import numpy as np, ml_dtypes
CORES = [16,17,18,19,32,33,34,35]
N = 8
BF = ml_dtypes.bfloat16
def gentries(a):
    return np.ascontiguousarray(a.reshape(8, 16, -1).transpose(0, 2, 1)).reshape(8, -1)
def gtable(e):
    e = np.asarray(e); return np.ascontiguousarray(e.reshape(8, -1, 16).transpose(0, 2, 1)).reshape(128, -1).astype(np.int32)
B, M, D, T = 512, 256, 2, 4
def laid(k):
    return np.array(np.transpose(k, (1, 2, 0, 3))).reshape(8, 16, N * B)
def look(K, L, cur):
    at = np.arange(N)[:, None] * B + D * np.arange(M)[None, :] + cur
    S, best, blk, C = [], [], [], []
    for q in range(N):
        own = K[:, :, at[q]]
        x = np.take_along_axis(K, L[q].reshape(8, 1, M * 16), 2).reshape(8, 16, M, 16)
        s = np.add.reduce(x * own[..., None], axis=1) - 8 * np.arange(16)
        kb = np.argmax(s, axis=2)
        b = np.take_along_axis(L[q], kb[..., None], 2)[..., 0]
        S.append(s); best.append(kb); blk.append(b)
        C.append(np.maximum(own, np.take_along_axis(K, b[:, None, :], 2)))
    return at, np.stack(S), np.stack(best), np.stack(blk), np.stack(C)
def settle(L, cur, fin, at, kb, b, tot, lim):
    who = b // B
    donor = L[who, np.arange(8)[None, :, None], (b % B) // D]
    take = (who != np.arange(N)[:, None, None]) & ~fin[b]
    L2 = np.where(take[..., None] & (np.arange(16) > kb[..., None]), donor, L)
    done = tot >= lim
    fin2 = np.array(fin); fin2[at[done]] = True
    cur2 = np.minimum(cur + done, D - 1)
    order = np.argsort(~fin2[L2], axis=-1, kind="stable")
    return np.take_along_axis(L2, order, -1), cur2, fin2
def tune(k, L, plan, slack):
    K = laid(k).astype(np.int64); cur = np.zeros((N, M), np.int64); fin = np.zeros(N * B, bool); th = np.zeros((N, T, M), np.int64)
    for t in range(T):
        at, s, kb, b, C = look(K, L, cur); tot = np.add.reduce(C, axis=(1, 2))
        th[:, t] = np.clip(np.where(plan[:, t], tot - slack[:, t], tot + 1 + slack[:, t]), 0, 1921)
        for q in range(N): K[:, :, at[q]] = C[q]
        L, cur, fin = settle(L, cur, fin, at, kb, b, tot, th[:, t])
    return th
def payload(rng):
    size = np.exp2(rng.integers(-2, 1, (1, 8, 16, 1)))
    return size * (0.5 + 1.5 * rng.random((N, 8, 16, B)))
def parts(rng):
    k = np.minimum(rng.integers(0, 16, (N, 8, 16, B)), rng.integers(0, 16, (N, 8, 16, B)))
    h = (N, 8, M, 16); e = np.minimum(rng.integers(0, D, h), rng.integers(0, D, h))
    return k, D * rng.integers(0, N * M, h) + e, payload(rng)
def pack(k, L, v, th):
    return {"k0": np.ascontiguousarray(k.reshape(N, 128, B)).astype(np.float32).astype(BF), "v0": np.ascontiguousarray(v.reshape(N, 128, B)).astype(np.float32).astype(BF),
            "vl": np.stack([gtable(a.reshape(8, -1)) for a in L]), "th": np.ascontiguousarray(th).astype(np.int32)}
def setup_inputs(rng):
    k, L, v = parts(rng)
    plan = rng.random((N, T, M)) < rng.choice(np.array([0.1, 0.3, 0.6, 0.9]), (N, 1, M))
    return pack(k, L, v, tune(k, L, plan, rng.integers(0, 40, (N, T, M))))
def setup_inputs_spread(rng):
    k, L, v = parts(rng)
    k = np.minimum(np.exp2(4.1 * rng.random((N, 8, 16, B)) * rng.random((N, 1, 1, B))).astype(np.int64) - 1, 15)
    pop = rng.permutation(N * B); h = (N, 8, M, 16)
    L = np.where(rng.random(h) < 0.6, pop[np.minimum(np.exp2(np.log2(N * B) * rng.random(h)).astype(np.int64) - 1, N * B - 1)], L)
    v = np.clip(v * np.exp2(rng.integers(-2, 3, (N, 1, 1, B))), 0.125, 8.0)
    v = np.where(rng.random((N, 1, 1, B)) > 0.0625, v, 0.125)
    return pack(k, L, v, rng.integers(0, 1922, (N, T, M)))
def setup_inputs_ends(rng):
    k, L, v = parts(rng); h = (N, 8, M, 16); W = N * B
    k = 15 * (rng.random((N, 8, 16, B)) < rng.choice(np.array([0.0, 0.1, 0.2, 0.4, 0.5, 0.6, 0.8, 0.9]), (N, 1, 1, B)))
    for q, c in ((0, 0), (N - 1, B - 1)):
        k[q, :, :, c] = 15 * rng.integers(0, 2, (8, 16)); k[q, 0, :, c] = 15; k[q, 7, :, c] = 15
    k[0, :, :, 2 * D] = 15; k[N - 1, :, :, D * (M - 1)] = 15; k[0, :, :, D] = 0; k[N - 1, :, :, D * (M - 2)] = 0
    L = np.where(rng.random(h) < 0.7, rng.choice(np.array([0, W - 1]), h), L)
    L[N - 1, :, M - 1] = W - 1; L[N - 1, :, M - 1, 15] = D; L[0, :, 2] = 0; L[0, :, 2, 15] = (N - 1) * B + D * (M - 2)
    th = np.where(rng.random((N, T, M)) < rng.choice(np.array([0.1, 0.8]), (N, 1, M)), 0, 1921)
    return pack(k, L, v, th)
def setup_inputs_corners(rng):
    k, L, v = parts(rng); W = N * B; w = np.arange(M); j = np.arange(16); a = rng.integers(0, 8, N); lad = np.zeros((N, 16), np.int64)
    for q in range(N):
        c = D * w[(w + a[q]) % 8 == 2][:16] + D - 1
        k[q][:, :, c] = 0; k[q][:, 3, c] = j; lad[q] = q * B + c
    for q in range(N):
        kd = (w + a[q]) % 8; o = (q + 1) % N
        z = w[kd == 1]; k[q][:, :, D * z] = 0; k[q][:, 3, D * z] = 8
        t = rng.integers(0, 8, (8, len(z), 1)); val = j + ((j >= t) & (j < 15)); src = np.where((z // 8) % 2 == 0, q, o)
        L[q][:, z] = lad[src[None, :, None], val]
        z = w[kd == 0]; L[q][:, z] = (q * B + D * z)[None, :, None]
        z = w[kd == 3]; L[q][:, z] = (o * B + D * z)[None, :, None] + j % D
        z = w[kd == 4]; L[q][:, z] = (((q + 1 + j) % N) * B)[None, None, :] + (D * z)[None, :, None]
        z = w[kd == 5]; L[q][:, z] = rng.choice(np.array([0, W - 1, q * B, q * B + B - 1]), (8, len(z), 16))
        z = w[kd == 6]; k[q][:, :, D * z] = 15
    pl = ((w // 8) % 4)[None, None, :]; t = np.arange(T)[None, :, None]
    plan = np.broadcast_to(((pl == 0) & (t < D)) | (pl == 1) | ((pl == 2) & (t == T - 1)) | ((pl == 3) & (t == 0)), (N, T, M))
    return pack(k, L, v, tune(k, L, plan, np.zeros((N, T, M), np.int64)))
def setup_inputs_crowd(rng):
    k, L, v = parts(rng); g = np.arange(8)[None, :]
    X = D * 2 * rng.integers(0, N * M // 2, (N, 8)); Y = D * (2 * rng.integers(0, N * M // 2, (N, 8)) + 1)
    X[:, ::2] = X[:1, ::2]; X[:, 5] = X[0, 5]
    v[X // B, np.broadcast_to(g, (N, 8)), :, X % B] = 8.0
    plan = rng.random((N, T, M)) < 0.4
    plan[(Y // B).reshape(-1), :, ((Y % B) // D).reshape(-1)] = False
    plan[X // B, np.broadcast_to(g // 4, (N, 8)), (X % B) // D] = True
    for i in range(8):
        if i % 4 < 2: L[:, i] = X[:, i, None, None]
        if i % 4 == 1: L[:, i, :, i] = Y[:, i, None]
        if i % 4 == 2:
            pool = np.stack([X[:, i], Y[:, i], np.zeros(N, np.int64), np.full(N, N * B - 1, np.int64)], 1)
            L[:, i] = np.take_along_axis(pool, rng.integers(0, 4, (N, M * 16)), 1).reshape(N, M, 16)
    return pack(k, L, v, tune(k, L, plan, rng.integers(0, 2, (N, T, M))))
def setup_inputs_calm(rng):
    k, L, v = parts(rng); k = rng.integers(0, 4, (N, 8, 16, B)); h = (N, 8, M, 16)
    stay = D * 4 * rng.integers(0, N * M // 4, h) + rng.integers(0, D, h)
    goes = D * (4 * rng.integers(0, N * M // 4, h) + rng.integers(1, 4, h))
    far = np.arange(16) >= 16 - (np.arange(8) % 4)[None, :, None, None]
    L = np.where(far, goes, stay)
    w = np.arange(M); base = np.arange(N)[:, None] * B
    for i in range(4):
        z = w[((w // 4) % 8 == 0) & ((w // 32) % 4 == i)]; hz = (N, 8, len(z), 16)
        c = (D * z[:, None] + np.arange(D)[None, :]).reshape(-1)
        k[:, :, :, c] = 0
        for j in range(i): k[:, 3 * j + 1, 15 - 5 * j, c] = rng.random((N, len(c))) < 0.7
        low = (base + D * z[z % 4 == 0][None, :]).reshape(-1); top = (base + D * z[z % 4 > 0][None, :]).reshape(-1)
        L[:, :, z] = np.where(far, rng.choice(top, hz), rng.choice(low, hz) + rng.integers(0, D, hz))
    plan = np.broadcast_to(np.arange(T)[None, :, None] < (np.arange(M) % 4)[None, None, :], (N, T, M))
    return pack(k, L, v, tune(k, L, plan, np.zeros((N, T, M), np.int64)))
def check_ranges(d):
    bad = []
    x = np.asarray(d["k0"]).astype(np.float32)
    if not (np.all(x >= 0) and np.all(x <= 15) and np.all(x == np.floor(x))): bad.append("range of k0")
    x = np.asarray(d["v0"]).astype(np.float32)
    if not (np.all(x >= 0.125) and np.all(x <= 8)): bad.append("range of v0")
    for i, lo, hi in (("vl", 0, N * B - 1), ("th", 0, 1921)):
        if np.min(d[i]) < lo or np.max(d[i]) > hi: bad.append("range of " + i)
    return bad
def reference(k0, v0, vl, th):
    K = laid(k0.astype(np.float64).reshape(N, 8, 16, B)).astype(np.int64); V = laid(v0.astype(np.float64).reshape(N, 8, 16, B))
    L = np.stack([gentries(a) for a in vl]).astype(np.int64).reshape(N, 8, M, 16)
    lim = th.astype(np.int64); cur = np.zeros((N, M), np.int64); fin = np.zeros(N * B, bool)
    for t in range(T):
        at, s, kb, b, C = look(K, L, cur)
        new = []
        for q in range(N):
            m = np.max(s[q], axis=2)[..., None]
            e = np.exp((s[q] - m) * 0.00390625)
            y = np.take_along_axis(V, L[q].reshape(8, 1, M * 16), 2).reshape(8, 16, M, 16)
            new.append(np.tanh(np.add.reduce(e[:, None] * y, axis=3) * 0.0625))
        for q in range(N):
            K[:, :, at[q]] = C[q]; V[:, :, at[q]] = new[q]
        L, cur, fin = settle(L, cur, fin, at, kb, b, np.add.reduce(C, axis=(1, 2)), lim[:, t])
    return {"yk": np.stack([K[:, :, q * B:(q + 1) * B].reshape(128, B) for q in range(N)]).astype(np.float32),
            "yv": np.stack([V[:, :, q * B:(q + 1) * B].reshape(128, B) for q in range(N)]).astype(np.float32),
            "yl": np.stack([gtable(a.reshape(8, -1)) for a in L]).astype(np.float32)}

def check_inputs(d):
    bad = list(check_ranges(d))
    if not bad:
        for name, y in reference(**d).items():
            for q in range(N):
                v = np.abs(np.asarray(y[q], np.float64)); s = np.sqrt(np.mean(v * v))
                if v.max() > 21 * s or s < 2.0 ** -3: bad.append('%s of rank %d is uneven or too small' % (name, q))
    return bad

@@ -1,0 +1,692 @@
+import numpy as np
+from concourse.bass import DstId, RemoteDMATransfer
+from concourse.mybir import AluOpType as OP, ActivationFunctionType as AF
+
+F, BF, HF, I, U = "float32", "bfloat16", "float16", "int32", "uint16"
+NS = 4
+SC = float(2 ** 18)
+C8 = 129.0 / 16
+EPS = 2.0 ** -18
+PE_NS, WAKE = 0.5, 80.0
+TRIES, KEPT = 6000, {}
+SHARE = (7,)
+SCRATCH = {}
+
+
+def _sb(dtype, **kw):
+    for n, c in kw.items():
+        SCRATCH[n] = ("sbuf", [128, c], dtype)
+
+
+_sb(BF, Tt=4096, P=4096, OX=4096, Kb=512, Vb=512, Ko1=256, G=256, Tc=512, sig=512, ownp=256, own1=256, fl=256, tt=256, gk=256, Kn=256,
+    RTs=128, rc0=128, rc1=128, rc2=128, rc3=128, BO=128, EB=144, SEL=1024, R16=128, LE=128, Am=128, LT=128, IDb=128, Bm=128, nU=128,
+    Mf=128, Mt=128, Mc=256, M128=128, I128=128, m8A=128, m8I=128, m8L=128, hI=128, nhI=128, nI=128, eI=128, bI=128, I2k=256,
+    Hs=256, ones=256, PMb=128, tmp=128)
+_sb(F, Vt=4096, E=4096, Y=4096, Vc=512, Vp=512, Ko=512, Lf=256, Lo=256, aS=256, Mx=256, us=256, d1=256, Bx=256, MR=32, MTs=128, yp=256,
+    yn=256, ga=256, gb=256, As=256, em=256, iot=256, ioq=128, iok=256, pc=16, mk=24, c8=8, c4=8, ID32=128, ISC=128, I16=128, PM32=128,
+    Hr=256, Hm=256, rm=256, qL=16, cL=16)
+_sb(HF, Lh=256, Lc=256, Z=128, Qs=512, R=4096, x16=256, thT=128, XK=2048, CB=240, SB=256, GB=248, GB63=248,
+    SB63=128, PMT=128, IDh=128, n63=128, Ht=1024)
+_sb(I, VT=2048, Li=256, Lp=256, thI=128, pi=8, si=128)
+_sb(U, lu=1280, wl=256, bl=16, dl=16, ol=16, cl0=16, cl1=16)
+PART = {}
+for _n in "Bm nU Mf Mt M128 I128 m8A m8I m8L hI nhI nI eI bI PMb Am LT LE".split():
+    PART[_n] = 128 * len(PART)
+    del SCRATCH[_n]
+_sb(BF, cmat=128 * len(PART))
+for _i in range(8):
+    SCRATCH["p%d" % _i] = ("psum", [128, 512], F)
+for _n, _c, _d in (("K", 64, BF), ("V", 64, BF), ("L", 32, I), ("k", 64, F), ("v", 64, F), ("l", 32, F)):
+    SCRATCH["S" + _n + "d"] = ("dram", [8, 128, _c], _d)
+    SCRATCH["R" + _n + "d"] = ("dram", [8, 128, _c], _d)
+SCRATCH["Std"] = ("dram", [128, 8], I)
+SCRATCH["Rtd"] = ("dram", [8, 128, 8], I)
+SEMAPHORES = ["pe", "v", "s", "g", "sent"] + ["d%d" % i for i in range(48)] + ["a%d" % i for i in range(12)]
+
+
+def spread(topo, src, dsts, per):
+    far = [d for d in dsts if topo.chip(d) != topo.chip(src)]
+    near = [d for d in dsts if topo.chip(d) == topo.chip(src)]
+    fe = topo.engines(src, far[0]) if far else []
+    ne = [e for e in topo.engines(src, near[0]) if e not in fe] if near else []
+    out = {}
+    for ds, es in ((far, fe), (near, ne)):
+        if ds:
+            n = 1
+            while 2 * n * per * len(ds) <= len(es):
+                n *= 2
+            for i, d in enumerate(ds):
+                out[d] = [(sum(1 << e for e in es[(i * per + j) * n:(i * per + j + 1) * n]), n) for j in range(per)]
+    return out
+
+
+def rank_program(g, core, T, topo):
+    r = T.rank_of(core)
+    if r is None:
+        return
+    cores = list(T.cores)
+    others = [c for c in cores if c != core]
+    QU = {"pe": g.tensor, "v": g.vector, "s": g.scalar, "g": g, "y": g.sync}
+    ops, acc, nd = [], {}, [0]
+
+    def A(n, a=0, b=None, st=1, p0=0, p1=128):
+        if n in PART:
+            n, a, b = "cmat", PART[n], PART[n] + 128
+        if b is None:
+            b = SCRATCH[n][1][1]
+        ap = T[n][p0:p1, a:b:st] if st > 1 else T[n][p0:p1, a:b]
+        return (ap, [(n, a, b, st)])
+
+    def IND(w, o):
+        return (w[0].indirect(o[0]), w[1] + o[1])
+
+    def D(n, i=None):
+        return (T[n][:], [(n, 0, 8, 1)]) if i is None else (T[n][i], [(n, i, i + 1, 1)])
+
+    def meet(x, y):
+        if x[2] <= y[1] or y[2] <= x[1]:
+            return False
+        return not (x[3] == y[3] > 1 and (x[1] - y[1]) % x[3])
+
+    def rec(q, fn, rd, wr, sem=None, n=0, cost=60.0, lat=0.0, after=()):
+        deps, order = set(), set(after)
+        me = len(ops)
+        for kind, regs in ((0, rd), (1, wr)):
+            for x in regs:
+                ps = SCRATCH.get(x[0], "x")[0] == "psum"
+                for y, k2, o in acc.get(x[0], []):
+                    oq = ops[o]["q"] if ops[o]["sem"] is None else None
+                    if q == "pe" and oq == "pe":
+                        if ps:
+                            order.add(o)
+                        continue
+                    if (ps and oq != q) or ((kind or k2) and meet(x, y)):
+                        deps.add(o)
+        for kind, regs in ((0, rd), (1, wr)):
+            for x in regs:
+                lst = acc.setdefault(x[0], [])
+                if kind:
+                    lst[:] = [e for e in lst if not (e[0][1] >= x[1] and e[0][2] <= x[2] and (x[3] == 1 or e[0] == x))]
+                lst.append((x, kind, me))
+        ops.append({"q": q, "fn": fn, "deps": deps, "order": order, "sem": sem, "n": n, "cost": cost, "lat": lat, "hold": max(0.0, lat - 2000),
+                    "tag": (q, wr[0][0] if wr else None, rd[0][0] if rd and q == "pe" else None)})
+
+    def wide(x):
+        n, a, b, st = x[1][-1]
+        return 16 * (b - a) if len(x[1]) > 1 else (b - a + st - 1) // st
+
+    def size(x):
+        return 4 if SCRATCH[x[1][0][0]][2] in (F, I) else 2
+
+    def price(o, a, per):
+        if len(a[1]) > 1:
+            return 55 + 1.5 * wide(a)
+        if len(o[1]) > 1:
+            return 55 + 3.5 * wide(o)
+        return 60 + per * wide(o)
+
+    def regs(*xs):
+        return [p for x in xs if isinstance(x, tuple) for p in x[1]]
+
+    def val(x):
+        return x[0] if isinstance(x, tuple) else x
+
+    def outs(o):
+        return o[1][:1], o[1][1:]
+
+    def ts(o, a, s1, op0, s2=None, op1=None):
+        c = price(o, a, 0.5 if size(o) == 2 == size(a) else 1)
+        if op1 is None:
+            rec("v", lambda: g.vector.tensor_scalar(o[0], a[0], val(s1), None, op0), regs(a, s1), o[1], cost=c)
+        else:
+            rec("v", lambda: g.vector.tensor_scalar(o[0], a[0], val(s1), val(s2), op0, op1), regs(a, s1, s2), o[1], cost=c)
+
+    def tt(o, a, b, op):
+        c = price(o, a, 1 if "psum" in (SCRATCH[a[1][0][0]][0], SCRATCH[b[1][0][0]][0]) else 2)
+        rec("v", lambda: g.vector.tensor_tensor(o[0], a[0], b[0], op), regs(a, b), o[1], cost=c)
+
+    def cp(o, a):
+        w, x = outs(o)
+        rec("v", lambda: g.vector.tensor_copy(o[0], a[0]), regs(a) + x, w, cost=price(o, a, 0.5 if size(o) == 2 == size(a) else 1))
+
+    def fill(o, c):
+        rec("v", lambda: g.vector.memset(o[0], c), [], o[1], cost=price(o, o, 0.5))
+
+    def scan(o, a, b, op0, op1):
+        rec("v", lambda: g.vector.tensor_tensor_scan(o[0], a[0], b[0], 0.0, op0, op1), regs(a, b), o[1], cost=price(o, a, 1))
+
+    def act(o, a, f=AF.Copy, bias=None, scale=None):
+        w, x = outs(o)
+        kw = {}
+        if bias is not None:
+            kw["bias"] = val(bias)
+        if scale is not None:
+            kw["scale"] = val(scale)
+        c, after = price(o, a, 1), []
+        if f in (AF.Exp, AF.Tanh):
+            if f != table[0]:
+                c, after = c + 1800, table[1]
+                table[:] = [f, []]
+            else:
+                after = table[1][:1]
+            table[1].append(len(ops))
+        rec("s", lambda: g.scalar.activation(o[0], a[0], f, **kw), regs(a, bias, scale) + x, w, cost=c, after=after)
+
+    table = [None, []]
+
+    def pe_price(lst):
+        return sum(max(min(64, wide(l)), wide(x)) * (4 if size(x) == 4 else 1) * PE_NS for o, l, x in lst)
+
+    def mm(lst, start=True, stop=True):
+        def fn():
+            for j, (o, l, x) in enumerate(lst):
+                h = g.tensor.matmul(o[0], l[0], x[0], start and j == 0, stop and j == len(lst) - 1)
+            return h
+        rec("pe", fn, [p for o, l, x in lst for p in l[1] + x[1]], [p for o, l, x in lst for p in o[1]], cost=pe_price(lst))
+
+    def mms(lst):
+        def fn():
+            for o, l, x in lst:
+                h = g.tensor.matmul(o[0], l[0], x[0], True, True)
+            return h
+        rec("pe", fn, [p for o, l, x in lst for p in l[1] + x[1]], [p for o, l, x in lst for p in o[1]], cost=pe_price(lst))
+
+    def iota(o, pat, cm=0, flt=True):
+        if flt:
+            rec("g", lambda: g.iota(o[0], pat, 0, cm, allow_small_or_imprecise_dtypes=True), [], o[1], cost=130 + 2 * wide(o))
+        else:
+            rec("g", lambda: g.iota(o[0], pat, 0, cm), [], o[1], cost=130 + 2 * wide(o))
+
+    def dma(q, pairs, lat=2500.0):
+        sem = "d%d" % nd[0]
+        nd[0] += 1
+
+        def fn():
+            for o, x in pairs:
+                QU[q].dma_start(o[0], x[0]).then_inc(T.sem[sem], 16)
+        rec(q, fn, [p for o, x in pairs for p in x[1]], [p for o, x in pairs for p in o[1]], sem, 16 * len(pairs), 60.0 * len(pairs), lat)
+
+    sent = [0]
+
+    def dst(c):
+        a = topo.addr(c)
+        return DstId(rid=a[0], pnc=a[1])
+
+    def send(sem, per, src, land):
+        mk = spread(topo, core, others, per)
+        trs = [RemoteDMATransfer(dst_ids=[dst(c)], dma_engine_mask=mk[c][j][0], remote_sem=T.sem[sem],
+                                 src=src(j, T.rank_of(c))[0], dst=land(j, r)[0]) for c in others for j in range(per)]
+        sent[0] += sum(n for c in others for m, n in mk[c])
+        rec("g", lambda: g.remote_dma_fused(trs, local_sem=T.sem.sent), regs(*[src(j, q) for j in range(per) for q in range(8) if q != r]), [], "-", 0, 300.0,
+            after=list(calls.values())[-1:] if len(calls) < 4 else [])
+        calls[sem] = len(ops) - 1
+
+    calls = {}
+
+    def arrive(sem, per, land, lat=5500.0):
+        n = sum(k for c in others for m, k in spread(topo, c, [x for x in cores if x != c], per)[core])
+        rec(None, None, [], regs(*[land(j, q) for j in range(per) for q in range(8) if q != r]), sem, n, 0.0, lat, [calls[sem]])
+
+    X = lambda n, a, b: (T[n][a:b, :], [])
+    col = lambda n, j, p1=128: A(n, j, j + 1, p1=p1)
+    PS = lambda i, a=0, b=512, st=1, p1=128: A("p%d" % i, a, b, st, p1=p1)
+
+    dma("y", [(D("SKd"), X("k0", 0, 128))])
+    dma("s", [(D("SLd"), X("vl", 0, 128))])
+    dma("y", [(D("SVd"), X("v0", 0, 128))])
+    dma("s", [(D("Std"), X("th", 0, 4))])
+    dma("y", [(D("RKd", r), X("k0", 16 * r, 16 * r + 16)), (D("RLd", r), X("vl", 16 * r, 16 * r + 16))])
+    dma("s", [(D("RVd", r), X("v0", 16 * r, 16 * r + 16)), (D("Rtd", r), X("th", 0, 4))])
+    iota(col("pi", 0), [[0, 1]], 1, False)
+    iota(A("iot"), [[1, 256]])
+    iota(A("iok"), [[0, 16], [1, 16]])
+    iota(A("ioq"), [[1, 8], [0, 16]])
+    send("a0", 1, lambda j, q: D("SKd", q), lambda j, q: D("RKd", q))
+    send("a10", 1, lambda j, q: D("SLd", q), lambda j, q: D("RLd", q))
+    send("a1", 1, lambda j, q: D("SVd", q), lambda j, q: D("RVd", q))
+    send("a2", 1, lambda j, q: D("Std"), lambda j, q: D("Rtd", q))
+    arrive("a0", 1, lambda j, q: D("RKd", q), 6000.0)
+    arrive("a10", 1, lambda j, q: D("RLd", q), 6000.0)
+    arrive("a1", 1, lambda j, q: D("RVd", q), 6000.0)
+    arrive("a2", 1, lambda j, q: D("Rtd", q), 3000.0)
+    dma("y", [(A("Kb"), D("RKd"))])
+    dma("y", [(A("Li"), D("RLd"))])
+    dma("y", [(A("Vb"), D("RVd"))])
+    dma("y", [(A("thI", p1=64), D("Rtd"))])
+
+    p_, q_, k_, kq_, e_, qk_, w_, yb_, nyb_ = [col("pc", j) for j in range(9)]
+    ts(col("pi", 1), col("pi", 0), 4, OP.arith_shift_right)
+    ts(col("pi", 2), col("pi", 0), 15, OP.bitwise_and)
+    ts(col("pi", 3), col("pi", 0), 3, OP.arith_shift_right)
+    ts(col("pi", 4), col("pi", 0), 7, OP.bitwise_and)
+    cp(A("pc", 0, 3), A("pi", 0, 3))
+    cp(A("pc", 9, 11), A("pi", 3, 5))
+    ts(kq_, k_, 8.0, OP.mult, q_, OP.add)
+    ts(e_, q_, 16.0, OP.mult, 15.0, OP.add)
+    ts(qk_, col("pc", 10), 16.0, OP.mult, col("pc", 9), OP.add)
+    ts(w_, q_, 256.0, OP.mult, k_, OP.add)
+    ts(yb_, k_, -15.5, OP.add, 16384.0, OP.mult)
+    ts(nyb_, k_, -15.5, OP.add, -16384.0, OP.mult)
+    ts(A("mk", 0, 16), A("iot", 0, 16), k_, OP.is_equal)
+    ts(A("mk", 16, 24), A("iot", 0, 8), q_, OP.is_equal)
+    ts(A("R16"), A("iok", 0, 128), k_, OP.is_equal)
+    ts(A("BO"), A("ioq"), q_, OP.is_equal)
+    for j in range(8):
+        act(A("SEL", 128 * j, 128 * j + 128), A("R16"), AF.Identity, scale=col("mk", 16 + j))
+    cp(A("wl"), A("iot"))
+    ts(A("EB"), A("iot", 0, 144), e_, OP.is_equal)
+    io128 = A("iot", 0, 128)
+    for n in ("SB", "PM32", "PMb"):
+        ts(A(n, 0, 128), io128, kq_, OP.is_equal)
+    fill(A("ones"), 1.0)
+    fill(A("sig"), 1.0)
+    ts(A("LE"), A("iok", 0, 128), k_, OP.is_ge)
+    for n, c in (("IDb", 1), ("IDh", 1), ("n63", -63)):
+        ts(A(n, 0, 128), io128, p_, OP.is_equal, float(c), OP.mult)
+    for n, c in (("ID32", 1), ("ISC", 1 / SC), ("I16", 1 / 16), ("Mt", -C8 * SC), ("I128", 128), ("m8I", -8), ("hI", .5),
+                 ("nhI", -.5), ("nI", -1), ("eI", EPS), ("bI", SC), ("I2k", 2048)):
+        act(A(n, 0, 128), A("IDb"), scale=float(c))
+    act(A("I2k", 128, 256), A("IDb"), scale=2048.0)
+    tt(A("LE"), A("LE"), A("BO"), OP.mult)
+    tt(A("Am"), A("BO"), A("LE"), OP.subtract)
+    tt(A("LT"), A("LE"), A("IDb"), OP.subtract)
+    act(A("nU"), A("LE"), scale=-1.0)
+    tt(A("Bm"), A("LE"), A("Am"), OP.subtract)
+    act(A("m8A"), A("Am"), scale=-8.0)
+    act(A("m8L"), A("LT"), scale=-8.0)
+
+    def mix(o, a, ca, ci):
+        ts(o, a, ca, OP.mult)
+        ts(A("tmp"), A("IDb"), ci, OP.mult)
+        tt(o, o, A("tmp"), OP.add)
+    mix(A("Mf"), A("Am"), -C8 * SC, SC / 32)
+    mix(A("Mc", 0, 128), A("LT"), -C8 * SC, 136 * SC)
+    cp(A("Mc", 128, 256), A("Mc", 0, 128))
+    ts(A("rm"), A("iok"), 0.0, OP.not_equal)
+    ts(A("CB"), A("iot", 0, 240), -112.0, OP.add, k_, OP.is_equal)
+    ts(A("c4", 0, 4), A("iot", 0, 4), -8.0, OP.mult, p_, OP.add)
+    ts(A("c4", 4, 6), A("iot", 0, 2), -8.0, OP.mult, k_, OP.add)
+    ts(A("cL"), A("iot", 0, 16), 16.0, OP.mult, k_, OP.add)
+    cp(A("qL", 0, 8), A("iot", 0, 8))
+    cp(A("qL", 8, 16), A("iot", 0, 8))
+    ts(A("cl0"), A("cL"), 2.0, OP.mult)
+    for h in range(2):
+        ts(A("Hr", 128 * h, 128 * h + 128), A("ioq"), col("c4", h), OP.is_equal, 16384.0, OP.mult)
+        ts(A("Hm", 128 * h, 128 * h + 128), A("ioq"), col("c4", 2 + h), OP.is_equal, -1.0, OP.mult)
+    ts(A("cL"), A("cL"), -64.0, OP.mult, -16.0, OP.add)
+    for k in range(16):
+        ts(A("XK", 128 * k, 128 * k + 128), A("BO"), col("mk", k), OP.mult)
+
+    def spread_T(share):
+        for q in range(8):
+            b = (0, 3, 5, 6)[q % 4]
+            mms([(PS(b), A("SEL", 128 * q, 128 * q + 128), A("Tc"))])
+            (cp if q in share else act)(A("Tt", 512 * q, 512 * q + 512), PS(b))
+
+    def spread_dma(tab, src, q="y"):
+        dma(q, [(A(tab, p0=16 * a, p1=16 * a + 16), A(src)) for a in range(8)], 4500.0 + 10 * wide(A(src)))
+
+    ts(A("Tc"), A("Kb"), 1.0, OP.add)
+    ts(A("ownp"), A("Kb", 0, 512, 2), EPS, OP.max)
+    spread_T((1, 3, 5, 6, 7))
+    ts(A("Ko1"), A("Kb", 1, 512, 2), 1.0, OP.add)
+    ts(A("own1"), A("Kb", 0, 512, 2), 1.0, OP.add)
+    cp(A("lu", 0, 256), A("Li"))
+    cp(A("Lf"), A("Li"))
+
+    def late_constants():
+        ts(A("c8"), A("iot", 0, 8), p_, OP.subtract, -0.125, OP.mult)
+        ts(A("ol"), A("iot", 0, 16), 16.0, OP.mult, w_, OP.add)
+        for h in range(2):
+            ts(A("Hs", 128 * h, 128 * h + 128), A("ioq"), col("c4", 4 + h), OP.is_equal, -64.0, OP.mult)
+        for j in range(8):
+            ts(A("Ht", 128 * j, 128 * j + 128), A("ioq"), col("c8", j), OP.is_equal, 64.0, OP.mult)
+        cp(A("SB", 128, 256), A("SB", 0, 128))
+        ts(A("SB63"), A("SB", 0, 128), 63.0, OP.mult)
+        ts(A("PMT"), io128, qk_, OP.is_equal)
+        tt(A("GB"), A("SB", 0, 248), A("SB", 8, 256), OP.subtract)
+        mix(A("M128"), A("Am"), 128.0, 2048.0)
+        ts(A("GB63"), A("GB"), 63.0, OP.mult)
+
+    def contract(c):
+        mm([(PS(0, 64 * c, 64 * c + 64), A("EB", 15 - k, 143 - k), A("P", 1024 * c + k, 1024 * c + 1024, 16)) for k in range(16)])
+
+    def pieces():
+        ts(A("Lc"), A("Lf"), -2048.0, OP.add)
+        ts(A("Lh"), A("Lf"), 1.0 / 64, OP.mult, 1025 - 31.5 / 64, OP.add)
+
+    def marks():
+        mm([(PS(1, 0, 256), A("nU"), A("ones"))], True, False)
+        ts(A("fl"), PS(0, 0, 256), 0.0, OP.is_lt)
+        mm([(PS(1, 0, 256), A("Bm"), A("fl"))], False, True)
+        tt(A("tt"), A("fl"), PS(1, 0, 256), OP.mult)
+
+    def sort_keys():
+        lin = [(A("M128"), A("fl")), (A("I128"), A("tt"))]
+        mm([(PS(3, 0, 256), l, x) for l, x in [(A("IDh"), A("Lh"))] + lin])
+        mm([(PS(3, 256, 512), l, x) for l, x in [(A("IDh"), A("Lc")), (A("n63"), A("Lh"))] + lin])
+
+    def sort_evac():
+        ts(A("Qs", 0, 256), PS(3, 0, 256), -2113.0, OP.add)
+        ts(A("Qs", 256, 512), PS(3, 256, 512), 65535.0, OP.add)
+
+    def moves(d0, d1):
+        o = PS(3, 0, 256)
+        for d in range(d0, d1):
+            if d == 0:
+                mm([(o, A("SB63"), A("Qs", 0, 256)), (o, A("SB", 0, 128), A("Qs", 256, 512))], True, False)
+                continue
+            a = 512 * (d % 8)
+            ts(A("R", a, a + 512), A("Qs"), 128.0 * d - 1088, OP.max)
+            mm([(o, A("GB63", 128 - 8 * d, 256 - 8 * d), A("R", a, a + 256)), (o, A("GB", 128 - 8 * d, 256 - 8 * d), A("R", a + 256, a + 512))], False, d == 16)
+
+    def sort_end():
+        ts(A("Li"), PS(3, 0, 256), 69632.0, OP.add)
+        ts(A("Lp"), A("Li"), 4095, OP.bitwise_and)
+
+    def weights(k0, k1):
+        for k in range(k0, k1, 2):
+            b = 5 + (k // 2) % 2
+            mms([(PS(b, 256 * j, 256 * j + 256), A("XK", 128 * (k + j), 128 * (k + j + 1)), A("x16")) for j in range(2)])
+            for j in range(2):
+                act(A("E", k + j, 4096, 16), PS(b, 256 * j, 256 * j + 256), AF.Exp, scale=1.0 / 256)
+
+    def new_V(t):
+        act(IND(A("Vc"), A("cl%d" % (t % 2))), A("As"), AF.Tanh)
+
+    def hand_back(sem, n, src, y):
+        s, d = "S" + n + "d", "R" + n + "d"
+        dma("y", [(D(s), A(src))])
+        dma("y", [(D(d, r), A(src, p0=16 * r, p1=16 * r + 16))])
+        send(sem, 1, lambda j, q: D(s, q), lambda j, q: D(d, q))
+        arrive(sem, 1, lambda j, q: D(d, q), 2500.0 + 128 * SCRATCH[d][1][2])
+        return lambda: dma("y", [((T[y][:, :], []), D(d))])
+
+    si = lambda j: A("si", 16 * j, 16 * j + 16)
+    for t in range(NS):
+        for c in range(4):
+            s = (1024 * c, 1024 * c + 1024)
+            act(A("OX", *s), IND(A("ownp"), A("wl", 64 * c, 64 * c + 64)))
+            tt(A("P", *s), IND(A("Tt"), A("lu", 256 * t + 64 * c, 256 * t + 64 * c + 64)), A("OX", *s), OP.mult)
+            if c == 0 and t > 0:
+                tt(A("As"), A("em"), PS(4, 256, 512), OP.mult)
+            if c == 3 and t > 0:
+                act(A("own1"), A("ownp"), AF.Identity, bias=1.0)
+                act(A("Ko1"), PS(2, 0, 256))
+                new_V(t - 1)
+                mms([(PS(5), A("PM32"), A("Vc"))])
+                act(A("Vp"), PS(5))
+                spread_dma("Vt", "Vp")
+            if c == 3 and t == 0:
+                act(A("Vc"), A("Vb"))
+                mms([(PS(5), A("PMb"), A("Vb"))])
+                act(A("Vp"), PS(5))
+                spread_dma("Vt", "Vp")
+            contract(c)
+        pieces()
+        mm([(PS(2, 256, 512), A("ones", 0, 128), A("I2k"))] +
+           [(PS(2, 256 + 128 * h, 384 + 128 * h), A("Lc", 128 * h, 128 * h + 128), A("IDh")) for h in range(2)])
+        mm([(PS(2, 0, 256), A("ones", 0, 128), A("Mc"))], True, False)
+        marks()
+        act(A("aS"), PS(0, 0, 256), AF.Abs, scale=SC)
+        hs = [(PS(2, 128 * h, 128 * h + 128), 128 * h) for h in range(2)]
+        mm([(o, A("fl", a, a + 128), A("Mf")) for o, a in hs], False, False)
+        mm([(o, A("aS", a, a + 128), A("ID32")) for o, a in hs], False, False)
+        mm([(o, A("tt", a, a + 128), A("Mt")) for o, a in hs], False, True)
+        xl = PS(4, 0, 256)
+        mm([(xl, A("m8L"), A("ones")), (xl, A("m8A"), A("fl")), (xl, A("m8I"), A("tt")), (xl, A("ISC"), A("aS"))])
+        if t > 0:
+            sort_keys()
+        else:
+            mms([(PS(3, 0, 256), A("SB", 0, 128), A("Lc"))])
+        mv = moves if t > 0 else lambda a, b: None
+        scan(A("Mx"), A("rm"), PS(2, 0, 256), OP.mult, OP.max)
+        ts(A("x16"), xl, -1860.0, OP.add)
+        weights(0, 4)
+        tt(A("us"), A("Mx"), PS(2, 0, 256), OP.subtract)
+        tt(A("d1"), PS(2, 256, 512), A("us"), OP.subtract)
+        scan(A("Bx"), A("us"), A("d1"), OP.min, OP.max)
+        bs = A("Bx", 15, 256, 16)
+        for a in range(8):
+            ts(A("Z", a, 128, 8), bs, -2048.0, OP.add, col("mk", 16 + a), OP.mult)
+        for h in range(2):
+            mm([(PS(1, 256 + 8 * h, 264 + 8 * h), A("CB", 112 - 16 * q, 240 - 16 * q), A("Z", 64 * h + 8 * q, 64 * h + 8 * q + 8)) for q in range(8)])
+        ts(si(0), A("Mx", 15, 256, 16), 32 / SC, OP.mult, 30.0, OP.add)
+        ts(si(4), bs, 1.0 / 512, OP.mult, -255.5 / 512, OP.add)
+        if t > 0:
+            sort_evac()
+        else:
+            ts(A("Lp"), PS(3, 0, 256), 2048.0, OP.add)
+            spread_dma("VT", "Lp")
+        ts(A("bl"), PS(1, 256, 272), 2048.0, OP.add)
+        act(A("gk"), IND(A("Tt"), A("bl")), AF.Abs)
+        ts(si(1), si(0), 31, OP.bitwise_and, 1, OP.logical_shift_right)
+        ts(si(2), si(0), 1, OP.bitwise_and)
+        ts(si(3), si(0), 5, OP.arith_shift_right)
+        mv(0, 3)
+        tt(A("Kn"), A("gk"), A("own1"), OP.max)
+        mms([(PS(1, 272 + 8 * h, 280 + 8 * h), A("Kn", 128 * h, 128 * h + 128), A("BO", 0, 128, 16)) for h in range(2)])
+        rc = "rc%d" % t
+        act(A(rc, 16 * r, 16 * r + 16), PS(1, 272, 288))
+        if t == 0:
+            late_constants()
+        send("a%d" % (3 + t), 1, lambda j, q, rc=rc: A(rc, 16 * r, 16 * r + 16), lambda j, q, rc=rc: A(rc, 16 * q, 16 * q + 16))
+        arrive("a%d" % (3 + t), 1, lambda j, q, rc=rc: A(rc, 16 * q, 16 * q + 16))
+        tt(si(5), si(4), A("qL"), OP.not_equal)
+        cp(A("MR", 16, 32), si(3))
+        tt(si(6), si(5), si(2), OP.is_gt)
+        ts(si(7), PS(1, 256, 272), 0.5, OP.mult, 1023.75, OP.add)
+        tt(A("MR", 0, 16), si(6), si(1), OP.mult)
+        cp(A("dl"), si(7))
+        weights(4, 6)
+        mms([(PS(1, 288, 416, p1=32), A("MR"), A("ID32"))])
+        weights(6, 8)
+        mv(3, 5)
+        act(A("MTs", p1=32), PS(1, 288, 416, p1=32))
+        mms([(PS(0, 128 * j, 128 * j + 128), A(("Hm", "Hr")[j // 2], 128 * (j % 2), 128 * (j % 2) + 128, p1=32), A("MTs", p1=32)) for j in range(4)])
+        half = [(A("hI"), A("Kn")), (A("hI"), A("Ko1"))]
+        mm([(PS(2, 0, 256), A("hI"), A("Kn")), (PS(2, 0, 256), A("nhI"), A("Ko1"))])
+        weights(8, 10)
+        mv(5, 7)
+        tt(A("G"), A("sig", 0, 256), PS(2, 0, 256), OP.mult)
+        mv(7, 9)
+        act(A("em"), PS(0, 0, 256), AF.Exp, bias=1996.0 / 256, scale=1.0 / 256)
+        weights(10, 12)
+        mm([(PS(2, 0, 256), l, x) for l, x in half + [(A("IDb"), A("G"))]])
+        mm([(PS(2, 256, 512), l, x) for l, x in half + [(A("nI"), A("G"))]])
+        mv(9, 11)
+        weights(12, 14)
+        mms([(PS(1, 0, 256), A("IDb"), A("G"))])
+        mm([(PS(1, 256, 512), l, x) for l, x in half + [(A("nI"), A("ones")), (A("eI"), A("ones"))]])
+        mv(11, 13)
+        weights(14, 16)
+        if t == 0:
+            cp(A("thT", p1=64), A("thI", p1=64))
+        mm([(PS(7), A("bI"), A("sig")), (PS(7, 256, 512), A("bI"), A("sig", 0, 256))] +
+           [(PS(7, 256 * e + 128 * h, 256 * e + 128 * h + 128), A("Ht", 128 * (2 * t + h), 128 * (2 * t + h + 1), p1=64), A("thT", p1=64))
+            for e in range(2) for h in range(2)], True, False)
+        act(A("yp"), PS(0, 256, 512), AF.Identity, bias=yb_)
+        act(A("yn"), PS(0, 256, 512), AF.Identity, bias=nyb_, scale=-1.0)
+        if t == NS - 1:
+            for e in range(2):
+                act(A("Ko", e, 512, 2), PS(2, 256 * e, 256 * e + 256), AF.Identity, bias=-1.0)
+            last_k = hand_back("a7", "k", "Ko", "yk")
+        mv(13, 17)
+
+        def values(c):
+            for j in (2 * c, 2 * c + 1):
+                s = (512 * j, 512 * j + 512)
+                tt(A("Y", *s), IND(A("Vt"), A("lu", 256 * t + 32 * j, 256 * t + 32 * j + 32)), A("E", *s), OP.mult)
+
+        def sums(c):
+            mm([(PS(4, 256 + 64 * c, 320 + 64 * c), A("I16"), A("Y", 1024 * c + k, 1024 * c + 1024, 16)) for k in range(16)])
+        mms([(PS(0, 0, 128), A(rc), A("IDb"))])
+        if t == 0:
+            values(0)
+        cp(A("RTs"), PS(0, 0, 128))
+        mm([(PS(7, 256 * e + 128 * h, 256 * e + 128 * h + 128), A("Hs", 128 * h, 128 * h + 128), A("RTs")) for e in range(2) for h in range(2)], False, True)
+        if t > 0:
+            sort_end()
+            spread_dma("VT", "Lp")
+        act(A("sig", 0, 256), PS(7, 0, 256), AF.Sign, bias=8160.0 - SC)
+        act(A("sig", 256, 512), PS(7, 256, 512), AF.Sign, bias=8160.0)
+        tt(A("Tc", 0, 512, 2), A("sig", 0, 256), PS(2, 0, 256), OP.mult)
+        tt(A("Tc", 1, 512, 2), A("sig", 256, 512), PS(2, 256, 512), OP.mult)
+        if t < NS - 1:
+            tt(A("gk"), A("sig", 0, 256), PS(1, 0, 256), OP.mult)
+            tt(A("ownp"), A("gk"), PS(1, 256, 512), OP.add)
+        if t > 0:
+            values(0)
+        spread_T(SHARE)
+        if t < NS - 1:
+            mm([(PS(7, 0, 16), A("ID32"), A("cL"))] + [(PS(7, 0, 16), A("EB", 15 - b, 143 - b), A("sig", b, 256, 16)) for b in range(16)])
+            mm([(PS(2, 0, 256), l, x) for l, x in half + [(A("nI"), A("gk"))]])
+        else:
+            last_k()
+        sums(0)
+        for c in range(1, 4):
+            values(c)
+            sums(c)
+        if t < NS - 1:
+            ts(A("cl%d" % ((t + 1) % 2)), PS(7, 0, 16), -1.0 / 32, OP.mult)
+        tt(A("ga"), IND(A("VT"), A("dl")), A("yp"), OP.min)
+        tt(A("gb"), IND(A("VT"), A("ol")), A("yn"), OP.min)
+        tt(A("Lf"), A("ga"), A("gb"), OP.max)
+        cp(A("lu", 256 * t + 256, 256 * t + 512), A("Lf"))
+
+    for c in (0, 2, 1, 3):
+        (cp if c < 2 else act)(A("P", 1024 * c, 1024 * c + 1024), IND(A("Tt"), A("lu", 256 * NS + 64 * c, 256 * NS + 64 * c + 64)))
+        contract(c)
+    tt(A("As"), A("em"), PS(4, 256, 512), OP.mult)
+    pieces()
+    new_V(NS - 1)
+    last_v = hand_back("a8", "v", "Vc", "yv")
+    marks()
+    sort_keys()
+    sort_evac()
+    moves(0, 17)
+    sort_end()
+    ts(A("Lc"), A("Lp"), -2048.0, OP.add)
+    mms([(PS(0, 0, 256), A("PMT"), A("Lc"))])
+    ts(A("Lo"), PS(0, 0, 256), 2048.0, OP.add)
+    last_l = hand_back("a9", "l", "Lo", "yl")
+    last_v()
+    last_l()
+    emit(g, T, QU, ops, sent[0])
+
+
+def arrange(ops):
+    n = len(ops)
+    rank = [0.0] * n
+    for i in range(n - 1, -1, -1):
+        o = ops[i]
+        rank[i] += o["cost"] + o["lat"]
+        for d in o["deps"] | o["order"]:
+            rank[d] = max(rank[d], rank[i] + WAKE)
+    deps = [sorted(o["deps"]) for o in ops]
+    order = [sorted(o["order"]) for o in ops]
+    cost = [o["cost"] for o in ops]
+
+    def lay(prio):
+        taken, at, end = {q: ([], []) for q in ("pe", "v", "s", "g", "y", "port", "dma")}, [0.0] * n, [0.0] * n
+        for i in sorted(range(n), key=lambda j: (-prio[j], j)):
+            t, c = 0.0, cost[i]
+            for d in deps[i]:
+                t = max(t, end[d] + WAKE)
+            for d in order[i]:
+                t = max(t, at[d] + cost[d])
+            if ops[i]["q"] is not None:
+                st, en = taken[ops[i]["q"]]
+                j = len(st)
+                while j > 0 and en[j - 1] > t:
+                    j -= 1
+                while j < len(st) and t + c > st[j]:
+                    t = max(t, en[j])
+                    j += 1
+                st.insert(j, t)
+                en.insert(j, t + c)
+            at[i], end[i] = t, t + c + ops[i]["lat"]
+            if ops[i]["hold"]:
+                st, en = taken["port" if ops[i]["q"] is None else "dma"]
+                t, c, j = t + c + 1400, ops[i]["hold"], len(st)
+                while j > 0 and en[j - 1] > t:
+                    j -= 1
+                while j < len(st) and t + c > st[j]:
+                    t = max(t, en[j])
+                    j += 1
+                st.insert(j, t)
+                en.insert(j, t + c)
+                end[i] = t + c + 600
+        return max(end), at, end
+
+    def mend(prio):
+        for i in range(n - 1, -1, -1):
+            for d in deps[i] + order[i]:
+                prio[d] = max(prio[d], prio[i] + 1e-3)
+        return prio
+
+    if n not in KEPT:
+        rng = np.random.default_rng(0)
+        best, at, end = lay(rank)
+        prio = [-x for x in at]
+        for it in range(TRIES):
+            p = list(prio)
+            for i in rng.integers(0, n, 3):
+                x, reach = float(rng.normal()) * 3000, int(rng.integers(0, 3)) * 30
+                for j in range(max(0, i - reach), min(n, i + reach + 1)):
+                    if ops[j]["tag"] == ops[i]["tag"]:
+                        p[j] += x
+            span, at2, end2 = lay(mend(p))
+            span += 1e-4 * sum(end2) / n
+            if span <= best:
+                best, at, prio = span, at2, [-x for x in at2]
+        KEPT[n] = sorted(range(n), key=lambda j: (at[j], j))
+    seq = KEPT[n]
+    place = {j: k for k, j in enumerate(seq)}
+    for j, o in enumerate(ops):
+        assert all(place[d] < place[j] for d in o["deps"] | o["order"])
+        o["deps"] = {place[d] for d in o["deps"]}
+    return [ops[j] for j in seq]
+
+
+def emit(g, T, QU, ops, sent):
+    ops = arrange(ops)
+    clock = {q: {} for q in QU}
+    marked = set()
+    for i, o in enumerate(ops):
+        o["waits"], o["snap"] = [], {}
+        if o["q"] is None:
+            continue
+        ck = clock[o["q"]]
+        for d in sorted(o["deps"], reverse=True):
+            key = ops[d]["sem"] or ops[d]["q"]
+            if ck.get(key, -1) >= d:
+                continue
+            o["waits"].append(d)
+            marked.add(d)
+            for k2, v2 in ops[d]["snap"].items():
+                ck[k2] = max(ck.get(k2, -1), v2)
+            ck[key] = d
+        o["snap"] = dict(ck)
+    last = {}
+    for i, o in enumerate(ops):
+        if o["sem"] is None:
+            last[o["q"]] = i
+    marked |= set(last.values())
+    count, done = {}, {}
+    for i, o in enumerate(ops):
+        for d in o["waits"]:
+            s = ops[d]["sem"] or ops[d]["q"]
+            QU[o["q"]].wait_ge(T.sem[s], ops[d]["n"])
+            done[s] = max(done.get(s, 0), ops[d]["n"])
+        h = o["fn"]() if o["fn"] else None
+        if o["sem"] is None:
+            if i in marked:
+                count[o["q"]] = o["n"] = count.get(o["q"], 0) + 1
+                h.then_inc(T.sem[o["q"]], 1)
+        elif o["sem"] != "-":
+            count[o["sem"]] = o["n"]
+    count["sent"] = sent
+    for s, n in count.items():
+        if done.get(s, 0) < n:
+            g.wait_ge(T.sem[s], n)

@@ -9,7 +9,8 @@ C8 = 129.0 / 16
 EPS = 2.0 ** -18
 PE_NS, WAKE = 0.5, 80.0
 TRIES, KEPT = 6000, {}
-SHARE = (7,)
+SHARE = (3,)
+S_MOVES = (3, 6, 9, 12, 15)
 SCRATCH = {}
 
 
@@ -18,29 +19,26 @@ def _sb(dtype, **kw):
         SCRATCH[n] = ("sbuf", [128, c], dtype)
 
 
-_sb(BF, Tt=4096, P=4096, OX=4096, Kb=512, Vb=512, Ko1=256, G=256, Tc=512, sig=512, ownp=256, own1=256, fl=256, tt=256, gk=256, Kn=256,
-    RTs=128, rc0=128, rc1=128, rc2=128, rc3=128, BO=128, EB=144, SEL=1024, R16=128, LE=128, Am=128, LT=128, IDb=128, Bm=128, nU=128,
-    Mf=128, Mt=128, Mc=256, M128=128, I128=128, m8A=128, m8I=128, m8L=128, hI=128, nhI=128, nI=128, eI=128, bI=128, I2k=256,
-    Hs=256, ones=256, PMb=128, tmp=128)
-_sb(F, Vt=4096, E=4096, Y=4096, Vc=512, Vp=512, Ko=512, Lf=256, Lo=256, aS=256, Mx=256, us=256, d1=256, Bx=256, MR=32, MTs=128, yp=256,
-    yn=256, ga=256, gb=256, As=256, em=256, iot=256, ioq=128, iok=256, pc=16, mk=24, c8=8, c4=8, ID32=128, ISC=128, I16=128, PM32=128,
-    Hr=256, Hm=256, rm=256, qL=16, cL=16)
-_sb(HF, Lh=256, Lc=256, Z=128, Qs=512, R=4096, x16=256, thT=128, XK=2048, CB=240, SB=256, GB=248, GB63=248,
-    SB63=128, PMT=128, IDh=128, n63=128, Ht=1024)
-_sb(I, VT=2048, Li=256, Lp=256, thI=128, pi=8, si=128)
-_sb(U, lu=1280, wl=256, bl=16, dl=16, ol=16, cl0=16, cl1=16)
+_sb(BF, Tt=4096, P=4096, Kb=512, Vb=512, KK=1536, Tc=512, own=512, fl=256, tt=256, BO=128, EB=144, SEL=1024, R16=128, IDb=128,
+    Mf=128, Mc=256, I2k=256, ones=256, tmp=128, IEb=272, Cs=512)
+_sb(F, Vt=4096, E=4096, Y=4096, Vc=512, Vp=512, Ko=512, Lo=256, aS=256, Mx=256, us=256, d1=256, Bx=256, ypn=512, ga=512, As=256,
+    iot=272, ioq=128, iok=256, ioj=256, pc=24, mk=24, ID32=128, ISC=128, I16=128, PM32=128, rm=256, qL=16, wL=16, olf=16, nb=16)
+_sb(HF, LcA=256, Lh=256, Lt=256, Qs=512, R=4096, x16=256, XK=2048, PM=128, IDh=128, nIh=128, n64=128, n8k=128, I256=128, n512=128,
+    IEh=272, Hs=256, Wt=64, thZ=128, cL=80, sg=32, MR=16, r16=16, MTs=128, rc0=128, rc1=128, rc2=128, rc3=128)
+_sb(I, VT=2048, Li=256, Lp=256, thI=16, pi=8, si=128)
+_sb(U, lu=1280, bl=16, dl=32, cl=320)
+SCRATCH["LcB"] = ("sbuf", [128, 16, 16], HF)
+_sb(BF, gkB=256)
 PART = {}
-for _n in "Bm nU Mf Mt M128 I128 m8A m8I m8L hI nhI nI eI bI PMb Am LT LE".split():
+for _n in "Bm nU Mt M64 I64 m8A m8I m8L PMb Am LT LE".split():
     PART[_n] = 128 * len(PART)
-    del SCRATCH[_n]
 _sb(BF, cmat=128 * len(PART))
 for _i in range(8):
-    SCRATCH["p%d" % _i] = ("psum", [128, 512], F)
+    SCRATCH["p%d" % _i] = ("psum", [128, 32, 16], F)
+SCRATCH["p1"] = ("psum", [128, 512], F)
 for _n, _c, _d in (("K", 64, BF), ("V", 64, BF), ("L", 32, I), ("k", 64, F), ("v", 64, F), ("l", 32, F)):
     SCRATCH["S" + _n + "d"] = ("dram", [8, 128, _c], _d)
     SCRATCH["R" + _n + "d"] = ("dram", [8, 128, _c], _d)
-SCRATCH["Std"] = ("dram", [128, 8], I)
-SCRATCH["Rtd"] = ("dram", [8, 128, 8], I)
 SEMAPHORES = ["pe", "v", "s", "g", "sent"] + ["d%d" % i for i in range(48)] + ["a%d" % i for i in range(12)]
 
 
@@ -60,6 +58,10 @@ def spread(topo, src, dsts, per):
     return out
 
 
+def bits(cols):
+    return sum(1 << c for c in cols)
+
+
 def rank_program(g, core, T, topo):
     r = T.rank_of(core)
     if r is None:
@@ -69,24 +71,29 @@ def rank_program(g, core, T, topo):
     QU = {"pe": g.tensor, "v": g.vector, "s": g.scalar, "g": g, "y": g.sync}
     ops, acc, nd = [], {}, [0]
 
+    def B(n, r0, r1, rs=1, c0=0, c1=16, cs=1, p0=0, p1=128):
+        cols = [16 * i + j for i in range(r0, r1, rs) for j in range(c0, c1, cs)]
+        rows = r0 if r1 - r0 <= rs else slice(r0, r1, rs)
+        return (T[n][p0:p1, rows, c0 if len(cols) > 1 and c1 - c0 <= cs else slice(c0, c1, cs)], [(n, bits(cols), len(cols))])
+
     def A(n, a=0, b=None, st=1, p0=0, p1=128):
         if n in PART:
             n, a, b = "cmat", PART[n], PART[n] + 128
+        shape = SCRATCH[n][1]
         if b is None:
-            b = SCRATCH[n][1][1]
+            b = int(np.prod(shape[1:]))
+        if len(shape) == 3:
+            if st >= 16:
+                return B(n, a // 16, (b + 15) // 16, st // 16, a % 16, a % 16 + 1, 1, p0, p1)
+            return B(n, a // 16, b // 16, 1, a % 16, 16, st, p0, p1)
         ap = T[n][p0:p1, a:b:st] if st > 1 else T[n][p0:p1, a:b]
-        return (ap, [(n, a, b, st)])
+        return (ap, [(n, bits(range(a, b, st)) if st > 1 else (1 << b) - (1 << a), len(range(a, b, st)))])
 
     def IND(w, o):
         return (w[0].indirect(o[0]), w[1] + o[1])
 
     def D(n, i=None):
-        return (T[n][:], [(n, 0, 8, 1)]) if i is None else (T[n][i], [(n, i, i + 1, 1)])
-
-    def meet(x, y):
-        if x[2] <= y[1] or y[2] <= x[1]:
-            return False
-        return not (x[3] == y[3] > 1 and (x[1] - y[1]) % x[3])
+        return (T[n][:], [(n, 255, 8)]) if i is None else (T[n][i], [(n, 1 << i, 1)])
 
     def rec(q, fn, rd, wr, sem=None, n=0, cost=60.0, lat=0.0, after=()):
         deps, order = set(), set(after)
@@ -100,20 +107,19 @@ def rank_program(g, core, T, topo):
                         if ps:
                             order.add(o)
                         continue
-                    if (ps and oq != q) or ((kind or k2) and meet(x, y)):
+                    if (ps and oq != q) or ((kind or k2) and x[1] & y[1]):
                         deps.add(o)
         for kind, regs in ((0, rd), (1, wr)):
             for x in regs:
                 lst = acc.setdefault(x[0], [])
                 if kind:
-                    lst[:] = [e for e in lst if not (e[0][1] >= x[1] and e[0][2] <= x[2] and (x[3] == 1 or e[0] == x))]
+                    lst[:] = [e for e in lst if e[0][1] & ~x[1]]
                 lst.append((x, kind, me))
         ops.append({"q": q, "fn": fn, "deps": deps, "order": order, "sem": sem, "n": n, "cost": cost, "lat": lat, "hold": max(0.0, lat - 2000),
                     "tag": (q, wr[0][0] if wr else None, rd[0][0] if rd and q == "pe" else None)})
 
     def wide(x):
-        n, a, b, st = x[1][-1]
-        return 16 * (b - a) if len(x[1]) > 1 else (b - a + st - 1) // st
+        return 16 * x[1][-1][2] if len(x[1]) > 1 else x[1][0][2]
 
     def size(x):
         return 4 if SCRATCH[x[1][0][0]][2] in (F, I) else 2
@@ -177,19 +183,18 @@ def rank_program(g, core, T, topo):
     def pe_price(lst):
         return sum(max(min(64, wide(l)), wide(x)) * (4 if size(x) == 4 else 1) * PE_NS for o, l, x in lst)
 
-    def mm(lst, start=True, stop=True):
+    def mm(lst, start=True, stop=True, each=0):
         def fn():
             for j, (o, l, x) in enumerate(lst):
-                h = g.tensor.matmul(o[0], l[0], x[0], start and j == 0, stop and j == len(lst) - 1)
+                if each:
+                    h = g.tensor.matmul(o[0], l[0], x[0], j % each == 0, j % each == each - 1)
+                else:
+                    h = g.tensor.matmul(o[0], l[0], x[0], start and j == 0, stop and j == len(lst) - 1)
             return h
         rec("pe", fn, [p for o, l, x in lst for p in l[1] + x[1]], [p for o, l, x in lst for p in o[1]], cost=pe_price(lst))
 
     def mms(lst):
-        def fn():
-            for o, l, x in lst:
-                h = g.tensor.matmul(o[0], l[0], x[0], True, True)
-            return h
-        rec("pe", fn, [p for o, l, x in lst for p in l[1] + x[1]], [p for o, l, x in lst for p in o[1]], cost=pe_price(lst))
+        mm(lst, each=1)
 
     def iota(o, pat, cm=0, flt=True):
         if flt:
@@ -218,7 +223,7 @@ def rank_program(g, core, T, topo):
                                  src=src(j, T.rank_of(c))[0], dst=land(j, r)[0]) for c in others for j in range(per)]
         sent[0] += sum(n for c in others for m, n in mk[c])
         rec("g", lambda: g.remote_dma_fused(trs, local_sem=T.sem.sent), regs(*[src(j, q) for j in range(per) for q in range(8) if q != r]), [], "-", 0, 300.0,
-            after=list(calls.values())[-1:] if len(calls) < 4 else [])
+            after=list(calls.values())[-1:] if len(calls) < 3 else [])
         calls[sem] = len(ops) - 1
 
     calls = {}
@@ -234,57 +239,55 @@ def rank_program(g, core, T, topo):
     dma("y", [(D("SKd"), X("k0", 0, 128))])
     dma("s", [(D("SLd"), X("vl", 0, 128))])
     dma("y", [(D("SVd"), X("v0", 0, 128))])
-    dma("s", [(D("Std"), X("th", 0, 4))])
+    dma("s", [(A("thI", p1=64), X("th", 0, 4))])
     dma("y", [(D("RKd", r), X("k0", 16 * r, 16 * r + 16)), (D("RLd", r), X("vl", 16 * r, 16 * r + 16))])
-    dma("s", [(D("RVd", r), X("v0", 16 * r, 16 * r + 16)), (D("Rtd", r), X("th", 0, 4))])
+    dma("s", [(D("RVd", r), X("v0", 16 * r, 16 * r + 16))])
     iota(col("pi", 0), [[0, 1]], 1, False)
-    iota(A("iot"), [[1, 256]])
+    iota(A("iot"), [[1, 272]])
     iota(A("iok"), [[0, 16], [1, 16]])
     iota(A("ioq"), [[1, 8], [0, 16]])
+    iota(A("ioj"), [[0, 2], [1, 16], [0, 8]])
+    iota(A("olf"), [[128, 2], [256, 8]], 1)
     send("a0", 1, lambda j, q: D("SKd", q), lambda j, q: D("RKd", q))
     send("a10", 1, lambda j, q: D("SLd", q), lambda j, q: D("RLd", q))
     send("a1", 1, lambda j, q: D("SVd", q), lambda j, q: D("RVd", q))
-    send("a2", 1, lambda j, q: D("Std"), lambda j, q: D("Rtd", q))
     arrive("a0", 1, lambda j, q: D("RKd", q), 6000.0)
     arrive("a10", 1, lambda j, q: D("RLd", q), 6000.0)
     arrive("a1", 1, lambda j, q: D("RVd", q), 6000.0)
-    arrive("a2", 1, lambda j, q: D("Rtd", q), 3000.0)
     dma("y", [(A("Kb"), D("RKd"))])
     dma("y", [(A("Li"), D("RLd"))])
     dma("y", [(A("Vb"), D("RVd"))])
-    dma("y", [(A("thI", p1=64), D("Rtd"))])
 
-    p_, q_, k_, kq_, e_, qk_, w_, yb_, nyb_ = [col("pc", j) for j in range(9)]
+    p_, q_, k_, kq_, e_, yb_, nyb_, c1_, c2_, cs1_, cs2_, ie_, h0_, h1_ = [col("pc", j) for j in range(14)]
     ts(col("pi", 1), col("pi", 0), 4, OP.arith_shift_right)
     ts(col("pi", 2), col("pi", 0), 15, OP.bitwise_and)
-    ts(col("pi", 3), col("pi", 0), 3, OP.arith_shift_right)
-    ts(col("pi", 4), col("pi", 0), 7, OP.bitwise_and)
     cp(A("pc", 0, 3), A("pi", 0, 3))
-    cp(A("pc", 9, 11), A("pi", 3, 5))
     ts(kq_, k_, 8.0, OP.mult, q_, OP.add)
     ts(e_, q_, 16.0, OP.mult, 15.0, OP.add)
-    ts(qk_, col("pc", 10), 16.0, OP.mult, col("pc", 9), OP.add)
-    ts(w_, q_, 256.0, OP.mult, k_, OP.add)
-    ts(yb_, k_, -15.5, OP.add, 16384.0, OP.mult)
-    ts(nyb_, k_, -15.5, OP.add, -16384.0, OP.mult)
+    ts(ie_, q_, 16.0, OP.mult, p_, OP.add)
     ts(A("mk", 0, 16), A("iot", 0, 16), k_, OP.is_equal)
     ts(A("mk", 16, 24), A("iot", 0, 8), q_, OP.is_equal)
-    ts(A("R16"), A("iok", 0, 128), k_, OP.is_equal)
+    ts(A("R16"), A("iok", 0, 128), k_, OP.is_equal, -2.0, OP.mult)
     ts(A("BO"), A("ioq"), q_, OP.is_equal)
     for j in range(8):
         act(A("SEL", 128 * j, 128 * j + 128), A("R16"), AF.Identity, scale=col("mk", 16 + j))
-    cp(A("wl"), A("iot"))
     ts(A("EB"), A("iot", 0, 144), e_, OP.is_equal)
     io128 = A("iot", 0, 128)
-    for n in ("SB", "PM32", "PMb"):
-        ts(A(n, 0, 128), io128, kq_, OP.is_equal)
+    for n in ("PM", "PM32", "PMb"):
+        ts(A(n), io128, kq_, OP.is_equal)
+    ts(A("IEh"), A("iot"), -16.0, OP.add, ie_, OP.is_equal)
+    cp(A("IEb"), A("IEh"))
     fill(A("ones"), 1.0)
-    fill(A("sig"), 1.0)
+    ts(A("sg"), A("iot", 0, 32), 0.0, OP.mult, -0.5, OP.add)
     ts(A("LE"), A("iok", 0, 128), k_, OP.is_ge)
-    for n, c in (("IDb", 1), ("IDh", 1), ("n63", -63)):
-        ts(A(n, 0, 128), io128, p_, OP.is_equal, float(c), OP.mult)
-    for n, c in (("ID32", 1), ("ISC", 1 / SC), ("I16", 1 / 16), ("Mt", -C8 * SC), ("I128", 128), ("m8I", -8), ("hI", .5),
-                 ("nhI", -.5), ("nI", -1), ("eI", EPS), ("bI", SC), ("I2k", 2048)):
+    ts(A("IDb"), io128, p_, OP.is_equal)
+    ts(A("IDh"), io128, p_, OP.is_equal)
+    for n, c in (("I256", 256), ("n512", -512), ("nIh", -1), ("n64", -64), ("n8k", -8192)):
+        ts(A(n), A("IDh"), float(c), OP.mult)
+    ts(A("wL"), A("iot", 0, 16), 16.0, OP.mult, k_, OP.add)
+    for j, (m, c) in enumerate(((1, 128), (1, 128), (1, 256), (1, 384), (2, 0.5))):
+        ts(A("cL", 16 * j, 16 * j + 16), A("wL"), float(m), OP.mult, float(c), OP.add)
+    for n, c in (("ID32", 1), ("ISC", 1 / SC), ("I16", 1 / 16), ("Mt", -C8 * SC), ("I64", 64), ("m8I", -8), ("I2k", 2048)):
         act(A(n, 0, 128), A("IDb"), scale=float(c))
     act(A("I2k", 128, 256), A("IDb"), scale=2048.0)
     tt(A("LE"), A("LE"), A("BO"), OP.mult)
@@ -292,8 +295,8 @@ def rank_program(g, core, T, topo):
     tt(A("LT"), A("LE"), A("IDb"), OP.subtract)
     act(A("nU"), A("LE"), scale=-1.0)
     tt(A("Bm"), A("LE"), A("Am"), OP.subtract)
-    act(A("m8A"), A("Am"), scale=-8.0)
-    act(A("m8L"), A("LT"), scale=-8.0)
+    for n, a, c in (("m8A", "Am", -8), ("m8L", "LT", -8), ("M64", "Am", 64)):
+        act(A(n), A(a), scale=float(c))
 
     def mix(o, a, ca, ci):
         ts(o, a, ca, OP.mult)
@@ -303,96 +306,123 @@ def rank_program(g, core, T, topo):
     mix(A("Mc", 0, 128), A("LT"), -C8 * SC, 136 * SC)
     cp(A("Mc", 128, 256), A("Mc", 0, 128))
     ts(A("rm"), A("iok"), 0.0, OP.not_equal)
-    ts(A("CB"), A("iot", 0, 240), -112.0, OP.add, k_, OP.is_equal)
-    ts(A("c4", 0, 4), A("iot", 0, 4), -8.0, OP.mult, p_, OP.add)
-    ts(A("c4", 4, 6), A("iot", 0, 2), -8.0, OP.mult, k_, OP.add)
-    ts(A("cL"), A("iot", 0, 16), 16.0, OP.mult, k_, OP.add)
     cp(A("qL", 0, 8), A("iot", 0, 8))
     cp(A("qL", 8, 16), A("iot", 0, 8))
-    ts(A("cl0"), A("cL"), 2.0, OP.mult)
-    for h in range(2):
-        ts(A("Hr", 128 * h, 128 * h + 128), A("ioq"), col("c4", h), OP.is_equal, 16384.0, OP.mult)
-        ts(A("Hm", 128 * h, 128 * h + 128), A("ioq"), col("c4", 2 + h), OP.is_equal, -1.0, OP.mult)
-    ts(A("cL"), A("cL"), -64.0, OP.mult, -16.0, OP.add)
+    for h, c in enumerate((h0_, h1_)):
+        ts(c, p_, -8.0 * h, OP.add)
+        ts(A("Hs", 128 * h, 128 * h + 128), A("ioq"), c, OP.is_equal, -1.0, OP.mult)
     for k in range(16):
         ts(A("XK", 128 * k, 128 * k + 128), A("BO"), col("mk", k), OP.mult)
+    ts(A("thZ", p1=64), A("iot", 0, 128, p1=64), 0.0, OP.mult)
+    ts(A("thZ", 16 * r, 16 * r + 16, p1=64), A("thI", p1=64), -1.0, OP.mult)
+    ts(yb_, k_, -15.5, OP.add, 16384.0, OP.mult)
+    ts(nyb_, k_, -15.5, OP.add, -16384.0, OP.mult)
+    cp(A("dl", 16, 32), A("olf"))
+
+    def late_constants():
+        ts(c1_, k_, 64.0, OP.mult, -1025.0, OP.add)
+        ts(c2_, k_, 64.0, OP.mult, 67648.0, OP.add)
+        ts(cs1_, p_, 0.0, OP.is_equal, 4032.0, OP.mult)
+        ts(cs2_, p_, 1.0, OP.is_le, 64.0, OP.mult)
+        tt(cs1_, cs1_, cs2_, OP.add)
+        ts(cs2_, p_, 2.0, OP.is_equal, -2048.0, OP.mult)
+        ts(col("pc", 14), cs1_, -15.0, OP.mult)
+        tt(cs2_, cs2_, col("pc", 14), OP.add)
+        ts(A("Cs", 0, 256), A("ioj"), cs1_, OP.mult, cs2_, OP.add)
+        ts(A("Cs", 256, 512), A("iok"), cs1_, OP.mult, cs2_, OP.add)
+        for j, c in enumerate((-64.0, 64.0, -1.0, 1.0)):
+            ts(A("Wt", 8 * j, 8 * j + 8), A("mk", 16, 24), c, OP.mult)
+            ts(A("Wt", 32 + 16 * (j // 2) + j % 2, 48 + 16 * (j // 2), 2), A("mk", 16, 24), c, OP.mult)
+        ts(A("nb"), A("iot", 0, 16), -64.0, OP.mult)
 
     def spread_T(share):
         for q in range(8):
-            b = (0, 3, 5, 6)[q % 4]
-            mms([(PS(b), A("SEL", 128 * q, 128 * q + 128), A("Tc"))])
+            b = (5, 6, 0, 4)[q % 4]
+            mms([(PS(b, e, 512, 2), A("SEL", 128 * q, 128 * q + 128), A("Tc", 256 * e, 256 * e + 256)) for e in range(2)])
             (cp if q in share else act)(A("Tt", 512 * q, 512 * q + 512), PS(b))
 
     def spread_dma(tab, src, q="y"):
         dma(q, [(A(tab, p0=16 * a, p1=16 * a + 16), A(src)) for a in range(8)], 4500.0 + 10 * wide(A(src)))
 
-    ts(A("Tc"), A("Kb"), 1.0, OP.add)
-    ts(A("ownp"), A("Kb", 0, 512, 2), EPS, OP.max)
-    spread_T((1, 3, 5, 6, 7))
-    ts(A("Ko1"), A("Kb", 1, 512, 2), 1.0, OP.add)
-    ts(A("own1"), A("Kb", 0, 512, 2), 1.0, OP.add)
-    cp(A("lu", 0, 256), A("Li"))
-    cp(A("Lf"), A("Li"))
+    def swap(out, ie, src):
+        mm([(out(x, 32 * a), A(ie, 32 * x + 16 - 16 * u, 32 * x + 48 - 16 * u), src(2 * a + u)) for x in range(8) for a in range(4) for u in range(2)], each=2)
 
-    def late_constants():
-        ts(A("c8"), A("iot", 0, 8), p_, OP.subtract, -0.125, OP.mult)
-        ts(A("ol"), A("iot", 0, 16), 16.0, OP.mult, w_, OP.add)
-        for h in range(2):
-            ts(A("Hs", 128 * h, 128 * h + 128), A("ioq"), col("c4", 4 + h), OP.is_equal, -64.0, OP.mult)
-        for j in range(8):
-            ts(A("Ht", 128 * j, 128 * j + 128), A("ioq"), col("c8", j), OP.is_equal, 64.0, OP.mult)
-        cp(A("SB", 128, 256), A("SB", 0, 128))
-        ts(A("SB63"), A("SB", 0, 128), 63.0, OP.mult)
-        ts(A("PMT"), io128, qk_, OP.is_equal)
-        tt(A("GB"), A("SB", 0, 248), A("SB", 8, 256), OP.subtract)
-        mix(A("M128"), A("Am"), 128.0, 2048.0)
-        ts(A("GB63"), A("GB"), 63.0, OP.mult)
+    def cur_lists(t):
+        mm([(PS(1, 432, 512), A("IDh"), A("cL"))] +
+           [(PS(1, 432 + 16 * j, 448 + 16 * j), A(n), A("sg", 0, 16)) for j, n in enumerate(("I256", "I256", "n512", "I256", "IDh"))])
+        cp(A("cl", 80 * t, 80 * t + 80), PS(1, 432, 512))
+
+    K2 = lambda t, a=0, b=512: A("KK", 768 * (t % 2) + a, 768 * (t % 2) + b)
+
+    def own_K(t):
+        act(A("own"), IND(K2(t), A("cl", 80 * t, 80 * t + 32)))
+
+    for e in range(2):
+        ts(A("Tc", 256 * e, 256 * e + 256), A("Kb", e, 512, 2), EPS, OP.max, -0.5, OP.mult)
+    spread_T((1, 3, 5, 7))
+    for e in range(2):
+        ts(K2(0, 256 * e, 256 * e + 256), A("Kb", e, 512, 2), EPS, OP.max)
+    cur_lists(0)
+    own_K(0)
+    ts(A("LcA"), A("Li"), -2048.0, OP.add)
+    mms([(B("p2", 0, 16, 1, 8 * y, 8 * y + 8), A("LcA", 128 * y, 128 * y + 128), A("PM")) for y in range(2)])
+    cp(A("LcB"), PS(2, 0, 256))
+    swap(lambda x, p: B("p2", 0, 16, 1, x, 16, 8, p, p + 32), "IEh", lambda q: B("LcB", 0, 16, 1, q, 16, 8))
+    ts(A("lu", 0, 256), PS(2, 0, 256), 2048.0, OP.add)
 
     def contract(c):
-        mm([(PS(0, 64 * c, 64 * c + 64), A("EB", 15 - k, 143 - k), A("P", 1024 * c + k, 1024 * c + 1024, 16)) for k in range(16)])
-
-    def pieces():
-        ts(A("Lc"), A("Lf"), -2048.0, OP.add)
-        ts(A("Lh"), A("Lf"), 1.0 / 64, OP.mult, 1025 - 31.5 / 64, OP.add)
+        mm([(PS(0, 0, 256), A("EB", 15 - k, 143 - k), A("P", 256 * k, 256 * k + 256)) for k in (2 * c, 2 * c + 1)], c == 0, c == 7)
 
     def marks():
-        mm([(PS(1, 0, 256), A("nU"), A("ones"))], True, False)
+        mm([(PS(2, 0, 256), A("nU"), A("ones"))], True, False)
         ts(A("fl"), PS(0, 0, 256), 0.0, OP.is_lt)
-        mm([(PS(1, 0, 256), A("Bm"), A("fl"))], False, True)
-        tt(A("tt"), A("fl"), PS(1, 0, 256), OP.mult)
+        mm([(PS(2, 0, 256), A("Bm"), A("fl"))], False, True)
+        tt(A("tt"), A("fl"), PS(2, 0, 256), OP.mult)
 
     def sort_keys():
-        lin = [(A("M128"), A("fl")), (A("I128"), A("tt"))]
+        lin = [(A("M64"), A("fl")), (A("I64"), A("tt"))]
         mm([(PS(3, 0, 256), l, x) for l, x in [(A("IDh"), A("Lh"))] + lin])
-        mm([(PS(3, 256, 512), l, x) for l, x in [(A("IDh"), A("Lc")), (A("n63"), A("Lh"))] + lin])
+        mm([(PS(3, 256, 512), l, x) for l, x in [(A("IDh"), A("LcA")), (A("n64"), A("Lh"))] + lin])
+        ts(A("Qs", 0, 256), PS(3, 0, 256), c1_, OP.add)
+        ts(A("Qs", 256, 512), PS(3, 256, 512), c2_, OP.add)
 
-    def sort_evac():
-        ts(A("Qs", 0, 256), PS(3, 0, 256), -2113.0, OP.add)
-        ts(A("Qs", 256, 512), PS(3, 256, 512), 65535.0, OP.add)
+    def moves(last):
+        mm([(PS(3, 0, 256), A("ones", 0, 128, p1=32), A("Cs", 256 * last, 256 * last + 256, p1=32))], True, False)
+        for j in range(16):
+            a = 512 * (j % 8)
+            n = "R" if j else "Qs"
+            if j in S_MOVES:
+                act(A("R", a, a + 512), A("Qs"), AF.Relu, bias=col("nb", j))
+            elif j:
+                ts(A("R", a, a + 512), A("Qs"), -64.0 * j, OP.add, 0.0, OP.max)
+            lst = []
+            for u in range(2):
+                for y in range(2):
+                    if last:
+                        o = B("p3", 8 * y, 8 * y + 8, 1, max(j - 1, 0), j + 1)
+                        w = A("Wt", 32 + 16 * u, 48 + 16 * u) if j else A("Wt", 33 + 16 * u, 48 + 16 * u, 2)
+                    else:
+                        o = B("p3", 8 * y, 8 * y + 1, 1, 0, 8) if j == 0 else PS(3, 128 * y + 8 * j - 8, 128 * y + 8 * j + 8) if j % 2 else None
+                        w = A("Wt", 16 * u + (0 if j else 8), 16 * u + 16)
+                    l = A(n, a + 256 * u + 128 * y, a + 256 * u + 128 * y + 128)
+                    if o is None:
+                        lst.append((B("p3", 8 * y + j // 2 - 1, 8 * y + j // 2, 1, 8, 16), l, A("Wt", 16 * u, 16 * u + 8)))
+                        lst.append((B("p3", 8 * y + j // 2, 8 * y + j // 2 + 1, 1, 0, 8), l, A("Wt", 16 * u + 8, 16 * u + 16)))
+                    else:
+                        lst.append((o, l, w))
+            mm(lst, False, j == 15)
+        cp(A("Lt"), PS(3, 0, 256))
+        mms([(PS(3, 256 + 128 * y, 384 + 128 * y), A("Lt", 128 * y, 128 * y + 128), A("IDh")) for y in range(2)])
 
-    def moves(d0, d1):
-        o = PS(3, 0, 256)
-        for d in range(d0, d1):
-            if d == 0:
-                mm([(o, A("SB63"), A("Qs", 0, 256)), (o, A("SB", 0, 128), A("Qs", 256, 512))], True, False)
-                continue
-            a = 512 * (d % 8)
-            ts(A("R", a, a + 512), A("Qs"), 128.0 * d - 1088, OP.max)
-            mm([(o, A("GB63", 128 - 8 * d, 256 - 8 * d), A("R", a, a + 256)), (o, A("GB", 128 - 8 * d, 256 - 8 * d), A("R", a + 256, a + 512))], False, d == 16)
-
-    def sort_end():
-        ts(A("Li"), PS(3, 0, 256), 69632.0, OP.add)
-        ts(A("Lp"), A("Li"), 4095, OP.bitwise_and)
-
-    def weights(k0, k1):
-        for k in range(k0, k1, 2):
+    def weights():
+        for k in range(0, 16, 2):
             b = 5 + (k // 2) % 2
             mms([(PS(b, 256 * j, 256 * j + 256), A("XK", 128 * (k + j), 128 * (k + j + 1)), A("x16")) for j in range(2)])
-            for j in range(2):
-                act(A("E", k + j, 4096, 16), PS(b, 256 * j, 256 * j + 256), AF.Exp, scale=1.0 / 256)
+            act(A("E", 256 * k, 256 * k + 512), PS(b), AF.Exp, bias=-1860.0 / 256, scale=1.0 / 256)
 
     def new_V(t):
-        act(IND(A("Vc"), A("cl%d" % (t % 2))), A("As"), AF.Tanh)
+        act(A("As"), PS(7, 0, 256))
+        act(IND(A("Vc"), A("cl", 80 * t + 64, 80 * t + 80)), A("As"), AF.Tanh)
 
     def hand_back(sem, n, src, y):
         s, d = "S" + n + "d", "R" + n + "d"
@@ -403,172 +433,114 @@ def rank_program(g, core, T, topo):
         return lambda: dma("y", [((T[y][:, :], []), D(d))])
 
     si = lambda j: A("si", 16 * j, 16 * j + 16)
+    lu = lambda t, c: A("lu", 256 * t + 32 * c, 256 * t + 32 * c + 32)
     for t in range(NS):
-        for c in range(4):
-            s = (1024 * c, 1024 * c + 1024)
-            act(A("OX", *s), IND(A("ownp"), A("wl", 64 * c, 64 * c + 64)))
-            tt(A("P", *s), IND(A("Tt"), A("lu", 256 * t + 64 * c, 256 * t + 64 * c + 64)), A("OX", *s), OP.mult)
-            if c == 0 and t > 0:
-                tt(A("As"), A("em"), PS(4, 256, 512), OP.mult)
-            if c == 3 and t > 0:
-                act(A("own1"), A("ownp"), AF.Identity, bias=1.0)
-                act(A("Ko1"), PS(2, 0, 256))
-                new_V(t - 1)
-                mms([(PS(5), A("PM32"), A("Vc"))])
-                act(A("Vp"), PS(5))
-                spread_dma("Vt", "Vp")
-            if c == 3 and t == 0:
-                act(A("Vc"), A("Vb"))
-                mms([(PS(5), A("PMb"), A("Vb"))])
-                act(A("Vp"), PS(5))
-                spread_dma("Vt", "Vp")
+        for c in range(8):
+            tt(A("P", 512 * c, 512 * c + 512), IND(A("Tt"), lu(t, c)), A("own"), OP.mult)
             contract(c)
-        pieces()
-        mm([(PS(2, 256, 512), A("ones", 0, 128), A("I2k"))] +
-           [(PS(2, 256 + 128 * h, 384 + 128 * h), A("Lc", 128 * h, 128 * h + 128), A("IDh")) for h in range(2)])
-        mm([(PS(2, 0, 256), A("ones", 0, 128), A("Mc"))], True, False)
+        if t > 0:
+            new_V(t - 1)
+            mms([(PS(4), A("PM32"), A("Vc"))])
+        else:
+            act(A("Vc"), A("Vb"))
+            mms([(PS(4), A("PMb"), A("Vb"))])
+        act(A("Vp"), PS(4))
+        spread_dma("Vt", "Vp")
+        mm([(PS(1, 256, 512), A("ones", 0, 128), A("I2k"))] +
+           [(PS(1, 256 + 128 * h, 384 + 128 * h), A("LcA", 128 * h, 128 * h + 128), A("IDh")) for h in range(2)])
+        mm([(PS(1, 0, 256), A("ones", 0, 128), A("Mc"))], True, False)
         marks()
         act(A("aS"), PS(0, 0, 256), AF.Abs, scale=SC)
-        hs = [(PS(2, 128 * h, 128 * h + 128), 128 * h) for h in range(2)]
+        hs = [(PS(1, 128 * h, 128 * h + 128), 128 * h) for h in range(2)]
         mm([(o, A("fl", a, a + 128), A("Mf")) for o, a in hs], False, False)
         mm([(o, A("aS", a, a + 128), A("ID32")) for o, a in hs], False, False)
         mm([(o, A("tt", a, a + 128), A("Mt")) for o, a in hs], False, True)
         xl = PS(4, 0, 256)
-        mm([(xl, A("m8L"), A("ones")), (xl, A("m8A"), A("fl")), (xl, A("m8I"), A("tt")), (xl, A("ISC"), A("aS"))])
-        if t > 0:
-            sort_keys()
-        else:
-            mms([(PS(3, 0, 256), A("SB", 0, 128), A("Lc"))])
-        mv = moves if t > 0 else lambda a, b: None
-        scan(A("Mx"), A("rm"), PS(2, 0, 256), OP.mult, OP.max)
-        ts(A("x16"), xl, -1860.0, OP.add)
-        weights(0, 4)
-        tt(A("us"), A("Mx"), PS(2, 0, 256), OP.subtract)
-        tt(A("d1"), PS(2, 256, 512), A("us"), OP.subtract)
+        mm([(xl, A("m8L"), A("ones")), (xl, A("m8A"), A("fl")), (xl, A("m8I"), A("tt")), (xl, A("ISC"), A("aS"))], True, False)
+        scan(A("Mx"), A("rm"), PS(1, 0, 256), OP.mult, OP.max)
+        tt(A("us"), A("Mx"), PS(1, 0, 256), OP.subtract)
+        tt(A("d1"), PS(1, 256, 512), A("us"), OP.subtract)
         scan(A("Bx"), A("us"), A("d1"), OP.min, OP.max)
         bs = A("Bx", 15, 256, 16)
-        for a in range(8):
-            ts(A("Z", a, 128, 8), bs, -2048.0, OP.add, col("mk", 16 + a), OP.mult)
-        for h in range(2):
-            mm([(PS(1, 256 + 8 * h, 264 + 8 * h), A("CB", 112 - 16 * q, 240 - 16 * q), A("Z", 64 * h + 8 * q, 64 * h + 8 * q + 8)) for q in range(8)])
-        ts(si(0), A("Mx", 15, 256, 16), 32 / SC, OP.mult, 30.0, OP.add)
-        ts(si(4), bs, 1.0 / 512, OP.mult, -255.5 / 512, OP.add)
-        if t > 0:
-            sort_evac()
-        else:
-            ts(A("Lp"), PS(3, 0, 256), 2048.0, OP.add)
-            spread_dma("VT", "Lp")
-        ts(A("bl"), PS(1, 256, 272), 2048.0, OP.add)
-        act(A("gk"), IND(A("Tt"), A("bl")), AF.Abs)
-        ts(si(1), si(0), 31, OP.bitwise_and, 1, OP.logical_shift_right)
-        ts(si(2), si(0), 1, OP.bitwise_and)
-        ts(si(3), si(0), 5, OP.arith_shift_right)
-        mv(0, 3)
-        tt(A("Kn"), A("gk"), A("own1"), OP.max)
-        mms([(PS(1, 272 + 8 * h, 280 + 8 * h), A("Kn", 128 * h, 128 * h + 128), A("BO", 0, 128, 16)) for h in range(2)])
+        for y in range(2):
+            cp(A("bl", y, 16, 2), A("Bx", 128 * y + 15, 128 * y + 128, 16))
+        act(A("gkB"), IND(A("Tt"), A("bl")), AF.Abs)
+        swap(lambda x, p: B("p0", x, 16, 8, 0, 16, 1, p, p + 32), "IEb", lambda q: A("gkB", 32 * q, 32 * q + 32))
+        Kn = K2(t, 512, 768)
+        tt(Kn, PS(0, 0, 256), A("own", 0, 256), OP.max)
+        kn = 768 * (t % 2) + 512
+        mm([(PS(1, 384, 400), A("thZ", p1=64), A("IDh", 16 * t, 16 * t + 16, p1=64))] +
+           [(PS(1, 384, 400), A("EB", 15 - b, 143 - b), A("KK", kn + b, kn + 256, 16)) for b in range(16)])
         rc = "rc%d" % t
-        act(A(rc, 16 * r, 16 * r + 16), PS(1, 272, 288))
-        if t == 0:
-            late_constants()
+        cp(A(rc, 16 * r, 16 * r + 16), PS(1, 384, 400))
         send("a%d" % (3 + t), 1, lambda j, q, rc=rc: A(rc, 16 * r, 16 * r + 16), lambda j, q, rc=rc: A(rc, 16 * q, 16 * q + 16))
         arrive("a%d" % (3 + t), 1, lambda j, q, rc=rc: A(rc, 16 * q, 16 * q + 16))
+        ts(si(0), A("Mx", 15, 256, 16), 32 / SC, OP.mult, 30.0, OP.add)
+        ts(si(3), si(0), 5, OP.arith_shift_right)
+        ts(A("MR"), si(3), -1860.0, OP.add)
+        mms([(PS(1, 256, 384, p1=16), A("MR"), A("IDh"))])
+        cp(A("MTs", p1=16), PS(1, 256, 384, p1=16))
+        mm([(PS(4, 128 * y, 128 * y + 128), A("Hs", 128 * y, 128 * y + 128, p1=16), A("MTs", p1=16)) for y in range(2)], False, True)
+        ts(A("x16"), xl, 136.0, OP.add)
+        weights()
+        act(K2(t + 1), IND(K2(t, 0, 768), A("cl", 80 * t + 32, 80 * t + 64)))
+        ts(si(4), bs, 1.0 / 512, OP.mult, -255.5 / 512, OP.add)
+        ts(si(1), si(0), 31, OP.bitwise_and, 1, OP.logical_shift_right)
+        ts(si(2), si(0), 1, OP.bitwise_and)
         tt(si(5), si(4), A("qL"), OP.not_equal)
-        cp(A("MR", 16, 32), si(3))
         tt(si(6), si(5), si(2), OP.is_gt)
-        ts(si(7), PS(1, 256, 272), 0.5, OP.mult, 1023.75, OP.add)
-        tt(A("MR", 0, 16), si(6), si(1), OP.mult)
-        cp(A("dl"), si(7))
-        weights(4, 6)
-        mms([(PS(1, 288, 416, p1=32), A("MR"), A("ID32"))])
-        weights(6, 8)
-        mv(3, 5)
-        act(A("MTs", p1=32), PS(1, 288, 416, p1=32))
-        mms([(PS(0, 128 * j, 128 * j + 128), A(("Hm", "Hr")[j // 2], 128 * (j % 2), 128 * (j % 2) + 128, p1=32), A("MTs", p1=32)) for j in range(4)])
-        half = [(A("hI"), A("Kn")), (A("hI"), A("Ko1"))]
-        mm([(PS(2, 0, 256), A("hI"), A("Kn")), (PS(2, 0, 256), A("nhI"), A("Ko1"))])
-        weights(8, 10)
-        mv(5, 7)
-        tt(A("G"), A("sig", 0, 256), PS(2, 0, 256), OP.mult)
-        mv(7, 9)
-        act(A("em"), PS(0, 0, 256), AF.Exp, bias=1996.0 / 256, scale=1.0 / 256)
-        weights(10, 12)
-        mm([(PS(2, 0, 256), l, x) for l, x in half + [(A("IDb"), A("G"))]])
-        mm([(PS(2, 256, 512), l, x) for l, x in half + [(A("nI"), A("G"))]])
-        mv(9, 11)
-        weights(12, 14)
-        mms([(PS(1, 0, 256), A("IDb"), A("G"))])
-        mm([(PS(1, 256, 512), l, x) for l, x in half + [(A("nI"), A("ones")), (A("eI"), A("ones"))]])
-        mv(11, 13)
-        weights(14, 16)
-        if t == 0:
-            cp(A("thT", p1=64), A("thI", p1=64))
-        mm([(PS(7), A("bI"), A("sig")), (PS(7, 256, 512), A("bI"), A("sig", 0, 256))] +
-           [(PS(7, 256 * e + 128 * h, 256 * e + 128 * h + 128), A("Ht", 128 * (2 * t + h), 128 * (2 * t + h + 1), p1=64), A("thT", p1=64))
-            for e in range(2) for h in range(2)], True, False)
-        act(A("yp"), PS(0, 256, 512), AF.Identity, bias=yb_)
-        act(A("yn"), PS(0, 256, 512), AF.Identity, bias=nyb_, scale=-1.0)
+        tt(A("r16"), si(6), si(1), OP.mult)
+        ts(si(7), bs, 0.5, OP.mult, -0.25, OP.add)
+        cp(A("dl", 0, 16), si(7))
+        mms([(PS(2, b, 256, 16), A("XK", 128 * b, 128 * b + 128), A("r16")) for b in range(16)])
+        act(A("ypn", 0, 256), PS(2, 0, 256), AF.Identity, bias=yb_, scale=16384.0)
+        act(A("ypn", 256, 512), PS(2, 0, 256), AF.Identity, bias=nyb_, scale=-16384.0)
         if t == NS - 1:
             for e in range(2):
-                act(A("Ko", e, 512, 2), PS(2, 256 * e, 256 * e + 256), AF.Identity, bias=-1.0)
+                ts(A("Ko", e, 512, 2), K2(NS, 256 * e, 256 * e + 256), 12582912.0, OP.add, -12582912.0, OP.add)
             last_k = hand_back("a7", "k", "Ko", "yk")
-        mv(13, 17)
-
-        def values(c):
-            for j in (2 * c, 2 * c + 1):
-                s = (512 * j, 512 * j + 512)
-                tt(A("Y", *s), IND(A("Vt"), A("lu", 256 * t + 32 * j, 256 * t + 32 * j + 32)), A("E", *s), OP.mult)
-
-        def sums(c):
-            mm([(PS(4, 256 + 64 * c, 320 + 64 * c), A("I16"), A("Y", 1024 * c + k, 1024 * c + 1024, 16)) for k in range(16)])
-        mms([(PS(0, 0, 128), A(rc), A("IDb"))])
-        if t == 0:
-            values(0)
-        cp(A("RTs"), PS(0, 0, 128))
-        mm([(PS(7, 256 * e + 128 * h, 256 * e + 128 * h + 128), A("Hs", 128 * h, 128 * h + 128), A("RTs")) for e in range(2) for h in range(2)], False, True)
         if t > 0:
-            sort_end()
-            spread_dma("VT", "Lp")
-        act(A("sig", 0, 256), PS(7, 0, 256), AF.Sign, bias=8160.0 - SC)
-        act(A("sig", 256, 512), PS(7, 256, 512), AF.Sign, bias=8160.0)
-        tt(A("Tc", 0, 512, 2), A("sig", 0, 256), PS(2, 0, 256), OP.mult)
-        tt(A("Tc", 1, 512, 2), A("sig", 256, 512), PS(2, 256, 512), OP.mult)
-        if t < NS - 1:
-            tt(A("gk"), A("sig", 0, 256), PS(1, 0, 256), OP.mult)
-            tt(A("ownp"), A("gk"), PS(1, 256, 512), OP.add)
-        if t > 0:
-            values(0)
-        spread_T(SHARE)
-        if t < NS - 1:
-            mm([(PS(7, 0, 16), A("ID32"), A("cL"))] + [(PS(7, 0, 16), A("EB", 15 - b, 143 - b), A("sig", b, 256, 16)) for b in range(16)])
-            mm([(PS(2, 0, 256), l, x) for l, x in half + [(A("nI"), A("gk"))]])
+            sort_keys()
+            moves(0)
         else:
-            last_k()
-        sums(0)
-        for c in range(1, 4):
-            values(c)
-            sums(c)
+            mms([(PS(3, 256, 512), A("PM"), A("LcA"))])
+            late_constants()
+        cp(A("Lp"), PS(3, 256, 512))
+        spread_dma("VT", "Lp")
+        tt(A("ga"), IND(A("VT"), A("dl")), A("ypn"), OP.min)
+        tt(A("LcB"), A("ga", 0, 256), A("ga", 256, 512), OP.max)
+        mms([(B("p2", 0, 16, 1, 8 * y, 8 * y + 8), A("LcB", 128 * y, 128 * y + 128), A("PM")) for y in range(2)])
+        ts(A("lu", 256 * t + 256, 256 * t + 512), PS(2, 0, 256), 2048.0, OP.add)
+        swap(lambda x, p: B("p2", 16 + x, 32, 8, 0, 16, 1, p, p + 32), "IEh", lambda q: B("LcB", q, 16, 8))
+        cp(A("LcA"), PS(2, 256, 512))
+        ts(A("Lh"), PS(2, 256, 512), 1.0 / 64, OP.mult, 1057 - 31.5 / 64, OP.add)
+        sg = [A("sg", 0, 16), A("sg", 16, 32)]
+        mm([(PS(1, 400, 432), A("n8k"), A("sg")), (PS(1, 416, 432), A("n8k"), sg[0])], True, False)
+        mm([(PS(1, 400 + 16 * e, 416 + 16 * e), A("nIh"), A(rc, 16 * h, 16 * h + 16)) for e in range(2) for h in range(8)], False, True)
+        for e in range(2):
+            ts(sg[e], PS(1, 400 + 16 * e, 416 + 16 * e), 4096.5 - 4096 * e, OP.is_lt, -0.5, OP.add)
+        mms([(PS(0, b, 512, 16), A("XK", 128 * b, 128 * b + 128), A("sg")) for b in range(16)])
+        tt(A("Tc"), PS(0), K2(t + 1), OP.mult)
         if t < NS - 1:
-            ts(A("cl%d" % ((t + 1) % 2)), PS(7, 0, 16), -1.0 / 32, OP.mult)
-        tt(A("ga"), IND(A("VT"), A("dl")), A("yp"), OP.min)
-        tt(A("gb"), IND(A("VT"), A("ol")), A("yn"), OP.min)
-        tt(A("Lf"), A("ga"), A("gb"), OP.max)
-        cp(A("lu", 256 * t + 256, 256 * t + 512), A("Lf"))
+            cur_lists(t + 1)
+            own_K(t + 1)
+        spread_T(SHARE)
+        if t == NS - 1:
+            last_k()
+        for c in range(8):
+            s = (512 * c, 512 * c + 512)
+            tt(A("Y", *s), IND(A("Vt"), lu(t, c)), A("E", *s), OP.mult)
+            mm([(PS(7, 0, 256), A("I16"), A("Y", 256 * k, 256 * k + 256)) for k in (2 * c, 2 * c + 1)], c == 0, c == 7)
 
-    for c in (0, 2, 1, 3):
-        (cp if c < 2 else act)(A("P", 1024 * c, 1024 * c + 1024), IND(A("Tt"), A("lu", 256 * NS + 64 * c, 256 * NS + 64 * c + 64)))
+    for c in range(8):
+        (cp if c % 2 else act)(A("P", 512 * c, 512 * c + 512), IND(A("Tt"), lu(NS, c)))
         contract(c)
-    tt(A("As"), A("em"), PS(4, 256, 512), OP.mult)
-    pieces()
     new_V(NS - 1)
     last_v = hand_back("a8", "v", "Vc", "yv")
     marks()
     sort_keys()
-    sort_evac()
-    moves(0, 17)
-    sort_end()
-    ts(A("Lc"), A("Lp"), -2048.0, OP.add)
-    mms([(PS(0, 0, 256), A("PMT"), A("Lc"))])
-    ts(A("Lo"), PS(0, 0, 256), 2048.0, OP.add)
+    moves(1)
+    ts(A("Lo"), PS(3, 256, 512), 2048.0, OP.add)
     last_l = hand_back("a9", "l", "Lo", "yl")
     last_v()
     last_l()
@@ -639,8 +611,9 @@ def arrange(ops):
             span, at2, end2 = lay(mend(p))
             span += 1e-4 * sum(end2) / n
             if span <= best:
-                best, at, prio = span, at2, [-x for x in at2]
+                best, at, end, prio = span, at2, end2, [-x for x in at2]
         KEPT[n] = sorted(range(n), key=lambda j: (at[j], j))
+        KEPT["times"] = (best, at, end)
     seq = KEPT[n]
     place = {j: k for k, j in enumerate(seq)}
     for j, o in enumerate(ops):

@@ -7,10 +7,12 @@ NS = 4
 SC = float(2 ** 18)
 C8 = 129.0 / 16
 EPS = 2.0 ** -18
-PE_NS, WAKE = 0.5, 80.0
-TRIES, KEPT = 6000, {}
-SHARE = (3,)
-S_MOVES = (3, 6, 9, 12, 15)
+PE_NS, WAKE, VLAT = 0.5, 80.0, 6500.0
+STARTS, FIRST, TRIES, STEP, SLACK, KEPT = 3, 2000, 14000, 4000.0, 400.0, {}
+SHARE, SHARE_ENDS = (3,), (1, 3, 5, 7)
+S_MOVES, S_LAST = (8,), (3, 6, 9, 12, 15)
+ON_S = {"Qs", "Lt", "LcA", "Lh", "x16", "MTs", "Lp", "W2"}
+WB, TB = (5, 6), (4, 0, 1)
 SCRATCH = {}
 
 
@@ -20,29 +22,28 @@ def _sb(dtype, **kw):
 
 
 _sb(BF, Tt=4096, P=4096, Kb=512, Vb=512, KK=1536, Tc=512, own=512, fl=256, tt=256, BO=128, EB=144, SEL=1024, R16=128, IDb=128,
-    Mf=128, Mc=256, I2k=256, ones=256, tmp=128, IEb=272, Cs=512)
-_sb(F, Vt=4096, E=4096, Y=4096, Vc=512, Vp=512, Ko=512, Lo=256, aS=256, Mx=256, us=256, d1=256, Bx=256, ypn=512, ga=512, As=256,
-    iot=272, ioq=128, iok=256, ioj=256, pc=24, mk=24, ID32=128, ISC=128, I16=128, PM32=128, rm=256, qL=16, wL=16, olf=16, nb=16)
-_sb(HF, LcA=256, Lh=256, Lt=256, Qs=512, R=4096, x16=256, XK=2048, PM=128, IDh=128, nIh=128, n64=128, n8k=128, I256=128, n512=128,
-    IEh=272, Hs=256, Wt=64, thZ=128, cL=80, sg=32, MR=16, r16=16, MTs=128, rc0=128, rc1=128, rc2=128, rc3=128)
-_sb(I, VT=2048, Li=256, Lp=256, thI=16, pi=8, si=128)
-_sb(U, lu=1280, bl=16, dl=32, cl=320)
-SCRATCH["LcB"] = ("sbuf", [128, 16, 16], HF)
-_sb(BF, gkB=256)
+    Mf=128, Mc=256, I2k=256, ones=256, tmp=128, IEb=272, Cs=512, Ko=512, gkB=256)
+_sb(F, Vt=4096, E=8192, Y=4096, Vc=512, Vp=512, VT=2048, Lo=256, aS=256, Mx=256, us=256, d1=256, Bx=256, ypn=512, ga=512, As=256, At=256, Lp=256,
+    iot=272, ioq=128, iok=256, ioj=256, pc=24, mk=24, ID32=128, ISC=128, PM32=128, rm=256, qL=16, wL=16, olf=16, nb=16, m16=16, gq=128)
+_sb(HF, LcA=256, Lh=256, Lt=256, Ls=256, L0=256, R0=256, Qs=512, R=4096, x16=256, XK=2048, XG=2048, PM=128, IDh=128, nIh=128, n64=128, n8k=128,
+    I256=128, n512=128, IEh=272, Hs=256, Wt=64, thZ=128, cL=80, sg=32, MR=16, r16=16, MTs=128, rc0=128, rc1=128, rc2=128, rc3=128)
+_sb(I, Li=256, thI=16, pi=8, si=128)
+_sb(U, lu=1280, lv=1024, bl=16, dl=32, cl=320)
+for _n in ("LcB", "W2", "Rl"):
+    SCRATCH[_n] = ("sbuf", [128, 16, 16], HF)
 PART = {}
-for _n in "Bm nU Mt M64 I64 m8A m8I m8L PMb Am LT LE".split():
+for _n in "Bm nU Mt M64 I64 m8A m8I PMb Am LT LE".split():
     PART[_n] = 128 * len(PART)
 _sb(BF, cmat=128 * len(PART))
 for _i in range(8):
-    SCRATCH["p%d" % _i] = ("psum", [128, 32, 16], F)
-SCRATCH["p1"] = ("psum", [128, 512], F)
-for _n, _c, _d in (("K", 64, BF), ("V", 64, BF), ("L", 32, I), ("k", 64, F), ("v", 64, F), ("l", 32, F)):
+    SCRATCH["p%d" % _i] = ("psum", [128, 512] if _i in (1, 3) else [128, 32, 16], F)
+for _n, _c, _d in (("K", 64, BF), ("V", 64, BF), ("k", 64, BF), ("v", 32, F), ("w", 32, F)):
     SCRATCH["S" + _n + "d"] = ("dram", [8, 128, _c], _d)
     SCRATCH["R" + _n + "d"] = ("dram", [8, 128, _c], _d)
 SEMAPHORES = ["pe", "v", "s", "g", "sent"] + ["d%d" % i for i in range(48)] + ["a%d" % i for i in range(12)]
 
 
-def spread(topo, src, dsts, per):
+def spread(topo, src, dsts):
     far = [d for d in dsts if topo.chip(d) != topo.chip(src)]
     near = [d for d in dsts if topo.chip(d) == topo.chip(src)]
     fe = topo.engines(src, far[0]) if far else []
@@ -51,10 +52,10 @@ def spread(topo, src, dsts, per):
     for ds, es in ((far, fe), (near, ne)):
         if ds:
             n = 1
-            while 2 * n * per * len(ds) <= len(es):
+            while 2 * n * len(ds) <= len(es):
                 n *= 2
             for i, d in enumerate(ds):
-                out[d] = [(sum(1 << e for e in es[(i * per + j) * n:(i * per + j + 1) * n]), n) for j in range(per)]
+                out[d] = (sum(1 << e for e in es[i * n:(i + 1) * n]), n)
     return out
 
 
@@ -152,8 +153,7 @@ def rank_program(g, core, T, topo):
         rec("v", lambda: g.vector.tensor_tensor(o[0], a[0], b[0], op), regs(a, b), o[1], cost=c)
 
     def cp(o, a):
-        w, x = outs(o)
-        rec("v", lambda: g.vector.tensor_copy(o[0], a[0]), regs(a) + x, w, cost=price(o, a, 0.5 if size(o) == 2 == size(a) else 1))
+        rec("v", lambda: g.vector.tensor_copy(o[0], a[0]), regs(a), o[1], cost=price(o, a, 0.5 if size(o) == 2 == size(a) else 1))
 
     def fill(o, c):
         rec("v", lambda: g.vector.memset(o[0], c), [], o[1], cost=price(o, o, 0.5))
@@ -180,8 +180,11 @@ def rank_program(g, core, T, topo):
 
     table = [None, []]
 
-    def pe_price(lst):
-        return sum(max(min(64, wide(l)), wide(x)) * (4 if size(x) == 4 else 1) * PE_NS for o, l, x in lst)
+    def lin(key, o, a, scale=1.0, bias=0.0):
+        if key in ON_S:
+            act(o, a, AF.Identity, bias=bias, scale=scale)
+        else:
+            ts(o, a, scale, OP.mult, bias, OP.add)
 
     def mm(lst, start=True, stop=True, each=0):
         def fn():
@@ -191,7 +194,8 @@ def rank_program(g, core, T, topo):
                 else:
                     h = g.tensor.matmul(o[0], l[0], x[0], start and j == 0, stop and j == len(lst) - 1)
             return h
-        rec("pe", fn, [p for o, l, x in lst for p in l[1] + x[1]], [p for o, l, x in lst for p in o[1]], cost=pe_price(lst))
+        rec("pe", fn, [p for o, l, x in lst for p in l[1] + x[1]], [p for o, l, x in lst for p in o[1]],
+            cost=sum(max(min(64, wide(l)), wide(x)) * (4 if size(x) == 4 else 1) * PE_NS for o, l, x in lst))
 
     def mms(lst):
         mm(lst, each=1)
@@ -211,36 +215,32 @@ def rank_program(g, core, T, topo):
                 QU[q].dma_start(o[0], x[0]).then_inc(T.sem[sem], 16)
         rec(q, fn, [p for o, x in pairs for p in x[1]], [p for o, x in pairs for p in o[1]], sem, 16 * len(pairs), 60.0 * len(pairs), lat)
 
-    sent = [0]
+    sent, calls = [0], []
 
     def dst(c):
         a = topo.addr(c)
         return DstId(rid=a[0], pnc=a[1])
 
-    def send(sem, per, src, land):
-        mk = spread(topo, core, others, per)
-        trs = [RemoteDMATransfer(dst_ids=[dst(c)], dma_engine_mask=mk[c][j][0], remote_sem=T.sem[sem],
-                                 src=src(j, T.rank_of(c))[0], dst=land(j, r)[0]) for c in others for j in range(per)]
-        sent[0] += sum(n for c in others for m, n in mk[c])
-        rec("g", lambda: g.remote_dma_fused(trs, local_sem=T.sem.sent), regs(*[src(j, q) for j in range(per) for q in range(8) if q != r]), [], "-", 0, 300.0,
-            after=list(calls.values())[-1:] if len(calls) < 3 else [])
-        calls[sem] = len(ops) - 1
-
-    calls = {}
-
-    def arrive(sem, per, land, lat=5500.0):
-        n = sum(k for c in others for m, k in spread(topo, c, [x for x in cores if x != c], per)[core])
-        rec(None, None, [], regs(*[land(j, q) for j in range(per) for q in range(8) if q != r]), sem, n, 0.0, lat, [calls[sem]])
+    def trade(src, land, lat=5500.0):
+        sem = "a%d" % len(calls)
+        mk = spread(topo, core, others)
+        trs = [RemoteDMATransfer(dst_ids=[dst(c)], dma_engine_mask=mk[c][0], remote_sem=T.sem[sem], src=src(T.rank_of(c))[0], dst=land(r)[0]) for c in others]
+        sent[0] += sum(mk[c][1] for c in others)
+        rec("g", lambda: g.remote_dma_fused(trs, local_sem=T.sem.sent), regs(*[src(q) for q in range(8) if q != r]), [], "-", 0, 300.0,
+            after=calls[-1:] if len(calls) < 3 else [])
+        calls.append(len(ops) - 1)
+        n = sum(spread(topo, c, [x for x in cores if x != c])[core][1] for c in others)
+        rec(None, None, [], regs(*[land(q) for q in range(8) if q != r]), sem, n, 0.0, lat, calls[-1:])
 
     X = lambda n, a, b: (T[n][a:b, :], [])
     col = lambda n, j, p1=128: A(n, j, j + 1, p1=p1)
     PS = lambda i, a=0, b=512, st=1, p1=128: A("p%d" % i, a, b, st, p1=p1)
 
     dma("y", [(D("SKd"), X("k0", 0, 128))])
-    dma("s", [(D("SLd"), X("vl", 0, 128))])
+    dma("s", [(A("Li"), X("vl", 0, 128))])
     dma("y", [(D("SVd"), X("v0", 0, 128))])
     dma("s", [(A("thI", p1=64), X("th", 0, 4))])
-    dma("y", [(D("RKd", r), X("k0", 16 * r, 16 * r + 16)), (D("RLd", r), X("vl", 16 * r, 16 * r + 16))])
+    dma("y", [(D("RKd", r), X("k0", 16 * r, 16 * r + 16))])
     dma("s", [(D("RVd", r), X("v0", 16 * r, 16 * r + 16))])
     iota(col("pi", 0), [[0, 1]], 1, False)
     iota(A("iot"), [[1, 272]])
@@ -248,20 +248,24 @@ def rank_program(g, core, T, topo):
     iota(A("ioq"), [[1, 8], [0, 16]])
     iota(A("ioj"), [[0, 2], [1, 16], [0, 8]])
     iota(A("olf"), [[128, 2], [256, 8]], 1)
-    send("a0", 1, lambda j, q: D("SKd", q), lambda j, q: D("RKd", q))
-    send("a10", 1, lambda j, q: D("SLd", q), lambda j, q: D("RLd", q))
-    send("a1", 1, lambda j, q: D("SVd", q), lambda j, q: D("RVd", q))
-    arrive("a0", 1, lambda j, q: D("RKd", q), 6000.0)
-    arrive("a10", 1, lambda j, q: D("RLd", q), 6000.0)
-    arrive("a1", 1, lambda j, q: D("RVd", q), 6000.0)
-    dma("y", [(A("Kb"), D("RKd"))])
-    dma("y", [(A("Li"), D("RLd"))])
-    dma("y", [(A("Vb"), D("RVd"))])
 
-    p_, q_, k_, kq_, e_, yb_, nyb_, c1_, c2_, cs1_, cs2_, ie_, h0_, h1_ = [col("pc", j) for j in range(14)]
+    p_, q_, k_, kq_, e_, yb_, nyb_, c1_, c2_, cs1_, cs2_, ie_, h0_, h1_, cs3_, xb_ = [col("pc", j) for j in range(16)]
     ts(col("pi", 1), col("pi", 0), 4, OP.arith_shift_right)
     ts(col("pi", 2), col("pi", 0), 15, OP.bitwise_and)
     cp(A("pc", 0, 3), A("pi", 0, 3))
+    io128 = A("iot", 0, 128)
+    ts(A("IDh"), io128, p_, OP.is_equal)
+
+    trade(lambda q: D("SKd", q), lambda q: D("RKd", q), 6000.0)
+    ts(A("Ls"), A("Li"), -2048.0, OP.add)
+    mms([(PS(2, y, 256, 2), A("Ls", 128 * y, 128 * y + 128), A("IDh")) for y in range(2)])
+    cp(A("L0"), PS(2, 0, 256))
+    trade(lambda q: A("L0", 32 * q, 32 * q + 32), lambda q: A("R0", 32 * q, 32 * q + 32), 4500.0)
+    cp(A("R0", 32 * r, 32 * r + 32), A("L0", 32 * r, 32 * r + 32))
+    trade(lambda q: D("SVd", q), lambda q: D("RVd", q), 6000.0)
+    dma("y", [(A("Kb"), D("RKd"))])
+    dma("y", [(A("Vb"), D("RVd"))])
+
     ts(kq_, k_, 8.0, OP.mult, q_, OP.add)
     ts(e_, q_, 16.0, OP.mult, 15.0, OP.add)
     ts(ie_, q_, 16.0, OP.mult, p_, OP.add)
@@ -272,7 +276,6 @@ def rank_program(g, core, T, topo):
     for j in range(8):
         act(A("SEL", 128 * j, 128 * j + 128), A("R16"), AF.Identity, scale=col("mk", 16 + j))
     ts(A("EB"), A("iot", 0, 144), e_, OP.is_equal)
-    io128 = A("iot", 0, 128)
     for n in ("PM", "PM32", "PMb"):
         ts(A(n), io128, kq_, OP.is_equal)
     ts(A("IEh"), A("iot"), -16.0, OP.add, ie_, OP.is_equal)
@@ -281,13 +284,13 @@ def rank_program(g, core, T, topo):
     ts(A("sg"), A("iot", 0, 32), 0.0, OP.mult, -0.5, OP.add)
     ts(A("LE"), A("iok", 0, 128), k_, OP.is_ge)
     ts(A("IDb"), io128, p_, OP.is_equal)
-    ts(A("IDh"), io128, p_, OP.is_equal)
     for n, c in (("I256", 256), ("n512", -512), ("nIh", -1), ("n64", -64), ("n8k", -8192)):
         ts(A(n), A("IDh"), float(c), OP.mult)
     ts(A("wL"), A("iot", 0, 16), 16.0, OP.mult, k_, OP.add)
     for j, (m, c) in enumerate(((1, 128), (1, 128), (1, 256), (1, 384), (2, 0.5))):
         ts(A("cL", 16 * j, 16 * j + 16), A("wL"), float(m), OP.mult, float(c), OP.add)
-    for n, c in (("ID32", 1), ("ISC", 1 / SC), ("I16", 1 / 16), ("Mt", -C8 * SC), ("I64", 64), ("m8I", -8), ("I2k", 2048)):
+    ts(A("cL", 72, 80), A("cL", 72, 80), -256.0, OP.add)
+    for n, c in (("ID32", 1), ("ISC", 1 / SC), ("Mt", -C8 * SC), ("I64", 64), ("m8I", -8), ("I2k", 2048)):
         act(A(n, 0, 128), A("IDb"), scale=float(c))
     act(A("I2k", 128, 256), A("IDb"), scale=2048.0)
     tt(A("LE"), A("LE"), A("BO"), OP.mult)
@@ -295,7 +298,7 @@ def rank_program(g, core, T, topo):
     tt(A("LT"), A("LE"), A("IDb"), OP.subtract)
     act(A("nU"), A("LE"), scale=-1.0)
     tt(A("Bm"), A("LE"), A("Am"), OP.subtract)
-    for n, a, c in (("m8A", "Am", -8), ("m8L", "LT", -8), ("M64", "Am", 64)):
+    for n, a, c in (("m8A", "Am", -8), ("M64", "Am", 64)):
         act(A(n), A(a), scale=float(c))
 
     def mix(o, a, ca, ci):
@@ -313,21 +316,28 @@ def rank_program(g, core, T, topo):
         ts(A("Hs", 128 * h, 128 * h + 128), A("ioq"), c, OP.is_equal, -1.0, OP.mult)
     for k in range(16):
         ts(A("XK", 128 * k, 128 * k + 128), A("BO"), col("mk", k), OP.mult)
+    ts(A("m16"), A("mk", 0, 16), 1.0 / 16, OP.mult)
+    for u in range(2):
+        ts(A("gq"), A("ioq"), 2.0, OP.mult, float(u), OP.add)
+        ts(A("tmp"), A("gq"), k_, OP.is_equal)
+        for q in range(8):
+            act(A("XG", 128 * (2 * q + u), 128 * (2 * q + u + 1)), A("tmp"), AF.Identity, scale=col("mk", 16 + q))
     ts(A("thZ", p1=64), A("iot", 0, 128, p1=64), 0.0, OP.mult)
     ts(A("thZ", 16 * r, 16 * r + 16, p1=64), A("thI", p1=64), -1.0, OP.mult)
     ts(yb_, k_, -15.5, OP.add, 16384.0, OP.mult)
     ts(nyb_, k_, -15.5, OP.add, -16384.0, OP.mult)
+    ts(xb_, k_, -8.0, OP.mult, 136.0, OP.add)
     cp(A("dl", 16, 32), A("olf"))
 
-    def late_constants():
+    def sort_constants():
         ts(c1_, k_, 64.0, OP.mult, -1025.0, OP.add)
         ts(c2_, k_, 64.0, OP.mult, 67648.0, OP.add)
         ts(cs1_, p_, 0.0, OP.is_equal, 4032.0, OP.mult)
         ts(cs2_, p_, 1.0, OP.is_le, 64.0, OP.mult)
         tt(cs1_, cs1_, cs2_, OP.add)
         ts(cs2_, p_, 2.0, OP.is_equal, -2048.0, OP.mult)
-        ts(col("pc", 14), cs1_, -15.0, OP.mult)
-        tt(cs2_, cs2_, col("pc", 14), OP.add)
+        ts(cs3_, cs1_, -15.0, OP.mult)
+        tt(cs2_, cs2_, cs3_, OP.add)
         ts(A("Cs", 0, 256), A("ioj"), cs1_, OP.mult, cs2_, OP.add)
         ts(A("Cs", 256, 512), A("iok"), cs1_, OP.mult, cs2_, OP.add)
         for j, c in enumerate((-64.0, 64.0, -1.0, 1.0)):
@@ -337,15 +347,27 @@ def rank_program(g, core, T, topo):
 
     def spread_T(share):
         for q in range(8):
-            b = (5, 6, 0, 4)[q % 4]
+            b = TB[q % len(TB)]
             mms([(PS(b, e, 512, 2), A("SEL", 128 * q, 128 * q + 128), A("Tc", 256 * e, 256 * e + 256)) for e in range(2)])
             (cp if q in share else act)(A("Tt", 512 * q, 512 * q + 512), PS(b))
 
-    def spread_dma(tab, src, q="y"):
-        dma(q, [(A(tab, p0=16 * a, p1=16 * a + 16), A(src)) for a in range(8)], 4500.0 + 10 * wide(A(src)))
+    def spread_V(t, y):
+        s = (256 * y, 256 * y + 256)
+        mms([(PS(WB[y], 0, 256), A("PM32"), A("Vc", *s)) if t else (PS(WB[y], 0, 256), A("PMb"), A("Vb", *s))])
+        act(A("Vp", *s), PS(WB[y], 0, 256))
+        if y:
+            dma("y", [(A("Vt", p0=16 * a, p1=16 * a + 16), A("Vp")) for a in range(8)], 1.5 * VLAT)
 
     def swap(out, ie, src):
         mm([(out(x, 32 * a), A(ie, 32 * x + 16 - 16 * u, 32 * x + 48 - 16 * u), src(2 * a + u)) for x in range(8) for a in range(4) for u in range(2)], each=2)
+
+    def lists(t):
+        lin("lu", A("lu", 256 * t, 256 * t + 256), PS(2, 0, 256), 1.0, 2048.0)
+        if t < NS:
+            for y in range(2):
+                lin("W2", A("W2", 128 * y, 128 * y + 128), B("p2", 0, 16, 1, 8 * y, 8 * y + 8))
+            swap(lambda q, p: B("p2", q, 16, 8, 0, 16, 1, p, p + 32), "IEh", lambda x: B("W2", x, 16, 8))
+            lin("lv", A("lv", 256 * t, 256 * t + 256), PS(2, 0, 256), 1.0, 2048.0)
 
     def cur_lists(t):
         mm([(PS(1, 432, 512), A("IDh"), A("cL"))] +
@@ -357,18 +379,17 @@ def rank_program(g, core, T, topo):
     def own_K(t):
         act(A("own"), IND(K2(t), A("cl", 80 * t, 80 * t + 32)))
 
+    swap(lambda x, p: B("p2", 0, 16, 1, x, 16, 8, p, p + 32), "IEh", lambda q: A("R0", 32 * q, 32 * q + 32))
+    lists(0)
+    mms([(PS(3, 128 * y, 128 * y + 128), A("R0", y, 256, 2), A("IDh")) for y in range(2)])
+    lin("LcA", A("LcA"), PS(3, 0, 256))
+    cur_lists(0)
     for e in range(2):
         ts(A("Tc", 256 * e, 256 * e + 256), A("Kb", e, 512, 2), EPS, OP.max, -0.5, OP.mult)
-    spread_T((1, 3, 5, 7))
+    spread_T(SHARE_ENDS)
     for e in range(2):
         ts(K2(0, 256 * e, 256 * e + 256), A("Kb", e, 512, 2), EPS, OP.max)
-    cur_lists(0)
     own_K(0)
-    ts(A("LcA"), A("Li"), -2048.0, OP.add)
-    mms([(B("p2", 0, 16, 1, 8 * y, 8 * y + 8), A("LcA", 128 * y, 128 * y + 128), A("PM")) for y in range(2)])
-    cp(A("LcB"), PS(2, 0, 256))
-    swap(lambda x, p: B("p2", 0, 16, 1, x, 16, 8, p, p + 32), "IEh", lambda q: B("LcB", 0, 16, 1, q, 16, 8))
-    ts(A("lu", 0, 256), PS(2, 0, 256), 2048.0, OP.add)
 
     def contract(c):
         mm([(PS(0, 0, 256), A("EB", 15 - k, 143 - k), A("P", 256 * k, 256 * k + 256)) for k in (2 * c, 2 * c + 1)], c == 0, c == 7)
@@ -380,57 +401,55 @@ def rank_program(g, core, T, topo):
         tt(A("tt"), A("fl"), PS(2, 0, 256), OP.mult)
 
     def sort_keys():
-        lin = [(A("M64"), A("fl")), (A("I64"), A("tt"))]
-        mm([(PS(3, 0, 256), l, x) for l, x in [(A("IDh"), A("Lh"))] + lin])
-        mm([(PS(3, 256, 512), l, x) for l, x in [(A("IDh"), A("LcA")), (A("n64"), A("Lh"))] + lin])
-        ts(A("Qs", 0, 256), PS(3, 0, 256), c1_, OP.add)
-        ts(A("Qs", 256, 512), PS(3, 256, 512), c2_, OP.add)
+        pos = [(A("M64"), A("fl")), (A("I64"), A("tt"))]
+        mm([(PS(3, 0, 256), l, x) for l, x in [(A("IDh"), A("Lh"))] + pos])
+        mm([(PS(3, 256, 512), l, x) for l, x in [(A("IDh"), A("LcA")), (A("n64"), A("Lh"))] + pos])
+        lin("Qs", A("Qs", 0, 256), PS(3, 0, 256), 1.0, c1_)
+        lin("Qs", A("Qs", 256, 512), PS(3, 256, 512), 1.0, c2_)
 
     def moves(last):
-        mm([(PS(3, 0, 256), A("ones", 0, 128, p1=32), A("Cs", 256 * last, 256 * last + 256, p1=32))], True, False)
+        b = 5 if last else 3
+        mm([(PS(b, 0, 256), A("ones", 0, 128, p1=32), A("Cs", 256 * last, 256 * last + 256, p1=32))], True, False)
         for j in range(16):
-            a = 512 * (j % 8)
-            n = "R" if j else "Qs"
-            if j in S_MOVES:
+            a, i = 512 * (j % 8), max(j - 1, 0)
+            if j in (S_LAST if last else S_MOVES):
                 act(A("R", a, a + 512), A("Qs"), AF.Relu, bias=col("nb", j))
             elif j:
                 ts(A("R", a, a + 512), A("Qs"), -64.0 * j, OP.add, 0.0, OP.max)
-            lst = []
-            for u in range(2):
-                for y in range(2):
-                    if last:
-                        o = B("p3", 8 * y, 8 * y + 8, 1, max(j - 1, 0), j + 1)
-                        w = A("Wt", 32 + 16 * u, 48 + 16 * u) if j else A("Wt", 33 + 16 * u, 48 + 16 * u, 2)
-                    else:
-                        o = B("p3", 8 * y, 8 * y + 1, 1, 0, 8) if j == 0 else PS(3, 128 * y + 8 * j - 8, 128 * y + 8 * j + 8) if j % 2 else None
-                        w = A("Wt", 16 * u + (0 if j else 8), 16 * u + 16)
-                    l = A(n, a + 256 * u + 128 * y, a + 256 * u + 128 * y + 128)
-                    if o is None:
-                        lst.append((B("p3", 8 * y + j // 2 - 1, 8 * y + j // 2, 1, 8, 16), l, A("Wt", 16 * u, 16 * u + 8)))
-                        lst.append((B("p3", 8 * y + j // 2, 8 * y + j // 2 + 1, 1, 0, 8), l, A("Wt", 16 * u + 8, 16 * u + 16)))
-                    else:
-                        lst.append((o, l, w))
-            mm(lst, False, j == 15)
-        cp(A("Lt"), PS(3, 0, 256))
-        mms([(PS(3, 256 + 128 * y, 384 + 128 * y), A("Lt", 128 * y, 128 * y + 128), A("IDh")) for y in range(2)])
+            mm([(B("p5", y, 16, 2, i, j + 1) if last else PS(3, 128 * y + 8 * i, 128 * y + 8 * j + 8),
+                 A("R" if j else "Qs", a + 256 * u + 128 * y, a + 256 * u + 128 * y + 128),
+                 A("Wt", 32 + 16 * u + (j == 0), 48 + 16 * u, 1 + (j == 0)) if last else A("Wt", 16 * u + 8 * (j == 0), 16 * u + 16))
+                for u in range(2) for y in range(2)], False, j == 15)
+        lin("Lt", A("Lt"), PS(b, 0, 256))
 
-    def weights():
-        for k in range(0, 16, 2):
-            b = 5 + (k // 2) % 2
-            mms([(PS(b, 256 * j, 256 * j + 256), A("XK", 128 * (k + j), 128 * (k + j + 1)), A("x16")) for j in range(2)])
-            act(A("E", 256 * k, 256 * k + 512), PS(b), AF.Exp, bias=-1860.0 / 256, scale=1.0 / 256)
+    def weights(t):
+        for c in range(8):
+            b, y, a = WB[c % len(WB)], c // 4, 4096 * (t % 2) + 512 * c
+            mms([(PS(b, 128 * j, 128 * j + 128), A("XG", 128 * (4 * c % 16 + j), 128 * (4 * c % 16 + j + 1)), A("x16", 128 * y, 128 * y + 128)) for j in range(4)])
+            act(A("E", a, a + 512), PS(b), AF.Exp, bias=-1860.0 / 256, scale=1.0 / 256)
 
-    def new_V(t):
-        act(A("As"), PS(7, 0, 256))
-        act(IND(A("Vc"), A("cl", 80 * t + 64, 80 * t + 80)), A("As"), AF.Tanh)
-
-    def hand_back(sem, n, src, y):
+    def hand_back(n, src, a, b, y, q="y"):
         s, d = "S" + n + "d", "R" + n + "d"
-        dma("y", [(D(s), A(src))])
-        dma("y", [(D(d, r), A(src, p0=16 * r, p1=16 * r + 16))])
-        send(sem, 1, lambda j, q: D(s, q), lambda j, q: D(d, q))
-        arrive(sem, 1, lambda j, q: D(d, q), 2500.0 + 128 * SCRATCH[d][1][2])
-        return lambda: dma("y", [((T[y][:, :], []), D(d))])
+        dma("y", [(D(s), A(src, a, b))])
+        dma("y", [(D(d, r), A(src, a, b, p0=16 * r, p1=16 * r + 16))])
+        trade(lambda q: D(s, q), lambda q: D(d, q), 6600.0)
+        dma(q, [((T[y][:, a:b], []), D(d))])
+
+    def values(t):
+        for c in range(8):
+            a, y, e = 512 * c, c // 4, 4096 * (t % 2) + 512 * c
+            tt(A("Y", a, a + 512), IND(A("Vt"), A("lv", 256 * t + 32 * c, 256 * t + 32 * c + 32)), A("E", e, e + 512), OP.mult)
+            mm([(PS(7, 32 * c + 16 * (j // 2), 32 * c + 16 * (j // 2) + 16), A("Y", a + 128 * j, a + 128 * j + 128), A("m16")) for j in range(4)], each=2)
+            if c % 4 == 3:
+                s = (128 * y, 128 * y + 128)
+                act(A("At", *s), PS(7, *s))
+                mms([(PS(7, 256 + s[0], 256 + s[1]), A("At", *s), A("ID32"))])
+                act(A("As", *s), PS(7, 256 + s[0], 256 + s[1]))
+                act(IND(A("Vc", 256 * y, 256 * y + 256), A("cl", 80 * t + 64 + 8 * y, 80 * t + 72 + 8 * y)), A("As", *s), AF.Tanh)
+                if t < NS - 1:
+                    spread_V(t + 1, y)
+                else:
+                    hand_back("vw"[y], "Vc", 256 * y, 256 * y + 256, "yv")
 
     si = lambda j: A("si", 16 * j, 16 * j + 16)
     lu = lambda t, c: A("lu", 256 * t + 32 * c, 256 * t + 32 * c + 32)
@@ -438,14 +457,10 @@ def rank_program(g, core, T, topo):
         for c in range(8):
             tt(A("P", 512 * c, 512 * c + 512), IND(A("Tt"), lu(t, c)), A("own"), OP.mult)
             contract(c)
-        if t > 0:
-            new_V(t - 1)
-            mms([(PS(4), A("PM32"), A("Vc"))])
-        else:
+        if t == 0:
             act(A("Vc"), A("Vb"))
-            mms([(PS(4), A("PMb"), A("Vb"))])
-        act(A("Vp"), PS(4))
-        spread_dma("Vt", "Vp")
+            spread_V(0, 0)
+            spread_V(0, 1)
         mm([(PS(1, 256, 512), A("ones", 0, 128), A("I2k"))] +
            [(PS(1, 256 + 128 * h, 384 + 128 * h), A("LcA", 128 * h, 128 * h + 128), A("IDh")) for h in range(2)])
         mm([(PS(1, 0, 256), A("ones", 0, 128), A("Mc"))], True, False)
@@ -456,7 +471,7 @@ def rank_program(g, core, T, topo):
         mm([(o, A("aS", a, a + 128), A("ID32")) for o, a in hs], False, False)
         mm([(o, A("tt", a, a + 128), A("Mt")) for o, a in hs], False, True)
         xl = PS(4, 0, 256)
-        mm([(xl, A("m8L"), A("ones")), (xl, A("m8A"), A("fl")), (xl, A("m8I"), A("tt")), (xl, A("ISC"), A("aS"))], True, False)
+        mm([(xl, A("m8A"), A("fl")), (xl, A("m8I"), A("tt")), (xl, A("ISC"), A("aS"))], True, False)
         scan(A("Mx"), A("rm"), PS(1, 0, 256), OP.mult, OP.max)
         tt(A("us"), A("Mx"), PS(1, 0, 256), OP.subtract)
         tt(A("d1"), PS(1, 256, 512), A("us"), OP.subtract)
@@ -464,25 +479,23 @@ def rank_program(g, core, T, topo):
         bs = A("Bx", 15, 256, 16)
         for y in range(2):
             cp(A("bl", y, 16, 2), A("Bx", 128 * y + 15, 128 * y + 128, 16))
+        ts(si(0), A("Mx", 15, 256, 16), 32 / SC, OP.mult, 30.0, OP.add)
+        ts(si(3), si(0), 5, OP.arith_shift_right)
+        ts(A("MR"), si(3), -1860.0, OP.add)
+        mms([(PS(1, 256, 384, p1=16), A("MR"), A("IDh"))])
+        lin("MTs", A("MTs", p1=16), PS(1, 256, 384, p1=16))
+        mm([(PS(4, 128 * y, 128 * y + 128), A("Hs", 128 * y, 128 * y + 128, p1=16), A("MTs", p1=16)) for y in range(2)], False, True)
+        lin("x16", A("x16"), xl, 1.0, xb_)
         act(A("gkB"), IND(A("Tt"), A("bl")), AF.Abs)
         swap(lambda x, p: B("p0", x, 16, 8, 0, 16, 1, p, p + 32), "IEb", lambda q: A("gkB", 32 * q, 32 * q + 32))
-        Kn = K2(t, 512, 768)
-        tt(Kn, PS(0, 0, 256), A("own", 0, 256), OP.max)
+        tt(K2(t, 512, 768), PS(0, 0, 256), A("own", 0, 256), OP.max)
         kn = 768 * (t % 2) + 512
         mm([(PS(1, 384, 400), A("thZ", p1=64), A("IDh", 16 * t, 16 * t + 16, p1=64))] +
            [(PS(1, 384, 400), A("EB", 15 - b, 143 - b), A("KK", kn + b, kn + 256, 16)) for b in range(16)])
         rc = "rc%d" % t
         cp(A(rc, 16 * r, 16 * r + 16), PS(1, 384, 400))
-        send("a%d" % (3 + t), 1, lambda j, q, rc=rc: A(rc, 16 * r, 16 * r + 16), lambda j, q, rc=rc: A(rc, 16 * q, 16 * q + 16))
-        arrive("a%d" % (3 + t), 1, lambda j, q, rc=rc: A(rc, 16 * q, 16 * q + 16))
-        ts(si(0), A("Mx", 15, 256, 16), 32 / SC, OP.mult, 30.0, OP.add)
-        ts(si(3), si(0), 5, OP.arith_shift_right)
-        ts(A("MR"), si(3), -1860.0, OP.add)
-        mms([(PS(1, 256, 384, p1=16), A("MR"), A("IDh"))])
-        cp(A("MTs", p1=16), PS(1, 256, 384, p1=16))
-        mm([(PS(4, 128 * y, 128 * y + 128), A("Hs", 128 * y, 128 * y + 128, p1=16), A("MTs", p1=16)) for y in range(2)], False, True)
-        ts(A("x16"), xl, 136.0, OP.add)
-        weights()
+        trade(lambda q: A(rc, 16 * r, 16 * r + 16), lambda q: A(rc, 16 * q, 16 * q + 16))
+        weights(t)
         act(K2(t + 1), IND(K2(t, 0, 768), A("cl", 80 * t + 32, 80 * t + 64)))
         ts(si(4), bs, 1.0 / 512, OP.mult, -255.5 / 512, OP.add)
         ts(si(1), si(0), 31, OP.bitwise_and, 1, OP.logical_shift_right)
@@ -498,22 +511,23 @@ def rank_program(g, core, T, topo):
         if t == NS - 1:
             for e in range(2):
                 ts(A("Ko", e, 512, 2), K2(NS, 256 * e, 256 * e + 256), 12582912.0, OP.add, -12582912.0, OP.add)
-            last_k = hand_back("a7", "k", "Ko", "yk")
+            hand_back("k", "Ko", 0, 512, "yk", "g")
         if t > 0:
             sort_keys()
             moves(0)
+            mms([(PS(3, 256 + 128 * y, 384 + 128 * y), A("Lt", 128 * y, 128 * y + 128), A("IDh")) for y in range(2)])
         else:
             mms([(PS(3, 256, 512), A("PM"), A("LcA"))])
-            late_constants()
-        cp(A("Lp"), PS(3, 256, 512))
-        spread_dma("VT", "Lp")
+            sort_constants()
+        lin("Lp", A("Lp"), PS(3, 256, 512))
+        dma("y", [(A("VT", p0=16 * a, p1=16 * a + 16), A("Lp")) for a in range(8)], VLAT)
         tt(A("ga"), IND(A("VT"), A("dl")), A("ypn"), OP.min)
         tt(A("LcB"), A("ga", 0, 256), A("ga", 256, 512), OP.max)
         mms([(B("p2", 0, 16, 1, 8 * y, 8 * y + 8), A("LcB", 128 * y, 128 * y + 128), A("PM")) for y in range(2)])
-        ts(A("lu", 256 * t + 256, 256 * t + 512), PS(2, 0, 256), 2048.0, OP.add)
+        lists(t + 1)
         swap(lambda x, p: B("p2", 16 + x, 32, 8, 0, 16, 1, p, p + 32), "IEh", lambda q: B("LcB", q, 16, 8))
-        cp(A("LcA"), PS(2, 256, 512))
-        ts(A("Lh"), PS(2, 256, 512), 1.0 / 64, OP.mult, 1057 - 31.5 / 64, OP.add)
+        lin("LcA", A("LcA"), PS(2, 256, 512))
+        lin("Lh", A("Lh"), PS(2, 256, 512), 1.0 / 64, 1057 - 31.5 / 64)
         sg = [A("sg", 0, 16), A("sg", 16, 32)]
         mm([(PS(1, 400, 432), A("n8k"), A("sg")), (PS(1, 416, 432), A("n8k"), sg[0])], True, False)
         mm([(PS(1, 400 + 16 * e, 416 + 16 * e), A("nIh"), A(rc, 16 * h, 16 * h + 16)) for e in range(2) for h in range(8)], False, True)
@@ -524,96 +538,114 @@ def rank_program(g, core, T, topo):
         if t < NS - 1:
             cur_lists(t + 1)
             own_K(t + 1)
-        spread_T(SHARE)
-        if t == NS - 1:
-            last_k()
-        for c in range(8):
-            s = (512 * c, 512 * c + 512)
-            tt(A("Y", *s), IND(A("Vt"), lu(t, c)), A("E", *s), OP.mult)
-            mm([(PS(7, 0, 256), A("I16"), A("Y", 256 * k, 256 * k + 256)) for k in (2 * c, 2 * c + 1)], c == 0, c == 7)
+        spread_T(SHARE if t < NS - 1 else SHARE_ENDS)
+        values(t)
 
     for c in range(8):
         (cp if c % 2 else act)(A("P", 512 * c, 512 * c + 512), IND(A("Tt"), lu(NS, c)))
         contract(c)
-    new_V(NS - 1)
-    last_v = hand_back("a8", "v", "Vc", "yv")
     marks()
     sort_keys()
     moves(1)
+    trade(lambda q: A("Lt", 32 * q, 32 * q + 32), lambda q: A("Rl", 32 * q, 32 * q + 32))
+    cp(A("Rl", 32 * r, 32 * r + 32), A("Lt", 32 * r, 32 * r + 32))
+    for y in range(2):
+        cp(A("Ls", 128 * y, 128 * y + 128), B("Rl", y, 16, 2))
+    mms([(PS(3, 256 + 128 * y, 384 + 128 * y), A("Ls", 128 * y, 128 * y + 128), A("IDh")) for y in range(2)])
     ts(A("Lo"), PS(3, 256, 512), 2048.0, OP.add)
-    last_l = hand_back("a9", "l", "Lo", "yl")
-    last_v()
-    last_l()
+    dma("s", [((T["yl"][:, :], []), A("Lo"))])
     emit(g, T, QU, ops, sent[0])
 
 
 def arrange(ops):
     n = len(ops)
-    rank = [0.0] * n
-    for i in range(n - 1, -1, -1):
-        o = ops[i]
-        rank[i] += o["cost"] + o["lat"]
-        for d in o["deps"] | o["order"]:
-            rank[d] = max(rank[d], rank[i] + WAKE)
-    deps = [sorted(o["deps"]) for o in ops]
-    order = [sorted(o["order"]) for o in ops]
     cost = [o["cost"] for o in ops]
+    full = [o["cost"] + o["lat"] for o in ops]
+    queue = [o["q"] for o in ops]
+    need = [[(d, True) for d in sorted(o["deps"])] + [(d, False) for d in sorted(o["order"] - o["deps"])] for o in ops]
+    after = [[] for o in ops]
+    for i in range(n):
+        for d, hard in need[i]:
+            after[d].append((i, hard))
 
-    def lay(prio):
+    def fit(taken, t, c):
+        st, en = taken
+        j = len(st)
+        while j > 0 and en[j - 1] > t:
+            j -= 1
+        while j < len(st) and t + c > st[j]:
+            if en[j] > t:
+                t = en[j]
+            j += 1
+        st.insert(j, t)
+        en.insert(j, t + c)
+        return t
+
+    def order(key):
+        key = list(key)
+        for i in range(n):
+            for d, hard in need[i]:
+                if key[d] >= key[i]:
+                    key[i] = key[d] + 1e-3
+        return sorted(range(n), key=lambda j: key[j])
+
+    def forth(key):
         taken, at, end = {q: ([], []) for q in ("pe", "v", "s", "g", "y", "port", "dma")}, [0.0] * n, [0.0] * n
-        for i in sorted(range(n), key=lambda j: (-prio[j], j)):
-            t, c = 0.0, cost[i]
-            for d in deps[i]:
-                t = max(t, end[d] + WAKE)
-            for d in order[i]:
-                t = max(t, at[d] + cost[d])
-            if ops[i]["q"] is not None:
-                st, en = taken[ops[i]["q"]]
-                j = len(st)
-                while j > 0 and en[j - 1] > t:
-                    j -= 1
-                while j < len(st) and t + c > st[j]:
-                    t = max(t, en[j])
-                    j += 1
-                st.insert(j, t)
-                en.insert(j, t + c)
-            at[i], end[i] = t, t + c + ops[i]["lat"]
+        for i in order(key):
+            t = 0.0
+            for d, hard in need[i]:
+                x = end[d] + WAKE if hard else at[d] + cost[d]
+                if x > t:
+                    t = x
+            if queue[i] is not None:
+                t = fit(taken[queue[i]], t, cost[i])
+            at[i], end[i] = t, t + full[i]
             if ops[i]["hold"]:
-                st, en = taken["port" if ops[i]["q"] is None else "dma"]
-                t, c, j = t + c + 1400, ops[i]["hold"], len(st)
-                while j > 0 and en[j - 1] > t:
-                    j -= 1
-                while j < len(st) and t + c > st[j]:
-                    t = max(t, en[j])
-                    j += 1
-                st.insert(j, t)
-                en.insert(j, t + c)
-                end[i] = t + c + 600
-        return max(end), at, end
+                end[i] = fit(taken["port" if queue[i] is None else "dma"], t + cost[i] + 1400, ops[i]["hold"]) + ops[i]["hold"] + 600
+        return max(end) + 1e-2 * sum(end) / n, at, end
 
-    def mend(prio):
-        for i in range(n - 1, -1, -1):
-            for d in deps[i] + order[i]:
-                prio[d] = max(prio[d], prio[i] + 1e-3)
-        return prio
+    def back(at, end):
+        taken, lead = {q: ([], []) for q in ("pe", "v", "s", "g", "y")}, [0.0] * n
+        for i in order(end)[::-1]:
+            t = 0.0 if after[i] else end[i] - at[i] - cost[i]
+            for d, hard in after[i]:
+                x = lead[d] + (end[i] - at[i] - cost[i] + WAKE if hard else 0.0)
+                if x > t:
+                    t = x
+            if queue[i] is not None:
+                t = fit(taken[queue[i]], t, cost[i])
+            lead[i] = t + cost[i]
+        return [-x for x in lead]
+
+    def lean(now, key, tries, kinds):
+        best = now
+        for it in range(tries):
+            p = list(key if kinds else now[1])
+            i = int(rng.integers(0, n))
+            x, reach = float(rng.normal()) * STEP, n if kinds else (0, 8, 30, 60)[int(rng.integers(0, 4))]
+            for j in kin[tags[i % len(tags)] if kinds else ops[i]["tag"]]:
+                if abs(j - i) <= reach:
+                    p[j] += x
+            new = forth(p)
+            if not kinds and it % 10 == 0:
+                new = min(new, forth(back(new[1], new[2])), key=lambda z: z[0])
+            if new[0] <= now[0] + SLACK * (1 - it / tries * (not kinds)) * float(rng.exponential()):
+                now, key = new, p
+                if new[0] < best[0]:
+                    best = new
+        return best
 
     if n not in KEPT:
         rng = np.random.default_rng(0)
-        best, at, end = lay(rank)
-        prio = [-x for x in at]
-        for it in range(TRIES):
-            p = list(prio)
-            for i in rng.integers(0, n, 3):
-                x, reach = float(rng.normal()) * 3000, int(rng.integers(0, 3)) * 30
-                for j in range(max(0, i - reach), min(n, i + reach + 1)):
-                    if ops[j]["tag"] == ops[i]["tag"]:
-                        p[j] += x
-            span, at2, end2 = lay(mend(p))
-            span += 1e-4 * sum(end2) / n
-            if span <= best:
-                best, at, end, prio = span, at2, end2, [-x for x in at2]
-        KEPT[n] = sorted(range(n), key=lambda j: (at[j], j))
-        KEPT["times"] = (best, at, end)
+        rank, kin = [0.0] * n, {}
+        for i in range(n - 1, -1, -1):
+            rank[i] = -full[i] + min([rank[d] - WAKE for d, hard in after[i]], default=0.0)
+            kin.setdefault(ops[i]["tag"], []).append(i)
+        tags = list(kin)
+        best = min([lean(forth(rank), rank, FIRST, True) for _ in range(STARTS)], key=lambda z: z[0])
+        best = lean(best, None, TRIES, False)
+        KEPT[n] = order(best[1])
+        KEPT["times"] = best
     seq = KEPT[n]
     place = {j: k for k, j in enumerate(seq)}
     for j, o in enumerate(ops):

@@ -1,3 +1,4 @@
+import math
 import numpy as np
 from concourse.bass import DstId, RemoteDMATransfer
 from concourse.mybir import AluOpType as OP, ActivationFunctionType as AF
@@ -7,37 +8,43 @@ NS = 4
 SC = float(2 ** 18)
 C8 = 129.0 / 16
 EPS = 2.0 ** -18
-PE_NS, WAKE, VLAT = 0.5, 80.0, 6500.0
-STARTS, FIRST, TRIES, STEP, SLACK, KEPT = 3, 2000, 14000, 4000.0, 400.0, {}
-SHARE, SHARE_ENDS = (3,), (1, 3, 5, 7)
-S_MOVES, S_LAST = (8,), (3, 6, 9, 12, 15)
-ON_S = {"Qs", "Lt", "LcA", "Lh", "x16", "MTs", "Lp", "W2"}
-WB, TB = (5, 6), (4, 0, 1)
+LN64 = math.log(64.0)
+LOW, POW = 16.0, 18
+PE_NS, WAKE, VLAT, LONG = 0.5, 80.0, 6500.0, 5500.0
+STARTS, FIRST, TRIES, STEP, SLACK, KEPT = 4, 3500, 22000, 4000.0, 400.0, {}
+SHARE, SHARE_ENDS, SHARE_VT = (3, 6), (1, 3, 5, 7), ()
+TURNS = 2
+GATHER = (1, 4, 6)
+ON_S = {"D0", "D1", "x16", "MTs", "Lp", "W2", "L0", "Vo", "Lh"}
+WB, TB, VB = (5, 6), (4, 0, 1), (3, 4)
 SCRATCH = {}
 
 
 def _sb(dtype, **kw):
     for n, c in kw.items():
-        SCRATCH[n] = ("sbuf", [128, c], dtype)
+        SCRATCH[n] = ("sbuf", [128] + (list(c) if isinstance(c, tuple) else [c]), dtype)
 
 
-_sb(BF, Tt=4096, P=4096, Kb=512, Vb=512, KK=1536, Tc=512, own=512, fl=256, tt=256, BO=128, EB=144, SEL=1024, R16=128, IDb=128,
-    Mf=128, Mc=256, I2k=256, ones=256, tmp=128, IEb=272, Cs=512, Ko=512, gkB=256)
-_sb(F, Vt=4096, E=8192, Y=4096, Vc=512, Vp=512, VT=2048, Lo=256, aS=256, Mx=256, us=256, d1=256, Bx=256, ypn=512, ga=512, As=256, At=256, Lp=256,
-    iot=272, ioq=128, iok=256, ioj=256, pc=24, mk=24, ID32=128, ISC=128, PM32=128, rm=256, qL=16, wL=16, olf=16, nb=16, m16=16, gq=128)
-_sb(HF, LcA=256, Lh=256, Lt=256, Ls=256, L0=256, R0=256, Qs=512, R=4096, x16=256, XK=2048, XG=2048, PM=128, IDh=128, nIh=128, n64=128, n8k=128,
-    I256=128, n512=128, IEh=272, Hs=256, Wt=64, thZ=128, cL=80, sg=32, MR=16, r16=16, MTs=128, rc0=128, rc1=128, rc2=128, rc3=128)
-_sb(I, Li=256, thI=16, pi=8, si=128)
-_sb(U, lu=1280, lv=1024, bl=16, dl=32, cl=320)
-for _n in ("LcB", "W2", "Rl"):
-    SCRATCH[_n] = ("sbuf", [128, 16, 16], HF)
+SL = (16, 16)
+RING = 4
+_sb(BF, Tt=4096, V0=4096, K0=512, Kb=512, Vb=512, KK=1536, Tc=512, own=640, P=2048, G=768 * RING, diag=1024, fl=SL, tt=SL, sS=256, pw=256, z=512, R=(128, 16), BO=128, EB=144,
+    SEL=1024, SEL0=1024, XK=2048, Hs=512, IE2=272, Mc=256, I2k=256, ones=256, tmp=128, Cs=256, Cz=384, Ko=512, gkB=256, Wt=64, Wt0=64, Q8=8)
+_sb(F, Vt=8192, E=(16, 512), Y=4096, Vc=512, Vp=512, VT=2048, Lf=256, Lo=256, aS=SL, Mx=256, us=256, d1=256, Bx=256, As=256, At=256,
+    iot=272, ioq=128, iok=256, ioa=256, ioj=256, pc=24, mk=24, ID32=128, ISC=128, ID320=128, ISC0=128, rm=256, wL=16, m16=16, iob=128)
+_sb(HF, LcB=SL, Lq=SL, Ly=SL, Lp=SL, Lh=SL, Ls=SL, R0=SL, L0=256, Rl=256, W2=256, ga=256, D=(32, 16), D2=(32, 16), x16=SL, IEh=272, thZ=128, cL=88, sg=32, MR=32,
+    d16=16, MTs=128, rc0=128, rc1=128, rc2=128, rc3=128)
+_sb(I, Li=256, thI=16, pi=8, si=160)
+_sb(U, lu=1280, lv=1024, bl=16, dl=16, dg=8, cl=352)
 PART = {}
-for _n in "Bm nU Mt M64 I64 m8A m8I PMb Am LT LE".split():
-    PART[_n] = 128 * len(PART)
+for _n in "Mf Mt m8A Bc Mf0 Mt0 m8A0 Bm0 Am0 m8I0 n640 I40 n600 Bm nU m8I PMb Am LE nI PMv PMt Iy Iq I4 n60 PMk IDh n64 n8k I256 n512 Ia Ib Ic Id".split():
+    PART[_n] = ("cmat", 128 * len(PART))
 _sb(BF, cmat=128 * len(PART))
 for _i in range(8):
-    SCRATCH["p%d" % _i] = ("psum", [128, 512] if _i in (1, 3) else [128, 32, 16], F)
-for _n, _c, _d in (("K", 64, BF), ("V", 64, BF), ("k", 64, BF), ("v", 32, F), ("w", 32, F)):
+    SCRATCH["p%d" % _i] = ("psum", [128, 512] if _i == 1 else [128, 32, 16], F)
+SCRATCH["SKd"] = ("dram", [8, 128, 64], BF)
+SCRATCH["Vd"] = ("dram", [4, 16, 8, 256], F)
+SCRATCH["V0d"] = ("dram", [16, 2, 8, 256], BF)
+for _n, _c, _d in (("V", 64, BF), ("k", 64, BF), ("v", 32, F), ("w", 32, F)):
     SCRATCH["S" + _n + "d"] = ("dram", [8, 128, _c], _d)
     SCRATCH["R" + _n + "d"] = ("dram", [8, 128, _c], _d)
 SEMAPHORES = ["pe", "v", "s", "g", "sent"] + ["d%d" % i for i in range(48)] + ["a%d" % i for i in range(12)]
@@ -70,23 +77,33 @@ def rank_program(g, core, T, topo):
     cores = list(T.cores)
     others = [c for c in cores if c != core]
     QU = {"pe": g.tensor, "v": g.vector, "s": g.scalar, "g": g, "y": g.sync}
-    ops, acc, nd = [], {}, [0]
+    ops, acc, nd, step, line = [], {}, [0], [-1], ["K"]
 
-    def B(n, r0, r1, rs=1, c0=0, c1=16, cs=1, p0=0, p1=128):
-        cols = [16 * i + j for i in range(r0, r1, rs) for j in range(c0, c1, cs)]
+    def on(name, fn, *a):
+        line.insert(0, name)
+        fn(*a)
+        line.pop(0)
+
+    def B(n, r0, r1, rs=1, c0=0, c1=None, cs=1, p0=0, p1=128):
+        w = SCRATCH[n][1][2]
+        c1 = w if c1 is None else c1
+        cols = [w * i + j for i in range(r0, r1, rs) for j in range(c0, c1, cs)]
         rows = r0 if r1 - r0 <= rs else slice(r0, r1, rs)
         return (T[n][p0:p1, rows, c0 if len(cols) > 1 and c1 - c0 <= cs else slice(c0, c1, cs)], [(n, bits(cols), len(cols))])
 
     def A(n, a=0, b=None, st=1, p0=0, p1=128):
         if n in PART:
-            n, a, b = "cmat", PART[n], PART[n] + 128
+            n, a, b = PART[n][0], PART[n][1] + a, PART[n][1] + (128 if b is None else b)
         shape = SCRATCH[n][1]
         if b is None:
             b = int(np.prod(shape[1:]))
         if len(shape) == 3:
-            if st >= 16:
-                return B(n, a // 16, (b + 15) // 16, st // 16, a % 16, a % 16 + 1, 1, p0, p1)
-            return B(n, a // 16, b // 16, 1, a % 16, 16, st, p0, p1)
+            w = shape[2]
+            if st >= w:
+                return B(n, a // w, (b + w - 1) // w, st // w, a % w, a % w + 1, 1, p0, p1)
+            if a // w == (b - 1) // w:
+                return B(n, a // w, a // w + 1, 1, a % w, (b - 1) % w + 1, st, p0, p1)
+            return B(n, a // w, b // w, 1, a % w, w, st, p0, p1)
         ap = T[n][p0:p1, a:b:st] if st > 1 else T[n][p0:p1, a:b]
         return (ap, [(n, bits(range(a, b, st)) if st > 1 else (1 << b) - (1 << a), len(range(a, b, st)))])
 
@@ -116,7 +133,7 @@ def rank_program(g, core, T, topo):
                 if kind:
                     lst[:] = [e for e in lst if e[0][1] & ~x[1]]
                 lst.append((x, kind, me))
-        ops.append({"q": q, "fn": fn, "deps": deps, "order": order, "sem": sem, "n": n, "cost": cost, "lat": lat, "hold": max(0.0, lat - 2000),
+        ops.append({"q": q, "fn": fn, "deps": deps, "order": order, "sem": sem, "n": n, "cost": cost, "lat": lat, "hold": max(0.0, lat - 2000), "step": step[0], "line": line[0],
                     "tag": (q, wr[0][0] if wr else None, rd[0][0] if rd and q == "pe" else None)})
 
     def wide(x):
@@ -143,17 +160,19 @@ def rank_program(g, core, T, topo):
 
     def ts(o, a, s1, op0, s2=None, op1=None):
         c = price(o, a, 0.5 if size(o) == 2 == size(a) else 1)
+        w, x = outs(o)
         if op1 is None:
-            rec("v", lambda: g.vector.tensor_scalar(o[0], a[0], val(s1), None, op0), regs(a, s1), o[1], cost=c)
+            rec("v", lambda: g.vector.tensor_scalar(o[0], a[0], val(s1), None, op0), regs(a, s1) + x, w, cost=c)
         else:
-            rec("v", lambda: g.vector.tensor_scalar(o[0], a[0], val(s1), val(s2), op0, op1), regs(a, s1, s2), o[1], cost=c)
+            rec("v", lambda: g.vector.tensor_scalar(o[0], a[0], val(s1), val(s2), op0, op1), regs(a, s1, s2) + x, w, cost=c)
 
     def tt(o, a, b, op):
         c = price(o, a, 1 if "psum" in (SCRATCH[a[1][0][0]][0], SCRATCH[b[1][0][0]][0]) else 2)
         rec("v", lambda: g.vector.tensor_tensor(o[0], a[0], b[0], op), regs(a, b), o[1], cost=c)
 
     def cp(o, a):
-        rec("v", lambda: g.vector.tensor_copy(o[0], a[0]), regs(a), o[1], cost=price(o, a, 0.5 if size(o) == 2 == size(a) else 1))
+        w, x = outs(o)
+        rec("v", lambda: g.vector.tensor_copy(o[0], a[0]), regs(a) + x, w, cost=price(o, a, 0.5 if size(o) == 2 == size(a) else 1))
 
     def fill(o, c):
         rec("v", lambda: g.vector.memset(o[0], c), [], o[1], cost=price(o, o, 0.5))
@@ -169,19 +188,15 @@ def rank_program(g, core, T, topo):
         if scale is not None:
             kw["scale"] = val(scale)
         c, after = price(o, a, 1), []
-        if f in (AF.Exp, AF.Tanh):
-            if f != table[0]:
-                c, after = c + 1800, table[1]
-                table[:] = [f, []]
-            else:
-                after = table[1][:1]
-            table[1].append(len(ops))
+        if f == AF.Sigmoid:
+            c, after = c + (0 if table else 1500), table[:1]
+            table.append(len(ops))
         rec("s", lambda: g.scalar.activation(o[0], a[0], f, **kw), regs(a, bias, scale) + x, w, cost=c, after=after)
 
-    table = [None, []]
+    table = []
 
     def lin(key, o, a, scale=1.0, bias=0.0):
-        if key in ON_S:
+        if key is True or key in ON_S:
             act(o, a, AF.Identity, bias=bias, scale=scale)
         else:
             ts(o, a, scale, OP.mult, bias, OP.add)
@@ -235,198 +250,274 @@ def rank_program(g, core, T, topo):
     X = lambda n, a, b: (T[n][a:b, :], [])
     col = lambda n, j, p1=128: A(n, j, j + 1, p1=p1)
     PS = lambda i, a=0, b=512, st=1, p1=128: A("p%d" % i, a, b, st, p1=p1)
+    half = lambda n, y, r0=0: B(n, r0 + 8 * y, r0 + 8 * y + 8)
+
+    def swap(out, src, ie="IEh"):
+        mm([(out(x, 32 * a), A(ie, 32 * x + 16 - 16 * u, 32 * x + 48 - 16 * u), src(2 * a + u)) for x in range(8) for a in range(4) for u in range(2)], each=2)
 
     dma("y", [(D("SKd"), X("k0", 0, 128))])
     dma("s", [(A("Li"), X("vl", 0, 128))])
     dma("y", [(D("SVd"), X("v0", 0, 128))])
     dma("s", [(A("thI", p1=64), X("th", 0, 4))])
-    dma("y", [(D("RKd", r), X("k0", 16 * r, 16 * r + 16))])
+    dma("y", [(A("K0", 64 * r, 64 * r + 64), X("k0", 16 * r, 16 * r + 16))])
     dma("s", [(D("RVd", r), X("v0", 16 * r, 16 * r + 16))])
     iota(col("pi", 0), [[0, 1]], 1, False)
     iota(A("iot"), [[1, 272]])
     iota(A("iok"), [[0, 16], [1, 16]])
     iota(A("ioq"), [[1, 8], [0, 16]])
-    iota(A("ioj"), [[0, 2], [1, 16], [0, 8]])
-    iota(A("olf"), [[128, 2], [256, 8]], 1)
+    iota(A("ioa"), [[0, 32], [1, 8]])
+    iota(A("ioj"), [[0, 4], [1, 8], [0, 8]])
+    iota(A("iob"), [[1, 16], [0, 8]])
 
-    p_, q_, k_, kq_, e_, yb_, nyb_, c1_, c2_, cs1_, cs2_, ie_, h0_, h1_, cs3_, xb_ = [col("pc", j) for j in range(16)]
+    p_, q_, k_, kq_, e_, yb_, pk_, pb_, lb_, cs1_, cs2_, ie_, h0_, h1_, cs3_, xb_, h2_, h3_, od_, kh_, kn_, pb0_ = [col("pc", j) for j in range(22)]
     ts(col("pi", 1), col("pi", 0), 4, OP.arith_shift_right)
     ts(col("pi", 2), col("pi", 0), 15, OP.bitwise_and)
     cp(A("pc", 0, 3), A("pi", 0, 3))
     io128 = A("iot", 0, 128)
-    ts(A("IDh"), io128, p_, OP.is_equal)
+    ts(ie_, q_, 16.0, OP.mult, p_, OP.add)
+    ts(A("IEh"), A("iot"), -16.0, OP.add, ie_, OP.is_equal)
 
-    trade(lambda q: D("SKd", q), lambda q: D("RKd", q), 6000.0)
-    ts(A("Ls"), A("Li"), -2048.0, OP.add)
-    mms([(PS(2, y, 256, 2), A("Ls", 128 * y, 128 * y + 128), A("IDh")) for y in range(2)])
-    cp(A("L0"), PS(2, 0, 256))
+    trade(lambda q: D("SKd", q), lambda q: A("K0", 64 * q, 64 * q + 64), 6300.0)
+    ts(A("Ls"), A("Li"), -2048.0, OP.add, 1.0 / 2048, OP.mult)
+    swap(lambda x, p: B("p2", 2 * x, 2 * x + 2, 1, 0, 16, 1, p, p + 32), lambda q: B("Ls", q, 16, 8))
+    lin("L0", A("L0"), PS(2, 0, 256))
     trade(lambda q: A("L0", 32 * q, 32 * q + 32), lambda q: A("R0", 32 * q, 32 * q + 32), 4500.0)
     cp(A("R0", 32 * r, 32 * r + 32), A("L0", 32 * r, 32 * r + 32))
     trade(lambda q: D("SVd", q), lambda q: D("RVd", q), 6000.0)
-    dma("y", [(A("Kb"), D("RKd"))])
+    dma("y", [(A("Kb", p0=16 * q, p1=16 * q + 16), A("K0", 64 * q, 64 * q + 64)) for q in range(8)])
     dma("y", [(A("Vb"), D("RVd"))])
 
+    for c in range(RING):
+        fill(A("G", 768 * c, 768 * c + 256), 0.0)
+
+    def pick(o, pat, c, base=0, src=None, p1=128):
+        src = src or A("G", 0, wide(o), p1=p1)
+        rec("g", lambda: g.affine_select(o[0], src[0], pat, OP.not_equal, float(c), base, 1), src[1], o[1], cost=170 + 2 * wide(o))
+
+    for j in range(4):
+        pick(A("SEL0", 256 * j, 256 * j + 256), [[-1, 2], [0, 8], [-8, 16]], 1, -2 * j)
+    for j in range(4):
+        pick(A("SEL", 256 * j, 256 * j + 256), [[-16, 2], [0, 8], [-1, 16]], -2, -32 * j)
+    for j in range(8):
+        pick(A("XK", 256 * j, 256 * j + 256), [[-1, 2], [-16, 8], [0, 16]], 1, -2 * j)
+    pick(A("Hs", 0, 256), [[-8, 2], [0, 16], [-1, 8]], -1)
+    pick(A("Hs", 256, 512), [[-8, 2], [-1, 8], [0, 16]], 1, -16)
+    for n, c in (("n64", -64), ("n8k", -8192), ("nI", -1), ("Ia", 1 / 32), ("Ib", -2), ("Ic", 1 / 2048), ("Id", -1 / 32), ("I4", 4), ("n60", -60)):
+        pick(A(n), [[-1, 128]], c)
+    pick(A("PMt"), [[-1, 8], [-8, 16]], 1)
+    pick(A("IE2", 0, 16), [[1, 16]], 0, 1)
+    pick(A("IE2", 16, 272), [[-1, 8], [999, 2], [-8, 16]], 1)
+    for j, (c0, c1) in enumerate(((-1024, 0), (67584, 65), (56320, 56))):
+        o = A("Cz", 128 * j, 128 * j + 128, p1=32)
+        pick(o, [[0, 128]], c0, p1=32)
+        if c1:
+            pick(o, [[0, 128]], c1, -1, o)
+
+    ts(A("IDh"), io128, p_, OP.is_equal)
     ts(kq_, k_, 8.0, OP.mult, q_, OP.add)
     ts(e_, q_, 16.0, OP.mult, 15.0, OP.add)
-    ts(ie_, q_, 16.0, OP.mult, p_, OP.add)
+    ts(col("pi", 3), col("pi", 0), 3, OP.arith_shift_right, 1, OP.bitwise_and)
+    ts(col("pi", 4), col("pi", 0), 16, OP.bitwise_and)
+    cp(A("pc", 18, 20), A("pi", 3, 5))
+    ts(pk_, kh_, -2.0, OP.mult, 16.0, OP.add)
+    ts(kh_, pk_, p_, OP.add)
+    ts(A("dg"), A("iot", 0, 8), 128.0, OP.mult, kq_, OP.add)
+    fill(A("diag"), 0.0)
+    ts(A("PMk"), io128, kh_, OP.is_equal, 2048.0, OP.mult)
+    ts(A("PMv"), io128, kq_, OP.is_equal, 2048.0, OP.mult)
+    for n, c in (("Iy", 1792 / 2048), ("Iq", -3840 / 2048)):
+        ts(A(n), A("IDh"), c, OP.mult)
+    lin("Lq", A("Lq"), A("R0"), 4.0, 1029 - 255.5 / 512)
+    lin("Ly", A("Ly"), A("R0"), 8.0, 1033 - 127.5 / 256)
+    mm([(PS(2, 128 * y, 128 * y + 128), A(m), B(n, y, 16, 2)) for y in range(2) for m, n in (("IDh", "R0"), ("Iy", "Ly"), ("Iq", "Lq"))], each=3)
+    lin("LcB", A("LcB"), PS(2, 0, 256), 1.0, 1025.0)
     ts(A("mk", 0, 16), A("iot", 0, 16), k_, OP.is_equal)
     ts(A("mk", 16, 24), A("iot", 0, 8), q_, OP.is_equal)
-    ts(A("R16"), A("iok", 0, 128), k_, OP.is_equal, -2.0, OP.mult)
+    cp(A("Q8"), A("mk", 16, 24))
     ts(A("BO"), A("ioq"), q_, OP.is_equal)
-    for j in range(8):
-        act(A("SEL", 128 * j, 128 * j + 128), A("R16"), AF.Identity, scale=col("mk", 16 + j))
     ts(A("EB"), A("iot", 0, 144), e_, OP.is_equal)
-    for n in ("PM", "PM32", "PMb"):
-        ts(A(n), io128, kq_, OP.is_equal)
-    ts(A("IEh"), A("iot"), -16.0, OP.add, ie_, OP.is_equal)
-    cp(A("IEb"), A("IEh"))
+    ts(A("PMb"), io128, kq_, OP.is_equal)
     fill(A("ones"), 1.0)
     ts(A("sg"), A("iot", 0, 32), 0.0, OP.mult, -0.5, OP.add)
     ts(A("LE"), A("iok", 0, 128), k_, OP.is_ge)
-    ts(A("IDb"), io128, p_, OP.is_equal)
-    for n, c in (("I256", 256), ("n512", -512), ("nIh", -1), ("n64", -64), ("n8k", -8192)):
-        ts(A(n), A("IDh"), float(c), OP.mult)
+    for n, c in (("I256", 256), ("n512", -512)):
+        act(A(n), A("IDh"), scale=float(c))
     ts(A("wL"), A("iot", 0, 16), 16.0, OP.mult, k_, OP.add)
-    for j, (m, c) in enumerate(((1, 128), (1, 128), (1, 256), (1, 384), (2, 0.5))):
-        ts(A("cL", 16 * j, 16 * j + 16), A("wL"), float(m), OP.mult, float(c), OP.add)
-    ts(A("cL", 72, 80), A("cL", 72, 80), -256.0, OP.add)
-    for n, c in (("ID32", 1), ("ISC", 1 / SC), ("Mt", -C8 * SC), ("I64", 64), ("m8I", -8), ("I2k", 2048)):
-        act(A(n, 0, 128), A("IDb"), scale=float(c))
-    act(A("I2k", 128, 256), A("IDb"), scale=2048.0)
+    for j in range(3):
+        ts(A("cL", 8 * j, 8 * j + 8), A("wL", 0, 8), 128.0, OP.add)
+    for j, (m, c) in enumerate(((1, 128), (1, 256), (1, 384), (2, 0.5))):
+        ts(A("cL", 24 + 16 * j, 40 + 16 * j), A("wL"), float(m), OP.mult, float(c), OP.add)
+    ts(A("cL", 80, 88), A("cL", 80, 88), -256.0, OP.add)
+    for n, c in (("ID32", 1), ("Mt", -C8 * SC), ("I2k", 2048)):
+        act(A(n, 0, 128), A("IDh"), scale=float(c))
+    act(A("I2k", 128, 256), A("IDh"), scale=2048.0)
     tt(A("LE"), A("LE"), A("BO"), OP.mult)
     tt(A("Am"), A("BO"), A("LE"), OP.subtract)
-    tt(A("LT"), A("LE"), A("IDb"), OP.subtract)
-    act(A("nU"), A("LE"), scale=-1.0)
+    ts(kn_, k_, -1.0, OP.mult, -1.0, OP.add)
+    act(A("nU"), A("IDh"), AF.Identity, scale=kn_)
     tt(A("Bm"), A("LE"), A("Am"), OP.subtract)
-    for n, a, c in (("m8A", "Am", -8), ("M64", "Am", 64)):
-        act(A(n), A(a), scale=float(c))
+    tt(A("Bm"), A("Bm"), A("nU"), OP.add)
+    act(A("ISC"), A("PMb"), scale=1 / SC)
+    act(A("m8I"), A("PMb"), scale=-8.0)
+    ts(A("m8A"), A("iob"), k_, OP.is_lt, -8.0, OP.mult)
+    ts(A("tmp"), A("ioa", 0, 128), q_, OP.is_equal)
+    tt(A("m8A"), A("m8A"), A("tmp"), OP.mult)
 
-    def mix(o, a, ca, ci):
-        ts(o, a, ca, OP.mult)
-        ts(A("tmp"), A("IDb"), ci, OP.mult)
-        tt(o, o, A("tmp"), OP.add)
-    mix(A("Mf"), A("Am"), -C8 * SC, SC / 32)
-    mix(A("Mc", 0, 128), A("LT"), -C8 * SC, 136 * SC)
-    cp(A("Mc", 128, 256), A("Mc", 0, 128))
+    for o, a, ci in ((A("Mf"), "Am", SC / 32), (A("Mc", 0, 128), "LE", 136 * SC), (A("Mc", 128, 256), "LE", 136 * SC)):
+        act(o, A(a), scale=-C8 * SC)
+        pick(o, [[-1, 128]], ci, 0, o)
+    ts(A("Bc"), A("m8A"), 0.25, OP.mult)
+    tt(A("Bc"), A("Bc"), A("tmp"), OP.add)
+    act(A("nU"), A("PMb"), AF.Identity, scale=kn_)
+    tt(A("Bc"), A("Bc"), A("nU"), OP.add)
+    mms([(PS(3), A("PMb"), A("Mf", 0, 512))])
+    act(A("Mf0", 0, 512), PS(3))
+    act(A("Am0"), A("m8A0"), scale=-0.125)
+    act(A("m8I0"), A("IDh"), scale=-8.0)
+    act(A("ISC0"), A("IDh"), scale=1 / SC)
+    act(A("ID320"), A("PMt"))
+    for n, c in (("n640", -64), ("I40", 4), ("n600", -60)):
+        pick(A(n), [[-1, 16], [-16, 8]], c)
+    M = lambda n, y, *a: A(n if y else {"IDh": "PMb", "I2k": "PMv"}.get(n, n + "0"), *a)
     ts(A("rm"), A("iok"), 0.0, OP.not_equal)
-    cp(A("qL", 0, 8), A("iot", 0, 8))
-    cp(A("qL", 8, 16), A("iot", 0, 8))
-    for h, c in enumerate((h0_, h1_)):
-        ts(c, p_, -8.0 * h, OP.add)
-        ts(A("Hs", 128 * h, 128 * h + 128), A("ioq"), c, OP.is_equal, -1.0, OP.mult)
-    for k in range(16):
-        ts(A("XK", 128 * k, 128 * k + 128), A("BO"), col("mk", k), OP.mult)
-    ts(A("m16"), A("mk", 0, 16), 1.0 / 16, OP.mult)
-    for u in range(2):
-        ts(A("gq"), A("ioq"), 2.0, OP.mult, float(u), OP.add)
-        ts(A("tmp"), A("gq"), k_, OP.is_equal)
-        for q in range(8):
-            act(A("XG", 128 * (2 * q + u), 128 * (2 * q + u + 1)), A("tmp"), AF.Identity, scale=col("mk", 16 + q))
+    ts(A("m16"), A("mk", 0, 16), math.exp(LOW) / 8, OP.mult)
     ts(A("thZ", p1=64), A("iot", 0, 128, p1=64), 0.0, OP.mult)
     ts(A("thZ", 16 * r, 16 * r + 16, p1=64), A("thI", p1=64), -1.0, OP.mult)
-    ts(yb_, k_, -15.5, OP.add, 16384.0, OP.mult)
-    ts(nyb_, k_, -15.5, OP.add, -16384.0, OP.mult)
-    ts(xb_, k_, -8.0, OP.mult, 136.0, OP.add)
-    cp(A("dl", 16, 32), A("olf"))
+    ts(yb_, k_, -15.5, OP.add)
+    ts(col("pi", 5), col("pi", 0), 120, OP.bitwise_and)
+    ts(xb_, col("pi", 5), -1.0, OP.mult, 136.0, OP.add)
 
     def sort_constants():
-        ts(c1_, k_, 64.0, OP.mult, -1025.0, OP.add)
-        ts(c2_, k_, 64.0, OP.mult, 67648.0, OP.add)
-        ts(cs1_, p_, 0.0, OP.is_equal, 4032.0, OP.mult)
-        ts(cs2_, p_, 1.0, OP.is_le, 64.0, OP.mult)
-        tt(cs1_, cs1_, cs2_, OP.add)
-        ts(cs2_, p_, 2.0, OP.is_equal, -2048.0, OP.mult)
-        ts(cs3_, cs1_, -15.0, OP.mult)
-        tt(cs2_, cs2_, cs3_, OP.add)
-        ts(A("Cs", 0, 256), A("ioj"), cs1_, OP.mult, cs2_, OP.add)
-        ts(A("Cs", 256, 512), A("iok"), cs1_, OP.mult, cs2_, OP.add)
-        for j, c in enumerate((-64.0, 64.0, -1.0, 1.0)):
-            ts(A("Wt", 8 * j, 8 * j + 8), A("mk", 16, 24), c, OP.mult)
-            ts(A("Wt", 32 + 16 * (j // 2) + j % 2, 48 + 16 * (j // 2), 2), A("mk", 16, 24), c, OP.mult)
-        ts(A("nb"), A("iot", 0, 16), -64.0, OP.mult)
+        ts(pb_, k_, -float(POW), OP.add, LN64, OP.mult)
+        even, odd = (65 * (2048 + 64 * 1025) - 2048) / 2048, -(65 * 1025 + 2048) / 2048
+        ts(lb_, od_, odd - even, OP.mult, even, OP.add)
+        row0, row1 = h0_, h1_
+        ts(row0, p_, 0.0, OP.is_equal)
+        ts(row1, p_, 1.0, OP.is_equal)
+        ts(cs1_, row1, -2.0, OP.mult)
+        ts(cs1_, row0, 8192.0, OP.mult, cs1_, OP.add)
+        ts(cs2_, row1, -65.0, OP.mult)
+        ts(cs2_, row0, -59392.0, OP.mult, cs2_, OP.add)
+        ts(A("Cs"), A("ioj"), cs1_, OP.mult, cs2_, OP.add)
+        for a in range(8):
+            ts(A("Wt", 8 * a, 8 * a + 8), A("mk", 16, 24), 8.0 ** (POW - 2 * a), OP.mult, 8.0 ** (POW - 2 * a), OP.mult)
+        mms([(PS(3, 0, 64), A("PMb"), A("Wt"))])
+        act(A("Wt0"), PS(3, 0, 64))
+        ts(pb0_, xb_, -LN64 / 8, OP.mult, (17 - POW) * LN64, OP.add)
+        act(B("D2", 0, 32, 1, 8, 16), A("ones"), scale=0.0)
 
-    def spread_T(share):
+    def spread_T(share, first=0):
         for q in range(8):
             b = TB[q % len(TB)]
-            mms([(PS(b, e, 512, 2), A("SEL", 128 * q, 128 * q + 128), A("Tc", 256 * e, 256 * e + 256)) for e in range(2)])
+            y, q0 = q // 4, 2 * (q % 4)
+            if first:
+                mms([(PS(b, 256 * j + 64 * h, 256 * j + 64 * h + 64), A("SEL0", 128 * (4 * y + h), 128 * (4 * y + h + 1)), A("Tc", 64 * (q0 + j), 64 * (q0 + j + 1)))
+                     for j in range(2) for h in range(4)])
+            else:
+                mms([(PS(b, 256 * j + e, 256 * j + 256, 2), A("SEL", 128 * (q0 + j), 128 * (q0 + j + 1)), A("Tc", 256 * e + 128 * y, 256 * e + 128 * y + 128))
+                     for j in range(2) for e in range(2)])
             (cp if q in share else act)(A("Tt", 512 * q, 512 * q + 512), PS(b))
 
     def spread_V(t, y):
-        s = (256 * y, 256 * y + 256)
-        mms([(PS(WB[y], 0, 256), A("PM32"), A("Vc", *s)) if t else (PS(WB[y], 0, 256), A("PMb"), A("Vb", *s))])
-        act(A("Vp", *s), PS(WB[y], 0, 256))
-        if y:
-            dma("y", [(A("Vt", p0=16 * a, p1=16 * a + 16), A("Vp")) for a in range(8)], 1.5 * VLAT)
+        j, o = 2 * (t % 2) + y, 4096 * (t % 2) + 2048 * y
+        dma("y", [((T["Vd"][j, :, q, :], D("Vd", j)[1]), A("Vp", 256 * y, 256 * y + 256, p0=16 * q, p1=16 * q + 16)) for q in range(8)])
+        dma("y", [(A("Vt", o, o + 2048, p0=16 * a, p1=16 * a + 16), D("Vd", j)) for a in range(8)], LONG)
 
-    def swap(out, ie, src):
-        mm([(out(x, 32 * a), A(ie, 32 * x + 16 - 16 * u, 32 * x + 48 - 16 * u), src(2 * a + u)) for x in range(8) for a in range(4) for u in range(2)], each=2)
+    def first_V():
+        dma("y", [((T["V0d"][:, :, q, :], D("V0d")[1]), D("RVd", q)) for q in range(8)])
+        dma("y", [(A("V0", p0=16 * a, p1=16 * a + 16), D("V0d")) for a in range(8)], LONG)
 
     def lists(t):
+        mms([(PS(2, 128 * y, 128 * y + 128), half("LcB", y), A(("PMv", "PMk")[y])) for y in range(2)])
         lin("lu", A("lu", 256 * t, 256 * t + 256), PS(2, 0, 256), 1.0, 2048.0)
         if t < NS:
-            for y in range(2):
-                lin("W2", A("W2", 128 * y, 128 * y + 128), B("p2", 0, 16, 1, 8 * y, 8 * y + 8))
-            swap(lambda q, p: B("p2", q, 16, 8, 0, 16, 1, p, p + 32), "IEh", lambda x: B("W2", x, 16, 8))
+            mms([(B("p2", 16 + y, 32, 2), half("LcB", y), A("PMv")) for y in range(2)])
+            lin("W2", A("W2"), PS(2, 256, 512))
+            swap(lambda q, p: B("p2", q, 16, 8, 0, 16, 1, p, p + 32), lambda x: A("W2", 32 * x, 32 * x + 32))
             lin("lv", A("lv", 256 * t, 256 * t + 256), PS(2, 0, 256), 1.0, 2048.0)
+        else:
+            lin("Lq", A("Lq"), A("LcB"), 1.0, 1026 - 1023.5 / 2048)
+            lin("Ly", A("Ly"), A("LcB"), 8.0, 1033 - 127.5 / 256)
+        if t:
+            lin("Lh", A("Lh"), A("LcB"), 32.0, 1057 - 31.5 / 64)
 
     def cur_lists(t):
-        mm([(PS(1, 432, 512), A("IDh"), A("cL"))] +
-           [(PS(1, 432 + 16 * j, 448 + 16 * j), A(n), A("sg", 0, 16)) for j, n in enumerate(("I256", "I256", "n512", "I256", "IDh"))])
-        cp(A("cl", 80 * t, 80 * t + 80), PS(1, 432, 512))
+        mm([(PS(1, 256, 344), A("IDh"), A("cL"))] + [(PS(1, 256 + 8 * j, 264 + 8 * j), A("I256"), A("sg", 0, 8)) for j in range(3)] +
+           [(PS(1, 280 + 16 * j, 296 + 16 * j), A(n), A("sg", 0, 16)) for j, n in enumerate(("I256", "n512", "I256", "IDh"))])
+        cp(A("cl", 88 * t, 88 * t + 88), PS(1, 256, 344))
 
     K2 = lambda t, a=0, b=512: A("KK", 768 * (t % 2) + a, 768 * (t % 2) + b)
 
     def own_K(t):
-        act(A("own"), IND(K2(t), A("cl", 80 * t, 80 * t + 32)))
+        act(A("own", 512, 640), IND(K2(t), A("cl", 88 * t + 32, 88 * t + 40)))
+        cp(IND(A("diag"), A("dg")), A("own", 512, 640))
+        act(A("own", 0, 512), IND(K2(t), A("cl", 88 * t, 88 * t + 32)))
 
-    swap(lambda x, p: B("p2", 0, 16, 1, x, 16, 8, p, p + 32), "IEh", lambda q: A("R0", 32 * q, 32 * q + 32))
+    own = lambda t: A("own", 384, 640)
+
     lists(0)
-    mms([(PS(3, 128 * y, 128 * y + 128), A("R0", y, 256, 2), A("IDh")) for y in range(2)])
-    lin("LcA", A("LcA"), PS(3, 0, 256))
     cur_lists(0)
-    for e in range(2):
-        ts(A("Tc", 256 * e, 256 * e + 256), A("Kb", e, 512, 2), EPS, OP.max, -0.5, OP.mult)
-    spread_T(SHARE_ENDS)
+    ts(A("Tc"), A("K0"), EPS, OP.max)
+    spread_T(SHARE_ENDS, 1)
     for e in range(2):
         ts(K2(0, 256 * e, 256 * e + 256), A("Kb", e, 512, 2), EPS, OP.max)
     own_K(0)
 
-    def contract(c):
-        mm([(PS(0, 0, 256), A("EB", 15 - k, 143 - k), A("P", 256 * k, 256 * k + 256)) for k in (2 * c, 2 * c + 1)], c == 0, c == 7)
+    def scores(t):
+        for a in range(4):
+            o = 768 * (a % RING)
+            if t < NS:
+                tt(A("P", 512 * a, 512 * a + 512), IND(A("Tt"), lu(t, a)), A("own", 0, 512), OP.mult)
+            else:
+                cp(A("P", 512 * a, 512 * a + 512), IND(A("Tt"), lu(t, a)))
+            act(A("G", o + 256, o + 768), IND(A("Tt"), lu(t, 4 + a)))
+            k = lambda u, w: A("diag", 128 * (2 * a + u) + 8 * w, 128 * (2 * a + u) + 8 * w + 8) if t < NS else A("Q8")
+            mm([(B("p0", 8, 16, 1, w, w + 1, 1, 32 * a, 32 * a + 16 + 16 * u), A("G", o + 512 * (1 - u) + w, o + 768 - 256 * u, 16), k(u, w))
+                for w in range(16) for u in (1, 0)], each=2)
+        mms([(B("p0", 0, 8, 1, w, w + 1), A("P", w, 2048, 16), A("Q8")) for w in range(16)])
 
     def marks():
-        mm([(PS(2, 0, 256), A("nU"), A("ones"))], True, False)
         ts(A("fl"), PS(0, 0, 256), 0.0, OP.is_lt)
-        mm([(PS(2, 0, 256), A("Bm"), A("fl"))], False, True)
+        mms([(half("p2", y), M("Bm", y), half("fl", y)) for y in range(2)])
         tt(A("tt"), A("fl"), PS(2, 0, 256), OP.mult)
 
-    def sort_keys():
-        pos = [(A("M64"), A("fl")), (A("I64"), A("tt"))]
-        mm([(PS(3, 0, 256), l, x) for l, x in [(A("IDh"), A("Lh"))] + pos])
-        mm([(PS(3, 256, 512), l, x) for l, x in [(A("IDh"), A("LcA")), (A("n64"), A("Lh"))] + pos])
-        lin("Qs", A("Qs", 0, 256), PS(3, 0, 256), 1.0, c1_)
-        lin("Qs", A("Qs", 256, 512), PS(3, 256, 512), 1.0, c2_)
+    def digits(last=0):
+        one = A("ones", p1=32)
+        mm([(PS(3, 0, 256), A("Cz", 256 * last, 256 * last + 128, p1=32), one)] +
+           [(half("p3", y), M(m, y), half(n, y)) for m, n in [("IDh", "Lh")] + [("I4", "Ly"), ("n60", "Lq")] * last for y in range(2)])
+        mm([(PS(3, 256, 512), A("Cz", 128, 256, p1=32), one)] +
+           [(half("p3", y, 16), M(m, y, 0, 128), half(n, y)) for m, n in (("I2k", "LcB"), ("n64", "Lh")) for y in range(2)])
 
-    def moves(last):
-        b = 5 if last else 3
-        mm([(PS(b, 0, 256), A("ones", 0, 128, p1=32), A("Cs", 256 * last, 256 * last + 256, p1=32))], True, False)
-        for j in range(16):
-            a, i = 512 * (j % 8), max(j - 1, 0)
-            if j in (S_LAST if last else S_MOVES):
-                act(A("R", a, a + 512), A("Qs"), AF.Relu, bias=col("nb", j))
-            elif j:
-                ts(A("R", a, a + 512), A("Qs"), -64.0 * j, OP.add, 0.0, OP.max)
-            mm([(B("p5", y, 16, 2, i, j + 1) if last else PS(3, 128 * y + 8 * i, 128 * y + 8 * j + 8),
-                 A("R" if j else "Qs", a + 256 * u + 128 * y, a + 256 * u + 128 * y + 128),
-                 A("Wt", 32 + 16 * u + (j == 0), 48 + 16 * u, 1 + (j == 0)) if last else A("Wt", 16 * u + 8 * (j == 0), 16 * u + 16))
-                for u in range(2) for y in range(2)], False, j == 15)
-        lin("Lt", A("Lt"), PS(b, 0, 256))
+    def powers():
+        mm([(half("p0", y, 16), M("Am", y), half("fl", y)) for y in range(2)] + [(PS(0, 256, 512), A("IDh"), A("tt"))])
+        for y in range(2):
+            act(A("pw", 128 * y, 128 * y + 128), half("p0", y, 16), AF.Sigmoid, bias=(pb0_, pb_)[y], scale=LN64)
+
+    def sort(last=0):
+        for h in range(2):
+            tt(A("z", 256 * h, 256 * h + 256), PS(3, 256 * h, 256 * h + 256), A("pw"), OP.mult)
+        mm([(PS(3, 0, 256), A("ones", 0, 128, p1=32), A("Cs", p1=32))], True, False)
+        for a in range(8):
+            o = 32 * (a % 4)
+            ts(B("R", o, o + 32), A("z"), 64.0 ** (2 * a - POW), OP.max, 64.0 ** (2 * a + 2 - POW), OP.min)
+            mm([(PS(3, 128 * h + 64 * y + 8 * a, 128 * h + 64 * y + 8 * a + 8), half("R", y, o + 16 * h), M("Wt", y, 8 * a, 8 * a + 8))
+                for h in range(2) for y in range(2)], False, a == 7)
+        lin("D1", B("D", 0, 32, 1, 8, 16), PS(3, 0, 256), 1.0 / 64, 1057 - 31.5 / 64)
+        lin("D0", B("D", 0, 32, 1, 0, 8), PS(3, 0, 256))
+        cp(B("D2", 0, 32, 1, 0, 8), B("D", 0, 32, 1, 8, 16))
+        mm([(B("p4", 16 + y, 32, 2) if last else half("p4", y, 16), half(d, y, 16 * h), A(n))
+            for y in range(2) for h, d, n in ((0, "D2", "Ib"), (1, "D2", "Id"), (0, "D", "Ia"), (1, "D", "Ic"))], each=4)
+        if not last:
+            lin("Lp", A("Lf"), PS(4, 256, 512), 1.0, lb_)
+        lin("Lp", A("Lp"), PS(4, 256, 512), 1.0, lb_)
 
     def weights(t):
+        lin("x16", A("x16"), PS(4, 0, 256), 1.0, xb_)
         for c in range(8):
-            b, y, a = WB[c % len(WB)], c // 4, 4096 * (t % 2) + 512 * c
-            mms([(PS(b, 128 * j, 128 * j + 128), A("XG", 128 * (4 * c % 16 + j), 128 * (4 * c % 16 + j + 1)), A("x16", 128 * y, 128 * y + 128)) for j in range(4)])
-            act(A("E", a, a + 512), PS(b), AF.Exp, bias=-1860.0 / 256, scale=1.0 / 256)
+            b, y, j, u = WB[c % len(WB)], c // 4, c // 2 % 2, c % 2
+            mms([(B("p%d" % b, x, 32, 8), A("XK", 128 * (8 * u + x), 128 * (8 * u + x + 1)), B("x16", 8 * y + j, 8 * y + 8, 2)) for x in range(8)])
+            o = 8 * (t % 2) + 4 * y
+            act(B("E", o, o + 4, 1, 256 * j + 128 * u, 256 * j + 128 * u + 128), PS(b), AF.Sigmoid, bias=-1860.0 / 256 - LOW, scale=1.0 / 256)
 
     def hand_back(n, src, a, b, y, q="y"):
         s, d = "S" + n + "d", "R" + n + "d"
@@ -437,100 +528,104 @@ def rank_program(g, core, T, topo):
 
     def values(t):
         for c in range(8):
-            a, y, e = 512 * c, c // 4, 4096 * (t % 2) + 512 * c
-            tt(A("Y", a, a + 512), IND(A("Vt"), A("lv", 256 * t + 32 * c, 256 * t + 32 * c + 32)), A("E", e, e + 512), OP.mult)
+            a, y, e = 512 * c, c // 4, 8 * (t % 2) + c
+            tt(A("Y", a, a + 512), IND(A("Vt", 4096 * (t % 2), 4096 * (t % 2) + 4096) if t else A("V0"), A("lv", 256 * t + 32 * c, 256 * t + 32 * c + 32)), B("E", e, e + 1), OP.mult)
             mm([(PS(7, 32 * c + 16 * (j // 2), 32 * c + 16 * (j // 2) + 16), A("Y", a + 128 * j, a + 128 * j + 128), A("m16")) for j in range(4)], each=2)
             if c % 4 == 3:
                 s = (128 * y, 128 * y + 128)
                 act(A("At", *s), PS(7, *s))
                 mms([(PS(7, 256 + s[0], 256 + s[1]), A("At", *s), A("ID32"))])
                 act(A("As", *s), PS(7, 256 + s[0], 256 + s[1]))
-                act(IND(A("Vc", 256 * y, 256 * y + 256), A("cl", 80 * t + 64 + 8 * y, 80 * t + 72 + 8 * y)), A("As", *s), AF.Tanh)
+                act(IND(A("Vc", 256 * y, 256 * y + 256), A("cl", 88 * t + 72 + 8 * y, 88 * t + 80 + 8 * y)), A("As", *s), AF.Sigmoid)
+                lin("Vo", A("Vp", 256 * y, 256 * y + 256), A("Vc", 256 * y, 256 * y + 256), 2.0, -1.0)
                 if t < NS - 1:
                     spread_V(t + 1, y)
                 else:
-                    hand_back("vw"[y], "Vc", 256 * y, 256 * y + 256, "yv")
+                    hand_back("vw"[y], "Vp", 256 * y, 256 * y + 256, "yv")
 
     si = lambda j: A("si", 16 * j, 16 * j + 16)
     lu = lambda t, c: A("lu", 256 * t + 32 * c, 256 * t + 32 * c + 32)
     for t in range(NS):
-        for c in range(8):
-            tt(A("P", 512 * c, 512 * c + 512), IND(A("Tt"), lu(t, c)), A("own"), OP.mult)
-            contract(c)
+        step[0] = t
+        scores(t)
         if t == 0:
-            act(A("Vc"), A("Vb"))
-            spread_V(0, 0)
-            spread_V(0, 1)
+            lin(True, A("Vc"), A("Vb"), 0.5, 0.5)
+            first_V()
+        else:
+            digits()
         mm([(PS(1, 256, 512), A("ones", 0, 128), A("I2k"))] +
-           [(PS(1, 256 + 128 * h, 384 + 128 * h), A("LcA", 128 * h, 128 * h + 128), A("IDh")) for h in range(2)])
+           [(PS(1, 256 + 128 * h, 384 + 128 * h), half("LcB", h), A("I2k", 0, 128)) for h in range(2)])
         mm([(PS(1, 0, 256), A("ones", 0, 128), A("Mc"))], True, False)
         marks()
         act(A("aS"), PS(0, 0, 256), AF.Abs, scale=SC)
-        hs = [(PS(1, 128 * h, 128 * h + 128), 128 * h) for h in range(2)]
-        mm([(o, A("fl", a, a + 128), A("Mf")) for o, a in hs], False, False)
-        mm([(o, A("aS", a, a + 128), A("ID32")) for o, a in hs], False, False)
-        mm([(o, A("tt", a, a + 128), A("Mt")) for o, a in hs], False, True)
-        xl = PS(4, 0, 256)
-        mm([(xl, A("m8A"), A("fl")), (xl, A("m8I"), A("tt")), (xl, A("ISC"), A("aS"))], True, False)
+        hs = [(PS(1, 128 * h, 128 * h + 128), h) for h in range(2)]
+        mm([(o, half("fl", h), M("Mf", h)) for o, h in hs], False, False)
+        mm([(o, half("aS", h), M("ID32", h)) for o, h in hs], False, False)
+        mm([(o, half("tt", h), M("Mt", h)) for o, h in hs], False, True)
+        if t > 0:
+            on("L", powers)
+        mm([(PS(4, 128 * y, 128 * y + 128), M(m, y), half(n, y)) for m, n in (("m8A", "fl"), ("m8I", "tt"), ("ISC", "aS")) for y in range(2)], True, False)
         scan(A("Mx"), A("rm"), PS(1, 0, 256), OP.mult, OP.max)
         tt(A("us"), A("Mx"), PS(1, 0, 256), OP.subtract)
         tt(A("d1"), PS(1, 256, 512), A("us"), OP.subtract)
         scan(A("Bx"), A("us"), A("d1"), OP.min, OP.max)
         bs = A("Bx", 15, 256, 16)
-        for y in range(2):
-            cp(A("bl", y, 16, 2), A("Bx", 128 * y + 15, 128 * y + 128, 16))
-        ts(si(0), A("Mx", 15, 256, 16), 32 / SC, OP.mult, 30.0, OP.add)
-        ts(si(3), si(0), 5, OP.arith_shift_right)
-        ts(A("MR"), si(3), -1860.0, OP.add)
-        mms([(PS(1, 256, 384, p1=16), A("MR"), A("IDh"))])
-        lin("MTs", A("MTs", p1=16), PS(1, 256, 384, p1=16))
-        mm([(PS(4, 128 * y, 128 * y + 128), A("Hs", 128 * y, 128 * y + 128, p1=16), A("MTs", p1=16)) for y in range(2)], False, True)
-        lin("x16", A("x16"), xl, 1.0, xb_)
+        cp(A("bl"), bs)
         act(A("gkB"), IND(A("Tt"), A("bl")), AF.Abs)
-        swap(lambda x, p: B("p0", x, 16, 8, 0, 16, 1, p, p + 32), "IEb", lambda q: A("gkB", 32 * q, 32 * q + 32))
-        tt(K2(t, 512, 768), PS(0, 0, 256), A("own", 0, 256), OP.max)
+        tt(K2(t, 512, 768), A("gkB"), own(t), OP.max)
         kn = 768 * (t % 2) + 512
         mm([(PS(1, 384, 400), A("thZ", p1=64), A("IDh", 16 * t, 16 * t + 16, p1=64))] +
            [(PS(1, 384, 400), A("EB", 15 - b, 143 - b), A("KK", kn + b, kn + 256, 16)) for b in range(16)])
         rc = "rc%d" % t
         cp(A(rc, 16 * r, 16 * r + 16), PS(1, 384, 400))
         trade(lambda q: A(rc, 16 * r, 16 * r + 16), lambda q: A(rc, 16 * q, 16 * q + 16))
-        weights(t)
-        act(K2(t + 1), IND(K2(t, 0, 768), A("cl", 80 * t + 32, 80 * t + 64)))
-        ts(si(4), bs, 1.0 / 512, OP.mult, -255.5 / 512, OP.add)
+        ts(si(0), A("Mx", 15, 256, 16), 32 / SC, OP.mult, 30.0, OP.add)
+        ts(si(3), si(0), 5, OP.arith_shift_right)
+        ts(A("MR", 0, 16), si(3), -1860.0, OP.add)
+        ts(si(7), bs, 0.5, OP.mult, -0.25, OP.add)
+        ts(si(4), si(7), 7, OP.arith_shift_right, 7, OP.bitwise_and)
         ts(si(1), si(0), 31, OP.bitwise_and, 1, OP.logical_shift_right)
         ts(si(2), si(0), 1, OP.bitwise_and)
-        tt(si(5), si(4), A("qL"), OP.not_equal)
+        ts(si(5), si(4), q_, OP.not_equal)
         tt(si(6), si(5), si(2), OP.is_gt)
-        tt(A("r16"), si(6), si(1), OP.mult)
-        ts(si(7), bs, 0.5, OP.mult, -0.25, OP.add)
-        cp(A("dl", 0, 16), si(7))
-        mms([(PS(2, b, 256, 16), A("XK", 128 * b, 128 * b + 128), A("r16")) for b in range(16)])
-        act(A("ypn", 0, 256), PS(2, 0, 256), AF.Identity, bias=yb_, scale=16384.0)
-        act(A("ypn", 256, 512), PS(2, 0, 256), AF.Identity, bias=nyb_, scale=-16384.0)
+        tt(A("MR", 16, 32), si(6), si(1), OP.mult)
+        ts(si(8), si(7), 4, OP.arith_shift_right)
+        ts(si(9), si(7), 7, OP.arith_shift_right)
+        ts(si(8), si(8), 240.0, OP.mult)
+        ts(si(9), si(9), -2032.0, OP.mult)
+        tt(si(8), si(8), si(9), OP.add)
+        tt(A("d16"), si(8), si(7), OP.add)
+        mms([(PS(1, 256, 384, p1=32), A("MR"), A("IDh"))])
+        lin("MTs", A("MTs", p1=32), PS(1, 256, 384, p1=32))
+        mm([(PS(4, 128 * y, 128 * y + 128), A("Hs", 128 * y, 128 * y + 128, p1=32), A("MTs", p1=32)) for y in range(2)], False, True)
+        on("V", weights, t)
+        line[0] = "L"
+        mms([(half("p2", y), A("Hs", 256 + 128 * y, 384 + 128 * y, p1=32), A("MTs", p1=32)) for y in range(2)])
+        act(A("sS"), PS(2, 0, 256), AF.Sign, bias=yb_)
+        swap(lambda q, p: B("p2", 16, 17, 1, q, 16, 8, p, p + 32), lambda x: A("d16", x, 16, 8))
+        cp(A("dl"), PS(2, 256, 272))
+        if t > 0:
+            sort()
+        else:
+            mms([(PS(3, 0, 256), A("PMb"), A("LcB"))])
+            lin("Lp", A("Lf"), PS(3, 0, 256))
+        act(K2(t + 1), IND(K2(t, 0, 768), A("cl", 88 * t + 40, 88 * t + 72)))
         if t == NS - 1:
             for e in range(2):
                 ts(A("Ko", e, 512, 2), K2(NS, 256 * e, 256 * e + 256), 12582912.0, OP.add, -12582912.0, OP.add)
             hand_back("k", "Ko", 0, 512, "yk", "g")
-        if t > 0:
-            sort_keys()
-            moves(0)
-            mms([(PS(3, 256 + 128 * y, 384 + 128 * y), A("Lt", 128 * y, 128 * y + 128), A("IDh")) for y in range(2)])
-        else:
-            mms([(PS(3, 256, 512), A("PM"), A("LcA"))])
+        dma("y", [(A("VT", p0=16 * a, p1=16 * a + 16), A("Lf")) for a in range(8)], VLAT)
+        mm([(PS(2, 256, 512), A("nI"), A("ones")), (PS(2, 256, 512), A("nI"), A("sS"))], True, False)
+        mm([(PS(2, 256, 512), A("PMt"), A("Lp")) if t else (PS(2, 256, 512), A("IDh"), A("LcB"))], False, True)
+        tt(A("ga"), IND(A("VT"), A("dl")), A("sS"), OP.min)
+        tt(A("LcB"), PS(2, 256, 512), A("ga"), OP.max)
+        if t == 0:
             sort_constants()
-        lin("Lp", A("Lp"), PS(3, 256, 512))
-        dma("y", [(A("VT", p0=16 * a, p1=16 * a + 16), A("Lp")) for a in range(8)], VLAT)
-        tt(A("ga"), IND(A("VT"), A("dl")), A("ypn"), OP.min)
-        tt(A("LcB"), A("ga", 0, 256), A("ga", 256, 512), OP.max)
-        mms([(B("p2", 0, 16, 1, 8 * y, 8 * y + 8), A("LcB", 128 * y, 128 * y + 128), A("PM")) for y in range(2)])
         lists(t + 1)
-        swap(lambda x, p: B("p2", 16 + x, 32, 8, 0, 16, 1, p, p + 32), "IEh", lambda q: B("LcB", q, 16, 8))
-        lin("LcA", A("LcA"), PS(2, 256, 512))
-        lin("Lh", A("Lh"), PS(2, 256, 512), 1.0 / 64, 1057 - 31.5 / 64)
+        line[0] = "K"
         sg = [A("sg", 0, 16), A("sg", 16, 32)]
         mm([(PS(1, 400, 432), A("n8k"), A("sg")), (PS(1, 416, 432), A("n8k"), sg[0])], True, False)
-        mm([(PS(1, 400 + 16 * e, 416 + 16 * e), A("nIh"), A(rc, 16 * h, 16 * h + 16)) for e in range(2) for h in range(8)], False, True)
+        mm([(PS(1, 400 + 16 * e, 416 + 16 * e), A("nI"), A(rc, 16 * h, 16 * h + 16)) for e in range(2) for h in range(8)], False, True)
         for e in range(2):
             ts(sg[e], PS(1, 400 + 16 * e, 416 + 16 * e), 4096.5 - 4096 * e, OP.is_lt, -0.5, OP.add)
         mms([(PS(0, b, 512, 16), A("XK", 128 * b, 128 * b + 128), A("sg")) for b in range(16)])
@@ -539,25 +634,23 @@ def rank_program(g, core, T, topo):
             cur_lists(t + 1)
             own_K(t + 1)
         spread_T(SHARE if t < NS - 1 else SHARE_ENDS)
-        values(t)
+        on("V", values, t)
 
-    for c in range(8):
-        (cp if c % 2 else act)(A("P", 512 * c, 512 * c + 512), IND(A("Tt"), lu(NS, c)))
-        contract(c)
+    step[0] = NS
+    scores(NS)
+    digits(1)
     marks()
-    sort_keys()
-    moves(1)
-    trade(lambda q: A("Lt", 32 * q, 32 * q + 32), lambda q: A("Rl", 32 * q, 32 * q + 32))
-    cp(A("Rl", 32 * r, 32 * r + 32), A("Lt", 32 * r, 32 * r + 32))
-    for y in range(2):
-        cp(A("Ls", 128 * y, 128 * y + 128), B("Rl", y, 16, 2))
-    mms([(PS(3, 256 + 128 * y, 384 + 128 * y), A("Ls", 128 * y, 128 * y + 128), A("IDh")) for y in range(2)])
-    ts(A("Lo"), PS(3, 256, 512), 2048.0, OP.add)
+    powers()
+    sort(1)
+    trade(lambda q: A("Lp", 32 * q, 32 * q + 32), lambda q: A("Rl", 32 * q, 32 * q + 32))
+    cp(A("Rl", 32 * r, 32 * r + 32), A("Lp", 32 * r, 32 * r + 32))
+    swap(lambda x, p: B("p2", x, 16, 8, 0, 16, 1, p, p + 32), lambda q: A("Rl", 32 * q, 32 * q + 32), "IE2")
+    ts(A("Lo"), PS(2, 0, 256), 2048.0, OP.mult, 2048.0, OP.add)
     dma("s", [((T["yl"][:, :], []), A("Lo"))])
     emit(g, T, QU, ops, sent[0])
 
 
-def arrange(ops):
+def former(ops):
     n = len(ops)
     cost = [o["cost"] for o in ops]
     full = [o["cost"] + o["lat"] for o in ops]
@@ -644,6 +737,146 @@ def arrange(ops):
         tags = list(kin)
         best = min([lean(forth(rank), rank, FIRST, True) for _ in range(STARTS)], key=lambda z: z[0])
         best = lean(best, None, TRIES, False)
+        KEPT[n] = order(best[1])
+        KEPT["times"] = best
+    seq = KEPT[n]
+    place = {j: k for k, j in enumerate(seq)}
+    for j, o in enumerate(ops):
+        assert all(place[d] < place[j] for d in o["deps"] | o["order"])
+        o["deps"] = {place[d] for d in o["deps"]}
+    return [ops[j] for j in seq]
+
+
+def arrange(ops):
+    n = len(ops)
+    cost, lat, hold = [o["cost"] for o in ops], [o["lat"] for o in ops], [o["hold"] for o in ops]
+    queue = [("pe", "v", "s", "g", "y", None).index(o["q"]) for o in ops]
+    hard, soft, behind = [], [], []
+    for o in ops:
+        seen = 0
+        for d in o["deps"] | o["order"]:
+            seen |= behind[d]
+        hard.append([d for d in sorted(o["deps"]) if not seen >> d & 1])
+        soft.append([d for d in sorted(o["order"] - o["deps"]) if not seen >> d & 1])
+        behind.append(seen | bits(o["deps"]))
+    both = [h + s for h, s in zip(hard, soft)]
+    after = [[] for o in ops]
+    for i in range(n):
+        for d in hard[i]:
+            after[d].append((i, True))
+        for d in soft[i]:
+            after[d].append((i, False))
+
+    def fit(st, en, t, c):
+        j = m = len(st)
+        while j and en[j - 1] > t:
+            j -= 1
+        while j < m and t + c > st[j]:
+            if en[j] > t:
+                t = en[j]
+            j += 1
+        st.insert(j, t)
+        en.insert(j, t + c)
+        return t
+
+    def order(key):
+        key = list(key)
+        for i in range(n):
+            k = key[i]
+            for d in both[i]:
+                if key[d] >= k:
+                    k = key[d] + 1e-3
+            key[i] = k
+        return [j for k, j in sorted(zip(key, range(n)))]
+
+    def forth(key):
+        st, en, at, end = [[] for q in range(7)], [[] for q in range(7)], [0.0] * n, [0.0] * n
+        for i in order(key):
+            t = 0.0
+            for d in hard[i]:
+                x = end[d] + WAKE
+                if x > t:
+                    t = x
+            for d in soft[i]:
+                x = at[d] + cost[d]
+                if x > t:
+                    t = x
+            q, c = queue[i], cost[i]
+            if q < 5:
+                s, e = st[q], en[q]
+                if e and e[-1] > t:
+                    t = fit(s, e, t, c)
+                else:
+                    s.append(t)
+                    e.append(t + c)
+            at[i] = t
+            if hold[i]:
+                q = 5 if q == 5 else 6
+                end[i] = fit(st[q], en[q], t + c + 1400, hold[i]) + hold[i] + 600
+            else:
+                end[i] = t + c + lat[i]
+        return max(end) + 1e-2 * sum(end) / n, at, end
+
+    def back(at, end):
+        st, en, lead = [[] for q in range(5)], [[] for q in range(5)], [0.0] * n
+        for i in order(end)[::-1]:
+            w = end[i] - at[i] - cost[i]
+            t = 0.0 if after[i] else w
+            for d, h in after[i]:
+                x = lead[d] + (w + WAKE if h else 0.0)
+                if x > t:
+                    t = x
+            if queue[i] < 5:
+                t = fit(st[queue[i]], en[queue[i]], t, cost[i])
+            lead[i] = t + cost[i]
+        return [-x for x in lead]
+
+    def lean(now, key, tries, kinds):
+        best = now
+        for it in range(tries):
+            p = list(key if kinds else now[1])
+            i = int(rng.integers(0, n))
+            x, how = float(rng.normal()) * STEP * (1.0, 0.3)[it % 2], int(rng.integers(0, 4))
+            if it % 8 == 4:
+                for j in line[ops[i]["line"]]:
+                    if how < 2 or seat[j][0] == seat[i][0]:
+                        p[j] += x
+            elif kinds:
+                t, k = seat[i]
+                for j in kin[ops[i]["tag"]]:
+                    if how == 0 or (seat[j][1] >= k, seat[j][1] <= k, seat[j][1] == k)[how - 1]:
+                        p[j] += x
+            else:
+                for j in kin[ops[i]["tag"]]:
+                    if abs(j - i) <= (0, 8, 30, 60)[how]:
+                        p[j] += x
+            new = forth(p)
+            if not kinds and it % 10 == 0:
+                new = min(new, forth(back(new[1], new[2])), key=lambda z: z[0])
+            if new[0] <= now[0] + SLACK * (1 - it / tries) * float(rng.exponential()):
+                now, key = new, p
+                if new[0] < best[0]:
+                    best = new
+        return best
+
+    if n not in KEPT:
+        rng = np.random.default_rng(0)
+        kin, line, seat, met, ranks = {}, {}, [], {}, []
+        for i in range(n):
+            kin.setdefault(ops[i]["tag"], []).append(i)
+            line.setdefault(ops[i]["line"], []).append(i)
+        for x in (1.0, 1.25, 1.5, 1.75, 2.0, 2.5):
+            for y in (1.0, 1.25, 1.5, 2.0):
+                rank = [0.0] * n
+                for i in range(n - 1, -1, -1):
+                    rank[i] = -cost[i] * {"V": x, "L": y}.get(ops[i]["line"], 1.0) - lat[i] + min([rank[d] - WAKE for d, h in after[i]], default=0.0)
+                ranks.append((forth(rank)[0], rank))
+        ranks.sort()
+        for o in ops:
+            met[o["step"], o["tag"]] = met.get((o["step"], o["tag"]), -1) + 1
+            seat.append((o["step"], met[o["step"], o["tag"]]))
+        best = [lean(lean(forth(rank), rank, FIRST, True), None, FIRST, False) for _, rank in ranks[:STARTS]]
+        best = lean(min(best, key=lambda z: z[0]), None, TRIES, False)
         KEPT[n] = order(best[1])
         KEPT["times"] = best
     seq = KEPT[n]

@@ -13,8 +13,8 @@ LOW, POW = 16.0, 18
 PE_NS, WAKE, VLAT, LONG = 0.5, 80.0, 6500.0, 5500.0
 STARTS, FIRST, TRIES, STEP, SLACK, KEPT = 4, 3500, 22000, 4000.0, 400.0, {}
 SHARE, SHARE_ENDS, SHARE_VT = (3, 6), (1, 3, 5, 7), ()
-TURNS = 2
-GATHER = (1, 4, 6)
+OWN = 2
+BY_DMA = (0, 1, 2)
 ON_S = {"D0", "D1", "x16", "MTs", "Lp", "W2", "L0", "Vo", "Lh"}
 WB, TB, VB = (5, 6), (4, 0, 1), (3, 4)
 SCRATCH = {}
@@ -28,11 +28,11 @@ def _sb(dtype, **kw):
 SL = (16, 16)
 RING = 4
 _sb(BF, Tt=4096, V0=4096, K0=512, Kb=512, Vb=512, KK=1536, Tc=512, own=640, P=2048, G=768 * RING, diag=1024, fl=SL, tt=SL, sS=256, pw=256, z=512, R=(128, 16), BO=128, EB=144,
-    SEL=1024, SEL0=1024, XK=2048, Hs=512, IE2=272, Mc=256, I2k=256, ones=256, tmp=128, Cs=256, Cz=384, Ko=512, gkB=256, Wt=64, Wt0=64, Q8=8)
+    SEL=1024, SEL0=1024, XK=2048, Hs=512, IE2=272, Mc=256, I2k=256, ones=256, tmp=128, Cs=256, Cz=384, Ko=512, gkB=256, Wt=64, Wt0=64, Q8=8, m05=16)
 _sb(F, Vt=8192, E=(16, 512), Y=4096, Vc=512, Vp=512, VT=2048, Lf=256, Lo=256, aS=SL, Mx=256, us=256, d1=256, Bx=256, As=256, At=256,
     iot=272, ioq=128, iok=256, ioa=256, ioj=256, pc=24, mk=24, ID32=128, ISC=128, ID320=128, ISC0=128, rm=256, wL=16, m16=16, iob=128)
 _sb(HF, LcB=SL, Lq=SL, Ly=SL, Lp=SL, Lh=SL, Ls=SL, R0=SL, L0=256, Rl=256, W2=256, ga=256, D=(32, 16), D2=(32, 16), x16=SL, IEh=272, thZ=128, cL=88, sg=32, MR=32,
-    d16=16, MTs=128, rc0=128, rc1=128, rc2=128, rc3=128)
+    d16=16, MTs=256, rc0=128, rc1=128, rc2=128, rc3=128)
 _sb(I, Li=256, thI=16, pi=8, si=160)
 _sb(U, lu=1280, lv=1024, bl=16, dl=16, dg=8, cl=352)
 PART = {}
@@ -301,7 +301,7 @@ def rank_program(g, core, T, topo):
     for j in range(8):
         pick(A("XK", 256 * j, 256 * j + 256), [[-1, 2], [-16, 8], [0, 16]], 1, -2 * j)
     pick(A("Hs", 0, 256), [[-8, 2], [0, 16], [-1, 8]], -1)
-    pick(A("Hs", 256, 512), [[-8, 2], [-1, 8], [0, 16]], 1, -16)
+    pick(A("Hs", 256, 512), [[-8, 2], [-1, 8], [0, 16]], 1)
     for n, c in (("n64", -64), ("n8k", -8192), ("nI", -1), ("Ia", 1 / 32), ("Ib", -2), ("Ic", 1 / 2048), ("Id", -1 / 32), ("I4", 4), ("n60", -60)):
         pick(A(n), [[-1, 128]], c)
     pick(A("PMt"), [[-1, 8], [-8, 16]], 1)
@@ -338,6 +338,7 @@ def rank_program(g, core, T, topo):
     ts(A("EB"), A("iot", 0, 144), e_, OP.is_equal)
     ts(A("PMb"), io128, kq_, OP.is_equal)
     fill(A("ones"), 1.0)
+    fill(A("m05"), 0.5)
     ts(A("sg"), A("iot", 0, 32), 0.0, OP.mult, -0.5, OP.add)
     ts(A("LE"), A("iok", 0, 128), k_, OP.is_ge)
     for n, c in (("I256", 256), ("n512", -512)):
@@ -472,12 +473,19 @@ def rank_program(g, core, T, topo):
                 cp(A("P", 512 * a, 512 * a + 512), IND(A("Tt"), lu(t, a)))
             act(A("G", o + 256, o + 768), IND(A("Tt"), lu(t, 4 + a)))
             k = lambda u, w: A("diag", 128 * (2 * a + u) + 8 * w, 128 * (2 * a + u) + 8 * w + 8) if t < NS else A("Q8")
-            mm([(B("p0", 8, 16, 1, w, w + 1, 1, 32 * a, 32 * a + 16 + 16 * u), A("G", o + 512 * (1 - u) + w, o + 768 - 256 * u, 16), k(u, w))
+            mm([(B("p4", 16, 24, 1, w, w + 1, 1, 32 * a, 32 * a + 16 + 16 * u), A("G", o + 512 * (1 - u) + w, o + 768 - 256 * u, 16), k(u, w))
                 for w in range(16) for u in (1, 0)], each=2)
         mms([(B("p0", 0, 8, 1, w, w + 1), A("P", w, 2048, 16), A("Q8")) for w in range(16)])
 
-    def marks():
-        ts(A("fl"), PS(0, 0, 256), 0.0, OP.is_lt)
+    raw = (PS(0, 0, 128), PS(4, 256, 384))
+
+    def marks(more=1):
+        for y in range(2):
+            if y == 0 and more:
+                act(half("aS", 1), raw[1], AF.Abs, scale=SC)
+            ts(half("fl", y), raw[y], 0.0, OP.is_lt)
+        if more:
+            act(half("aS", 0), raw[0], AF.Abs, scale=SC)
         mms([(half("p2", y), M("Bm", y), half("fl", y)) for y in range(2)])
         tt(A("tt"), A("fl"), PS(2, 0, 256), OP.mult)
 
@@ -493,7 +501,7 @@ def rank_program(g, core, T, topo):
         for y in range(2):
             act(A("pw", 128 * y, 128 * y + 128), half("p0", y, 16), AF.Sigmoid, bias=(pb0_, pb_)[y], scale=LN64)
 
-    def sort(last=0):
+    def sort(last=0, dma=0):
         for h in range(2):
             tt(A("z", 256 * h, 256 * h + 256), PS(3, 256 * h, 256 * h + 256), A("pw"), OP.mult)
         mm([(PS(3, 0, 256), A("ones", 0, 128, p1=32), A("Cs", p1=32))], True, False)
@@ -507,9 +515,18 @@ def rank_program(g, core, T, topo):
         cp(B("D2", 0, 32, 1, 0, 8), B("D", 0, 32, 1, 8, 16))
         mm([(B("p4", 16 + y, 32, 2) if last else half("p4", y, 16), half(d, y, 16 * h), A(n))
             for y in range(2) for h, d, n in ((0, "D2", "Ib"), (1, "D2", "Id"), (0, "D", "Ia"), (1, "D", "Ic"))], each=4)
-        if not last:
+        if dma:
             lin("Lp", A("Lf"), PS(4, 256, 512), 1.0, lb_)
         lin("Lp", A("Lp"), PS(4, 256, 512), 1.0, lb_)
+
+    def spread_views(t):
+        if t in BY_DMA:
+            dma("y", [(A("VT", p0=16 * a, p1=16 * a + 16), A("Lf")) for a in range(8)], VLAT)
+            return
+        for j in range(4):
+            b = "p%d" % VB[j % len(VB)]
+            mms([(B(b, x, 32, 8), A("SEL0" if t else "SEL", 128 * x, 128 * x + 128), A("Lp" if t else "LcB", 64 * j, 64 * j + 64)) for x in range(8)])
+            lin(j not in SHARE_VT, A("VT", 512 * j, 512 * j + 512), A(b), 1.0 if t else -0.5)
 
     def weights(t):
         lin("x16", A("x16"), PS(4, 0, 256), 1.0, xb_)
@@ -557,31 +574,39 @@ def rank_program(g, core, T, topo):
            [(PS(1, 256 + 128 * h, 384 + 128 * h), half("LcB", h), A("I2k", 0, 128)) for h in range(2)])
         mm([(PS(1, 0, 256), A("ones", 0, 128), A("Mc"))], True, False)
         marks()
-        act(A("aS"), PS(0, 0, 256), AF.Abs, scale=SC)
         hs = [(PS(1, 128 * h, 128 * h + 128), h) for h in range(2)]
+        for o, h in hs[::-1]:
+            mm([(o, half("aS", h), M("ID32", h))], False, False)
         mm([(o, half("fl", h), M("Mf", h)) for o, h in hs], False, False)
-        mm([(o, half("aS", h), M("ID32", h)) for o, h in hs], False, False)
         mm([(o, half("tt", h), M("Mt", h)) for o, h in hs], False, True)
         if t > 0:
             on("L", powers)
         mm([(PS(4, 128 * y, 128 * y + 128), M(m, y), half(n, y)) for m, n in (("m8A", "fl"), ("m8I", "tt"), ("ISC", "aS")) for y in range(2)], True, False)
         scan(A("Mx"), A("rm"), PS(1, 0, 256), OP.mult, OP.max)
+        line[0] = "V"
+        ts(si(3), A("Mx", 15, 256, 16), 1 / SC, OP.mult, 0.46, OP.add)
+        ts(A("MR", 0, 16), si(3), -1860.0, OP.add)
+        mms([(PS(2, 256, 384, p1=16), A("MR", 0, 16), A("IDh"))])
+        lin("MTs", A("MTs", 0, 128, p1=16), PS(2, 256, 384, p1=16))
+        mm([(PS(4, 128 * y, 128 * y + 128), A("Hs", 128 * y, 128 * y + 128, p1=16), A("MTs", 0, 128, p1=16)) for y in range(2)], False, True)
+        weights(t)
+        line[0] = "K"
         tt(A("us"), A("Mx"), PS(1, 0, 256), OP.subtract)
         tt(A("d1"), PS(1, 256, 512), A("us"), OP.subtract)
         scan(A("Bx"), A("us"), A("d1"), OP.min, OP.max)
         bs = A("Bx", 15, 256, 16)
         cp(A("bl"), bs)
+        mms([(PS(OWN, 0, 256), A("IDh"), own(t))])
         act(A("gkB"), IND(A("Tt"), A("bl")), AF.Abs)
-        tt(K2(t, 512, 768), A("gkB"), own(t), OP.max)
+        tt(K2(t, 512, 768), PS(OWN, 0, 256), A("gkB"), OP.max)
         kn = 768 * (t % 2) + 512
         mm([(PS(1, 384, 400), A("thZ", p1=64), A("IDh", 16 * t, 16 * t + 16, p1=64))] +
            [(PS(1, 384, 400), A("EB", 15 - b, 143 - b), A("KK", kn + b, kn + 256, 16)) for b in range(16)])
         rc = "rc%d" % t
         cp(A(rc, 16 * r, 16 * r + 16), PS(1, 384, 400))
         trade(lambda q: A(rc, 16 * r, 16 * r + 16), lambda q: A(rc, 16 * q, 16 * q + 16))
+        line[0] = "L"
         ts(si(0), A("Mx", 15, 256, 16), 32 / SC, OP.mult, 30.0, OP.add)
-        ts(si(3), si(0), 5, OP.arith_shift_right)
-        ts(A("MR", 0, 16), si(3), -1860.0, OP.add)
         ts(si(7), bs, 0.5, OP.mult, -0.25, OP.add)
         ts(si(4), si(7), 7, OP.arith_shift_right, 7, OP.bitwise_and)
         ts(si(1), si(0), 31, OP.bitwise_and, 1, OP.logical_shift_right)
@@ -589,24 +614,24 @@ def rank_program(g, core, T, topo):
         ts(si(5), si(4), q_, OP.not_equal)
         tt(si(6), si(5), si(2), OP.is_gt)
         tt(A("MR", 16, 32), si(6), si(1), OP.mult)
-        ts(si(8), si(7), 4, OP.arith_shift_right)
-        ts(si(9), si(7), 7, OP.arith_shift_right)
-        ts(si(8), si(8), 240.0, OP.mult)
-        ts(si(9), si(9), -2032.0, OP.mult)
-        tt(si(8), si(8), si(9), OP.add)
-        tt(A("d16"), si(8), si(7), OP.add)
-        mms([(PS(1, 256, 384, p1=32), A("MR"), A("IDh"))])
-        lin("MTs", A("MTs", p1=32), PS(1, 256, 384, p1=32))
-        mm([(PS(4, 128 * y, 128 * y + 128), A("Hs", 128 * y, 128 * y + 128, p1=32), A("MTs", p1=32)) for y in range(2)], False, True)
-        on("V", weights, t)
-        line[0] = "L"
-        mms([(half("p2", y), A("Hs", 256 + 128 * y, 384 + 128 * y, p1=32), A("MTs", p1=32)) for y in range(2)])
+        if t in BY_DMA:
+            ts(si(8), si(7), 4, OP.arith_shift_right)
+            ts(si(9), si(7), 7, OP.arith_shift_right)
+            ts(si(8), si(8), 240.0, OP.mult)
+            ts(si(9), si(9), -2032.0, OP.mult)
+            tt(si(8), si(8), si(9), OP.add)
+            tt(A("d16"), si(8), si(7), OP.add)
+        else:
+            cp(A("d16"), si(7))
+        mms([(PS(1, 256, 384, p1=16), A("MR", 16, 32), A("IDh"))])
+        lin("MTs", A("MTs", 128, 256, p1=16), PS(1, 256, 384, p1=16))
+        mms([(half("p2", y), A("Hs", 256 + 128 * y, 384 + 128 * y, p1=16), A("MTs", 128, 256, p1=16)) for y in range(2)])
         act(A("sS"), PS(2, 0, 256), AF.Sign, bias=yb_)
         swap(lambda q, p: B("p2", 16, 17, 1, q, 16, 8, p, p + 32), lambda x: A("d16", x, 16, 8))
         cp(A("dl"), PS(2, 256, 272))
         if t > 0:
-            sort()
-        else:
+            sort(0, t in BY_DMA)
+        elif t in BY_DMA:
             mms([(PS(3, 0, 256), A("PMb"), A("LcB"))])
             lin("Lp", A("Lf"), PS(3, 0, 256))
         act(K2(t + 1), IND(K2(t, 0, 768), A("cl", 88 * t + 40, 88 * t + 72)))
@@ -614,20 +639,26 @@ def rank_program(g, core, T, topo):
             for e in range(2):
                 ts(A("Ko", e, 512, 2), K2(NS, 256 * e, 256 * e + 256), 12582912.0, OP.add, -12582912.0, OP.add)
             hand_back("k", "Ko", 0, 512, "yk", "g")
-        dma("y", [(A("VT", p0=16 * a, p1=16 * a + 16), A("Lf")) for a in range(8)], VLAT)
+        spread_views(t)
         mm([(PS(2, 256, 512), A("nI"), A("ones")), (PS(2, 256, 512), A("nI"), A("sS"))], True, False)
         mm([(PS(2, 256, 512), A("PMt"), A("Lp")) if t else (PS(2, 256, 512), A("IDh"), A("LcB"))], False, True)
         tt(A("ga"), IND(A("VT"), A("dl")), A("sS"), OP.min)
         tt(A("LcB"), PS(2, 256, 512), A("ga"), OP.max)
         if t == 0:
             sort_constants()
+        if t == NS - 1:
+            for y in range(2):
+                cp(B("Ls", y, 16, 2), half("LcB", y))
+            trade(lambda q: A("Ls", 32 * q, 32 * q + 32), lambda q: A("R0", 32 * q, 32 * q + 32))
+            cp(A("R0", 32 * r, 32 * r + 32), A("Ls", 32 * r, 32 * r + 32))
+            for y in range(2):
+                cp(half("LcB", y), B("R0", y, 16, 2))
         lists(t + 1)
         line[0] = "K"
         sg = [A("sg", 0, 16), A("sg", 16, 32)]
-        mm([(PS(1, 400, 432), A("n8k"), A("sg")), (PS(1, 416, 432), A("n8k"), sg[0])], True, False)
+        mm([(PS(1, 400, 432), A("n8k"), A("sg")), (PS(1, 416, 432), A("n8k"), sg[0]), (PS(1, 400, 416), A("n8k"), A("m05"))], True, False)
         mm([(PS(1, 400 + 16 * e, 416 + 16 * e), A("nI"), A(rc, 16 * h, 16 * h + 16)) for e in range(2) for h in range(8)], False, True)
-        for e in range(2):
-            ts(sg[e], PS(1, 400 + 16 * e, 416 + 16 * e), 4096.5 - 4096 * e, OP.is_lt, -0.5, OP.add)
+        ts(A("sg"), PS(1, 400, 432), 0.5, OP.is_lt, -0.5, OP.add)
         mms([(PS(0, b, 512, 16), A("XK", 128 * b, 128 * b + 128), A("sg")) for b in range(16)])
         tt(A("Tc"), PS(0), K2(t + 1), OP.mult)
         if t < NS - 1:
@@ -639,12 +670,10 @@ def rank_program(g, core, T, topo):
     step[0] = NS
     scores(NS)
     digits(1)
-    marks()
+    marks(0)
     powers()
     sort(1)
-    trade(lambda q: A("Lp", 32 * q, 32 * q + 32), lambda q: A("Rl", 32 * q, 32 * q + 32))
-    cp(A("Rl", 32 * r, 32 * r + 32), A("Lp", 32 * r, 32 * r + 32))
-    swap(lambda x, p: B("p2", x, 16, 8, 0, 16, 1, p, p + 32), lambda q: A("Rl", 32 * q, 32 * q + 32), "IE2")
+    swap(lambda x, p: B("p2", x, 16, 8, 0, 16, 1, p, p + 32), lambda q: A("Lp", 32 * q, 32 * q + 32), "IE2")
     ts(A("Lo"), PS(2, 0, 256), 2048.0, OP.mult, 2048.0, OP.add)
     dma("s", [((T["yl"][:, :], []), A("Lo"))])
     emit(g, T, QU, ops, sent[0])

@@ -10,10 +10,11 @@ C8 = 129.0 / 16
 EPS = 2.0 ** -18
 LN64 = math.log(64.0)
 LOW, POW = 16.0, 18
-PE_NS, WAKE, VLAT, LONG = 0.5, 80.0, 6500.0, 5500.0
-STARTS, FIRST, TRIES, STEP, SLACK, KEPT = 4, 3500, 22000, 4000.0, 400.0, {}
-SHARE, SHARE_ENDS, SHARE_VT = (3, 6), (1, 3, 5, 7), ()
-OWN = 2
+RATES, BOTH, LATE = ((1.0, 1.5, 3.5, 0.5), (1.2, 2.3, 6.0, 0.6), (0.84, 1.1, 2.5, 0.42)), (0.4, 0.8), (1.0, 0.95)
+WAKE, VLAT, LONG = 80.0, 4400.0, 3500.0
+STARTS, FIRST, TRIES, STEP, SLACK, KEPT = 2, 1500, 5000, 4000.0, 300.0, {}
+SHARE, SHARE_ENDS, SHARE_VT = (1, 6), (1, 3, 5, 7), (1, 3)
+OWN, SEED, MORE = 2, 2, 3500
 BY_DMA = (0, 1, 2)
 ON_S = {"D0", "D1", "x16", "MTs", "Lp", "W2", "L0", "Vo", "Lh"}
 WB, TB, VB = (5, 6), (4, 0, 1), (3, 4)
@@ -31,7 +32,7 @@ _sb(BF, Tt=4096, V0=4096, K0=512, Kb=512, Vb=512, KK=1536, Tc=512, own=640, P=20
     SEL=1024, SEL0=1024, XK=2048, Hs=512, IE2=272, Mc=256, I2k=256, ones=256, tmp=128, Cs=256, Cz=384, Ko=512, gkB=256, Wt=64, Wt0=64, Q8=8, m05=16)
 _sb(F, Vt=8192, E=(16, 512), Y=4096, Vc=512, Vp=512, VT=2048, Lf=256, Lo=256, aS=SL, Mx=256, us=256, d1=256, Bx=256, As=256, At=256,
     iot=272, ioq=128, iok=256, ioa=256, ioj=256, pc=24, mk=24, ID32=128, ISC=128, ID320=128, ISC0=128, rm=256, wL=16, m16=16, iob=128)
-_sb(HF, LcB=SL, Lq=SL, Ly=SL, Lp=SL, Lh=SL, Ls=SL, R0=SL, L0=256, Rl=256, W2=256, ga=256, D=(32, 16), D2=(32, 16), x16=SL, IEh=272, thZ=128, cL=88, sg=32, MR=32,
+_sb(HF, LcB=SL, Lq=SL, Ly=SL, Lp=SL, Lh=SL, Ls=SL, R0=SL, L0=256, W2=256, ga=256, D=(32, 16), D2=(32, 16), x16=SL, IEh=272, thZ=128, cL=88, sg=32, MR=32,
     d16=16, MTs=256, rc0=128, rc1=128, rc2=128, rc3=128)
 _sb(I, Li=256, thI=16, pi=8, si=160)
 _sb(U, lu=1280, lv=1024, bl=16, dl=16, dg=8, cl=352)
@@ -47,7 +48,7 @@ SCRATCH["V0d"] = ("dram", [16, 2, 8, 256], BF)
 for _n, _c, _d in (("V", 64, BF), ("k", 64, BF), ("v", 32, F), ("w", 32, F)):
     SCRATCH["S" + _n + "d"] = ("dram", [8, 128, _c], _d)
     SCRATCH["R" + _n + "d"] = ("dram", [8, 128, _c], _d)
-SEMAPHORES = ["pe", "v", "s", "g", "sent"] + ["d%d" % i for i in range(48)] + ["a%d" % i for i in range(12)]
+SEMAPHORES = ["pe", "v", "s", "g", "sent"] + ["d%d" % i for i in range(48)] + ["a%d" % i for i in range(14)]
 
 
 def spread(topo, src, dsts):
@@ -133,7 +134,11 @@ def rank_program(g, core, T, topo):
                 if kind:
                     lst[:] = [e for e in lst if e[0][1] & ~x[1]]
                 lst.append((x, kind, me))
-        ops.append({"q": q, "fn": fn, "deps": deps, "order": order, "sem": sem, "n": n, "cost": cost, "lat": lat, "hold": max(0.0, lat - 2000), "step": step[0], "line": line[0],
+        j = 3 if q == "pe" else 0
+        cost, *other = cost if isinstance(cost, list) else [cost * x[j] / RATES[0][j] for x in RATES]
+        if q == "y":
+            other[1] = 1.5 * cost
+        ops.append({"q": q, "fn": fn, "other": other, "deps": deps, "order": order, "sem": sem, "n": n, "cost": cost, "lat": lat, "hold": max(0.0, lat - 2000), "step": step[0], "line": line[0],
                     "tag": (q, wr[0][0] if wr else None, rd[0][0] if rd and q == "pe" else None)})
 
     def wide(x):
@@ -143,11 +148,8 @@ def rank_program(g, core, T, topo):
         return 4 if SCRATCH[x[1][0][0]][2] in (F, I) else 2
 
     def price(o, a, per):
-        if len(a[1]) > 1:
-            return 55 + 1.5 * wide(a)
-        if len(o[1]) > 1:
-            return 55 + 3.5 * wide(o)
-        return 60 + per * wide(o)
+        kind, n = (1, wide(a)) if len(a[1]) > 1 else (2, wide(o)) if len(o[1]) > 1 else (0, per * wide(o))
+        return [60 + x[kind] * n for x in RATES]
 
     def regs(*xs):
         return [p for x in xs if isinstance(x, tuple) for p in x[1]]
@@ -189,7 +191,7 @@ def rank_program(g, core, T, topo):
             kw["scale"] = val(scale)
         c, after = price(o, a, 1), []
         if f == AF.Sigmoid:
-            c, after = c + (0 if table else 1500), table[:1]
+            c, after = [x + (0 if table else 1400) for x in c], table[:1]
             table.append(len(ops))
         rec("s", lambda: g.scalar.activation(o[0], a[0], f, **kw), regs(a, bias, scale) + x, w, cost=c, after=after)
 
@@ -210,7 +212,7 @@ def rank_program(g, core, T, topo):
                     h = g.tensor.matmul(o[0], l[0], x[0], start and j == 0, stop and j == len(lst) - 1)
             return h
         rec("pe", fn, [p for o, l, x in lst for p in l[1] + x[1]], [p for o, l, x in lst for p in o[1]],
-            cost=sum(max(min(64, wide(l)), wide(x)) * (4 if size(x) == 4 else 1) * PE_NS for o, l, x in lst))
+            cost=sum(max(min(64, wide(l)), wide(x)) * (4 if size(x) == 4 else 1) * RATES[0][3] for o, l, x in lst))
 
     def mms(lst):
         mm(lst, each=1)
@@ -221,7 +223,7 @@ def rank_program(g, core, T, topo):
         else:
             rec("g", lambda: g.iota(o[0], pat, 0, cm), [], o[1], cost=130 + 2 * wide(o))
 
-    def dma(q, pairs, lat=2500.0):
+    def dma(q, pairs, lat=2250.0):
         sem = "d%d" % nd[0]
         nd[0] += 1
 
@@ -236,7 +238,7 @@ def rank_program(g, core, T, topo):
         a = topo.addr(c)
         return DstId(rid=a[0], pnc=a[1])
 
-    def trade(src, land, lat=5500.0):
+    def trade(src, land, lat=4800.0):
         sem = "a%d" % len(calls)
         mk = spread(topo, core, others)
         trs = [RemoteDMATransfer(dst_ids=[dst(c)], dma_engine_mask=mk[c][0], remote_sem=T.sem[sem], src=src(T.rank_of(c))[0], dst=land(r)[0]) for c in others]
@@ -278,7 +280,14 @@ def rank_program(g, core, T, topo):
     ts(A("IEh"), A("iot"), -16.0, OP.add, ie_, OP.is_equal)
 
     trade(lambda q: D("SKd", q), lambda q: A("K0", 64 * q, 64 * q + 64), 6300.0)
-    ts(A("Ls"), A("Li"), -2048.0, OP.add, 1.0 / 2048, OP.mult)
+    ts(A("IDh"), io128, p_, OP.is_equal)
+    ts(A("L0"), A("Li"), -2048.0, OP.add, 1.0 / 2048, OP.mult)
+    for n, c in (("Iy", 1792 / 2048), ("Iq", -3840 / 2048)):
+        ts(A(n), A("IDh"), c, OP.mult)
+    lin("Lq", A("Lq"), A("L0"), 4.0, 1029 - 255.5 / 512)
+    lin("Ly", A("Ly"), A("L0"), 8.0, 1033 - 127.5 / 256)
+    mm([(PS(3, 0, 256), A(m), A(n)) for m, n in (("IDh", "L0"), ("Iy", "Ly"), ("Iq", "Lq"))])
+    lin("Ls", A("Ls"), PS(3, 0, 256), 1.0, 1025.0)
     swap(lambda x, p: B("p2", 2 * x, 2 * x + 2, 1, 0, 16, 1, p, p + 32), lambda q: B("Ls", q, 16, 8))
     lin("L0", A("L0"), PS(2, 0, 256))
     trade(lambda q: A("L0", 32 * q, 32 * q + 32), lambda q: A("R0", 32 * q, 32 * q + 32), 4500.0)
@@ -313,7 +322,6 @@ def rank_program(g, core, T, topo):
         if c1:
             pick(o, [[0, 128]], c1, -1, o)
 
-    ts(A("IDh"), io128, p_, OP.is_equal)
     ts(kq_, k_, 8.0, OP.mult, q_, OP.add)
     ts(e_, q_, 16.0, OP.mult, 15.0, OP.add)
     ts(col("pi", 3), col("pi", 0), 3, OP.arith_shift_right, 1, OP.bitwise_and)
@@ -325,12 +333,8 @@ def rank_program(g, core, T, topo):
     fill(A("diag"), 0.0)
     ts(A("PMk"), io128, kh_, OP.is_equal, 2048.0, OP.mult)
     ts(A("PMv"), io128, kq_, OP.is_equal, 2048.0, OP.mult)
-    for n, c in (("Iy", 1792 / 2048), ("Iq", -3840 / 2048)):
-        ts(A(n), A("IDh"), c, OP.mult)
-    lin("Lq", A("Lq"), A("R0"), 4.0, 1029 - 255.5 / 512)
-    lin("Ly", A("Ly"), A("R0"), 8.0, 1033 - 127.5 / 256)
-    mm([(PS(2, 128 * y, 128 * y + 128), A(m), B(n, y, 16, 2)) for y in range(2) for m, n in (("IDh", "R0"), ("Iy", "Ly"), ("Iq", "Lq"))], each=3)
-    lin("LcB", A("LcB"), PS(2, 0, 256), 1.0, 1025.0)
+    for y in range(2):
+        cp(half("LcB", y), B("R0", y, 16, 2))
     ts(A("mk", 0, 16), A("iot", 0, 16), k_, OP.is_equal)
     ts(A("mk", 16, 24), A("iot", 0, 8), q_, OP.is_equal)
     cp(A("Q8"), A("mk", 16, 24))
@@ -338,14 +342,12 @@ def rank_program(g, core, T, topo):
     ts(A("EB"), A("iot", 0, 144), e_, OP.is_equal)
     ts(A("PMb"), io128, kq_, OP.is_equal)
     fill(A("ones"), 1.0)
-    fill(A("m05"), 0.5)
+    act(A("m05"), A("ones", 0, 16), AF.Sigmoid, scale=0.0)
     ts(A("sg"), A("iot", 0, 32), 0.0, OP.mult, -0.5, OP.add)
     ts(A("LE"), A("iok", 0, 128), k_, OP.is_ge)
     for n, c in (("I256", 256), ("n512", -512)):
         act(A(n), A("IDh"), scale=float(c))
     ts(A("wL"), A("iot", 0, 16), 16.0, OP.mult, k_, OP.add)
-    for j in range(3):
-        ts(A("cL", 8 * j, 8 * j + 8), A("wL", 0, 8), 128.0, OP.add)
     for j, (m, c) in enumerate(((1, 128), (1, 256), (1, 384), (2, 0.5))):
         ts(A("cL", 24 + 16 * j, 40 + 16 * j), A("wL"), float(m), OP.mult, float(c), OP.add)
     ts(A("cL", 80, 88), A("cL", 80, 88), -256.0, OP.add)
@@ -411,6 +413,13 @@ def rank_program(g, core, T, topo):
         for q in range(8):
             b = TB[q % len(TB)]
             y, q0 = q // 4, 2 * (q % 4)
+            if first != 1:
+                e, y, q0 = q // 4, q // 2 % 2, 4 * (q % 2)
+                if e == 0 or first == 0:
+                    o = 256 * e + 128 * y
+                    mms([(PS(b, 128 * j, 128 * j + 128), A("SEL", 128 * (q0 + j), 128 * (q0 + j + 1)), A("Tc", o, o + 128)) for j in range(4)])
+                    (cp if q in share else act)(A("Tt", 1024 * (q % 4) + e, 1024 * (q % 4) + 1024, 2), PS(b))
+                continue
             if first:
                 mms([(PS(b, 256 * j + 64 * h, 256 * j + 64 * h + 64), A("SEL0", 128 * (4 * y + h), 128 * (4 * y + h + 1)), A("Tc", 64 * (q0 + j), 64 * (q0 + j + 1)))
                      for j in range(2) for h in range(4)])
@@ -443,16 +452,17 @@ def rank_program(g, core, T, topo):
             lin("Lh", A("Lh"), A("LcB"), 32.0, 1057 - 31.5 / 64)
 
     def cur_lists(t):
-        mm([(PS(1, 256, 344), A("IDh"), A("cL"))] + [(PS(1, 256 + 8 * j, 264 + 8 * j), A("I256"), A("sg", 0, 8)) for j in range(3)] +
+        mm([(PS(1, 280, 344), A("IDh"), A("cL", 24, 88))] +
            [(PS(1, 280 + 16 * j, 296 + 16 * j), A(n), A("sg", 0, 16)) for j, n in enumerate(("I256", "n512", "I256", "IDh"))])
-        cp(A("cl", 88 * t, 88 * t + 88), PS(1, 256, 344))
+        cp(A("cl", 88 * t + 24, 88 * t + 88), PS(1, 280, 344))
 
     K2 = lambda t, a=0, b=512: A("KK", 768 * (t % 2) + a, 768 * (t % 2) + b)
 
     def own_K(t):
-        act(A("own", 512, 640), IND(K2(t), A("cl", 88 * t + 32, 88 * t + 40)))
+        act(A("own", 384, 640), IND(K2(t), A("cl", 88 * t + 24, 88 * t + 40)))
         cp(IND(A("diag"), A("dg")), A("own", 512, 640))
-        act(A("own", 0, 512), IND(K2(t), A("cl", 88 * t, 88 * t + 32)))
+        cp(A("own", 256, 384), A("own", 384, 512))
+        cp(A("own", 0, 256), A("own", 256, 512))
 
     own = lambda t: A("own", 384, 640)
 
@@ -512,7 +522,10 @@ def rank_program(g, core, T, topo):
                 for h in range(2) for y in range(2)], False, a == 7)
         lin("D1", B("D", 0, 32, 1, 8, 16), PS(3, 0, 256), 1.0 / 64, 1057 - 31.5 / 64)
         lin("D0", B("D", 0, 32, 1, 0, 8), PS(3, 0, 256))
-        cp(B("D2", 0, 32, 1, 0, 8), B("D", 0, 32, 1, 8, 16))
+        if "D2" in ON_S:
+            lin("D2", B("D2", 0, 32, 1, 0, 8), PS(3, 0, 256), 1.0 / 64, 1057 - 31.5 / 64)
+        else:
+            cp(B("D2", 0, 32, 1, 0, 8), B("D", 0, 32, 1, 8, 16))
         mm([(B("p4", 16 + y, 32, 2) if last else half("p4", y, 16), half(d, y, 16 * h), A(n))
             for y in range(2) for h, d, n in ((0, "D2", "Ib"), (1, "D2", "Id"), (0, "D", "Ia"), (1, "D", "Ic"))], each=4)
         if dma:
@@ -541,7 +554,7 @@ def rank_program(g, core, T, topo):
         dma("y", [(D(s), A(src, a, b))])
         dma("y", [(D(d, r), A(src, a, b, p0=16 * r, p1=16 * r + 16))])
         trade(lambda q: D(s, q), lambda q: D(d, q), 6600.0)
-        dma(q, [((T[y][:, a:b], []), D(d))])
+        dma(q, [(y, D(d))])
 
     def values(t):
         for c in range(8):
@@ -550,15 +563,16 @@ def rank_program(g, core, T, topo):
             mm([(PS(7, 32 * c + 16 * (j // 2), 32 * c + 16 * (j // 2) + 16), A("Y", a + 128 * j, a + 128 * j + 128), A("m16")) for j in range(4)], each=2)
             if c % 4 == 3:
                 s = (128 * y, 128 * y + 128)
+                v, back = (256 * y, 256 * y + 256), PS(7, 256 + s[0], 256 + s[1])
                 act(A("At", *s), PS(7, *s))
-                mms([(PS(7, 256 + s[0], 256 + s[1]), A("At", *s), A("ID32"))])
-                act(A("As", *s), PS(7, 256 + s[0], 256 + s[1]))
-                act(IND(A("Vc", 256 * y, 256 * y + 256), A("cl", 88 * t + 72 + 8 * y, 88 * t + 80 + 8 * y)), A("As", *s), AF.Sigmoid)
-                lin("Vo", A("Vp", 256 * y, 256 * y + 256), A("Vc", 256 * y, 256 * y + 256), 2.0, -1.0)
+                mms([(back, A("At", *s), A("ID32"))])
+                act(A("As", *s), back)
+                act(IND(A("Vc", *v), A("cl", 88 * t + 72 + 8 * y, 88 * t + 80 + 8 * y)), A("As", *s), AF.Sigmoid)
+                lin("Vo", A("Vp", *v), A("Vc", *v), 2.0, -1.0)
                 if t < NS - 1:
                     spread_V(t + 1, y)
                 else:
-                    hand_back("vw"[y], "Vp", 256 * y, 256 * y + 256, "yv")
+                    hand_back("vw"[y], "Vp", *v, (T["yv"][:, v[0]:v[1]], []))
 
     si = lambda j: A("si", 16 * j, 16 * j + 16)
     lu = lambda t, c: A("lu", 256 * t + 32 * c, 256 * t + 32 * c + 32)
@@ -573,15 +587,20 @@ def rank_program(g, core, T, topo):
         mm([(PS(1, 256, 512), A("ones", 0, 128), A("I2k"))] +
            [(PS(1, 256 + 128 * h, 384 + 128 * h), half("LcB", h), A("I2k", 0, 128)) for h in range(2)])
         mm([(PS(1, 0, 256), A("ones", 0, 128), A("Mc"))], True, False)
-        marks()
+        if t:
+            marks()
+        else:
+            act(half("aS", 1), raw[1], scale=SC)
+            ts(half("aS", 0), raw[0], SC, OP.mult)
         hs = [(PS(1, 128 * h, 128 * h + 128), h) for h in range(2)]
         for o, h in hs[::-1]:
-            mm([(o, half("aS", h), M("ID32", h))], False, False)
-        mm([(o, half("fl", h), M("Mf", h)) for o, h in hs], False, False)
-        mm([(o, half("tt", h), M("Mt", h)) for o, h in hs], False, True)
-        if t > 0:
+            mm([(o, half("aS", h), M("ID32", h))], False, t == h == 0)
+        if t:
+            mm([(o, half("fl", h), M("Mf", h)) for o, h in hs], False, False)
+            mm([(o, half("tt", h), M("Mt", h)) for o, h in hs], False, True)
             on("L", powers)
-        mm([(PS(4, 128 * y, 128 * y + 128), M(m, y), half(n, y)) for m, n in (("m8A", "fl"), ("m8I", "tt"), ("ISC", "aS")) for y in range(2)], True, False)
+        mm([(PS(4, 128 * y, 128 * y + 128), M(m, y), half(n, y)) for m, n in (("ISC", "aS"), ("m8A", "fl"), ("m8I", "tt"))[:3 if t else 1] for y in range(2)],
+           True, False)
         scan(A("Mx"), A("rm"), PS(1, 0, 256), OP.mult, OP.max)
         line[0] = "V"
         ts(si(3), A("Mx", 15, 256, 16), 1 / SC, OP.mult, 0.46, OP.add)
@@ -638,7 +657,7 @@ def rank_program(g, core, T, topo):
         if t == NS - 1:
             for e in range(2):
                 ts(A("Ko", e, 512, 2), K2(NS, 256 * e, 256 * e + 256), 12582912.0, OP.add, -12582912.0, OP.add)
-            hand_back("k", "Ko", 0, 512, "yk", "g")
+            hand_back("k", "Ko", 0, 512, (T["yk"][:, :], []), "g")
         spread_views(t)
         mm([(PS(2, 256, 512), A("nI"), A("ones")), (PS(2, 256, 512), A("nI"), A("sS"))], True, False)
         mm([(PS(2, 256, 512), A("PMt"), A("Lp")) if t else (PS(2, 256, 512), A("IDh"), A("LcB"))], False, True)
@@ -659,12 +678,14 @@ def rank_program(g, core, T, topo):
         mm([(PS(1, 400, 432), A("n8k"), A("sg")), (PS(1, 416, 432), A("n8k"), sg[0]), (PS(1, 400, 416), A("n8k"), A("m05"))], True, False)
         mm([(PS(1, 400 + 16 * e, 416 + 16 * e), A("nI"), A(rc, 16 * h, 16 * h + 16)) for e in range(2) for h in range(8)], False, True)
         ts(A("sg"), PS(1, 400, 432), 0.5, OP.is_lt, -0.5, OP.add)
-        mms([(PS(0, b, 512, 16), A("XK", 128 * b, 128 * b + 128), A("sg")) for b in range(16)])
-        tt(A("Tc"), PS(0), K2(t + 1), OP.mult)
+        n = 512 if t else 256
+        mms([(PS(0, b, n, 16), A("XK", 128 * b, 128 * b + 128), A("sg", 0, n // 16)) for b in range(16)])
+        for o in range(0, n, 256):
+            tt(A("Tc", o, o + 256), PS(0, o, o + 256), K2(t + 1, o, o + 256), OP.mult)
         if t < NS - 1:
             cur_lists(t + 1)
             own_K(t + 1)
-        spread_T(SHARE if t < NS - 1 else SHARE_ENDS)
+        spread_T(SHARE if t < NS - 1 else SHARE_ENDS, 0 if t else 2)
         on("V", values, t)
 
     step[0] = NS
@@ -679,105 +700,9 @@ def rank_program(g, core, T, topo):
     emit(g, T, QU, ops, sent[0])
 
 
-def former(ops):
-    n = len(ops)
-    cost = [o["cost"] for o in ops]
-    full = [o["cost"] + o["lat"] for o in ops]
-    queue = [o["q"] for o in ops]
-    need = [[(d, True) for d in sorted(o["deps"])] + [(d, False) for d in sorted(o["order"] - o["deps"])] for o in ops]
-    after = [[] for o in ops]
-    for i in range(n):
-        for d, hard in need[i]:
-            after[d].append((i, hard))
-
-    def fit(taken, t, c):
-        st, en = taken
-        j = len(st)
-        while j > 0 and en[j - 1] > t:
-            j -= 1
-        while j < len(st) and t + c > st[j]:
-            if en[j] > t:
-                t = en[j]
-            j += 1
-        st.insert(j, t)
-        en.insert(j, t + c)
-        return t
-
-    def order(key):
-        key = list(key)
-        for i in range(n):
-            for d, hard in need[i]:
-                if key[d] >= key[i]:
-                    key[i] = key[d] + 1e-3
-        return sorted(range(n), key=lambda j: key[j])
-
-    def forth(key):
-        taken, at, end = {q: ([], []) for q in ("pe", "v", "s", "g", "y", "port", "dma")}, [0.0] * n, [0.0] * n
-        for i in order(key):
-            t = 0.0
-            for d, hard in need[i]:
-                x = end[d] + WAKE if hard else at[d] + cost[d]
-                if x > t:
-                    t = x
-            if queue[i] is not None:
-                t = fit(taken[queue[i]], t, cost[i])
-            at[i], end[i] = t, t + full[i]
-            if ops[i]["hold"]:
-                end[i] = fit(taken["port" if queue[i] is None else "dma"], t + cost[i] + 1400, ops[i]["hold"]) + ops[i]["hold"] + 600
-        return max(end) + 1e-2 * sum(end) / n, at, end
-
-    def back(at, end):
-        taken, lead = {q: ([], []) for q in ("pe", "v", "s", "g", "y")}, [0.0] * n
-        for i in order(end)[::-1]:
-            t = 0.0 if after[i] else end[i] - at[i] - cost[i]
-            for d, hard in after[i]:
-                x = lead[d] + (end[i] - at[i] - cost[i] + WAKE if hard else 0.0)
-                if x > t:
-                    t = x
-            if queue[i] is not None:
-                t = fit(taken[queue[i]], t, cost[i])
-            lead[i] = t + cost[i]
-        return [-x for x in lead]
-
-    def lean(now, key, tries, kinds):
-        best = now
-        for it in range(tries):
-            p = list(key if kinds else now[1])
-            i = int(rng.integers(0, n))
-            x, reach = float(rng.normal()) * STEP, n if kinds else (0, 8, 30, 60)[int(rng.integers(0, 4))]
-            for j in kin[tags[i % len(tags)] if kinds else ops[i]["tag"]]:
-                if abs(j - i) <= reach:
-                    p[j] += x
-            new = forth(p)
-            if not kinds and it % 10 == 0:
-                new = min(new, forth(back(new[1], new[2])), key=lambda z: z[0])
-            if new[0] <= now[0] + SLACK * (1 - it / tries * (not kinds)) * float(rng.exponential()):
-                now, key = new, p
-                if new[0] < best[0]:
-                    best = new
-        return best
-
-    if n not in KEPT:
-        rng = np.random.default_rng(0)
-        rank, kin = [0.0] * n, {}
-        for i in range(n - 1, -1, -1):
-            rank[i] = -full[i] + min([rank[d] - WAKE for d, hard in after[i]], default=0.0)
-            kin.setdefault(ops[i]["tag"], []).append(i)
-        tags = list(kin)
-        best = min([lean(forth(rank), rank, FIRST, True) for _ in range(STARTS)], key=lambda z: z[0])
-        best = lean(best, None, TRIES, False)
-        KEPT[n] = order(best[1])
-        KEPT["times"] = best
-    seq = KEPT[n]
-    place = {j: k for k, j in enumerate(seq)}
-    for j, o in enumerate(ops):
-        assert all(place[d] < place[j] for d in o["deps"] | o["order"])
-        o["deps"] = {place[d] for d in o["deps"]}
-    return [ops[j] for j in seq]
-
-
 def arrange(ops):
     n = len(ops)
+    other = [[o["other"][j] for o in ops] for j in range(2)]
     cost, lat, hold = [o["cost"] for o in ops], [o["lat"] for o in ops], [o["hold"] for o in ops]
     queue = [("pe", "v", "s", "g", "y", None).index(o["q"]) for o in ops]
     hard, soft, behind = [], [], []
@@ -846,6 +771,35 @@ def arrange(ops):
                 end[i] = t + c + lat[i]
         return max(end) + 1e-2 * sum(end) / n, at, end
 
+    def again(new):
+        seq = [i for k, i in sorted(zip(new[1], range(n)))]
+        spans = [span(seq, other[j], LATE[j]) for j in range(2)]
+        return new[0] + BOTH[0] * spans[0] + BOTH[1] * spans[1], new[1], new[2], new[0], spans
+
+    def span(seq, slow, f):
+        free, at, end = [0.0] * 8, [0.0] * n, [0.0] * n
+        for i in seq:
+            q, c = queue[i], slow[i]
+            t = free[q]
+            for d in hard[i]:
+                x = end[d] + WAKE
+                if x > t:
+                    t = x
+            for d in soft[i]:
+                x = at[d] + slow[d]
+                if x > t:
+                    t = x
+            if q < 5:
+                free[q] = t + c
+            at[i] = t
+            if hold[i]:
+                q = 6 if q == 5 else 7
+                free[q] = max(free[q], t + c + 1400 * f) + hold[i] * f
+                end[i] = free[q] + 600 * f
+            else:
+                end[i] = t + c + lat[i] * f
+        return max(end)
+
     def back(at, end):
         st, en, lead = [[] for q in range(5)], [[] for q in range(5)], [0.0] * n
         for i in order(end)[::-1]:
@@ -860,7 +814,7 @@ def arrange(ops):
             lead[i] = t + cost[i]
         return [-x for x in lead]
 
-    def lean(now, key, tries, kinds):
+    def lean(now, key, tries, kinds, both_ways=False):
         best = now
         for it in range(tries):
             p = list(key if kinds else now[1])
@@ -882,14 +836,19 @@ def arrange(ops):
             new = forth(p)
             if not kinds and it % 10 == 0:
                 new = min(new, forth(back(new[1], new[2])), key=lambda z: z[0])
-            if new[0] <= now[0] + SLACK * (1 - it / tries) * float(rng.exponential()):
+            room = SLACK * (1 - it / tries) * float(rng.exponential())
+            if both_ways:
+                if new[0] > now[3] + room + 1500:
+                    continue
+                new = again(new)
+            if new[0] <= now[0] + room:
                 now, key = new, p
                 if new[0] < best[0]:
                     best = new
         return best
 
     if n not in KEPT:
-        rng = np.random.default_rng(0)
+        rng = np.random.default_rng(SEED)
         kin, line, seat, met, ranks = {}, {}, [], {}, []
         for i in range(n):
             kin.setdefault(ops[i]["tag"], []).append(i)
@@ -905,7 +864,9 @@ def arrange(ops):
             met[o["step"], o["tag"]] = met.get((o["step"], o["tag"]), -1) + 1
             seat.append((o["step"], met[o["step"], o["tag"]]))
         best = [lean(lean(forth(rank), rank, FIRST, True), None, FIRST, False) for _, rank in ranks[:STARTS]]
-        best = lean(min(best, key=lambda z: z[0]), None, TRIES, False)
+        best = [lean(again(z), None, MORE, False, True) for z in best]
+        best = lean(min(best, key=lambda z: z[0]), None, TRIES, False, True)
+        best = lean(best, None, 4 * TRIES, False, True)
         KEPT[n] = order(best[1])
         KEPT["times"] = best
     seq = KEPT[n]

@@ -12,11 +12,15 @@ LN64 = math.log(64.0)
 LOW, POW = 16.0, 18
 RATES, BOTH, LATE = ((1.0, 1.5, 3.5, 0.5), (1.2, 2.3, 6.0, 0.6), (0.84, 1.1, 2.5, 0.42)), (0.4, 0.8), (1.0, 0.95)
 WAKE, VLAT, LONG = 80.0, 4400.0, 3500.0
-STARTS, FIRST, TRIES, STEP, SLACK, KEPT = 2, 1500, 5000, 4000.0, 300.0, {}
-SHARE, SHARE_ENDS, SHARE_VT = (1, 6), (1, 3, 5, 7), (1, 3)
+STARTS, FIRST, TRIES, STEP, SLACK, KEPT = 2, 300, 100000, 4000.0, 300.0, {}
+SHARE, SHARE_ENDS, SHARE_VT = (3,), (1, 3, 5, 7), (1,)
+SHARE_LAST, LAST_S = (1, 5), ()
+P_LAST = 1
+T_DMA, TP, TLAT = ((), (), (), ()), 4, 3800.0
 OWN, SEED, MORE = 2, 2, 3500
+V_PUT = (0, 1, 2, 3)
 BY_DMA = (0, 1, 2)
-ON_S = {"D0", "D1", "x16", "MTs", "Lp", "W2", "L0", "Vo", "Lh"}
+ON_S = {"D0", "D1", "D2", "x16", "MTs", "Lp", "L0", "Vo", "Lh", "dx", "fl0", "fl1", "Ko", "Lo", "Ly", "rc", "Tp"}
 WB, TB, VB = (5, 6), (4, 0, 1), (3, 4)
 SCRATCH = {}
 
@@ -28,27 +32,27 @@ def _sb(dtype, **kw):
 
 SL = (16, 16)
 RING = 4
-_sb(BF, Tt=4096, V0=4096, K0=512, Kb=512, Vb=512, KK=1536, Tc=512, own=640, P=2048, G=768 * RING, diag=1024, fl=SL, tt=SL, sS=256, pw=256, z=512, R=(128, 16), BO=128, EB=144,
-    SEL=1024, SEL0=1024, XK=2048, Hs=512, IE2=272, Mc=256, I2k=256, ones=256, tmp=128, Cs=256, Cz=384, Ko=512, gkB=256, Wt=64, Wt0=64, Q8=8, m05=16)
-_sb(F, Vt=8192, E=(16, 512), Y=4096, Vc=512, Vp=512, VT=2048, Lf=256, Lo=256, aS=SL, Mx=256, us=256, d1=256, Bx=256, As=256, At=256,
-    iot=272, ioq=128, iok=256, ioa=256, ioj=256, pc=24, mk=24, ID32=128, ISC=128, ID320=128, ISC0=128, rm=256, wL=16, m16=16, iob=128)
-_sb(HF, LcB=SL, Lq=SL, Ly=SL, Lp=SL, Lh=SL, Ls=SL, R0=SL, L0=256, W2=256, ga=256, D=(32, 16), D2=(32, 16), x16=SL, IEh=272, thZ=128, cL=88, sg=32, MR=32,
-    d16=16, MTs=256, rc0=128, rc1=128, rc2=128, rc3=128)
+_sb(BF, Tt=4096, V0=4096, K0=512, V1=512, Kb=512, Vb=512, KK=1536, Tc=512, Tp=512, own=640, P=2048, G=768 * RING, diag=1024, fl=SL, tt=SL, sS=256, pw=256, z=512, R=(128, 16), BO=128, EB=144,
+    SEL=1024, SEL0=1024, XK=2048, Hs=512, IE2=272, Mc=256, I2k=256, ones=256, rm=256, Cs=256, Cz=384, Ko=512, gkB=256, Wt=64, Wt0=64, Q8=8, m05=16)
+_sb(F, Vt=8192, E=8192, Y=4096, d16=32, Vc=512, Vp=512, VT=2048, Lf=256, Lo=256, aS=SL, Mx=256, us=256, d1=256, Bx=256, As=256, At=256,
+    iot=272, ioq=128, ioj=256, pc=24, mk=24, ID32=128, ISC=128, ID320=128, ISC0=128, wL=16, m16=16)
+_sb(HF, LcB=SL, Lq=SL, Ly=SL, Lp=SL, Lh=SL, Ls=SL, R0=256, L0=256, ga=256, D=(32, 16), D2=(32, 16), x16=SL, IEh=272, thZ=128, cL=88, sg=32, MR=112,
+    dx=128, W16=48, xf=8, MTs=256, rc0=128, rc1=128, rc2=128, rc3=128)
 _sb(I, Li=256, thI=16, pi=8, si=160)
-_sb(U, lu=1280, lv=1024, bl=16, dl=16, dg=8, cl=352)
+_sb(U, lu=1280, lv=1024, bl=16, dl=16, dg=8, xl=8, cl=352)
 PART = {}
-for _n in "Mf Mt m8A Bc Mf0 Mt0 m8A0 Bm0 Am0 m8I0 n640 I40 n600 Bm nU m8I PMb Am LE nI PMv PMt Iy Iq I4 n60 PMk IDh n64 n8k I256 n512 Ia Ib Ic Id".split():
+for _n in "Bm m8A Mf Mt Bc m8A0 Mf0 Mt0 Bm0 Am0 m8I0 n640 I40 n600 Us nU m8I PMb Am LE nI PMv PMw PMh PMy PMq PMt Iy Iq I4 n60 PMk IDh n64 n8k I256 n512 Ia Ib Ic Id I240 n2032".split():
     PART[_n] = ("cmat", 128 * len(PART))
 _sb(BF, cmat=128 * len(PART))
 for _i in range(8):
     SCRATCH["p%d" % _i] = ("psum", [128, 512] if _i == 1 else [128, 32, 16], F)
 SCRATCH["SKd"] = ("dram", [8, 128, 64], BF)
 SCRATCH["Vd"] = ("dram", [4, 16, 8, 256], F)
-SCRATCH["V0d"] = ("dram", [16, 2, 8, 256], BF)
-for _n, _c, _d in (("V", 64, BF), ("k", 64, BF), ("v", 32, F), ("w", 32, F)):
+SCRATCH["SVd"] = ("dram", [8, 128, 64], BF)
+for _n, _c, _d in (("k", 64, BF), ("v", 32, F), ("w", 32, F)):
     SCRATCH["S" + _n + "d"] = ("dram", [8, 128, _c], _d)
     SCRATCH["R" + _n + "d"] = ("dram", [8, 128, _c], _d)
-SEMAPHORES = ["pe", "v", "s", "g", "sent"] + ["d%d" % i for i in range(48)] + ["a%d" % i for i in range(14)]
+SEMAPHORES = ["pe", "v", "s", "g", "sent"] + ["d%d" % i for i in range(64)] + [_c + str(i) for _c in "ab" for i in range(14)]
 
 
 def spread(topo, src, dsts):
@@ -238,21 +242,32 @@ def rank_program(g, core, T, topo):
         a = topo.addr(c)
         return DstId(rid=a[0], pnc=a[1])
 
-    def trade(src, land, lat=4800.0):
-        sem = "a%d" % len(calls)
+    near = [q for q in range(8) if topo.chip(cores[q]) == topo.chip(core)]
+    far = [q for q in range(8) if q not in near]
+
+    def trade(src, land, lat=4800.0, soon=0):
+        sem = lambda q: "%s%d" % ("b" if soon and q in near else "a", len(calls))
         mk = spread(topo, core, others)
-        trs = [RemoteDMATransfer(dst_ids=[dst(c)], dma_engine_mask=mk[c][0], remote_sem=T.sem[sem], src=src(T.rank_of(c))[0], dst=land(r)[0]) for c in others]
+        trs = [RemoteDMATransfer(dst_ids=[dst(c)], dma_engine_mask=mk[c][0], remote_sem=T.sem[sem(T.rank_of(c))], src=src(T.rank_of(c))[0], dst=land(r)[0]) for c in others]
         sent[0] += sum(mk[c][1] for c in others)
         rec("g", lambda: g.remote_dma_fused(trs, local_sem=T.sem.sent), regs(*[src(q) for q in range(8) if q != r]), [], "-", 0, 300.0,
             after=calls[-1:] if len(calls) < 3 else [])
-        calls.append(len(ops) - 1)
-        n = sum(spread(topo, c, [x for x in cores if x != c])[core][1] for c in others)
-        rec(None, None, [], regs(*[land(q) for q in range(8) if q != r]), sem, n, 0.0, lat, calls[-1:])
+        call = len(ops) - 1
+        for qs, ns in ((near, soon), (far, lat)) if soon else ((near + far, lat),):
+            qs = [q for q in qs if q != r]
+            n = sum(spread(topo, cores[q], [x for x in cores if x != cores[q]])[core][1] for q in qs)
+            rec(None, None, [], regs(*[land(q) for q in qs]), sem(qs[0]), n, 0.0, ns, [call])
+            if ns == soon:
+                ops[-1]["hold"] = 0.0
+        calls.append(call)
 
     X = lambda n, a, b: (T[n][a:b, :], [])
     col = lambda n, j, p1=128: A(n, j, j + 1, p1=p1)
     PS = lambda i, a=0, b=512, st=1, p1=128: A("p%d" % i, a, b, st, p1=p1)
     half = lambda n, y, r0=0: B(n, r0 + 8 * y, r0 + 8 * y + 8)
+
+    def view(t, y, n="LcB"):
+        return A("R0" if n == "LcB" else n, y, 256, 2) if t % NS == 0 else half(n, y)
 
     def swap(out, src, ie="IEh"):
         mm([(out(x, 32 * a), A(ie, 32 * x + 16 - 16 * u, 32 * x + 48 - 16 * u), src(2 * a + u)) for x in range(8) for a in range(4) for u in range(2)], each=2)
@@ -262,16 +277,13 @@ def rank_program(g, core, T, topo):
     dma("y", [(D("SVd"), X("v0", 0, 128))])
     dma("s", [(A("thI", p1=64), X("th", 0, 4))])
     dma("y", [(A("K0", 64 * r, 64 * r + 64), X("k0", 16 * r, 16 * r + 16))])
-    dma("s", [(D("RVd", r), X("v0", 16 * r, 16 * r + 16))])
+    dma("s", [(A("V1", 64 * r, 64 * r + 64), X("v0", 16 * r, 16 * r + 16))])
     iota(col("pi", 0), [[0, 1]], 1, False)
     iota(A("iot"), [[1, 272]])
-    iota(A("iok"), [[0, 16], [1, 16]])
     iota(A("ioq"), [[1, 8], [0, 16]])
-    iota(A("ioa"), [[0, 32], [1, 8]])
     iota(A("ioj"), [[0, 4], [1, 8], [0, 8]])
-    iota(A("iob"), [[1, 16], [0, 8]])
 
-    p_, q_, k_, kq_, e_, yb_, pk_, pb_, lb_, cs1_, cs2_, ie_, h0_, h1_, cs3_, xb_, h2_, h3_, od_, kh_, kn_, pb0_ = [col("pc", j) for j in range(22)]
+    p_, q_, k_, kq_, e_, yb_, pk_, pb_, lb_, cs1_, cs2_, ie_, h0_, h1_, cs3_, xb_, h2_, h3_, od_, kh_, kn_, pb0_, eb_ = [col("pc", j) for j in range(23)]
     ts(col("pi", 1), col("pi", 0), 4, OP.arith_shift_right)
     ts(col("pi", 2), col("pi", 0), 15, OP.bitwise_and)
     cp(A("pc", 0, 3), A("pi", 0, 3))
@@ -279,7 +291,7 @@ def rank_program(g, core, T, topo):
     ts(ie_, q_, 16.0, OP.mult, p_, OP.add)
     ts(A("IEh"), A("iot"), -16.0, OP.add, ie_, OP.is_equal)
 
-    trade(lambda q: D("SKd", q), lambda q: A("K0", 64 * q, 64 * q + 64), 6300.0)
+    trade(lambda q: D("SKd", q), lambda q: A("K0", 64 * q, 64 * q + 64), 6300.0, 4300.0)
     ts(A("IDh"), io128, p_, OP.is_equal)
     ts(A("L0"), A("Li"), -2048.0, OP.add, 1.0 / 2048, OP.mult)
     for n, c in (("Iy", 1792 / 2048), ("Iq", -3840 / 2048)):
@@ -289,19 +301,23 @@ def rank_program(g, core, T, topo):
     mm([(PS(3, 0, 256), A(m), A(n)) for m, n in (("IDh", "L0"), ("Iy", "Ly"), ("Iq", "Lq"))])
     lin("Ls", A("Ls"), PS(3, 0, 256), 1.0, 1025.0)
     swap(lambda x, p: B("p2", 2 * x, 2 * x + 2, 1, 0, 16, 1, p, p + 32), lambda q: B("Ls", q, 16, 8))
-    lin("L0", A("L0"), PS(2, 0, 256))
+    for y in range(2):
+        lin("L0", A("L0", y, 256, 2), B("p2", y, 16, 2))
     trade(lambda q: A("L0", 32 * q, 32 * q + 32), lambda q: A("R0", 32 * q, 32 * q + 32), 4500.0)
     cp(A("R0", 32 * r, 32 * r + 32), A("L0", 32 * r, 32 * r + 32))
-    trade(lambda q: D("SVd", q), lambda q: D("RVd", q), 6000.0)
-    dma("y", [(A("Kb", p0=16 * q, p1=16 * q + 16), A("K0", 64 * q, 64 * q + 64)) for q in range(8)])
-    dma("y", [(A("Vb"), D("RVd"))])
+    trade(lambda q: D("SVd", q), lambda q: A("V1", 64 * q, 64 * q + 64), 6000.0)
+    for n in "KV":
+        dma("y", [(A(n + "b", p0=16 * q, p1=16 * q + 16), A({"K": "K0", "V": "V1"}[n], 64 * q, 64 * q + 64)) for q in range(8)])
 
-    for c in range(RING):
-        fill(A("G", 768 * c, 768 * c + 256), 0.0)
+    fill(A("G", 0, 256), 0.0)
+    dma("y", [(A("G", 768 * c, 768 * c + 256), A("G", 0, 256)) for c in range(1, RING)] + [(A("diag", c, c + 256), A("G", 0, 256)) for c in range(0, 1024, 256)])
 
     def pick(o, pat, c, base=0, src=None, p1=128):
         src = src or A("G", 0, wide(o), p1=p1)
         rec("g", lambda: g.affine_select(o[0], src[0], pat, OP.not_equal, float(c), base, 1), src[1], o[1], cost=170 + 2 * wide(o))
+
+    def keep(o, src, pat, op, cm):
+        rec("g", lambda: g.affine_select(o[0], src[0], pat, op, 0.0, 0, cm), src[1], o[1], cost=170 + 2 * wide(o))
 
     for j in range(4):
         pick(A("SEL0", 256 * j, 256 * j + 256), [[-1, 2], [0, 8], [-8, 16]], 1, -2 * j)
@@ -311,7 +327,7 @@ def rank_program(g, core, T, topo):
         pick(A("XK", 256 * j, 256 * j + 256), [[-1, 2], [-16, 8], [0, 16]], 1, -2 * j)
     pick(A("Hs", 0, 256), [[-8, 2], [0, 16], [-1, 8]], -1)
     pick(A("Hs", 256, 512), [[-8, 2], [-1, 8], [0, 16]], 1)
-    for n, c in (("n64", -64), ("n8k", -8192), ("nI", -1), ("Ia", 1 / 32), ("Ib", -2), ("Ic", 1 / 2048), ("Id", -1 / 32), ("I4", 4), ("n60", -60)):
+    for n, c in (("n64", -64), ("n8k", -8192), ("nI", -1), ("Ia", 1 / 32), ("Ib", -2), ("Ic", 1 / 2048), ("Id", -1 / 32), ("I4", 4), ("n60", -60), ("I240", 240), ("n2032", -2032)):
         pick(A(n), [[-1, 128]], c)
     pick(A("PMt"), [[-1, 8], [-8, 16]], 1)
     pick(A("IE2", 0, 16), [[1, 16]], 0, 1)
@@ -330,11 +346,14 @@ def rank_program(g, core, T, topo):
     ts(pk_, kh_, -2.0, OP.mult, 16.0, OP.add)
     ts(kh_, pk_, p_, OP.add)
     ts(A("dg"), A("iot", 0, 8), 128.0, OP.mult, kq_, OP.add)
-    fill(A("diag"), 0.0)
     ts(A("PMk"), io128, kh_, OP.is_equal, 2048.0, OP.mult)
     ts(A("PMv"), io128, kq_, OP.is_equal, 2048.0, OP.mult)
-    for y in range(2):
-        cp(half("LcB", y), B("R0", y, 16, 2))
+    ts(col("pi", 7), col("pi", 0), 1, OP.bitwise_and)
+    ts(eb_, col("pi", 7), -7.0, OP.mult, kq_, OP.add)
+    ts(eb_, eb_, q_, OP.add)
+    ts(A("PMw"), io128, eb_, OP.is_equal, 2048.0, OP.mult)
+    for n, c in (("PMh", 448), ("PMy", -1984), ("PMq", 1536)):
+        act(A(n), A("PMw"), scale=c / 2048)
     ts(A("mk", 0, 16), A("iot", 0, 16), k_, OP.is_equal)
     ts(A("mk", 16, 24), A("iot", 0, 8), q_, OP.is_equal)
     cp(A("Q8"), A("mk", 16, 24))
@@ -344,51 +363,64 @@ def rank_program(g, core, T, topo):
     fill(A("ones"), 1.0)
     act(A("m05"), A("ones", 0, 16), AF.Sigmoid, scale=0.0)
     ts(A("sg"), A("iot", 0, 32), 0.0, OP.mult, -0.5, OP.add)
-    ts(A("LE"), A("iok", 0, 128), k_, OP.is_ge)
+    keep(A("LE"), A("BO"), [[1, 128]], OP.is_ge, -1)
+    keep(A("rm"), A("ones"), [[0, 16], [1, 16]], OP.not_equal, 0)
     for n, c in (("I256", 256), ("n512", -512)):
         act(A(n), A("IDh"), scale=float(c))
     ts(A("wL"), A("iot", 0, 16), 16.0, OP.mult, k_, OP.add)
     for j, (m, c) in enumerate(((1, 128), (1, 256), (1, 384), (2, 0.5))):
         ts(A("cL", 24 + 16 * j, 40 + 16 * j), A("wL"), float(m), OP.mult, float(c), OP.add)
     ts(A("cL", 80, 88), A("cL", 80, 88), -256.0, OP.add)
+    for y in range(2):
+        ts(cs3_, q_, 256.0, OP.mult, 1792.0 * y, OP.add)
+        ts(A("cl", 8 * y, 8 * y + 8), A("wL", 8 * y, 8 * y + 8), 2.0, OP.mult, cs3_, OP.add)
     for n, c in (("ID32", 1), ("Mt", -C8 * SC), ("I2k", 2048)):
         act(A(n, 0, 128), A("IDh"), scale=float(c))
     act(A("I2k", 128, 256), A("IDh"), scale=2048.0)
-    tt(A("LE"), A("LE"), A("BO"), OP.mult)
-    tt(A("Am"), A("BO"), A("LE"), OP.subtract)
-    ts(kn_, k_, -1.0, OP.mult, -1.0, OP.add)
-    act(A("nU"), A("IDh"), AF.Identity, scale=kn_)
-    tt(A("Bm"), A("LE"), A("Am"), OP.subtract)
-    tt(A("Bm"), A("Bm"), A("nU"), OP.add)
     act(A("ISC"), A("PMb"), scale=1 / SC)
-    act(A("m8I"), A("PMb"), scale=-8.0)
-    ts(A("m8A"), A("iob"), k_, OP.is_lt, -8.0, OP.mult)
-    ts(A("tmp"), A("ioa", 0, 128), q_, OP.is_equal)
-    tt(A("m8A"), A("m8A"), A("tmp"), OP.mult)
 
-    for o, a, ci in ((A("Mf"), "Am", SC / 32), (A("Mc", 0, 128), "LE", 136 * SC), (A("Mc", 128, 256), "LE", 136 * SC)):
+    def sloped(o, a, ci):
         act(o, A(a), scale=-C8 * SC)
         pick(o, [[-1, 128]], ci, 0, o)
-    ts(A("Bc"), A("m8A"), 0.25, OP.mult)
-    tt(A("Bc"), A("Bc"), A("tmp"), OP.add)
-    act(A("nU"), A("PMb"), AF.Identity, scale=kn_)
-    tt(A("Bc"), A("Bc"), A("nU"), OP.add)
-    mms([(PS(3), A("PMb"), A("Mf", 0, 512))])
-    act(A("Mf0", 0, 512), PS(3))
-    act(A("Am0"), A("m8A0"), scale=-0.125)
-    act(A("m8I0"), A("IDh"), scale=-8.0)
+
+    for h in range(2):
+        sloped(A("Mc", 128 * h, 128 * h + 128), "LE", 136 * SC)
+
+    def mark_constants():
+        keep(A("Am"), A("BO"), [[-1, 128]], OP.is_gt, 1)
+        keep(A("Us"), A("BO"), [[1, 128]], OP.is_gt, -1)
+        sloped(A("Mf"), "Am", SC / 32)
+        ts(kn_, k_, -1.0, OP.mult, -1.0, OP.add)
+        act(A("nU"), A("IDh"), AF.Identity, scale=kn_)
+        act(A("m8I"), A("PMb"), scale=-8.0)
+        mm([(PS(3, 0, 128), A(m), A(n)) for m, n in (("IDh", "BO"), ("Ib", "Am"), ("IDh", "nU"))])
+        mms([(PS(3, 128, 256), A("Us"), A("m8I"))])
+        act(A("Bm", 0, 256), PS(3, 0, 256))
+        mms([(PS(3, 0, 128), A("Bm"), A("PMb"))])
+        act(A("Bc"), PS(3, 0, 128))
+        mms([(PS(3, 0, 384), A("PMb"), A("m8A", 0, 384)), (PS(3, 384, 512), A("Bc"), A("PMb"))])
+        act(A("m8A0", 0, 512), PS(3))
+        act(A("Am0"), A("m8A0"), scale=-0.125)
+        act(A("m8I0"), A("IDh"), scale=-8.0)
+
     act(A("ISC0"), A("IDh"), scale=1 / SC)
     act(A("ID320"), A("PMt"))
     for n, c in (("n640", -64), ("I40", 4), ("n600", -60)):
         pick(A(n), [[-1, 16], [-16, 8]], c)
     M = lambda n, y, *a: A(n if y else {"IDh": "PMb", "I2k": "PMv"}.get(n, n + "0"), *a)
-    ts(A("rm"), A("iok"), 0.0, OP.not_equal)
     ts(A("m16"), A("mk", 0, 16), math.exp(LOW) / 8, OP.mult)
     ts(A("thZ", p1=64), A("iot", 0, 128, p1=64), 0.0, OP.mult)
     ts(A("thZ", 16 * r, 16 * r + 16, p1=64), A("thI", p1=64), -1.0, OP.mult)
     ts(yb_, k_, -15.5, OP.add)
     ts(col("pi", 5), col("pi", 0), 120, OP.bitwise_and)
     ts(xb_, col("pi", 5), -1.0, OP.mult, 136.0, OP.add)
+    ts(col("pi", 6), col("pi", 0), 7, OP.bitwise_and)
+    ts(h2_, col("pi", 6), q_, OP.is_equal)
+    ts(h3_, od_, 8.0, OP.mult, -16.0, OP.add)
+    ts(A("xf"), A("iot", 0, 8), h3_, OP.add, h2_, OP.mult)
+    ts(A("xl"), A("xf"), 16.0, OP.add)
+    ts(A("d16", 16, 32), A("iot", 0, 16), 0.0, OP.mult)
+    ts(A("W16"), A("iot", 0, 48), -16.0, OP.add, k_, OP.is_equal)
 
     def sort_constants():
         ts(pb_, k_, -float(POW), OP.add, LN64, OP.mult)
@@ -409,24 +441,25 @@ def rank_program(g, core, T, topo):
         ts(pb0_, xb_, -LN64 / 8, OP.mult, (17 - POW) * LN64, OP.add)
         act(B("D2", 0, 32, 1, 8, 16), A("ones"), scale=0.0)
 
-    def spread_T(share, first=0):
+    def spread_T(share, first=0, copied=()):
+        for y in copied:
+            mms([(PS(TP, 256 * y + e, 256 * y + 256, 2), A("m8I"), A("Tc", 256 * e + 128 * y, 256 * e + 128 * y + 128)) for e in range(2)])
+            lin("Tp", A("Tp", 256 * y, 256 * y + 256), PS(TP, 256 * y, 256 * y + 256), 0.25)
+            dma("y", [(A("Tt", 2048 * y, 2048 * y + 2048, p0=16 * a, p1=16 * a + 16), A("Tp", 256 * y, 256 * y + 256)) for a in range(8)], TLAT)
         for q in range(8):
             b = TB[q % len(TB)]
             y, q0 = q // 4, 2 * (q % 4)
             if first != 1:
                 e, y, q0 = q // 4, q // 2 % 2, 4 * (q % 2)
-                if e == 0 or first == 0:
+                if (e == 0 or first == 0) and y not in copied:
                     o = 256 * e + 128 * y
                     mms([(PS(b, 128 * j, 128 * j + 128), A("SEL", 128 * (q0 + j), 128 * (q0 + j + 1)), A("Tc", o, o + 128)) for j in range(4)])
                     (cp if q in share else act)(A("Tt", 1024 * (q % 4) + e, 1024 * (q % 4) + 1024, 2), PS(b))
                 continue
-            if first:
-                mms([(PS(b, 256 * j + 64 * h, 256 * j + 64 * h + 64), A("SEL0", 128 * (4 * y + h), 128 * (4 * y + h + 1)), A("Tc", 64 * (q0 + j), 64 * (q0 + j + 1)))
-                     for j in range(2) for h in range(4)])
-            else:
-                mms([(PS(b, 256 * j + e, 256 * j + 256, 2), A("SEL", 128 * (q0 + j), 128 * (q0 + j + 1)), A("Tc", 256 * e + 128 * y, 256 * e + 128 * y + 128))
-                     for j in range(2) for e in range(2)])
-            (cp if q in share else act)(A("Tt", 512 * q, 512 * q + 512), PS(b))
+            y, q0 = q % 2, (near + far)[2 * (q // 2)]
+            mms([(PS(b, 256 * j + 64 * h, 256 * j + 64 * h + 64), A("SEL0", 128 * (4 * y + h), 128 * (4 * y + h + 1)), A("Tc", 64 * (q0 + j), 64 * (q0 + j + 1)))
+                 for j in range(2) for h in range(4)])
+            (cp if q in share else act)(A("Tt", 2048 * y + 256 * q0, 2048 * y + 256 * q0 + 512), PS(b))
 
     def spread_V(t, y):
         j, o = 2 * (t % 2) + y, 4096 * (t % 2) + 2048 * y
@@ -434,22 +467,19 @@ def rank_program(g, core, T, topo):
         dma("y", [(A("Vt", o, o + 2048, p0=16 * a, p1=16 * a + 16), D("Vd", j)) for a in range(8)], LONG)
 
     def first_V():
-        dma("y", [((T["V0d"][:, :, q, :], D("V0d")[1]), D("RVd", q)) for q in range(8)])
-        dma("y", [(A("V0", p0=16 * a, p1=16 * a + 16), D("V0d")) for a in range(8)], LONG)
+        dma("y", [(A("V0", p0=16 * a, p1=16 * a + 16), A("V1")) for a in range(8)], VLAT)
 
     def lists(t):
-        mms([(PS(2, 128 * y, 128 * y + 128), half("LcB", y), A(("PMv", "PMk")[y])) for y in range(2)])
+        mms([(PS(2, 128 * y, 128 * y + 128), view(t, y), A(("PMv", "PMk")[y])) for y in range(2)])
         lin("lu", A("lu", 256 * t, 256 * t + 256), PS(2, 0, 256), 1.0, 2048.0)
+        if t % NS == 0:
+            lin("Lq", A("Lq"), A("R0"), 1.0, 1026 - 1023.5 / 2048)
+            lin("Ly", A("Ly"), A("R0"), 8.0, 1033 - 127.5 / 256)
+        lin("Lh", A("Lh"), A("LcB" if t % NS else "R0"), 32.0, 1057 - 31.5 / 64)
         if t < NS:
-            mms([(B("p2", 16 + y, 32, 2), half("LcB", y), A("PMv")) for y in range(2)])
-            lin("W2", A("W2"), PS(2, 256, 512))
-            swap(lambda q, p: B("p2", q, 16, 8, 0, 16, 1, p, p + 32), lambda x: A("W2", 32 * x, 32 * x + 32))
-            lin("lv", A("lv", 256 * t, 256 * t + 256), PS(2, 0, 256), 1.0, 2048.0)
-        else:
-            lin("Lq", A("Lq"), A("LcB"), 1.0, 1026 - 1023.5 / 2048)
-            lin("Ly", A("Ly"), A("LcB"), 8.0, 1033 - 127.5 / 256)
-        if t:
-            lin("Lh", A("Lh"), A("LcB"), 32.0, 1057 - 31.5 / 64)
+            terms = (("PMw", "LcB"),) if t else (("PMw", "LcB"), ("PMh", "Lh"), ("PMy", "Ly"), ("PMq", "Lq"))
+            mm([(PS(2, 256 + 128 * y, 384 + 128 * y), A(m), view(t, y, n)) for y in range(2) for m, n in terms], each=len(terms))
+            lin("lv", A("lv", 256 * t, 256 * t + 256), PS(2, 256, 512), 1.0, 2048.0)
 
     def cur_lists(t):
         mm([(PS(1, 280, 344), A("IDh"), A("cL", 24, 88))] +
@@ -459,7 +489,7 @@ def rank_program(g, core, T, topo):
     K2 = lambda t, a=0, b=512: A("KK", 768 * (t % 2) + a, 768 * (t % 2) + b)
 
     def own_K(t):
-        act(A("own", 384, 640), IND(K2(t), A("cl", 88 * t + 24, 88 * t + 40)))
+        act(A("own", 384, 640), IND(K2(t), A("cl", 88 * t + 24, 88 * t + 40)) if t else IND(A("Tt"), A("cl", 0, 16)))
         cp(IND(A("diag"), A("dg")), A("own", 512, 640))
         cp(A("own", 256, 384), A("own", 384, 512))
         cp(A("own", 0, 256), A("own", 256, 512))
@@ -468,7 +498,8 @@ def rank_program(g, core, T, topo):
 
     lists(0)
     cur_lists(0)
-    ts(A("Tc"), A("K0"), EPS, OP.max)
+    for qs in (near, far):
+        ts(A("Tc", 64 * qs[0], 64 * qs[-1] + 64), A("K0", 64 * qs[0], 64 * qs[-1] + 64), EPS, OP.max)
     spread_T(SHARE_ENDS, 1)
     for e in range(2):
         ts(K2(0, 256 * e, 256 * e + 256), A("Kb", e, 512, 2), EPS, OP.max)
@@ -480,21 +511,29 @@ def rank_program(g, core, T, topo):
             if t < NS:
                 tt(A("P", 512 * a, 512 * a + 512), IND(A("Tt"), lu(t, a)), A("own", 0, 512), OP.mult)
             else:
-                cp(A("P", 512 * a, 512 * a + 512), IND(A("Tt"), lu(t, a)))
+                (act if a in LAST_S else cp)(A("P", 512 * a, 512 * a + 512), IND(A("Tt"), lu(t, a)))
             act(A("G", o + 256, o + 768), IND(A("Tt"), lu(t, 4 + a)))
             k = lambda u, w: A("diag", 128 * (2 * a + u) + 8 * w, 128 * (2 * a + u) + 8 * w + 8) if t < NS else A("Q8")
             mm([(B("p4", 16, 24, 1, w, w + 1, 1, 32 * a, 32 * a + 16 + 16 * u), A("G", o + 512 * (1 - u) + w, o + 768 - 256 * u, 16), k(u, w))
                 for w in range(16) for u in (1, 0)], each=2)
-        mms([(B("p0", 0, 8, 1, w, w + 1), A("P", w, 2048, 16), A("Q8")) for w in range(16)])
+            if a >= 4 - P_LAST:
+                mms([(B("p0", 0, 8, 1, w, w + 1, 1, 32 * a, 32 * a + 32), A("P", 512 * a + w, 512 * a + 512, 16), A("Q8")) for w in range(16)])
+            elif a == 3 - P_LAST:
+                mms([(B("p0", 0, 8, 1, w, w + 1, 1, 0, 32 * a + 32), A("P", w, 512 * a + 512, 16), A("Q8")) for w in range(16)])
 
     raw = (PS(0, 0, 128), PS(4, 256, 384))
 
     def marks(more=1):
         for y in range(2):
-            if y == 0 and more:
+            if y == 0 and more and "fl1" not in ON_S:
                 act(half("aS", 1), raw[1], AF.Abs, scale=SC)
-            ts(half("fl", y), raw[y], 0.0, OP.is_lt)
+            if more and "fl%d" % y in ON_S:
+                act(half("fl", y), raw[y], AF.Sigmoid, scale=-16.0 / EPS ** 2)
+            else:
+                ts(half("fl", y), raw[y], 0.0, OP.is_lt)
         if more:
+            if "fl1" in ON_S:
+                act(half("aS", 1), raw[1], AF.Abs, scale=SC)
             act(half("aS", 0), raw[0], AF.Abs, scale=SC)
         mms([(half("p2", y), M("Bm", y), half("fl", y)) for y in range(2)])
         tt(A("tt"), A("fl"), PS(2, 0, 256), OP.mult)
@@ -502,9 +541,9 @@ def rank_program(g, core, T, topo):
     def digits(last=0):
         one = A("ones", p1=32)
         mm([(PS(3, 0, 256), A("Cz", 256 * last, 256 * last + 128, p1=32), one)] +
-           [(half("p3", y), M(m, y), half(n, y)) for m, n in [("IDh", "Lh")] + [("I4", "Ly"), ("n60", "Lq")] * last for y in range(2)])
+           [(half("p3", y), M(m, y), view(1 - last, y, n)) for m, n in [("IDh", "Lh")] + [("I4", "Ly"), ("n60", "Lq")] * last for y in range(2)])
         mm([(PS(3, 256, 512), A("Cz", 128, 256, p1=32), one)] +
-           [(half("p3", y, 16), M(m, y, 0, 128), half(n, y)) for m, n in (("I2k", "LcB"), ("n64", "Lh")) for y in range(2)])
+           [(half("p3", y, 16), M(m, y, 0, 128), view(1 - last, y, n)) for m, n in (("I2k", "LcB"), ("n64", "Lh")) for y in range(2)])
 
     def powers():
         mm([(half("p0", y, 16), M("Am", y), half("fl", y)) for y in range(2)] + [(PS(0, 256, 512), A("IDh"), A("tt"))])
@@ -522,7 +561,7 @@ def rank_program(g, core, T, topo):
                 for h in range(2) for y in range(2)], False, a == 7)
         lin("D1", B("D", 0, 32, 1, 8, 16), PS(3, 0, 256), 1.0 / 64, 1057 - 31.5 / 64)
         lin("D0", B("D", 0, 32, 1, 0, 8), PS(3, 0, 256))
-        if "D2" in ON_S:
+        if "D2" in ON_S and not last:
             lin("D2", B("D2", 0, 32, 1, 0, 8), PS(3, 0, 256), 1.0 / 64, 1057 - 31.5 / 64)
         else:
             cp(B("D2", 0, 32, 1, 0, 8), B("D", 0, 32, 1, 8, 16))
@@ -544,10 +583,10 @@ def rank_program(g, core, T, topo):
     def weights(t):
         lin("x16", A("x16"), PS(4, 0, 256), 1.0, xb_)
         for c in range(8):
-            b, y, j, u = WB[c % len(WB)], c // 4, c // 2 % 2, c % 2
-            mms([(B("p%d" % b, x, 32, 8), A("XK", 128 * (8 * u + x), 128 * (8 * u + x + 1)), B("x16", 8 * y + j, 8 * y + 8, 2)) for x in range(8)])
-            o = 8 * (t % 2) + 4 * y
-            act(B("E", o, o + 4, 1, 256 * j + 128 * u, 256 * j + 128 * u + 128), PS(b), AF.Sigmoid, bias=-1860.0 / 256 - LOW, scale=1.0 / 256)
+            b, j, u = WB[c % len(WB)], c // 2, c % 2
+            mms([(PS(b, x, 512, 8), A("XK", 128 * (8 * u + x), 128 * (8 * u + x + 1)), B("x16", 4 * j, 4 * j + 4)) for x in range(8)])
+            o = 4096 * (t % 2) + 1024 * j
+            act(A("E", o + u, o + 1024, 2), PS(b), AF.Sigmoid, bias=-1860.0 / 256 - LOW, scale=1.0 / 256)
 
     def hand_back(n, src, a, b, y, q="y"):
         s, d = "S" + n + "d", "R" + n + "d"
@@ -558,17 +597,22 @@ def rank_program(g, core, T, topo):
 
     def values(t):
         for c in range(8):
-            a, y, e = 512 * c, c // 4, 8 * (t % 2) + c
-            tt(A("Y", a, a + 512), IND(A("Vt", 4096 * (t % 2), 4096 * (t % 2) + 4096) if t else A("V0"), A("lv", 256 * t + 32 * c, 256 * t + 32 * c + 32)), B("E", e, e + 1), OP.mult)
-            mm([(PS(7, 32 * c + 16 * (j // 2), 32 * c + 16 * (j // 2) + 16), A("Y", a + 128 * j, a + 128 * j + 128), A("m16")) for j in range(4)], each=2)
+            a, y, e = 512 * c, c // 4, 4096 * (t % 2) + 512 * c
+            tt(A("Y", a, a + 512), IND(A("Vt", 4096 * (t % 2), 4096 * (t % 2) + 4096) if t else A("V0"), A("lv", 256 * t + 32 * c, 256 * t + 32 * c + 32)), A("E", e, e + 512), OP.mult)
+            mm([(PS(7, 32 * c + 16 * j, 32 * c + 16 * j + 16), A("Y", a + 256 * j + u, a + 256 * j + 256, 2), A("m16")) for j in range(2) for u in range(2)], each=2)
             if c % 4 == 3:
                 s = (128 * y, 128 * y + 128)
                 v, back = (256 * y, 256 * y + 256), PS(7, 256 + s[0], 256 + s[1])
                 act(A("At", *s), PS(7, *s))
-                mms([(back, A("At", *s), A("ID32"))])
-                act(A("As", *s), back)
-                act(IND(A("Vc", *v), A("cl", 88 * t + 72 + 8 * y, 88 * t + 80 + 8 * y)), A("As", *s), AF.Sigmoid)
-                lin("Vo", A("Vp", *v), A("Vc", *v), 2.0, -1.0)
+                mms([(back, A("At", *s), A("ID320"))])
+                place = A("cl", 88 * t + 72 + 8 * y, 88 * t + 80 + 8 * y)
+                if t in V_PUT:
+                    act(A("As", *s), back, AF.Sigmoid)
+                    ts(IND(A("Vp", *v), place), A("As", *s), 2.0, OP.mult, -1.0, OP.add)
+                else:
+                    act(A("As", *s), back)
+                    act(IND(A("Vc", *v), place), A("As", *s), AF.Sigmoid)
+                    lin("Vo", A("Vp", *v), A("Vc", *v), 2.0, -1.0)
                 if t < NS - 1:
                     spread_V(t + 1, y)
                 else:
@@ -580,12 +624,15 @@ def rank_program(g, core, T, topo):
         step[0] = t
         scores(t)
         if t == 0:
-            lin(True, A("Vc"), A("Vb"), 0.5, 0.5)
+            if V_PUT:
+                lin(True, A("Vp"), A("Vb"))
+            else:
+                lin(True, A("Vc"), A("Vb"), 0.5, 0.5)
             first_V()
         else:
             digits()
         mm([(PS(1, 256, 512), A("ones", 0, 128), A("I2k"))] +
-           [(PS(1, 256 + 128 * h, 384 + 128 * h), half("LcB", h), A("I2k", 0, 128)) for h in range(2)])
+           [(PS(1, 256 + 128 * h, 384 + 128 * h), view(t, h), A("I2k", 0, 128)) for h in range(2)])
         mm([(PS(1, 0, 256), A("ones", 0, 128), A("Mc"))], True, False)
         if t:
             marks()
@@ -622,61 +669,65 @@ def rank_program(g, core, T, topo):
         mm([(PS(1, 384, 400), A("thZ", p1=64), A("IDh", 16 * t, 16 * t + 16, p1=64))] +
            [(PS(1, 384, 400), A("EB", 15 - b, 143 - b), A("KK", kn + b, kn + 256, 16)) for b in range(16)])
         rc = "rc%d" % t
-        cp(A(rc, 16 * r, 16 * r + 16), PS(1, 384, 400))
-        trade(lambda q: A(rc, 16 * r, 16 * r + 16), lambda q: A(rc, 16 * q, 16 * q + 16))
+        lin("rc", A(rc, 16 * r, 16 * r + 16), PS(1, 384, 400))
+        trade(lambda q: A(rc, 16 * r, 16 * r + 16), lambda q: A(rc, 16 * q, 16 * q + 16), 4800.0, 3000.0)
         line[0] = "L"
         ts(si(0), A("Mx", 15, 256, 16), 32 / SC, OP.mult, 30.0, OP.add)
         ts(si(7), bs, 0.5, OP.mult, -0.25, OP.add)
         ts(si(4), si(7), 7, OP.arith_shift_right, 7, OP.bitwise_and)
-        ts(si(1), si(0), 31, OP.bitwise_and, 1, OP.logical_shift_right)
-        ts(si(2), si(0), 1, OP.bitwise_and)
-        ts(si(5), si(4), q_, OP.not_equal)
-        tt(si(6), si(5), si(2), OP.is_gt)
-        tt(A("MR", 16, 32), si(6), si(1), OP.mult)
+        ts(si(5), si(0), 31, OP.bitwise_and)
+        ts(si(6), si(0), 1, OP.bitwise_and)
+        ts(A("MR", 16, 32), si(4), q_, OP.is_equal)
+        mr = lambda j: A("MR", 16 * j - 48, 16 * j - 32)
         if t in BY_DMA:
             ts(si(8), si(7), 4, OP.arith_shift_right)
             ts(si(9), si(7), 7, OP.arith_shift_right)
-            ts(si(8), si(8), 240.0, OP.mult)
-            ts(si(9), si(9), -2032.0, OP.mult)
-            tt(si(8), si(8), si(9), OP.add)
-            tt(A("d16"), si(8), si(7), OP.add)
+            cp(A("MR", 32, 112), A("si", 80, 160))
+            mm([(PS(1, 432, 448), A(m), mr(j)) for m, j in (("IDh", 7), ("I240", 8), ("n2032", 9))])
+            act(A("d16", 0, 16), PS(1, 432, 448))
         else:
-            cp(A("d16"), si(7))
-        mms([(PS(1, 256, 384, p1=16), A("MR", 16, 32), A("IDh"))])
+            cp(A("MR", 32, 64), A("si", 80, 112))
+            cp(A("d16", 0, 16), si(7))
+        mm([(PS(1, 256, 384, p1=16), x, A(m)) for x, m in ((mr(5), "IDh"), (mr(6), "n64"), (mr(4), "n64"))])
         lin("MTs", A("MTs", 128, 256, p1=16), PS(1, 256, 384, p1=16))
         mms([(half("p2", y), A("Hs", 256 + 128 * y, 384 + 128 * y, p1=16), A("MTs", 128, 256, p1=16)) for y in range(2)])
-        act(A("sS"), PS(2, 0, 256), AF.Sign, bias=yb_)
-        swap(lambda q, p: B("p2", 16, 17, 1, q, 16, 8, p, p + 32), lambda x: A("d16", x, 16, 8))
+        act(A("sS"), PS(2, 0, 256), AF.Sign, bias=yb_, scale=0.5)
+        (act if "dx" in ON_S else cp)(A("dx"), IND(A("d16"), A("xl")))
+        mm([(A("p2", 256, 272, 1, 32 * a, 32 * a + 32), A("W16", 16 - 16 * u, 48 - 16 * u), A("dx", 32 * a + 16 * u, 32 * a + 16 * u + 16)) for a in range(4) for u in range(2)], each=2)
         cp(A("dl"), PS(2, 256, 272))
         if t > 0:
             sort(0, t in BY_DMA)
         elif t in BY_DMA:
-            mms([(PS(3, 0, 256), A("PMb"), A("LcB"))])
+            mms([(PS(3, 128 * y, 128 * y + 128), A("PMb"), view(t, y)) for y in range(2)])
             lin("Lp", A("Lf"), PS(3, 0, 256))
         act(K2(t + 1), IND(K2(t, 0, 768), A("cl", 88 * t + 40, 88 * t + 72)))
         if t == NS - 1:
             for e in range(2):
-                ts(A("Ko", e, 512, 2), K2(NS, 256 * e, 256 * e + 256), 12582912.0, OP.add, -12582912.0, OP.add)
+                if "Ko" in ON_S:
+                    act(A("Ko", e, 512, 2), K2(NS, 256 * e, 256 * e + 256), AF.Relu, bias=-2 * EPS)
+                else:
+                    ts(A("Ko", e, 512, 2), K2(NS, 256 * e, 256 * e + 256), 12582912.0, OP.add, -12582912.0, OP.add)
             hand_back("k", "Ko", 0, 512, (T["yk"][:, :], []), "g")
         spread_views(t)
         mm([(PS(2, 256, 512), A("nI"), A("ones")), (PS(2, 256, 512), A("nI"), A("sS"))], True, False)
-        mm([(PS(2, 256, 512), A("PMt"), A("Lp")) if t else (PS(2, 256, 512), A("IDh"), A("LcB"))], False, True)
+        mm([(PS(2, 256, 512), A("PMt"), A("Lp"))] if t else [(PS(2, 256 + 128 * y, 384 + 128 * y), A("IDh"), view(t, y)) for y in range(2)], False, True)
         tt(A("ga"), IND(A("VT"), A("dl")), A("sS"), OP.min)
-        tt(A("LcB"), PS(2, 256, 512), A("ga"), OP.max)
+        if t < NS - 1:
+            tt(A("LcB"), PS(2, 256, 512), A("ga"), OP.max)
         if t == 0:
+            mark_constants()
             sort_constants()
         if t == NS - 1:
             for y in range(2):
-                cp(B("Ls", y, 16, 2), half("LcB", y))
+                tt(A("Ls", y, 256, 2), PS(2, 256 + 128 * y, 384 + 128 * y), A("ga", 128 * y, 128 * y + 128), OP.max)
             trade(lambda q: A("Ls", 32 * q, 32 * q + 32), lambda q: A("R0", 32 * q, 32 * q + 32))
             cp(A("R0", 32 * r, 32 * r + 32), A("Ls", 32 * r, 32 * r + 32))
-            for y in range(2):
-                cp(half("LcB", y), B("R0", y, 16, 2))
         lists(t + 1)
         line[0] = "K"
         sg = [A("sg", 0, 16), A("sg", 16, 32)]
         mm([(PS(1, 400, 432), A("n8k"), A("sg")), (PS(1, 416, 432), A("n8k"), sg[0]), (PS(1, 400, 416), A("n8k"), A("m05"))], True, False)
-        mm([(PS(1, 400 + 16 * e, 416 + 16 * e), A("nI"), A(rc, 16 * h, 16 * h + 16)) for e in range(2) for h in range(8)], False, True)
+        for hs in (near, far):
+            mm([(PS(1, 400 + 16 * e, 416 + 16 * e), A("nI"), A(rc, 16 * h, 16 * h + 16)) for e in range(2) for h in hs], False, hs == far)
         ts(A("sg"), PS(1, 400, 432), 0.5, OP.is_lt, -0.5, OP.add)
         n = 512 if t else 256
         mms([(PS(0, b, n, 16), A("XK", 128 * b, 128 * b + 128), A("sg", 0, n // 16)) for b in range(16)])
@@ -685,7 +736,7 @@ def rank_program(g, core, T, topo):
         if t < NS - 1:
             cur_lists(t + 1)
             own_K(t + 1)
-        spread_T(SHARE if t < NS - 1 else SHARE_ENDS, 0 if t else 2)
+        spread_T(SHARE if t < NS - 1 else SHARE_LAST, 0 if t else 2, T_DMA[t])
         on("V", values, t)
 
     step[0] = NS
@@ -695,7 +746,7 @@ def rank_program(g, core, T, topo):
     powers()
     sort(1)
     swap(lambda x, p: B("p2", x, 16, 8, 0, 16, 1, p, p + 32), lambda q: A("Lp", 32 * q, 32 * q + 32), "IE2")
-    ts(A("Lo"), PS(2, 0, 256), 2048.0, OP.mult, 2048.0, OP.add)
+    lin("Lo", A("Lo"), PS(2, 0, 256), 2048.0, 2048.0)
     dma("s", [((T["yl"][:, :], []), A("Lo"))])
     emit(g, T, QU, ops, sent[0])
 
@@ -847,7 +898,101 @@ def arrange(ops):
                     best = new
         return best
 
+    def play(seq, j, p=0, old=None):
+        c_, f = costs[j], late[j]
+        free, last = [0.0] * 8, [-1] * 8
+        at, end, why = ([0.0] * n, [0.0] * n, [-1] * n) if old is None else (old[3][:], old[4][:], old[1][:])
+        todo = {0, 1, 2, 3, 4, 6, 7}
+        for k in range(p - 1, -1, -1):
+            i = seq[k]
+            q = queue[i]
+            if q in todo:
+                todo.remove(q)
+                free[q], last[q] = at[i] + c_[i], i
+            if hold[i] and 6 + (q != 5) in todo:
+                todo.remove(6 + (q != 5))
+                free[6 + (q != 5)], last[6 + (q != 5)] = end[i] - 600 * f, i
+            if not todo:
+                break
+        for i in seq[p:]:
+            q, c = queue[i], c_[i]
+            t, w = free[q], -2 - last[q]
+            for d in hard[i]:
+                x = end[d] + WAKE
+                if x > t:
+                    t, w = x, d
+            for d in soft[i]:
+                x = at[d] + c_[d]
+                if x > t:
+                    t, w = x, d
+            if q < 5:
+                free[q], last[q] = t + c, i
+            at[i] = t
+            if hold[i]:
+                q = 6 + (q != 5)
+                x = t + c + 1400 * f
+                if free[q] > x:
+                    x, w = free[q], -2 - last[q]
+                free[q], last[q] = x + hold[i] * f, i
+                end[i] = free[q] + 600 * f
+            else:
+                end[i] = t + c + lat[i] * f
+            why[i] = w
+        m = max(end)
+        return m + 3e-3 * sum(end) / n, why, end.index(m), at, end
+
+    def blocked(run):
+        out, i = [], run[2]
+        while i != -1:
+            w = run[1][i]
+            if w < -1:
+                w = -2 - w
+                if not needs[i] >> w & 1:
+                    out.append((w, i))
+            i = w
+        return out
+
+    def polish(seq, tries):
+        now = [play(seq, j) for j in range(len(costs))]
+        val = sum(w * x[0] for w, x in zip(weight, now))
+        best, pairs, cum = (val, seq, now), [blocked(x) for x in now], np.cumsum(weight) / sum(weight)
+        for it in range(tries):
+            j = int(np.searchsorted(cum, rng.random()))
+            if not pairs[j]:
+                continue
+            a, b = pairs[j][int(rng.integers(len(pairs[j])))]
+            pa, pb, more = seq.index(a), seq.index(b), int(rng.integers(0, 3))
+            if rng.random() < 0.5:
+                while more and pa > 0 and not needs[b] >> seq[pa - 1] & (queue[seq[pa - 1]] == queue[b]):
+                    pa -= 1
+                    more -= queue[seq[pa]] == queue[b]
+                first = [x for x in seq[pa:pb + 1] if x == b or needs[b] >> x & 1]
+            else:
+                while more and pb < n - 1 and not needs[seq[pb + 1]] >> a & (queue[seq[pb + 1]] == queue[a]):
+                    pb += 1
+                    more -= queue[seq[pb]] == queue[a]
+                first = [x for x in seq[pa:pb + 1] if x != a and not needs[x] >> a & 1]
+            moved = set(first)
+            new = seq[:pa] + first + [x for x in seq[pa:pb + 1] if x not in moved] + seq[pb + 1:]
+            room = SLACK * (1 - it / tries) * float(rng.exponential())
+            one = play(new, j, pa, now[j])
+            if weight[j] * (one[0] - now[j][0]) > room + 400:
+                continue
+            runs = [one if k == j else play(new, k, pa, now[k]) for k in range(len(costs))]
+            v = sum(w * x[0] for w, x in zip(weight, runs))
+            if v <= val + room:
+                seq, now, val, pairs = new, runs, v, [blocked(x) for x in runs]
+                if v < best[0]:
+                    best = (v, seq, now)
+        return best
+
     if n not in KEPT:
+        costs, late, weight, needs = [cost] + other, (1.0,) + LATE, (1.0,) + BOTH, []
+        for o in ops:
+            m = bits(o["deps"] | o["order"])
+            for d in o["deps"] | o["order"]:
+                m |= needs[d]
+            needs.append(m)
         rng = np.random.default_rng(SEED)
         kin, line, seat, met, ranks = {}, {}, [], {}, []
         for i in range(n):
@@ -864,11 +1009,10 @@ def arrange(ops):
             met[o["step"], o["tag"]] = met.get((o["step"], o["tag"]), -1) + 1
             seat.append((o["step"], met[o["step"], o["tag"]]))
         best = [lean(lean(forth(rank), rank, FIRST, True), None, FIRST, False) for _, rank in ranks[:STARTS]]
-        best = [lean(again(z), None, MORE, False, True) for z in best]
-        best = lean(min(best, key=lambda z: z[0]), None, TRIES, False, True)
-        best = lean(best, None, 4 * TRIES, False, True)
-        KEPT[n] = order(best[1])
-        KEPT["times"] = best
+        best = min([polish(order(z[1]), MORE) for z in best], key=lambda z: z[0])
+        best = polish(best[1], TRIES)
+        KEPT[n] = best[1]
+        KEPT["times"] = (best[0], best[2][0][3], best[2][0][4], best[2][0][0], [x[0] for x in best[2][1:]])
     seq = KEPT[n]
     place = {j: k for k, j in enumerate(seq)}
     for j, o in enumerate(ops):

@@ -8,20 +8,21 @@ NS = 4
 SC = float(2 ** 18)
 C8 = 129.0 / 16
 EPS = 2.0 ** -18
+OFF = 1656
 LN64 = math.log(64.0)
 LOW, POW = 16.0, 18
-RATES, BOTH, LATE = ((1.0, 1.5, 3.5, 0.5), (1.2, 2.3, 6.0, 0.6), (0.84, 1.1, 2.5, 0.42)), (0.4, 0.8), (1.0, 0.95)
-WAKE, VLAT, LONG = 80.0, 4400.0, 3500.0
-STARTS, FIRST, TRIES, STEP, SLACK, KEPT = 2, 300, 100000, 4000.0, 300.0, {}
-SHARE, SHARE_ENDS, SHARE_VT = (3,), (1, 3, 5, 7), (1,)
-SHARE_LAST, LAST_S = (1, 5), ()
-P_LAST = 1
-T_DMA, TP, TLAT = ((), (), (), ()), 4, 3800.0
-OWN, SEED, MORE = 2, 2, 3500
-V_PUT = (0, 1, 2, 3)
+RATES = ((0.92, 1.3, 3.0, 0.48), (1.2, 2.2, 6.0, 0.6), (0.95, 1.4, 3.2, 0.48))
+WEIGHTS, LATE, WAKES, ISSUE = (1.0, 0.4, 0.5), (1.0, 1.1, 0.95), (170.0, 170.0, 90.0), (80.0, 100.0, 60.0)
+VLAT, LONG = 4400.0, 3500.0
+STARTS, FIRST, TRIES, STEP, SLACK, KEPT = 2, 300, 70000, 4000.0, 300.0, {}
+SHARE_ENDS, SHARE_VT = (1, 3, 5, 7), (1,)
+ON_V = ((0, 2, 4, 6), (1, 3, 5), (1, 3, 5), (1, 3, 5), (1, 3, 5))
+TLAT, HLAT = 2150.0, 3600.0
+SEED, MORE = 2, 3500
+DIAG_Q = "yy"
 BY_DMA = (0, 1, 2)
-ON_S = {"D0", "D1", "D2", "x16", "MTs", "Lp", "L0", "Vo", "Lh", "dx", "fl0", "fl1", "Ko", "Lo", "Ly", "rc", "Tp"}
-WB, TB, VB = (5, 6), (4, 0, 1), (3, 4)
+ON_S = {"D0", "D1", "D2", "x16", "MTs", "Lp", "L0", "Vo", "Lh", "dx", "fl0", "fl1", "Ko", "Lo", "Ly", "rc", "aS0", "aS1", "nb0", "nb1", "lu", "lv", "Lu"}
+WB, TB, VB, KB, SB = (6, 5), (4, 0, 1), (3, 4), (1, 5), (3, 6)
 SCRATCH = {}
 
 
@@ -31,28 +32,28 @@ def _sb(dtype, **kw):
 
 
 SL = (16, 16)
-RING = 4
-_sb(BF, Tt=4096, V0=4096, K0=512, V1=512, Kb=512, Vb=512, KK=1536, Tc=512, Tp=512, own=640, P=2048, G=768 * RING, diag=1024, fl=SL, tt=SL, sS=256, pw=256, z=512, R=(128, 16), BO=128, EB=144,
-    SEL=1024, SEL0=1024, XK=2048, Hs=512, IE2=272, Mc=256, I2k=256, ones=256, rm=256, Cs=256, Cz=384, Ko=512, gkB=256, Wt=64, Wt0=64, Q8=8, m05=16)
-_sb(F, Vt=8192, E=8192, Y=4096, d16=32, Vc=512, Vp=512, VT=2048, Lf=256, Lo=256, aS=SL, Mx=256, us=256, d1=256, Bx=256, As=256, At=256,
-    iot=272, ioq=128, ioj=256, pc=24, mk=24, ID32=128, ISC=128, ID320=128, ISC0=128, wL=16, m16=16)
-_sb(HF, LcB=SL, Lq=SL, Ly=SL, Lp=SL, Lh=SL, Ls=SL, R0=256, L0=256, ga=256, D=(32, 16), D2=(32, 16), x16=SL, IEh=272, thZ=128, cL=88, sg=32, MR=112,
+_sb(BF, Tt=4096, V0=4096, K0=512, V1=512, Kb=512, Vb=512, KK=2048, Tc=512, Z=512, own=256, G=768 * 8, diag=(16, 256), fl=SL, nb=SL, tt=SL, sS=256, pw=256, z=512, R=(128, 16), BO=128, EB=144,
+    S16=264, SEL0=1024, XK=2048, Hs=512, IE2=272, Mc=128, I2k=128, ones=256, rm=128, Cs=256, Cz=384, Ko=512, gkB=256, Wt=64, Q8=8, m05=16)
+_sb(F, Vt=8192, E=8192, Y=4096, d16=32, Vp=512, Vo=512, Vf=512, Ah=256, VT=2048, Lf=256, Lo=256, Mx=256, us=256, d1=256, Bx=256, As=256, At=256,
+    iot=272, ioq=128, ioj=256, pc=32, mk=24, ID32=128, ID320=128, wL=16, m16=16)
+_sb(HF, LcB=SL, Lq=SL, Ly=SL, Lp=SL, Lh=SL, Ls=SL, Lu=SL, aS=SL, R0=256, L0=256, ga=256, D=(32, 16), D2=(32, 16), x16=SL, IEh=272, thZ=128, cL=88, sg=32, MR=128,
     dx=128, W16=48, xf=8, MTs=256, rc0=128, rc1=128, rc2=128, rc3=128)
-_sb(I, Li=256, thI=16, pi=8, si=160)
-_sb(U, lu=1280, lv=1024, bl=16, dl=16, dg=8, xl=8, cl=352)
+_sb(I, Li=256, thI=16, pi=8, si=176)
+_sb(U, lu=1280, lv=1024, bl=16, dl=16, xl=8, cl=400)
 PART = {}
-for _n in "Bm m8A Mf Mt Bc m8A0 Mf0 Mt0 Bm0 Am0 m8I0 n640 I40 n600 Us nU m8I PMb Am LE nI PMv PMw PMh PMy PMq PMt Iy Iq I4 n60 PMk IDh n64 n8k I256 n512 Ia Ib Ic Id I240 n2032".split():
+for _n in "Bm m8A Mf Mt Us nU m8I PMb Am LE nI PMv PMw PMh PMy PMq PMt Iy Iq I4 n60 PMk IDh n64 n8k I512 n512 Ia Ib Ic Id I112 n1008 I896 ISC Hm nHm".split():
     PART[_n] = ("cmat", 128 * len(PART))
 _sb(BF, cmat=128 * len(PART))
 for _i in range(8):
-    SCRATCH["p%d" % _i] = ("psum", [128, 512] if _i == 1 else [128, 32, 16], F)
+    SCRATCH["p%d" % _i] = ("psum", [128, 512] if _i in KB else [128, 32, 16], F)
 SCRATCH["SKd"] = ("dram", [8, 128, 64], BF)
 SCRATCH["Vd"] = ("dram", [4, 16, 8, 256], F)
 SCRATCH["SVd"] = ("dram", [8, 128, 64], BF)
-for _n, _c, _d in (("k", 64, BF), ("v", 32, F), ("w", 32, F)):
+SCRATCH["Kd"] = ("dram", [16, 2, 8, 256], BF)
+for _n, _c, _d in (("k", 64, BF), ("v", 32, F)):
     SCRATCH["S" + _n + "d"] = ("dram", [8, 128, _c], _d)
     SCRATCH["R" + _n + "d"] = ("dram", [8, 128, _c], _d)
-SEMAPHORES = ["pe", "v", "s", "g", "sent"] + ["d%d" % i for i in range(64)] + [_c + str(i) for _c in "ab" for i in range(14)]
+SEMAPHORES = ["pe", "v", "s", "g", "sent"] + ["d%d" % i for i in range(80)] + [_c + str(i) for _c in "ab" for i in range(14)]
 
 
 def spread(topo, src, dsts):
@@ -140,8 +141,6 @@ def rank_program(g, core, T, topo):
                 lst.append((x, kind, me))
         j = 3 if q == "pe" else 0
         cost, *other = cost if isinstance(cost, list) else [cost * x[j] / RATES[0][j] for x in RATES]
-        if q == "y":
-            other[1] = 1.5 * cost
         ops.append({"q": q, "fn": fn, "other": other, "deps": deps, "order": order, "sem": sem, "n": n, "cost": cost, "lat": lat, "hold": max(0.0, lat - 2000), "step": step[0], "line": line[0],
                     "tag": (q, wr[0][0] if wr else None, rd[0][0] if rd and q == "pe" else None)})
 
@@ -153,7 +152,7 @@ def rank_program(g, core, T, topo):
 
     def price(o, a, per):
         kind, n = (1, wide(a)) if len(a[1]) > 1 else (2, wide(o)) if len(o[1]) > 1 else (0, per * wide(o))
-        return [60 + x[kind] * n for x in RATES]
+        return [60 + x[kind] * n if kind else x[0] * max(64, n) for x in RATES]
 
     def regs(*xs):
         return [p for x in xs if isinstance(x, tuple) for p in x[1]]
@@ -234,7 +233,7 @@ def rank_program(g, core, T, topo):
         def fn():
             for o, x in pairs:
                 QU[q].dma_start(o[0], x[0]).then_inc(T.sem[sem], 16)
-        rec(q, fn, [p for o, x in pairs for p in x[1]], [p for o, x in pairs for p in o[1]], sem, 16 * len(pairs), 60.0 * len(pairs), lat)
+        rec(q, fn, [p for o, x in pairs for p in x[1]], [p for o, x in pairs for p in o[1]], sem, 16 * len(pairs), [x * len(pairs) for x in ISSUE], lat)
 
     sent, calls = [0], []
 
@@ -283,7 +282,7 @@ def rank_program(g, core, T, topo):
     iota(A("ioq"), [[1, 8], [0, 16]])
     iota(A("ioj"), [[0, 4], [1, 8], [0, 8]])
 
-    p_, q_, k_, kq_, e_, yb_, pk_, pb_, lb_, cs1_, cs2_, ie_, h0_, h1_, cs3_, xb_, h2_, h3_, od_, kh_, kn_, pb0_, eb_ = [col("pc", j) for j in range(23)]
+    p_, q_, k_, kq_, e_, yb_, pk_, pb_, lb_, cs1_, cs2_, ie_, h0_, h1_, cs3_, xb_, h2_, h3_, od_, kh_, kn_, pb0_, eb_, r0_, xe_ = [col("pc", j) for j in range(25)]
     ts(col("pi", 1), col("pi", 0), 4, OP.arith_shift_right)
     ts(col("pi", 2), col("pi", 0), 15, OP.bitwise_and)
     cp(A("pc", 0, 3), A("pi", 0, 3))
@@ -310,7 +309,13 @@ def rank_program(g, core, T, topo):
         dma("y", [(A(n + "b", p0=16 * q, p1=16 * q + 16), A({"K": "K0", "V": "V1"}[n], 64 * q, 64 * q + 64)) for q in range(8)])
 
     fill(A("G", 0, 256), 0.0)
-    dma("y", [(A("G", 768 * c, 768 * c + 256), A("G", 0, 256)) for c in range(1, RING)] + [(A("diag", c, c + 256), A("G", 0, 256)) for c in range(0, 1024, 256)])
+    dma("y", [(A("G", 768 * c, 768 * c + 256), A("G", 0, 256)) for c in range(1, 8)])
+    fill(A("KK", 512, 1024), 0.0)
+    fill(A("diag", 0, 1024), 0.0)
+    dma("y", [(A("diag", c, c + 1024), A("diag", 0, 1024)) for c in (1024, 2048, 3072)] + [(A("KK", 1536, 2048), A("KK", 512, 1024))], 3200.0)
+    mine = lambda q: A("diag", 512 * q, 512 * q + 512, p0=16 * q, p1=16 * q + 16)
+    for qs in (near, far):
+        dma("y", [(mine(q), A("K0", 64 * q, 64 * q + 64)) for q in qs], 2100.0)
 
     def pick(o, pat, c, base=0, src=None, p1=128):
         src = src or A("G", 0, wide(o), p1=p1)
@@ -321,15 +326,17 @@ def rank_program(g, core, T, topo):
 
     for j in range(4):
         pick(A("SEL0", 256 * j, 256 * j + 256), [[-1, 2], [0, 8], [-8, 16]], 1, -2 * j)
-    for j in range(4):
-        pick(A("SEL", 256 * j, 256 * j + 256), [[-16, 2], [0, 8], [-1, 16]], -2, -32 * j)
+    pick(A("S16", 0, 8), [[1, 8]], 0, 1)
+    pick(A("S16", 8, 264), [[-1, 16], [999, 2], [-16, 8]], -2)
     for j in range(8):
         pick(A("XK", 256 * j, 256 * j + 256), [[-1, 2], [-16, 8], [0, 16]], 1, -2 * j)
     pick(A("Hs", 0, 256), [[-8, 2], [0, 16], [-1, 8]], -1)
     pick(A("Hs", 256, 512), [[-8, 2], [-1, 8], [0, 16]], 1)
-    for n, c in (("n64", -64), ("n8k", -8192), ("nI", -1), ("Ia", 1 / 32), ("Ib", -2), ("Ic", 1 / 2048), ("Id", -1 / 32), ("I4", 4), ("n60", -60), ("I240", 240), ("n2032", -2032)):
+    for n, c in (("n64", -64), ("n8k", -8192), ("nI", -1), ("Ia", 1 / 32), ("Ib", -2), ("Ic", 1 / 2048), ("Id", -1 / 32), ("I4", 4), ("n60", -60), ("I112", 112), ("n1008", -1008), ("I896", 896)):
         pick(A(n), [[-1, 128]], c)
     pick(A("PMt"), [[-1, 8], [-8, 16]], 1)
+    for n, c in (("Hm", 1), ("nHm", -1)):
+        pick(A(n), [[0, 8], [-1, 16]], c, -16 * r)
     pick(A("IE2", 0, 16), [[1, 16]], 0, 1)
     pick(A("IE2", 16, 272), [[-1, 8], [999, 2], [-8, 16]], 1)
     for j, (c0, c1) in enumerate(((-1024, 0), (67584, 65), (56320, 56))):
@@ -345,9 +352,8 @@ def rank_program(g, core, T, topo):
     cp(A("pc", 18, 20), A("pi", 3, 5))
     ts(pk_, kh_, -2.0, OP.mult, 16.0, OP.add)
     ts(kh_, pk_, p_, OP.add)
-    ts(A("dg"), A("iot", 0, 8), 128.0, OP.mult, kq_, OP.add)
+    ts(r0_, k_, 0.0, OP.is_equal)
     ts(A("PMk"), io128, kh_, OP.is_equal, 2048.0, OP.mult)
-    ts(A("PMv"), io128, kq_, OP.is_equal, 2048.0, OP.mult)
     ts(col("pi", 7), col("pi", 0), 1, OP.bitwise_and)
     ts(eb_, col("pi", 7), -7.0, OP.mult, kq_, OP.add)
     ts(eb_, eb_, q_, OP.add)
@@ -356,7 +362,7 @@ def rank_program(g, core, T, topo):
         act(A(n), A("PMw"), scale=c / 2048)
     ts(A("mk", 0, 16), A("iot", 0, 16), k_, OP.is_equal)
     ts(A("mk", 16, 24), A("iot", 0, 8), q_, OP.is_equal)
-    cp(A("Q8"), A("mk", 16, 24))
+    ts(A("Q8"), A("mk", 16, 24), r0_, OP.mult)
     ts(A("BO"), A("ioq"), q_, OP.is_equal)
     ts(A("EB"), A("iot", 0, 144), e_, OP.is_equal)
     ts(A("PMb"), io128, kq_, OP.is_equal)
@@ -364,27 +370,25 @@ def rank_program(g, core, T, topo):
     act(A("m05"), A("ones", 0, 16), AF.Sigmoid, scale=0.0)
     ts(A("sg"), A("iot", 0, 32), 0.0, OP.mult, -0.5, OP.add)
     keep(A("LE"), A("BO"), [[1, 128]], OP.is_ge, -1)
-    keep(A("rm"), A("ones"), [[0, 16], [1, 16]], OP.not_equal, 0)
-    for n, c in (("I256", 256), ("n512", -512)):
+    keep(A("rm"), A("ones", 0, 128), [[0, 8], [1, 16]], OP.not_equal, 0)
+    for n, c in (("I512", 512), ("n512", -512)):
         act(A(n), A("IDh"), scale=float(c))
     ts(A("wL"), A("iot", 0, 16), 16.0, OP.mult, k_, OP.add)
-    for j, (m, c) in enumerate(((1, 128), (1, 256), (1, 384), (2, 0.5))):
+    for j, (m, c) in enumerate(((2, 0.5), (2, 256), (2, 256.5), (2, 0.5))):
         ts(A("cL", 24 + 16 * j, 40 + 16 * j), A("wL"), float(m), OP.mult, float(c), OP.add)
     ts(A("cL", 80, 88), A("cL", 80, 88), -256.0, OP.add)
     for y in range(2):
         ts(cs3_, q_, 256.0, OP.mult, 1792.0 * y, OP.add)
         ts(A("cl", 8 * y, 8 * y + 8), A("wL", 8 * y, 8 * y + 8), 2.0, OP.mult, cs3_, OP.add)
-    for n, c in (("ID32", 1), ("Mt", -C8 * SC), ("I2k", 2048)):
+    for n, c in (("Mt", -C8 * SC), ("I2k", 2048)):
         act(A(n, 0, 128), A("IDh"), scale=float(c))
-    act(A("I2k", 128, 256), A("IDh"), scale=2048.0)
-    act(A("ISC"), A("PMb"), scale=1 / SC)
+    act(A("ISC"), A("IDh"), scale=SC)
 
     def sloped(o, a, ci):
         act(o, A(a), scale=-C8 * SC)
         pick(o, [[-1, 128]], ci, 0, o)
 
-    for h in range(2):
-        sloped(A("Mc", 128 * h, 128 * h + 128), "LE", 136 * SC)
+    sloped(A("Mc"), "LE", (136 + OFF) * SC)
 
     def mark_constants():
         keep(A("Am"), A("BO"), [[-1, 128]], OP.is_gt, 1)
@@ -396,24 +400,14 @@ def rank_program(g, core, T, topo):
         mm([(PS(3, 0, 128), A(m), A(n)) for m, n in (("IDh", "BO"), ("Ib", "Am"), ("IDh", "nU"))])
         mms([(PS(3, 128, 256), A("Us"), A("m8I"))])
         act(A("Bm", 0, 256), PS(3, 0, 256))
-        mms([(PS(3, 0, 128), A("Bm"), A("PMb"))])
-        act(A("Bc"), PS(3, 0, 128))
-        mms([(PS(3, 0, 384), A("PMb"), A("m8A", 0, 384)), (PS(3, 384, 512), A("Bc"), A("PMb"))])
-        act(A("m8A0", 0, 512), PS(3))
-        act(A("Am0"), A("m8A0"), scale=-0.125)
-        act(A("m8I0"), A("IDh"), scale=-8.0)
 
-    act(A("ISC0"), A("IDh"), scale=1 / SC)
     act(A("ID320"), A("PMt"))
-    for n, c in (("n640", -64), ("I40", 4), ("n600", -60)):
-        pick(A(n), [[-1, 16], [-16, 8]], c)
-    M = lambda n, y, *a: A(n if y else {"IDh": "PMb", "I2k": "PMv"}.get(n, n + "0"), *a)
     ts(A("m16"), A("mk", 0, 16), math.exp(LOW) / 8, OP.mult)
     ts(A("thZ", p1=64), A("iot", 0, 128, p1=64), 0.0, OP.mult)
     ts(A("thZ", 16 * r, 16 * r + 16, p1=64), A("thI", p1=64), -1.0, OP.mult)
     ts(yb_, k_, -15.5, OP.add)
     ts(col("pi", 5), col("pi", 0), 120, OP.bitwise_and)
-    ts(xb_, col("pi", 5), -1.0, OP.mult, 136.0, OP.add)
+    ts(xb_, col("pi", 5), -1.0, OP.mult, 136.0 + OFF, OP.add)
     ts(col("pi", 6), col("pi", 0), 7, OP.bitwise_and)
     ts(h2_, col("pi", 6), q_, OP.is_equal)
     ts(h3_, od_, 8.0, OP.mult, -16.0, OP.add)
@@ -436,26 +430,25 @@ def rank_program(g, core, T, topo):
         ts(A("Cs"), A("ioj"), cs1_, OP.mult, cs2_, OP.add)
         for a in range(8):
             ts(A("Wt", 8 * a, 8 * a + 8), A("mk", 16, 24), 8.0 ** (POW - 2 * a), OP.mult, 8.0 ** (POW - 2 * a), OP.mult)
-        mms([(PS(3, 0, 64), A("PMb"), A("Wt"))])
-        act(A("Wt0"), PS(3, 0, 64))
-        ts(pb0_, xb_, -LN64 / 8, OP.mult, (17 - POW) * LN64, OP.add)
         act(B("D2", 0, 32, 1, 8, 16), A("ones"), scale=0.0)
 
-    def spread_T(share, first=0, copied=()):
-        for y in copied:
-            mms([(PS(TP, 256 * y + e, 256 * y + 256, 2), A("m8I"), A("Tc", 256 * e + 128 * y, 256 * e + 128 * y + 128)) for e in range(2)])
-            lin("Tp", A("Tp", 256 * y, 256 * y + 256), PS(TP, 256 * y, 256 * y + 256), 0.25)
-            dma("y", [(A("Tt", 2048 * y, 2048 * y + 2048, p0=16 * a, p1=16 * a + 16), A("Tp", 256 * y, 256 * y + 256)) for a in range(8)], TLAT)
+    ROW0 = 1 << 4096
+    Tt = (T["Tt"][:, :], [("Tt", 2 * ROW0 - 1, 4096)])
+
+    def spread_K(t):
+        dma("y", [((T["Kd"][:, :, q, :], D("Kd")[1]), A("KK", 1024 * (t % 2), 1024 * (t % 2) + 512, p0=16 * q, p1=16 * q + 16)) for q in range(8)])
+        dma("y", [(A("Z", 0, 256, p1=16), (T["Kd"][0], D("Kd")[1]))], 2050.0)
+        dma("y", [(A("Tt", p0=16 * a + 1, p1=16 * a + 16), (T["Kd"][1:16], D("Kd")[1])) for a in range(8)], LONG)
+
+    def sign_T():
+        mm([(B("p0", w // 8, 16, 2, 2 * (w % 8), 2 * (w % 8) + 2, 1, 0, 16), A("S16", 16 * w + 8 - 8 * y, 16 * w + 24 - 8 * y), A("sg", 16 * y, 16 * y + 16))
+            for w in range(16) for y in range(2)], each=2)
+        tt(A("Z", 256, 512, p1=16), PS(0, 0, 256, p1=16), A("Z", 0, 256, p1=16), OP.mult)
+        dma("y", [((T["Tt"][16 * a:16 * a + 1, :], [("Tt", ROW0, 4096)]), A("Z", 256, 512, p1=16)) for a in range(8)], TLAT)
+
+    def first_T(share):
         for q in range(8):
             b = TB[q % len(TB)]
-            y, q0 = q // 4, 2 * (q % 4)
-            if first != 1:
-                e, y, q0 = q // 4, q // 2 % 2, 4 * (q % 2)
-                if (e == 0 or first == 0) and y not in copied:
-                    o = 256 * e + 128 * y
-                    mms([(PS(b, 128 * j, 128 * j + 128), A("SEL", 128 * (q0 + j), 128 * (q0 + j + 1)), A("Tc", o, o + 128)) for j in range(4)])
-                    (cp if q in share else act)(A("Tt", 1024 * (q % 4) + e, 1024 * (q % 4) + 1024, 2), PS(b))
-                continue
             y, q0 = q % 2, (near + far)[2 * (q // 2)]
             mms([(PS(b, 256 * j + 64 * h, 256 * j + 64 * h + 64), A("SEL0", 128 * (4 * y + h), 128 * (4 * y + h + 1)), A("Tc", 64 * (q0 + j), 64 * (q0 + j + 1)))
                  for j in range(2) for h in range(4)])
@@ -470,7 +463,7 @@ def rank_program(g, core, T, topo):
         dma("y", [(A("V0", p0=16 * a, p1=16 * a + 16), A("V1")) for a in range(8)], VLAT)
 
     def lists(t):
-        mms([(PS(2, 128 * y, 128 * y + 128), view(t, y), A(("PMv", "PMk")[y])) for y in range(2)])
+        mms([(PS(2, 128 * y, 128 * y + 128), view(t, y), A("PMk")) for y in range(2)])
         lin("lu", A("lu", 256 * t, 256 * t + 256), PS(2, 0, 256), 1.0, 2048.0)
         if t % NS == 0:
             lin("Lq", A("Lq"), A("R0"), 1.0, 1026 - 1023.5 / 2048)
@@ -483,97 +476,91 @@ def rank_program(g, core, T, topo):
 
     def cur_lists(t):
         mm([(PS(1, 280, 344), A("IDh"), A("cL", 24, 88))] +
-           [(PS(1, 280 + 16 * j, 296 + 16 * j), A(n), A("sg", 0, 16)) for j, n in enumerate(("I256", "n512", "I256", "IDh"))])
+           [(PS(1, 280 + 16 * j, 296 + 16 * j), A(n), A("sg", 0, 32, 2)) for j, n in ((0, "IDh"), (1, "n512"), (2, "I512"), (2, "nI"), (3, "IDh"))])
         cp(A("cl", 88 * t + 24, 88 * t + 88), PS(1, 280, 344))
+        if t == NS - 1:
+            mm([(PS(1, 280 + 16 * j, 296 + 16 * j), A(m), x) for j, c, n in ((0, 24, "nI"), (1, 72, "Hm"), (2, 24, "nHm"))
+                for m, x in (("IDh", A("cL", c, c + 16)), (n, A("sg", 0, 32, 2)))], each=2)
+            cp(A("cl", 352, 400), PS(1, 280, 328))
 
-    K2 = lambda t, a=0, b=512: A("KK", 768 * (t % 2) + a, 768 * (t % 2) + b)
+    K2 = lambda t, a=0, b=512, st=1: A("KK", 1024 * (t % 2) + a, 1024 * (t % 2) + b, st)
 
     def own_K(t):
-        act(A("own", 384, 640), IND(K2(t), A("cl", 88 * t + 24, 88 * t + 40)) if t else IND(A("Tt"), A("cl", 0, 16)))
-        cp(IND(A("diag"), A("dg")), A("own", 512, 640))
-        cp(A("own", 256, 384), A("own", 384, 512))
-        cp(A("own", 0, 256), A("own", 256, 512))
-
-    own = lambda t: A("own", 384, 640)
+        act(A("own"), IND(K2(t), A("cl", 88 * t + 24, 88 * t + 40)) if t else IND(Tt, A("cl", 0, 16)))
+        for b in range(2 if t else 0):
+            dma(DIAG_Q[b], [(B("diag", 8 * b + q, 8 * b + q + 1, p0=16 * q, p1=16 * q + 16 - 15 * b), A("own", p0=16 * q, p1=16 * q + 16 - 15 * b)) for q in range(8)], 2050.0)
 
     lists(0)
     cur_lists(0)
     for qs in (near, far):
         ts(A("Tc", 64 * qs[0], 64 * qs[-1] + 64), A("K0", 64 * qs[0], 64 * qs[-1] + 64), EPS, OP.max)
-    spread_T(SHARE_ENDS, 1)
-    for e in range(2):
-        ts(K2(0, 256 * e, 256 * e + 256), A("Kb", e, 512, 2), EPS, OP.max)
+    first_T(SHARE_ENDS)
+    ts(K2(0), A("Kb"), EPS, OP.max)
     own_K(0)
 
     def scores(t):
-        for a in range(4):
-            o = 768 * (a % RING)
-            if t < NS:
-                tt(A("P", 512 * a, 512 * a + 512), IND(A("Tt"), lu(t, a)), A("own", 0, 512), OP.mult)
-            else:
-                (act if a in LAST_S else cp)(A("P", 512 * a, 512 * a + 512), IND(A("Tt"), lu(t, a)))
-            act(A("G", o + 256, o + 768), IND(A("Tt"), lu(t, 4 + a)))
-            k = lambda u, w: A("diag", 128 * (2 * a + u) + 8 * w, 128 * (2 * a + u) + 8 * w + 8) if t < NS else A("Q8")
-            mm([(B("p4", 16, 24, 1, w, w + 1, 1, 32 * a, 32 * a + 16 + 16 * u), A("G", o + 512 * (1 - u) + w, o + 768 - 256 * u, 16), k(u, w))
+        n0, n1 = 8 * (t == NS), 16 if t else 8
+        for c in range(8):
+            o, y, a = 768 * c, c // 4, c % 4
+            (cp if c in ON_V[t] else act)(A("G", o + 256, o + 768), IND(Tt, lu(t, c)))
+            j = lambda u, w: 32 * c + 16 * u + w
+            k = lambda u, w: A("Q8") if t == NS else B("diag", 0, n1, 1, j(u, w), j(u, w) + 1) if t else A("diag", 2 * j(u, w), 4096, 512)
+            mm([(B(("p0", "p4")[y], 16 * y + n0, 16 * y + n1, 1, w, w + 1, 1, 32 * a, 32 * a + 16 + 16 * u), A("G", o + 512 * (1 - u) + w, o + 768 - 256 * u, 16), k(u, w))
                 for w in range(16) for u in (1, 0)], each=2)
-            if a >= 4 - P_LAST:
-                mms([(B("p0", 0, 8, 1, w, w + 1, 1, 32 * a, 32 * a + 32), A("P", 512 * a + w, 512 * a + 512, 16), A("Q8")) for w in range(16)])
-            elif a == 3 - P_LAST:
-                mms([(B("p0", 0, 8, 1, w, w + 1, 1, 0, 32 * a + 32), A("P", w, 512 * a + 512, 16), A("Q8")) for w in range(16)])
 
-    raw = (PS(0, 0, 128), PS(4, 256, 384))
+    raw, row = (PS(0, 0, 128), PS(4, 256, 384)), (PS(0, 128, 256), PS(4, 384, 512))
 
-    def marks(more=1):
-        for y in range(2):
-            if y == 0 and more and "fl1" not in ON_S:
-                act(half("aS", 1), raw[1], AF.Abs, scale=SC)
-            if more and "fl%d" % y in ON_S:
-                act(half("fl", y), raw[y], AF.Sigmoid, scale=-16.0 / EPS ** 2)
-            else:
-                ts(half("fl", y), raw[y], 0.0, OP.is_lt)
-        if more:
-            if "fl1" in ON_S:
-                act(half("aS", 1), raw[1], AF.Abs, scale=SC)
-            act(half("aS", 0), raw[0], AF.Abs, scale=SC)
-        mms([(half("p2", y), M("Bm", y), half("fl", y)) for y in range(2)])
-        tt(A("tt"), A("fl"), PS(2, 0, 256), OP.mult)
-
-    def digits(last=0):
-        one = A("ones", p1=32)
-        mm([(PS(3, 0, 256), A("Cz", 256 * last, 256 * last + 128, p1=32), one)] +
-           [(half("p3", y), M(m, y), view(1 - last, y, n)) for m, n in [("IDh", "Lh")] + [("I4", "Ly"), ("n60", "Lq")] * last for y in range(2)])
-        mm([(PS(3, 256, 512), A("Cz", 128, 256, p1=32), one)] +
-           [(half("p3", y, 16), M(m, y, 0, 128), view(1 - last, y, n)) for m, n in (("I2k", "LcB"), ("n64", "Lh")) for y in range(2)])
-
-    def powers():
-        mm([(half("p0", y, 16), M("Am", y), half("fl", y)) for y in range(2)] + [(PS(0, 256, 512), A("IDh"), A("tt"))])
-        for y in range(2):
-            act(A("pw", 128 * y, 128 * y + 128), half("p0", y, 16), AF.Sigmoid, bias=(pb0_, pb_)[y], scale=LN64)
-
-    def sort(last=0, dma=0):
-        for h in range(2):
-            tt(A("z", 256 * h, 256 * h + 256), PS(3, 256 * h, 256 * h + 256), A("pw"), OP.mult)
-        mm([(PS(3, 0, 256), A("ones", 0, 128, p1=32), A("Cs", p1=32))], True, False)
-        for a in range(8):
-            o = 32 * (a % 4)
-            ts(B("R", o, o + 32), A("z"), 64.0 ** (2 * a - POW), OP.max, 64.0 ** (2 * a + 2 - POW), OP.min)
-            mm([(PS(3, 128 * h + 64 * y + 8 * a, 128 * h + 64 * y + 8 * a + 8), half("R", y, o + 16 * h), M("Wt", y, 8 * a, 8 * a + 8))
-                for h in range(2) for y in range(2)], False, a == 7)
-        lin("D1", B("D", 0, 32, 1, 8, 16), PS(3, 0, 256), 1.0 / 64, 1057 - 31.5 / 64)
-        lin("D0", B("D", 0, 32, 1, 0, 8), PS(3, 0, 256))
-        if "D2" in ON_S and not last:
-            lin("D2", B("D2", 0, 32, 1, 0, 8), PS(3, 0, 256), 1.0 / 64, 1057 - 31.5 / 64)
+    def marks(y, more=1):
+        if "fl%d%s" % (y, "" if more else "z") in ON_S:
+            act(half("fl", y), row[y], AF.Sigmoid, scale=-256.0 / EPS ** 2)
         else:
-            cp(B("D2", 0, 32, 1, 0, 8), B("D", 0, 32, 1, 8, 16))
-        mm([(B("p4", 16 + y, 32, 2) if last else half("p4", y, 16), half(d, y, 16 * h), A(n))
-            for y in range(2) for h, d, n in ((0, "D2", "Ib"), (1, "D2", "Id"), (0, "D", "Ia"), (1, "D", "Ic"))], each=4)
+            ts(half("fl", y), row[y], 0.0, OP.is_lt)
+        if more:
+            lin("aS%d" % y, half("aS", y), raw[y], 1.0, -float(OFF))
+            if "nb%d" % y in ON_S:
+                act(half("nb", y), row[y], AF.Relu, scale=-2.0)
+            else:
+                ts(half("nb", y), row[y], -2.0, OP.mult, 0.0, OP.max)
+        o = half("p2", y) if more else PS(KB[y], 0, 128)
+        mms([(o, A("Bm"), half("fl", y))])
+        tt(half("tt", y), half("fl", y), o, OP.mult)
+
+    def digits(y, b, o, last=0):
+        one = A("ones", 0, 128, p1=32)
+        mm([(PS(b, o, o + 128), A("Cz", 256 * last, 256 * last + 128, p1=32), one)] +
+           [(PS(b, o, o + 128), A(m), view(1 - last, y, k)) for m, k in [("IDh", "Lh")] + [("I4", "Ly"), ("n60", "Lq")] * last])
+        mm([(PS(b, o + 128, o + 256), A("Cz", 128, 256, p1=32), one)] + [(PS(b, o + 128, o + 256), A(m), view(1 - last, y, k)) for m, k in (("I2k", "LcB"), ("n64", "Lh"))])
+
+    def powers(y, o):
+        mm([(o, A("Am"), half("fl", y)), (o, A("IDh"), half("tt", y))])
+        act(A("pw", 128 * y, 128 * y + 128), o, AF.Sigmoid, bias=pb_, scale=LN64)
+
+    def sort(y, b, o, last=0, dma=0):
+        z, sums = 256 * y, PS(b, o, o + 128)
+        for h in range(2):
+            tt(A("z", z + 128 * h, z + 128 * h + 128), PS(b, o + 128 * h, o + 128 * h + 128), A("pw", 128 * y, 128 * y + 128), OP.mult)
+        mm([(sums, A("ones", 0, 128, p1=32), A("Cs", 0, 128, p1=32))], True, False)
+        for a in range(8):
+            ring = 64 * y + 16 * (a % 4)
+            ts(B("R", ring, ring + 16), A("z", z, z + 256), 64.0 ** (2 * a - POW), OP.max, 64.0 ** (2 * a + 2 - POW), OP.min)
+            mm([(PS(b, o + 64 * h + 8 * a, o + 64 * h + 8 * a + 8), half("R", h, ring), A("Wt", 8 * a, 8 * a + 8)) for h in range(2)], False, a == 7)
+        rows = (16 * y, 16 * y + 16, 1)
+        lin("D1", B("D", *rows, 8, 16), sums, 1.0 / 64, 1057 - 31.5 / 64)
+        lin("D0", B("D", *rows, 0, 8), sums)
+        if "D2" in ON_S and not last:
+            lin("D2", B("D2", *rows, 0, 8), sums, 1.0 / 64, 1057 - 31.5 / 64)
+        else:
+            cp(B("D2", *rows, 0, 8), B("D", *rows, 8, 16))
+        out = B("p2", 16 + y, 32, 2) if last else half("p0", y)
+        mm([(out, half(d, h, 16 * y), A(k)) for h, d, k in ((0, "D2", "Ib"), (1, "D2", "Id"), (0, "D", "Ia"), (1, "D", "Ic"))])
         if dma:
-            lin("Lp", A("Lf"), PS(4, 256, 512), 1.0, lb_)
-        lin("Lp", A("Lp"), PS(4, 256, 512), 1.0, lb_)
+            lin("Lp", A("Lf", 128 * y, 128 * y + 128), out, 1.0, lb_)
+        lin("Lp", B("Lp", y, 16, 2) if last else half("Lp", y), out, 1.0, lb_)
 
     def spread_views(t):
         if t in BY_DMA:
-            dma("y", [(A("VT", p0=16 * a, p1=16 * a + 16), A("Lf")) for a in range(8)], VLAT)
+            for y in range(2):
+                dma("y", [(A("VT", 1024 * y, 1024 * y + 1024, p0=16 * a, p1=16 * a + 16), A("Lf", 128 * y, 128 * y + 128)) for a in range(8)], HLAT)
             return
         for j in range(4):
             b = "p%d" % VB[j % len(VB)]
@@ -595,28 +582,35 @@ def rank_program(g, core, T, topo):
         trade(lambda q: D(s, q), lambda q: D(d, q), 6600.0)
         dma(q, [(y, D(d))])
 
+    def new_V(y, sums, into, place):
+        s, back = (128 * y, 128 * y + 128), PS(7, 256 + 128 * y, 384 + 128 * y)
+        mms([(back, A(sums, *s), A("ID320"))])
+        act(A("As", *s), back, AF.Sigmoid)
+        ts(IND(A(into, 256 * y, 256 * y + 256), A("cl", place + 8 * y, place + 8 * y + 8)), A("As", *s), 2.0, OP.mult, -1.0, OP.add)
+
     def values(t):
+        table = A("Vt", 4096 * (t % 2), 4096 * (t % 2) + 4096) if t else A("V0")
         for c in range(8):
             a, y, e = 512 * c, c // 4, 4096 * (t % 2) + 512 * c
-            tt(A("Y", a, a + 512), IND(A("Vt", 4096 * (t % 2), 4096 * (t % 2) + 4096) if t else A("V0"), A("lv", 256 * t + 32 * c, 256 * t + 32 * c + 32)), A("E", e, e + 512), OP.mult)
-            mm([(PS(7, 32 * c + 16 * j, 32 * c + 16 * j + 16), A("Y", a + 256 * j + u, a + 256 * j + 256, 2), A("m16")) for j in range(2) for u in range(2)], each=2)
+            tt(A("Y", a, a + 512), IND(table, A("lv", 256 * t + 32 * c, 256 * t + 32 * c + 32)), A("E", e, e + 512), OP.mult)
+            for j in range(2):
+                mm([(PS(7, 32 * c + 16 * j, 32 * c + 16 * j + 16), A("Y", a + 256 * j + u, a + 256 * j + 256, 2), A("m16")) for u in range(2)])
             if c % 4 == 3:
-                s = (128 * y, 128 * y + 128)
-                v, back = (256 * y, 256 * y + 256), PS(7, 256 + s[0], 256 + s[1])
-                act(A("At", *s), PS(7, *s))
-                mms([(back, A("At", *s), A("ID320"))])
-                place = A("cl", 88 * t + 72 + 8 * y, 88 * t + 80 + 8 * y)
-                if t in V_PUT:
-                    act(A("As", *s), back, AF.Sigmoid)
-                    ts(IND(A("Vp", *v), place), A("As", *s), 2.0, OP.mult, -1.0, OP.add)
-                else:
-                    act(A("As", *s), back)
-                    act(IND(A("Vc", *v), place), A("As", *s), AF.Sigmoid)
-                    lin("Vo", A("Vp", *v), A("Vc", *v), 2.0, -1.0)
+                act(A("At", 128 * y, 128 * y + 128), PS(7, 128 * y, 128 * y + 128))
                 if t < NS - 1:
+                    new_V(y, "At", "Vp", 88 * t + 72)
                     spread_V(t + 1, y)
                 else:
-                    hand_back("vw"[y], "Vp", *v, (T["yv"][:, v[0]:v[1]], []))
+                    piece = lambda n, q, y=y: A(n, 128 * y + 16 * q, 128 * y + 16 * q + 16)
+                    trade(lambda q: piece("At", q), lambda q: piece("Ah", q))
+                    act(piece("Ah", r), piece("At", r))
+        for y in range(2 if t == NS - 1 else 0):
+            new_V(y, "Ah", "Vf", 368)
+            dma("y", [((T["yv"][:, 256 * y:256 * y + 256], []), A("Vf", 256 * y, 256 * y + 256))])
+        if t == NS - 2:
+            act(A("Vo", 0, 256), IND(A("Vp"), A("cl", 352, 368)))
+            hand_back("v", "Vo", 0, 256, A("Vo", 256, 512))
+            cp(IND(A("Vf"), A("cl", 384, 400)), A("Vo", 256, 512))
 
     si = lambda j: A("si", 16 * j, 16 * j + 16)
     lu = lambda t, c: A("lu", 256 * t + 32 * c, 256 * t + 32 * c + 32)
@@ -624,31 +618,36 @@ def rank_program(g, core, T, topo):
         step[0] = t
         scores(t)
         if t == 0:
-            if V_PUT:
-                lin(True, A("Vp"), A("Vb"))
-            else:
-                lin(True, A("Vc"), A("Vb"), 0.5, 0.5)
+            lin(True, A("Vp"), A("Vb"))
             first_V()
+            dma("y", [(mine(q), A("KK", 1536, 2048, p0=16 * q, p1=16 * q + 16)) for q in range(8)], 2100.0)
         else:
-            digits()
-        mm([(PS(1, 256, 512), A("ones", 0, 128), A("I2k"))] +
-           [(PS(1, 256 + 128 * h, 384 + 128 * h), view(t, h), A("I2k", 0, 128)) for h in range(2)])
-        mm([(PS(1, 0, 256), A("ones", 0, 128), A("Mc"))], True, False)
-        if t:
-            marks()
-        else:
-            act(half("aS", 1), raw[1], scale=SC)
-            ts(half("aS", 0), raw[0], SC, OP.mult)
-        hs = [(PS(1, 128 * h, 128 * h + 128), h) for h in range(2)]
-        for o, h in hs[::-1]:
-            mm([(o, half("aS", h), M("ID32", h))], False, t == h == 0)
-        if t:
-            mm([(o, half("fl", h), M("Mf", h)) for o, h in hs], False, False)
-            mm([(o, half("tt", h), M("Mt", h)) for o, h in hs], False, True)
-            on("L", powers)
-        mm([(PS(4, 128 * y, 128 * y + 128), M(m, y), half(n, y)) for m, n in (("ISC", "aS"), ("m8A", "fl"), ("m8I", "tt"))[:3 if t else 1] for y in range(2)],
-           True, False)
-        scan(A("Mx"), A("rm"), PS(1, 0, 256), OP.mult, OP.max)
+            for y in range(2):
+                on("L", digits, y, 3, 256 * y)
+        for h in range(2):
+            b, s = KB[h], (128 * h, 128 * h + 128)
+            key = PS(b, 0, 128)
+            mm([(PS(b, 128, 256), A("ones", 0, 128), A("I2k")), (PS(b, 128, 256), view(t, h), A("I2k"))])
+            mms([(PS(b, 256, 384), A("IDh"), A("own", *s))])
+            mm([(key, A("ones", 0, 128), A("Mc"))], True, False)
+            if t:
+                marks(h)
+                mm([(key, half("fl", h), A("Mf"))], False, False)
+            else:
+                lin(h == 1, half("aS", h), raw[h], 1.0, -float(OFF))
+            mm([(key, half(n, h), A("ISC")) for n in ("aS", "nb")[:2 if t else 1]], False, t == 0)
+            if t:
+                mm([(key, half("tt", h), A("Mt"))], False, True)
+            scan(A("Mx", *s), A("rm"), key, OP.mult, OP.max)
+            tt(A("us", *s), A("Mx", *s), key, OP.subtract)
+            tt(A("d1", *s), PS(b, 128, 256), A("us", *s), OP.subtract)
+            scan(A("Bx", *s), A("us", *s), A("d1", *s), OP.min, OP.max)
+            cp(A("bl", 8 * h, 8 * h + 8), A("Bx", s[0] + 15, s[1], 16))
+            act(A("gkB", *s), IND(Tt, A("bl", 8 * h, 8 * h + 8)), AF.Abs)
+            tt(K2(t, 512 + 2 * s[0], 512 + 2 * s[1], 2), PS(b, 256, 384), A("gkB", *s), OP.max)
+            if t:
+                on("L", powers, h, half("p0", h, 16))
+        mm([(PS(4, 0, 256), A(m), A(n)) for m, n in (("PMb", "aS"), ("PMb", "nb"), ("m8A", "fl"), ("m8I", "tt"))[:4 if t else 1]], True, False)
         line[0] = "V"
         ts(si(3), A("Mx", 15, 256, 16), 1 / SC, OP.mult, 0.46, OP.add)
         ts(A("MR", 0, 16), si(3), -1860.0, OP.add)
@@ -657,17 +656,9 @@ def rank_program(g, core, T, topo):
         mm([(PS(4, 128 * y, 128 * y + 128), A("Hs", 128 * y, 128 * y + 128, p1=16), A("MTs", 0, 128, p1=16)) for y in range(2)], False, True)
         weights(t)
         line[0] = "K"
-        tt(A("us"), A("Mx"), PS(1, 0, 256), OP.subtract)
-        tt(A("d1"), PS(1, 256, 512), A("us"), OP.subtract)
-        scan(A("Bx"), A("us"), A("d1"), OP.min, OP.max)
         bs = A("Bx", 15, 256, 16)
-        cp(A("bl"), bs)
-        mms([(PS(OWN, 0, 256), A("IDh"), own(t))])
-        act(A("gkB"), IND(A("Tt"), A("bl")), AF.Abs)
-        tt(K2(t, 512, 768), PS(OWN, 0, 256), A("gkB"), OP.max)
-        kn = 768 * (t % 2) + 512
         mm([(PS(1, 384, 400), A("thZ", p1=64), A("IDh", 16 * t, 16 * t + 16, p1=64))] +
-           [(PS(1, 384, 400), A("EB", 15 - b, 143 - b), A("KK", kn + b, kn + 256, 16)) for b in range(16)])
+           [(PS(1, 384, 400), A("EB", 15 - b, 143 - b), K2(t, 512 + 2 * b, 1024, 32)) for b in range(16)])
         rc = "rc%d" % t
         lin("rc", A(rc, 16 * r, 16 * r + 16), PS(1, 384, 400))
         trade(lambda q: A(rc, 16 * r, 16 * r + 16), lambda q: A(rc, 16 * q, 16 * q + 16), 4800.0, 3000.0)
@@ -680,10 +671,10 @@ def rank_program(g, core, T, topo):
         ts(A("MR", 16, 32), si(4), q_, OP.is_equal)
         mr = lambda j: A("MR", 16 * j - 48, 16 * j - 32)
         if t in BY_DMA:
-            ts(si(8), si(7), 4, OP.arith_shift_right)
-            ts(si(9), si(7), 7, OP.arith_shift_right)
-            cp(A("MR", 32, 112), A("si", 80, 160))
-            mm([(PS(1, 432, 448), A(m), mr(j)) for m, j in (("IDh", 7), ("I240", 8), ("n2032", 9))])
+            for j, bit in ((8, 4), (9, 7), (10, 10)):
+                ts(si(j), si(7), bit, OP.arith_shift_right)
+            cp(A("MR", 32, 128), A("si", 80, 176))
+            mm([(PS(1, 432, 448), A(m), mr(j)) for m, j in (("IDh", 7), ("I112", 8), ("n1008", 9), ("I896", 10))])
             act(A("d16", 0, 16), PS(1, 432, 448))
         else:
             cp(A("MR", 32, 64), A("si", 80, 112))
@@ -696,17 +687,22 @@ def rank_program(g, core, T, topo):
         mm([(A("p2", 256, 272, 1, 32 * a, 32 * a + 32), A("W16", 16 - 16 * u, 48 - 16 * u), A("dx", 32 * a + 16 * u, 32 * a + 16 * u + 16)) for a in range(4) for u in range(2)], each=2)
         cp(A("dl"), PS(2, 256, 272))
         if t > 0:
-            sort(0, t in BY_DMA)
+            for y in range(2):
+                sort(y, 3, 256 * y, 0, t in BY_DMA)
         elif t in BY_DMA:
             mms([(PS(3, 128 * y, 128 * y + 128), A("PMb"), view(t, y)) for y in range(2)])
             lin("Lp", A("Lf"), PS(3, 0, 256))
-        act(K2(t + 1), IND(K2(t, 0, 768), A("cl", 88 * t + 40, 88 * t + 72)))
+        line[0] = "K"
+        for e in range(2):
+            act(K2(t + 1, e, 512, 2), IND(K2(t, 0, 1024), A("cl", 88 * t + 40 + 16 * e, 88 * t + 56 + 16 * e)))
+        if t < NS - 1:
+            spread_K(t + 1)
+        line[0] = "L"
         if t == NS - 1:
-            for e in range(2):
-                if "Ko" in ON_S:
-                    act(A("Ko", e, 512, 2), K2(NS, 256 * e, 256 * e + 256), AF.Relu, bias=-2 * EPS)
-                else:
-                    ts(A("Ko", e, 512, 2), K2(NS, 256 * e, 256 * e + 256), 12582912.0, OP.add, -12582912.0, OP.add)
+            if "Ko" in ON_S:
+                act(A("Ko"), K2(NS), AF.Relu, bias=-2 * EPS)
+            else:
+                ts(A("Ko"), K2(NS), -2 * EPS, OP.add, 0.0, OP.max)
             hand_back("k", "Ko", 0, 512, (T["yk"][:, :], []), "g")
         spread_views(t)
         mm([(PS(2, 256, 512), A("nI"), A("ones")), (PS(2, 256, 512), A("nI"), A("sS"))], True, False)
@@ -724,27 +720,24 @@ def rank_program(g, core, T, topo):
             cp(A("R0", 32 * r, 32 * r + 32), A("Ls", 32 * r, 32 * r + 32))
         lists(t + 1)
         line[0] = "K"
-        sg = [A("sg", 0, 16), A("sg", 16, 32)]
-        mm([(PS(1, 400, 432), A("n8k"), A("sg")), (PS(1, 416, 432), A("n8k"), sg[0]), (PS(1, 400, 416), A("n8k"), A("m05"))], True, False)
+        mm([(PS(1, 400, 432), A("n8k"), A("sg")), (PS(1, 401, 432, 2), A("n8k"), A("sg", 0, 32, 2)), (PS(1, 400, 432, 2), A("n8k"), A("m05"))], True, False)
         for hs in (near, far):
-            mm([(PS(1, 400 + 16 * e, 416 + 16 * e), A("nI"), A(rc, 16 * h, 16 * h + 16)) for e in range(2) for h in hs], False, hs == far)
+            mm([(PS(1, 400 + e, 432, 2), A("nI"), A(rc, 16 * h, 16 * h + 16)) for e in range(2) for h in hs], False, hs == far)
         ts(A("sg"), PS(1, 400, 432), 0.5, OP.is_lt, -0.5, OP.add)
-        n = 512 if t else 256
-        mms([(PS(0, b, n, 16), A("XK", 128 * b, 128 * b + 128), A("sg", 0, n // 16)) for b in range(16)])
-        for o in range(0, n, 256):
-            tt(A("Tc", o, o + 256), PS(0, o, o + 256), K2(t + 1, o, o + 256), OP.mult)
+        sign_T()
         if t < NS - 1:
             cur_lists(t + 1)
             own_K(t + 1)
-        spread_T(SHARE if t < NS - 1 else SHARE_LAST, 0 if t else 2, T_DMA[t])
         on("V", values, t)
 
     step[0] = NS
     scores(NS)
-    digits(1)
-    marks(0)
-    powers()
-    sort(1)
+    for y in range(2):
+        digits(y, SB[y], 0, 1)
+        marks(y, 0)
+        powers(y, PS(KB[y], 256, 384))
+    for y in range(2):
+        sort(y, SB[y], 0, 1)
     swap(lambda x, p: B("p2", x, 16, 8, 0, 16, 1, p, p + 32), lambda q: A("Lp", 32 * q, 32 * q + 32), "IE2")
     lin("Lo", A("Lo"), PS(2, 0, 256), 2048.0, 2048.0)
     dma("s", [((T["yl"][:, :], []), A("Lo"))])
@@ -752,7 +745,7 @@ def rank_program(g, core, T, topo):
 
 
 def arrange(ops):
-    n = len(ops)
+    n, WAKE = len(ops), WAKES[0]
     other = [[o["other"][j] for o in ops] for j in range(2)]
     cost, lat, hold = [o["cost"] for o in ops], [o["lat"] for o in ops], [o["hold"] for o in ops]
     queue = [("pe", "v", "s", "g", "y", None).index(o["q"]) for o in ops]
@@ -822,35 +815,6 @@ def arrange(ops):
                 end[i] = t + c + lat[i]
         return max(end) + 1e-2 * sum(end) / n, at, end
 
-    def again(new):
-        seq = [i for k, i in sorted(zip(new[1], range(n)))]
-        spans = [span(seq, other[j], LATE[j]) for j in range(2)]
-        return new[0] + BOTH[0] * spans[0] + BOTH[1] * spans[1], new[1], new[2], new[0], spans
-
-    def span(seq, slow, f):
-        free, at, end = [0.0] * 8, [0.0] * n, [0.0] * n
-        for i in seq:
-            q, c = queue[i], slow[i]
-            t = free[q]
-            for d in hard[i]:
-                x = end[d] + WAKE
-                if x > t:
-                    t = x
-            for d in soft[i]:
-                x = at[d] + slow[d]
-                if x > t:
-                    t = x
-            if q < 5:
-                free[q] = t + c
-            at[i] = t
-            if hold[i]:
-                q = 6 if q == 5 else 7
-                free[q] = max(free[q], t + c + 1400 * f) + hold[i] * f
-                end[i] = free[q] + 600 * f
-            else:
-                end[i] = t + c + lat[i] * f
-        return max(end)
-
     def back(at, end):
         st, en, lead = [[] for q in range(5)], [[] for q in range(5)], [0.0] * n
         for i in order(end)[::-1]:
@@ -865,7 +829,7 @@ def arrange(ops):
             lead[i] = t + cost[i]
         return [-x for x in lead]
 
-    def lean(now, key, tries, kinds, both_ways=False):
+    def lean(now, key, tries, kinds):
         best = now
         for it in range(tries):
             p = list(key if kinds else now[1])
@@ -888,18 +852,22 @@ def arrange(ops):
             if not kinds and it % 10 == 0:
                 new = min(new, forth(back(new[1], new[2])), key=lambda z: z[0])
             room = SLACK * (1 - it / tries) * float(rng.exponential())
-            if both_ways:
-                if new[0] > now[3] + room + 1500:
-                    continue
-                new = again(new)
             if new[0] <= now[0] + room:
                 now, key = new, p
                 if new[0] < best[0]:
                     best = new
         return best
 
-    def play(seq, j, p=0, old=None):
-        c_, f = costs[j], late[j]
+    seats = [(1 << q if q < 5 else 0) | (1 << 6 + (q != 5) if h else 0) for q, h in zip(queue, hold)]
+    reach = [0] * n
+
+    def spot(seq):
+        for k, i in enumerate(seq):
+            for d in both[i]:
+                reach[d] = k
+
+    def play(seq, j, p=0, old=None, stop=n):
+        c_, f, wake = costs[j], LATE[j], WAKES[j]
         free, last = [0.0] * 8, [-1] * 8
         at, end, why = ([0.0] * n, [0.0] * n, [-1] * n) if old is None else (old[3][:], old[4][:], old[1][:])
         todo = {0, 1, 2, 3, 4, 6, 7}
@@ -914,11 +882,13 @@ def arrange(ops):
                 free[6 + (q != 5)], last[6 + (q != 5)] = end[i] - 600 * f, i
             if not todo:
                 break
-        for i in seq[p:]:
+        odd, owed = 0, 0
+        for k in range(p, n):
+            i = seq[k]
             q, c = queue[i], c_[i]
             t, w = free[q], -2 - last[q]
             for d in hard[i]:
-                x = end[d] + WAKE
+                x = end[d] + wake
                 if x > t:
                     t, w = x, d
             for d in soft[i]:
@@ -927,17 +897,27 @@ def arrange(ops):
                     t, w = x, d
             if q < 5:
                 free[q], last[q] = t + c, i
-            at[i] = t
             if hold[i]:
                 q = 6 + (q != 5)
                 x = t + c + 1400 * f
                 if free[q] > x:
                     x, w = free[q], -2 - last[q]
                 free[q], last[q] = x + hold[i] * f, i
-                end[i] = free[q] + 600 * f
+                e = free[q] + 600 * f
             else:
-                end[i] = t + c + lat[i] * f
+                e = t + c + lat[i] * f
             why[i] = w
+            if t != at[i] or e != end[i]:
+                at[i], end[i] = t, e
+                odd |= seats[i]
+                if reach[i] > owed:
+                    owed = reach[i]
+            elif k <= stop:
+                odd |= seats[i]
+            else:
+                odd &= ~seats[i]
+                if not odd and k >= owed:
+                    break
         m = max(end)
         return m + 3e-3 * sum(end) / n, why, end.index(m), at, end
 
@@ -954,6 +934,7 @@ def arrange(ops):
 
     def polish(seq, tries):
         now = [play(seq, j) for j in range(len(costs))]
+        spot(seq)
         val = sum(w * x[0] for w, x in zip(weight, now))
         best, pairs, cum = (val, seq, now), [blocked(x) for x in now], np.cumsum(weight) / sum(weight)
         for it in range(tries):
@@ -975,19 +956,20 @@ def arrange(ops):
             moved = set(first)
             new = seq[:pa] + first + [x for x in seq[pa:pb + 1] if x not in moved] + seq[pb + 1:]
             room = SLACK * (1 - it / tries) * float(rng.exponential())
-            one = play(new, j, pa, now[j])
+            one = play(new, j, pa, now[j], pb)
             if weight[j] * (one[0] - now[j][0]) > room + 400:
                 continue
-            runs = [one if k == j else play(new, k, pa, now[k]) for k in range(len(costs))]
+            runs = [one if k == j else play(new, k, pa, now[k], pb) for k in range(len(costs))]
             v = sum(w * x[0] for w, x in zip(weight, runs))
             if v <= val + room:
                 seq, now, val, pairs = new, runs, v, [blocked(x) for x in runs]
+                spot(seq)
                 if v < best[0]:
                     best = (v, seq, now)
         return best
 
     if n not in KEPT:
-        costs, late, weight, needs = [cost] + other, (1.0,) + LATE, (1.0,) + BOTH, []
+        costs, weight, needs = [cost] + other, WEIGHTS, []
         for o in ops:
             m = bits(o["deps"] | o["order"])
             for d in o["deps"] | o["order"]:
@@ -1012,7 +994,7 @@ def arrange(ops):
         best = min([polish(order(z[1]), MORE) for z in best], key=lambda z: z[0])
         best = polish(best[1], TRIES)
         KEPT[n] = best[1]
-        KEPT["times"] = (best[0], best[2][0][3], best[2][0][4], best[2][0][0], [x[0] for x in best[2][1:]])
+        KEPT["times"] = (best[0], best[2][0][3], best[2][0][4], best[2][0][0], [x[0] for x in best[2][1:]], best[2][0][1])
     seq = KEPT[n]
     place = {j: k for k, j in enumerate(seq)}
     for j, o in enumerate(ops):

import math
import numpy as np
from concourse.bass import DstId, RemoteDMATransfer
from concourse.mybir import AluOpType as OP, ActivationFunctionType as AF

F, BF, HF, I, U = "float32", "bfloat16", "float16", "int32", "uint16"
NS = 4
SC = float(2 ** 18)
C8 = 129.0 / 16
EPS = 2.0 ** -18
OFF = 1656
LN64 = math.log(64.0)
LOW, POW = 16.0, 18
RATES = ((0.92, 1.3, 3.0, 0.48), (1.2, 2.2, 6.0, 0.6), (0.95, 1.4, 3.2, 0.48))
WEIGHTS, LATE, WAKES, ISSUE = (1.0, 0.4, 0.5), (1.0, 1.1, 0.95), (170.0, 170.0, 90.0), (80.0, 100.0, 60.0)
VLAT, LONG = 4400.0, 3500.0
STARTS, FIRST, TRIES, STEP, SLACK, KEPT = 2, 300, 70000, 4000.0, 300.0, {}
SHARE_ENDS, SHARE_VT = (1, 3, 5, 7), (1,)
ON_V = ((0, 2, 4, 6), (1, 3, 5), (1, 3, 5), (1, 3, 5), (1, 3, 5))
TLAT, HLAT = 2150.0, 3600.0
SEED, MORE = 2, 3500
DIAG_Q = "yy"
BY_DMA = (0, 1, 2)
ON_S = {"D0", "D1", "D2", "x16", "MTs", "Lp", "L0", "Vo", "Lh", "dx", "fl0", "fl1", "Ko", "Lo", "Ly", "rc", "aS0", "aS1", "nb0", "nb1", "lu", "lv", "Lu"}
WB, TB, VB, KB, SB = (6, 5), (4, 0, 1), (3, 4), (1, 5), (3, 6)
SCRATCH = {}


def _sb(dtype, **kw):
    for n, c in kw.items():
        SCRATCH[n] = ("sbuf", [128] + (list(c) if isinstance(c, tuple) else [c]), dtype)


SL = (16, 16)
_sb(BF, Tt=4096, V0=4096, K0=512, V1=512, Kb=512, Vb=512, KK=2048, Tc=512, Z=512, own=256, G=768 * 8, diag=(16, 256), fl=SL, nb=SL, tt=SL, sS=256, pw=256, z=512, R=(128, 16), BO=128, EB=144,
    S16=264, SEL0=1024, XK=2048, Hs=512, IE2=272, Mc=128, I2k=128, ones=256, rm=128, Cs=256, Cz=384, Ko=512, gkB=256, Wt=64, Q8=8, m05=16)
_sb(F, Vt=8192, E=8192, Y=4096, d16=32, Vp=512, Vo=512, Vf=512, Ah=256, VT=2048, Lf=256, Lo=256, Mx=256, us=256, d1=256, Bx=256, As=256, At=256,
    iot=272, ioq=128, ioj=256, pc=32, mk=24, ID32=128, ID320=128, wL=16, m16=16)
_sb(HF, LcB=SL, Lq=SL, Ly=SL, Lp=SL, Lh=SL, Ls=SL, Lu=SL, aS=SL, R0=256, L0=256, ga=256, D=(32, 16), D2=(32, 16), x16=SL, IEh=272, thZ=128, cL=88, sg=32, MR=128,
    dx=128, W16=48, xf=8, MTs=256, rc0=128, rc1=128, rc2=128, rc3=128)
_sb(I, Li=256, thI=16, pi=8, si=176)
_sb(U, lu=1280, lv=1024, bl=16, dl=16, xl=8, cl=400)
PART = {}
for _n in "Bm m8A Mf Mt Us nU m8I PMb Am LE nI PMv PMw PMh PMy PMq PMt Iy Iq I4 n60 PMk IDh n64 n8k I512 n512 Ia Ib Ic Id I112 n1008 I896 ISC Hm nHm".split():
    PART[_n] = ("cmat", 128 * len(PART))
_sb(BF, cmat=128 * len(PART))
for _i in range(8):
    SCRATCH["p%d" % _i] = ("psum", [128, 512] if _i in KB else [128, 32, 16], F)
SCRATCH["SKd"] = ("dram", [8, 128, 64], BF)
SCRATCH["Vd"] = ("dram", [4, 16, 8, 256], F)
SCRATCH["SVd"] = ("dram", [8, 128, 64], BF)
SCRATCH["Kd"] = ("dram", [16, 2, 8, 256], BF)
for _n, _c, _d in (("k", 64, BF), ("v", 32, F)):
    SCRATCH["S" + _n + "d"] = ("dram", [8, 128, _c], _d)
    SCRATCH["R" + _n + "d"] = ("dram", [8, 128, _c], _d)
SEMAPHORES = ["pe", "v", "s", "g", "sent"] + ["d%d" % i for i in range(80)] + [_c + str(i) for _c in "ab" for i in range(14)]


def spread(topo, src, dsts):
    far = [d for d in dsts if topo.chip(d) != topo.chip(src)]
    near = [d for d in dsts if topo.chip(d) == topo.chip(src)]
    fe = topo.engines(src, far[0]) if far else []
    ne = [e for e in topo.engines(src, near[0]) if e not in fe] if near else []
    out = {}
    for ds, es in ((far, fe), (near, ne)):
        if ds:
            n = 1
            while 2 * n * len(ds) <= len(es):
                n *= 2
            for i, d in enumerate(ds):
                out[d] = (sum(1 << e for e in es[i * n:(i + 1) * n]), n)
    return out


def bits(cols):
    return sum(1 << c for c in cols)


def rank_program(g, core, T, topo):
    r = T.rank_of(core)
    if r is None:
        return
    cores = list(T.cores)
    others = [c for c in cores if c != core]
    QU = {"pe": g.tensor, "v": g.vector, "s": g.scalar, "g": g, "y": g.sync}
    ops, acc, nd, step, line = [], {}, [0], [-1], ["K"]

    def on(name, fn, *a):
        line.insert(0, name)
        fn(*a)
        line.pop(0)

    def B(n, r0, r1, rs=1, c0=0, c1=None, cs=1, p0=0, p1=128):
        w = SCRATCH[n][1][2]
        c1 = w if c1 is None else c1
        cols = [w * i + j for i in range(r0, r1, rs) for j in range(c0, c1, cs)]
        rows = r0 if r1 - r0 <= rs else slice(r0, r1, rs)
        return (T[n][p0:p1, rows, c0 if len(cols) > 1 and c1 - c0 <= cs else slice(c0, c1, cs)], [(n, bits(cols), len(cols))])

    def A(n, a=0, b=None, st=1, p0=0, p1=128):
        if n in PART:
            n, a, b = PART[n][0], PART[n][1] + a, PART[n][1] + (128 if b is None else b)
        shape = SCRATCH[n][1]
        if b is None:
            b = int(np.prod(shape[1:]))
        if len(shape) == 3:
            w = shape[2]
            if st >= w:
                return B(n, a // w, (b + w - 1) // w, st // w, a % w, a % w + 1, 1, p0, p1)
            if a // w == (b - 1) // w:
                return B(n, a // w, a // w + 1, 1, a % w, (b - 1) % w + 1, st, p0, p1)
            return B(n, a // w, b // w, 1, a % w, w, st, p0, p1)
        ap = T[n][p0:p1, a:b:st] if st > 1 else T[n][p0:p1, a:b]
        return (ap, [(n, bits(range(a, b, st)) if st > 1 else (1 << b) - (1 << a), len(range(a, b, st)))])

    def IND(w, o):
        return (w[0].indirect(o[0]), w[1] + o[1])

    def D(n, i=None):
        return (T[n][:], [(n, 255, 8)]) if i is None else (T[n][i], [(n, 1 << i, 1)])

    def rec(q, fn, rd, wr, sem=None, n=0, cost=60.0, lat=0.0, after=()):
        deps, order = set(), set(after)
        me = len(ops)
        for kind, regs in ((0, rd), (1, wr)):
            for x in regs:
                ps = SCRATCH.get(x[0], "x")[0] == "psum"
                for y, k2, o in acc.get(x[0], []):
                    oq = ops[o]["q"] if ops[o]["sem"] is None else None
                    if q == "pe" and oq == "pe":
                        if ps:
                            order.add(o)
                        continue
                    if (ps and oq != q) or ((kind or k2) and x[1] & y[1]):
                        deps.add(o)
        for kind, regs in ((0, rd), (1, wr)):
            for x in regs:
                lst = acc.setdefault(x[0], [])
                if kind:
                    lst[:] = [e for e in lst if e[0][1] & ~x[1]]
                lst.append((x, kind, me))
        j = 3 if q == "pe" else 0
        cost, *other = cost if isinstance(cost, list) else [cost * x[j] / RATES[0][j] for x in RATES]
        ops.append({"q": q, "fn": fn, "other": other, "deps": deps, "order": order, "sem": sem, "n": n, "cost": cost, "lat": lat, "hold": max(0.0, lat - 2000), "step": step[0], "line": line[0],
                    "tag": (q, wr[0][0] if wr else None, rd[0][0] if rd and q == "pe" else None)})

    def wide(x):
        return 16 * x[1][-1][2] if len(x[1]) > 1 else x[1][0][2]

    def size(x):
        return 4 if SCRATCH[x[1][0][0]][2] in (F, I) else 2

    def price(o, a, per):
        kind, n = (1, wide(a)) if len(a[1]) > 1 else (2, wide(o)) if len(o[1]) > 1 else (0, per * wide(o))
        return [60 + x[kind] * n if kind else x[0] * max(64, n) for x in RATES]

    def regs(*xs):
        return [p for x in xs if isinstance(x, tuple) for p in x[1]]

    def val(x):
        return x[0] if isinstance(x, tuple) else x

    def outs(o):
        return o[1][:1], o[1][1:]

    def ts(o, a, s1, op0, s2=None, op1=None):
        c = price(o, a, 0.5 if size(o) == 2 == size(a) else 1)
        w, x = outs(o)
        if op1 is None:
            rec("v", lambda: g.vector.tensor_scalar(o[0], a[0], val(s1), None, op0), regs(a, s1) + x, w, cost=c)
        else:
            rec("v", lambda: g.vector.tensor_scalar(o[0], a[0], val(s1), val(s2), op0, op1), regs(a, s1, s2) + x, w, cost=c)

    def tt(o, a, b, op):
        c = price(o, a, 1 if "psum" in (SCRATCH[a[1][0][0]][0], SCRATCH[b[1][0][0]][0]) else 2)
        rec("v", lambda: g.vector.tensor_tensor(o[0], a[0], b[0], op), regs(a, b), o[1], cost=c)

    def cp(o, a):
        w, x = outs(o)
        rec("v", lambda: g.vector.tensor_copy(o[0], a[0]), regs(a) + x, w, cost=price(o, a, 0.5 if size(o) == 2 == size(a) else 1))

    def fill(o, c):
        rec("v", lambda: g.vector.memset(o[0], c), [], o[1], cost=price(o, o, 0.5))

    def scan(o, a, b, op0, op1):
        rec("v", lambda: g.vector.tensor_tensor_scan(o[0], a[0], b[0], 0.0, op0, op1), regs(a, b), o[1], cost=price(o, a, 1))

    def act(o, a, f=AF.Copy, bias=None, scale=None):
        w, x = outs(o)
        kw = {}
        if bias is not None:
            kw["bias"] = val(bias)
        if scale is not None:
            kw["scale"] = val(scale)
        c, after = price(o, a, 1), []
        if f == AF.Sigmoid:
            c, after = [x + (0 if table else 1400) for x in c], table[:1]
            table.append(len(ops))
        rec("s", lambda: g.scalar.activation(o[0], a[0], f, **kw), regs(a, bias, scale) + x, w, cost=c, after=after)

    table = []

    def lin(key, o, a, scale=1.0, bias=0.0):
        if key is True or key in ON_S:
            act(o, a, AF.Identity, bias=bias, scale=scale)
        else:
            ts(o, a, scale, OP.mult, bias, OP.add)

    def mm(lst, start=True, stop=True, each=0):
        def fn():
            for j, (o, l, x) in enumerate(lst):
                if each:
                    h = g.tensor.matmul(o[0], l[0], x[0], j % each == 0, j % each == each - 1)
                else:
                    h = g.tensor.matmul(o[0], l[0], x[0], start and j == 0, stop and j == len(lst) - 1)
            return h
        rec("pe", fn, [p for o, l, x in lst for p in l[1] + x[1]], [p for o, l, x in lst for p in o[1]],
            cost=sum(max(min(64, wide(l)), wide(x)) * (4 if size(x) == 4 else 1) * RATES[0][3] for o, l, x in lst))

    def mms(lst):
        mm(lst, each=1)

    def iota(o, pat, cm=0, flt=True):
        if flt:
            rec("g", lambda: g.iota(o[0], pat, 0, cm, allow_small_or_imprecise_dtypes=True), [], o[1], cost=130 + 2 * wide(o))
        else:
            rec("g", lambda: g.iota(o[0], pat, 0, cm), [], o[1], cost=130 + 2 * wide(o))

    def dma(q, pairs, lat=2250.0):
        sem = "d%d" % nd[0]
        nd[0] += 1

        def fn():
            for o, x in pairs:
                QU[q].dma_start(o[0], x[0]).then_inc(T.sem[sem], 16)
        rec(q, fn, [p for o, x in pairs for p in x[1]], [p for o, x in pairs for p in o[1]], sem, 16 * len(pairs), [x * len(pairs) for x in ISSUE], lat)

    sent, calls = [0], []

    def dst(c):
        a = topo.addr(c)
        return DstId(rid=a[0], pnc=a[1])

    near = [q for q in range(8) if topo.chip(cores[q]) == topo.chip(core)]
    far = [q for q in range(8) if q not in near]

    def trade(src, land, lat=4800.0, soon=0):
        sem = lambda q: "%s%d" % ("b" if soon and q in near else "a", len(calls))
        mk = spread(topo, core, others)
        trs = [RemoteDMATransfer(dst_ids=[dst(c)], dma_engine_mask=mk[c][0], remote_sem=T.sem[sem(T.rank_of(c))], src=src(T.rank_of(c))[0], dst=land(r)[0]) for c in others]
        sent[0] += sum(mk[c][1] for c in others)
        rec("g", lambda: g.remote_dma_fused(trs, local_sem=T.sem.sent), regs(*[src(q) for q in range(8) if q != r]), [], "-", 0, 300.0,
            after=calls[-1:] if len(calls) < 3 else [])
        call = len(ops) - 1
        for qs, ns in ((near, soon), (far, lat)) if soon else ((near + far, lat),):
            qs = [q for q in qs if q != r]
            n = sum(spread(topo, cores[q], [x for x in cores if x != cores[q]])[core][1] for q in qs)
            rec(None, None, [], regs(*[land(q) for q in qs]), sem(qs[0]), n, 0.0, ns, [call])
            if ns == soon:
                ops[-1]["hold"] = 0.0
        calls.append(call)

    X = lambda n, a, b: (T[n][a:b, :], [])
    col = lambda n, j, p1=128: A(n, j, j + 1, p1=p1)
    PS = lambda i, a=0, b=512, st=1, p1=128: A("p%d" % i, a, b, st, p1=p1)
    half = lambda n, y, r0=0: B(n, r0 + 8 * y, r0 + 8 * y + 8)

    def view(t, y, n="LcB"):
        return A("R0" if n == "LcB" else n, y, 256, 2) if t % NS == 0 else half(n, y)

    def swap(out, src, ie="IEh"):
        mm([(out(x, 32 * a), A(ie, 32 * x + 16 - 16 * u, 32 * x + 48 - 16 * u), src(2 * a + u)) for x in range(8) for a in range(4) for u in range(2)], each=2)

    dma("y", [(D("SKd"), X("k0", 0, 128))])
    dma("s", [(A("Li"), X("vl", 0, 128))])
    dma("y", [(D("SVd"), X("v0", 0, 128))])
    dma("s", [(A("thI", p1=64), X("th", 0, 4))])
    dma("y", [(A("K0", 64 * r, 64 * r + 64), X("k0", 16 * r, 16 * r + 16))])
    dma("s", [(A("V1", 64 * r, 64 * r + 64), X("v0", 16 * r, 16 * r + 16))])
    iota(col("pi", 0), [[0, 1]], 1, False)
    iota(A("iot"), [[1, 272]])
    iota(A("ioq"), [[1, 8], [0, 16]])
    iota(A("ioj"), [[0, 4], [1, 8], [0, 8]])

    p_, q_, k_, kq_, e_, yb_, pk_, pb_, lb_, cs1_, cs2_, ie_, h0_, h1_, cs3_, xb_, h2_, h3_, od_, kh_, kn_, pb0_, eb_, r0_, xe_ = [col("pc", j) for j in range(25)]
    ts(col("pi", 1), col("pi", 0), 4, OP.arith_shift_right)
    ts(col("pi", 2), col("pi", 0), 15, OP.bitwise_and)
    cp(A("pc", 0, 3), A("pi", 0, 3))
    io128 = A("iot", 0, 128)
    ts(ie_, q_, 16.0, OP.mult, p_, OP.add)
    ts(A("IEh"), A("iot"), -16.0, OP.add, ie_, OP.is_equal)

    trade(lambda q: D("SKd", q), lambda q: A("K0", 64 * q, 64 * q + 64), 6300.0, 4300.0)
    ts(A("IDh"), io128, p_, OP.is_equal)
    ts(A("L0"), A("Li"), -2048.0, OP.add, 1.0 / 2048, OP.mult)
    for n, c in (("Iy", 1792 / 2048), ("Iq", -3840 / 2048)):
        ts(A(n), A("IDh"), c, OP.mult)
    lin("Lq", A("Lq"), A("L0"), 4.0, 1029 - 255.5 / 512)
    lin("Ly", A("Ly"), A("L0"), 8.0, 1033 - 127.5 / 256)
    mm([(PS(3, 0, 256), A(m), A(n)) for m, n in (("IDh", "L0"), ("Iy", "Ly"), ("Iq", "Lq"))])
    lin("Ls", A("Ls"), PS(3, 0, 256), 1.0, 1025.0)
    swap(lambda x, p: B("p2", 2 * x, 2 * x + 2, 1, 0, 16, 1, p, p + 32), lambda q: B("Ls", q, 16, 8))
    for y in range(2):
        lin("L0", A("L0", y, 256, 2), B("p2", y, 16, 2))
    trade(lambda q: A("L0", 32 * q, 32 * q + 32), lambda q: A("R0", 32 * q, 32 * q + 32), 4500.0)
    cp(A("R0", 32 * r, 32 * r + 32), A("L0", 32 * r, 32 * r + 32))
    trade(lambda q: D("SVd", q), lambda q: A("V1", 64 * q, 64 * q + 64), 6000.0)
    for n in "KV":
        dma("y", [(A(n + "b", p0=16 * q, p1=16 * q + 16), A({"K": "K0", "V": "V1"}[n], 64 * q, 64 * q + 64)) for q in range(8)])

    fill(A("G", 0, 256), 0.0)
    dma("y", [(A("G", 768 * c, 768 * c + 256), A("G", 0, 256)) for c in range(1, 8)])
    fill(A("KK", 512, 1024), 0.0)
    fill(A("diag", 0, 1024), 0.0)
    dma("y", [(A("diag", c, c + 1024), A("diag", 0, 1024)) for c in (1024, 2048, 3072)] + [(A("KK", 1536, 2048), A("KK", 512, 1024))], 3200.0)
    mine = lambda q: A("diag", 512 * q, 512 * q + 512, p0=16 * q, p1=16 * q + 16)
    for qs in (near, far):
        dma("y", [(mine(q), A("K0", 64 * q, 64 * q + 64)) for q in qs], 2100.0)

    def pick(o, pat, c, base=0, src=None, p1=128):
        src = src or A("G", 0, wide(o), p1=p1)
        rec("g", lambda: g.affine_select(o[0], src[0], pat, OP.not_equal, float(c), base, 1), src[1], o[1], cost=170 + 2 * wide(o))

    def keep(o, src, pat, op, cm):
        rec("g", lambda: g.affine_select(o[0], src[0], pat, op, 0.0, 0, cm), src[1], o[1], cost=170 + 2 * wide(o))

    for j in range(4):
        pick(A("SEL0", 256 * j, 256 * j + 256), [[-1, 2], [0, 8], [-8, 16]], 1, -2 * j)
    pick(A("S16", 0, 8), [[1, 8]], 0, 1)
    pick(A("S16", 8, 264), [[-1, 16], [999, 2], [-16, 8]], -2)
    for j in range(8):
        pick(A("XK", 256 * j, 256 * j + 256), [[-1, 2], [-16, 8], [0, 16]], 1, -2 * j)
    pick(A("Hs", 0, 256), [[-8, 2], [0, 16], [-1, 8]], -1)
    pick(A("Hs", 256, 512), [[-8, 2], [-1, 8], [0, 16]], 1)
    for n, c in (("n64", -64), ("n8k", -8192), ("nI", -1), ("Ia", 1 / 32), ("Ib", -2), ("Ic", 1 / 2048), ("Id", -1 / 32), ("I4", 4), ("n60", -60), ("I112", 112), ("n1008", -1008), ("I896", 896)):
        pick(A(n), [[-1, 128]], c)
    pick(A("PMt"), [[-1, 8], [-8, 16]], 1)
    for n, c in (("Hm", 1), ("nHm", -1)):
        pick(A(n), [[0, 8], [-1, 16]], c, -16 * r)
    pick(A("IE2", 0, 16), [[1, 16]], 0, 1)
    pick(A("IE2", 16, 272), [[-1, 8], [999, 2], [-8, 16]], 1)
    for j, (c0, c1) in enumerate(((-1024, 0), (67584, 65), (56320, 56))):
        o = A("Cz", 128 * j, 128 * j + 128, p1=32)
        pick(o, [[0, 128]], c0, p1=32)
        if c1:
            pick(o, [[0, 128]], c1, -1, o)

    ts(kq_, k_, 8.0, OP.mult, q_, OP.add)
    ts(e_, q_, 16.0, OP.mult, 15.0, OP.add)
    ts(col("pi", 3), col("pi", 0), 3, OP.arith_shift_right, 1, OP.bitwise_and)
    ts(col("pi", 4), col("pi", 0), 16, OP.bitwise_and)
    cp(A("pc", 18, 20), A("pi", 3, 5))
    ts(pk_, kh_, -2.0, OP.mult, 16.0, OP.add)
    ts(kh_, pk_, p_, OP.add)
    ts(r0_, k_, 0.0, OP.is_equal)
    ts(A("PMk"), io128, kh_, OP.is_equal, 2048.0, OP.mult)
    ts(col("pi", 7), col("pi", 0), 1, OP.bitwise_and)
    ts(eb_, col("pi", 7), -7.0, OP.mult, kq_, OP.add)
    ts(eb_, eb_, q_, OP.add)
    ts(A("PMw"), io128, eb_, OP.is_equal, 2048.0, OP.mult)
    for n, c in (("PMh", 448), ("PMy", -1984), ("PMq", 1536)):
        act(A(n), A("PMw"), scale=c / 2048)
    ts(A("mk", 0, 16), A("iot", 0, 16), k_, OP.is_equal)
    ts(A("mk", 16, 24), A("iot", 0, 8), q_, OP.is_equal)
    ts(A("Q8"), A("mk", 16, 24), r0_, OP.mult)
    ts(A("BO"), A("ioq"), q_, OP.is_equal)
    ts(A("EB"), A("iot", 0, 144), e_, OP.is_equal)
    ts(A("PMb"), io128, kq_, OP.is_equal)
    fill(A("ones"), 1.0)
    act(A("m05"), A("ones", 0, 16), AF.Sigmoid, scale=0.0)
    ts(A("sg"), A("iot", 0, 32), 0.0, OP.mult, -0.5, OP.add)
    keep(A("LE"), A("BO"), [[1, 128]], OP.is_ge, -1)
    keep(A("rm"), A("ones", 0, 128), [[0, 8], [1, 16]], OP.not_equal, 0)
    for n, c in (("I512", 512), ("n512", -512)):
        act(A(n), A("IDh"), scale=float(c))
    ts(A("wL"), A("iot", 0, 16), 16.0, OP.mult, k_, OP.add)
    for j, (m, c) in enumerate(((2, 0.5), (2, 256), (2, 256.5), (2, 0.5))):
        ts(A("cL", 24 + 16 * j, 40 + 16 * j), A("wL"), float(m), OP.mult, float(c), OP.add)
    ts(A("cL", 80, 88), A("cL", 80, 88), -256.0, OP.add)
    for y in range(2):
        ts(cs3_, q_, 256.0, OP.mult, 1792.0 * y, OP.add)
        ts(A("cl", 8 * y, 8 * y + 8), A("wL", 8 * y, 8 * y + 8), 2.0, OP.mult, cs3_, OP.add)
    for n, c in (("Mt", -C8 * SC), ("I2k", 2048)):
        act(A(n, 0, 128), A("IDh"), scale=float(c))
    act(A("ISC"), A("IDh"), scale=SC)

    def sloped(o, a, ci):
        act(o, A(a), scale=-C8 * SC)
        pick(o, [[-1, 128]], ci, 0, o)

    sloped(A("Mc"), "LE", (136 + OFF) * SC)

    def mark_constants():
        keep(A("Am"), A("BO"), [[-1, 128]], OP.is_gt, 1)
        keep(A("Us"), A("BO"), [[1, 128]], OP.is_gt, -1)
        sloped(A("Mf"), "Am", SC / 32)
        ts(kn_, k_, -1.0, OP.mult, -1.0, OP.add)
        act(A("nU"), A("IDh"), AF.Identity, scale=kn_)
        act(A("m8I"), A("PMb"), scale=-8.0)
        mm([(PS(3, 0, 128), A(m), A(n)) for m, n in (("IDh", "BO"), ("Ib", "Am"), ("IDh", "nU"))])
        mms([(PS(3, 128, 256), A("Us"), A("m8I"))])
        act(A("Bm", 0, 256), PS(3, 0, 256))

    act(A("ID320"), A("PMt"))
    ts(A("m16"), A("mk", 0, 16), math.exp(LOW) / 8, OP.mult)
    ts(A("thZ", p1=64), A("iot", 0, 128, p1=64), 0.0, OP.mult)
    ts(A("thZ", 16 * r, 16 * r + 16, p1=64), A("thI", p1=64), -1.0, OP.mult)
    ts(yb_, k_, -15.5, OP.add)
    ts(col("pi", 5), col("pi", 0), 120, OP.bitwise_and)
    ts(xb_, col("pi", 5), -1.0, OP.mult, 136.0 + OFF, OP.add)
    ts(col("pi", 6), col("pi", 0), 7, OP.bitwise_and)
    ts(h2_, col("pi", 6), q_, OP.is_equal)
    ts(h3_, od_, 8.0, OP.mult, -16.0, OP.add)
    ts(A("xf"), A("iot", 0, 8), h3_, OP.add, h2_, OP.mult)
    ts(A("xl"), A("xf"), 16.0, OP.add)
    ts(A("d16", 16, 32), A("iot", 0, 16), 0.0, OP.mult)
    ts(A("W16"), A("iot", 0, 48), -16.0, OP.add, k_, OP.is_equal)

    def sort_constants():
        ts(pb_, k_, -float(POW), OP.add, LN64, OP.mult)
        even, odd = (65 * (2048 + 64 * 1025) - 2048) / 2048, -(65 * 1025 + 2048) / 2048
        ts(lb_, od_, odd - even, OP.mult, even, OP.add)
        row0, row1 = h0_, h1_
        ts(row0, p_, 0.0, OP.is_equal)
        ts(row1, p_, 1.0, OP.is_equal)
        ts(cs1_, row1, -2.0, OP.mult)
        ts(cs1_, row0, 8192.0, OP.mult, cs1_, OP.add)
        ts(cs2_, row1, -65.0, OP.mult)
        ts(cs2_, row0, -59392.0, OP.mult, cs2_, OP.add)
        ts(A("Cs"), A("ioj"), cs1_, OP.mult, cs2_, OP.add)
        for a in range(8):
            ts(A("Wt", 8 * a, 8 * a + 8), A("mk", 16, 24), 8.0 ** (POW - 2 * a), OP.mult, 8.0 ** (POW - 2 * a), OP.mult)
        act(B("D2", 0, 32, 1, 8, 16), A("ones"), scale=0.0)

    ROW0 = 1 << 4096
    Tt = (T["Tt"][:, :], [("Tt", 2 * ROW0 - 1, 4096)])

    def spread_K(t):
        dma("y", [((T["Kd"][:, :, q, :], D("Kd")[1]), A("KK", 1024 * (t % 2), 1024 * (t % 2) + 512, p0=16 * q, p1=16 * q + 16)) for q in range(8)])
        dma("y", [(A("Z", 0, 256, p1=16), (T["Kd"][0], D("Kd")[1]))], 2050.0)
        dma("y", [(A("Tt", p0=16 * a + 1, p1=16 * a + 16), (T["Kd"][1:16], D("Kd")[1])) for a in range(8)], LONG)

    def sign_T():
        mm([(B("p0", w // 8, 16, 2, 2 * (w % 8), 2 * (w % 8) + 2, 1, 0, 16), A("S16", 16 * w + 8 - 8 * y, 16 * w + 24 - 8 * y), A("sg", 16 * y, 16 * y + 16))
            for w in range(16) for y in range(2)], each=2)
        tt(A("Z", 256, 512, p1=16), PS(0, 0, 256, p1=16), A("Z", 0, 256, p1=16), OP.mult)
        dma("y", [((T["Tt"][16 * a:16 * a + 1, :], [("Tt", ROW0, 4096)]), A("Z", 256, 512, p1=16)) for a in range(8)], TLAT)

    def first_T(share):
        for q in range(8):
            b = TB[q % len(TB)]
            y, q0 = q % 2, (near + far)[2 * (q // 2)]
            mms([(PS(b, 256 * j + 64 * h, 256 * j + 64 * h + 64), A("SEL0", 128 * (4 * y + h), 128 * (4 * y + h + 1)), A("Tc", 64 * (q0 + j), 64 * (q0 + j + 1)))
                 for j in range(2) for h in range(4)])
            (cp if q in share else act)(A("Tt", 2048 * y + 256 * q0, 2048 * y + 256 * q0 + 512), PS(b))

    def spread_V(t, y):
        j, o = 2 * (t % 2) + y, 4096 * (t % 2) + 2048 * y
        dma("y", [((T["Vd"][j, :, q, :], D("Vd", j)[1]), A("Vp", 256 * y, 256 * y + 256, p0=16 * q, p1=16 * q + 16)) for q in range(8)])
        dma("y", [(A("Vt", o, o + 2048, p0=16 * a, p1=16 * a + 16), D("Vd", j)) for a in range(8)], LONG)

    def first_V():
        dma("y", [(A("V0", p0=16 * a, p1=16 * a + 16), A("V1")) for a in range(8)], VLAT)

    def lists(t):
        mms([(PS(2, 128 * y, 128 * y + 128), view(t, y), A("PMk")) for y in range(2)])
        lin("lu", A("lu", 256 * t, 256 * t + 256), PS(2, 0, 256), 1.0, 2048.0)
        if t % NS == 0:
            lin("Lq", A("Lq"), A("R0"), 1.0, 1026 - 1023.5 / 2048)
            lin("Ly", A("Ly"), A("R0"), 8.0, 1033 - 127.5 / 256)
        lin("Lh", A("Lh"), A("LcB" if t % NS else "R0"), 32.0, 1057 - 31.5 / 64)
        if t < NS:
            terms = (("PMw", "LcB"),) if t else (("PMw", "LcB"), ("PMh", "Lh"), ("PMy", "Ly"), ("PMq", "Lq"))
            mm([(PS(2, 256 + 128 * y, 384 + 128 * y), A(m), view(t, y, n)) for y in range(2) for m, n in terms], each=len(terms))
            lin("lv", A("lv", 256 * t, 256 * t + 256), PS(2, 256, 512), 1.0, 2048.0)

    def cur_lists(t):
        mm([(PS(1, 280, 344), A("IDh"), A("cL", 24, 88))] +
           [(PS(1, 280 + 16 * j, 296 + 16 * j), A(n), A("sg", 0, 32, 2)) for j, n in ((0, "IDh"), (1, "n512"), (2, "I512"), (2, "nI"), (3, "IDh"))])
        cp(A("cl", 88 * t + 24, 88 * t + 88), PS(1, 280, 344))
        if t == NS - 1:
            mm([(PS(1, 280 + 16 * j, 296 + 16 * j), A(m), x) for j, c, n in ((0, 24, "nI"), (1, 72, "Hm"), (2, 24, "nHm"))
                for m, x in (("IDh", A("cL", c, c + 16)), (n, A("sg", 0, 32, 2)))], each=2)
            cp(A("cl", 352, 400), PS(1, 280, 328))

    K2 = lambda t, a=0, b=512, st=1: A("KK", 1024 * (t % 2) + a, 1024 * (t % 2) + b, st)

    def own_K(t):
        act(A("own"), IND(K2(t), A("cl", 88 * t + 24, 88 * t + 40)) if t else IND(Tt, A("cl", 0, 16)))
        for b in range(2 if t else 0):
            dma(DIAG_Q[b], [(B("diag", 8 * b + q, 8 * b + q + 1, p0=16 * q, p1=16 * q + 16 - 15 * b), A("own", p0=16 * q, p1=16 * q + 16 - 15 * b)) for q in range(8)], 2050.0)

    lists(0)
    cur_lists(0)
    for qs in (near, far):
        ts(A("Tc", 64 * qs[0], 64 * qs[-1] + 64), A("K0", 64 * qs[0], 64 * qs[-1] + 64), EPS, OP.max)
    first_T(SHARE_ENDS)
    ts(K2(0), A("Kb"), EPS, OP.max)
    own_K(0)

    def scores(t):
        n0, n1 = 8 * (t == NS), 16 if t else 8
        for c in range(8):
            o, y, a = 768 * c, c // 4, c % 4
            (cp if c in ON_V[t] else act)(A("G", o + 256, o + 768), IND(Tt, lu(t, c)))
            j = lambda u, w: 32 * c + 16 * u + w
            k = lambda u, w: A("Q8") if t == NS else B("diag", 0, n1, 1, j(u, w), j(u, w) + 1) if t else A("diag", 2 * j(u, w), 4096, 512)
            mm([(B(("p0", "p4")[y], 16 * y + n0, 16 * y + n1, 1, w, w + 1, 1, 32 * a, 32 * a + 16 + 16 * u), A("G", o + 512 * (1 - u) + w, o + 768 - 256 * u, 16), k(u, w))
                for w in range(16) for u in (1, 0)], each=2)

    raw, row = (PS(0, 0, 128), PS(4, 256, 384)), (PS(0, 128, 256), PS(4, 384, 512))

    def marks(y, more=1):
        if "fl%d%s" % (y, "" if more else "z") in ON_S:
            act(half("fl", y), row[y], AF.Sigmoid, scale=-256.0 / EPS ** 2)
        else:
            ts(half("fl", y), row[y], 0.0, OP.is_lt)
        if more:
            lin("aS%d" % y, half("aS", y), raw[y], 1.0, -float(OFF))
            if "nb%d" % y in ON_S:
                act(half("nb", y), row[y], AF.Relu, scale=-2.0)
            else:
                ts(half("nb", y), row[y], -2.0, OP.mult, 0.0, OP.max)
        o = half("p2", y) if more else PS(KB[y], 0, 128)
        mms([(o, A("Bm"), half("fl", y))])
        tt(half("tt", y), half("fl", y), o, OP.mult)

    def digits(y, b, o, last=0):
        one = A("ones", 0, 128, p1=32)
        mm([(PS(b, o, o + 128), A("Cz", 256 * last, 256 * last + 128, p1=32), one)] +
           [(PS(b, o, o + 128), A(m), view(1 - last, y, k)) for m, k in [("IDh", "Lh")] + [("I4", "Ly"), ("n60", "Lq")] * last])
        mm([(PS(b, o + 128, o + 256), A("Cz", 128, 256, p1=32), one)] + [(PS(b, o + 128, o + 256), A(m), view(1 - last, y, k)) for m, k in (("I2k", "LcB"), ("n64", "Lh"))])

    def powers(y, o):
        mm([(o, A("Am"), half("fl", y)), (o, A("IDh"), half("tt", y))])
        act(A("pw", 128 * y, 128 * y + 128), o, AF.Sigmoid, bias=pb_, scale=LN64)

    def sort(y, b, o, last=0, dma=0):
        z, sums = 256 * y, PS(b, o, o + 128)
        for h in range(2):
            tt(A("z", z + 128 * h, z + 128 * h + 128), PS(b, o + 128 * h, o + 128 * h + 128), A("pw", 128 * y, 128 * y + 128), OP.mult)
        mm([(sums, A("ones", 0, 128, p1=32), A("Cs", 0, 128, p1=32))], True, False)
        for a in range(8):
            ring = 64 * y + 16 * (a % 4)
            ts(B("R", ring, ring + 16), A("z", z, z + 256), 64.0 ** (2 * a - POW), OP.max, 64.0 ** (2 * a + 2 - POW), OP.min)
            mm([(PS(b, o + 64 * h + 8 * a, o + 64 * h + 8 * a + 8), half("R", h, ring), A("Wt", 8 * a, 8 * a + 8)) for h in range(2)], False, a == 7)
        rows = (16 * y, 16 * y + 16, 1)
        lin("D1", B("D", *rows, 8, 16), sums, 1.0 / 64, 1057 - 31.5 / 64)
        lin("D0", B("D", *rows, 0, 8), sums)
        if "D2" in ON_S and not last:
            lin("D2", B("D2", *rows, 0, 8), sums, 1.0 / 64, 1057 - 31.5 / 64)
        else:
            cp(B("D2", *rows, 0, 8), B("D", *rows, 8, 16))
        out = B("p2", 16 + y, 32, 2) if last else half("p0", y)
        mm([(out, half(d, h, 16 * y), A(k)) for h, d, k in ((0, "D2", "Ib"), (1, "D2", "Id"), (0, "D", "Ia"), (1, "D", "Ic"))])
        if dma:
            lin("Lp", A("Lf", 128 * y, 128 * y + 128), out, 1.0, lb_)
        lin("Lp", B("Lp", y, 16, 2) if last else half("Lp", y), out, 1.0, lb_)

    def spread_views(t):
        if t in BY_DMA:
            for y in range(2):
                dma("y", [(A("VT", 1024 * y, 1024 * y + 1024, p0=16 * a, p1=16 * a + 16), A("Lf", 128 * y, 128 * y + 128)) for a in range(8)], HLAT)
            return
        for j in range(4):
            b = "p%d" % VB[j % len(VB)]
            mms([(B(b, x, 32, 8), A("SEL0" if t else "SEL", 128 * x, 128 * x + 128), A("Lp" if t else "LcB", 64 * j, 64 * j + 64)) for x in range(8)])
            lin(j not in SHARE_VT, A("VT", 512 * j, 512 * j + 512), A(b), 1.0 if t else -0.5)

    def weights(t):
        lin("x16", A("x16"), PS(4, 0, 256), 1.0, xb_)
        for c in range(8):
            b, j, u = WB[c % len(WB)], c // 2, c % 2
            mms([(PS(b, x, 512, 8), A("XK", 128 * (8 * u + x), 128 * (8 * u + x + 1)), B("x16", 4 * j, 4 * j + 4)) for x in range(8)])
            o = 4096 * (t % 2) + 1024 * j
            act(A("E", o + u, o + 1024, 2), PS(b), AF.Sigmoid, bias=-1860.0 / 256 - LOW, scale=1.0 / 256)

    def hand_back(n, src, a, b, y, q="y"):
        s, d = "S" + n + "d", "R" + n + "d"
        dma("y", [(D(s), A(src, a, b))])
        dma("y", [(D(d, r), A(src, a, b, p0=16 * r, p1=16 * r + 16))])
        trade(lambda q: D(s, q), lambda q: D(d, q), 6600.0)
        dma(q, [(y, D(d))])

    def new_V(y, sums, into, place):
        s, back = (128 * y, 128 * y + 128), PS(7, 256 + 128 * y, 384 + 128 * y)
        mms([(back, A(sums, *s), A("ID320"))])
        act(A("As", *s), back, AF.Sigmoid)
        ts(IND(A(into, 256 * y, 256 * y + 256), A("cl", place + 8 * y, place + 8 * y + 8)), A("As", *s), 2.0, OP.mult, -1.0, OP.add)

    def values(t):
        table = A("Vt", 4096 * (t % 2), 4096 * (t % 2) + 4096) if t else A("V0")
        for c in range(8):
            a, y, e = 512 * c, c // 4, 4096 * (t % 2) + 512 * c
            tt(A("Y", a, a + 512), IND(table, A("lv", 256 * t + 32 * c, 256 * t + 32 * c + 32)), A("E", e, e + 512), OP.mult)
            for j in range(2):
                mm([(PS(7, 32 * c + 16 * j, 32 * c + 16 * j + 16), A("Y", a + 256 * j + u, a + 256 * j + 256, 2), A("m16")) for u in range(2)])
            if c % 4 == 3:
                act(A("At", 128 * y, 128 * y + 128), PS(7, 128 * y, 128 * y + 128))
                if t < NS - 1:
                    new_V(y, "At", "Vp", 88 * t + 72)
                    spread_V(t + 1, y)
                else:
                    piece = lambda n, q, y=y: A(n, 128 * y + 16 * q, 128 * y + 16 * q + 16)
                    trade(lambda q: piece("At", q), lambda q: piece("Ah", q))
                    act(piece("Ah", r), piece("At", r))
        for y in range(2 if t == NS - 1 else 0):
            new_V(y, "Ah", "Vf", 368)
            dma("y", [((T["yv"][:, 256 * y:256 * y + 256], []), A("Vf", 256 * y, 256 * y + 256))])
        if t == NS - 2:
            act(A("Vo", 0, 256), IND(A("Vp"), A("cl", 352, 368)))
            hand_back("v", "Vo", 0, 256, A("Vo", 256, 512))
            cp(IND(A("Vf"), A("cl", 384, 400)), A("Vo", 256, 512))

    si = lambda j: A("si", 16 * j, 16 * j + 16)
    lu = lambda t, c: A("lu", 256 * t + 32 * c, 256 * t + 32 * c + 32)
    for t in range(NS):
        step[0] = t
        scores(t)
        if t == 0:
            lin(True, A("Vp"), A("Vb"))
            first_V()
            dma("y", [(mine(q), A("KK", 1536, 2048, p0=16 * q, p1=16 * q + 16)) for q in range(8)], 2100.0)
        else:
            for y in range(2):
                on("L", digits, y, 3, 256 * y)
        for h in range(2):
            b, s = KB[h], (128 * h, 128 * h + 128)
            key = PS(b, 0, 128)
            mm([(PS(b, 128, 256), A("ones", 0, 128), A("I2k")), (PS(b, 128, 256), view(t, h), A("I2k"))])
            mms([(PS(b, 256, 384), A("IDh"), A("own", *s))])
            mm([(key, A("ones", 0, 128), A("Mc"))], True, False)
            if t:
                marks(h)
                mm([(key, half("fl", h), A("Mf"))], False, False)
            else:
                lin(h == 1, half("aS", h), raw[h], 1.0, -float(OFF))
            mm([(key, half(n, h), A("ISC")) for n in ("aS", "nb")[:2 if t else 1]], False, t == 0)
            if t:
                mm([(key, half("tt", h), A("Mt"))], False, True)
            scan(A("Mx", *s), A("rm"), key, OP.mult, OP.max)
            tt(A("us", *s), A("Mx", *s), key, OP.subtract)
            tt(A("d1", *s), PS(b, 128, 256), A("us", *s), OP.subtract)
            scan(A("Bx", *s), A("us", *s), A("d1", *s), OP.min, OP.max)
            cp(A("bl", 8 * h, 8 * h + 8), A("Bx", s[0] + 15, s[1], 16))
            act(A("gkB", *s), IND(Tt, A("bl", 8 * h, 8 * h + 8)), AF.Abs)
            tt(K2(t, 512 + 2 * s[0], 512 + 2 * s[1], 2), PS(b, 256, 384), A("gkB", *s), OP.max)
            if t:
                on("L", powers, h, half("p0", h, 16))
        mm([(PS(4, 0, 256), A(m), A(n)) for m, n in (("PMb", "aS"), ("PMb", "nb"), ("m8A", "fl"), ("m8I", "tt"))[:4 if t else 1]], True, False)
        line[0] = "V"
        ts(si(3), A("Mx", 15, 256, 16), 1 / SC, OP.mult, 0.46, OP.add)
        ts(A("MR", 0, 16), si(3), -1860.0, OP.add)
        mms([(PS(2, 256, 384, p1=16), A("MR", 0, 16), A("IDh"))])
        lin("MTs", A("MTs", 0, 128, p1=16), PS(2, 256, 384, p1=16))
        mm([(PS(4, 128 * y, 128 * y + 128), A("Hs", 128 * y, 128 * y + 128, p1=16), A("MTs", 0, 128, p1=16)) for y in range(2)], False, True)
        weights(t)
        line[0] = "K"
        bs = A("Bx", 15, 256, 16)
        mm([(PS(1, 384, 400), A("thZ", p1=64), A("IDh", 16 * t, 16 * t + 16, p1=64))] +
           [(PS(1, 384, 400), A("EB", 15 - b, 143 - b), K2(t, 512 + 2 * b, 1024, 32)) for b in range(16)])
        rc = "rc%d" % t
        lin("rc", A(rc, 16 * r, 16 * r + 16), PS(1, 384, 400))
        trade(lambda q: A(rc, 16 * r, 16 * r + 16), lambda q: A(rc, 16 * q, 16 * q + 16), 4800.0, 3000.0)
        line[0] = "L"
        ts(si(0), A("Mx", 15, 256, 16), 32 / SC, OP.mult, 30.0, OP.add)
        ts(si(7), bs, 0.5, OP.mult, -0.25, OP.add)
        ts(si(4), si(7), 7, OP.arith_shift_right, 7, OP.bitwise_and)
        ts(si(5), si(0), 31, OP.bitwise_and)
        ts(si(6), si(0), 1, OP.bitwise_and)
        ts(A("MR", 16, 32), si(4), q_, OP.is_equal)
        mr = lambda j: A("MR", 16 * j - 48, 16 * j - 32)
        if t in BY_DMA:
            for j, bit in ((8, 4), (9, 7), (10, 10)):
                ts(si(j), si(7), bit, OP.arith_shift_right)
            cp(A("MR", 32, 128), A("si", 80, 176))
            mm([(PS(1, 432, 448), A(m), mr(j)) for m, j in (("IDh", 7), ("I112", 8), ("n1008", 9), ("I896", 10))])
            act(A("d16", 0, 16), PS(1, 432, 448))
        else:
            cp(A("MR", 32, 64), A("si", 80, 112))
            cp(A("d16", 0, 16), si(7))
        mm([(PS(1, 256, 384, p1=16), x, A(m)) for x, m in ((mr(5), "IDh"), (mr(6), "n64"), (mr(4), "n64"))])
        lin("MTs", A("MTs", 128, 256, p1=16), PS(1, 256, 384, p1=16))
        mms([(half("p2", y), A("Hs", 256 + 128 * y, 384 + 128 * y, p1=16), A("MTs", 128, 256, p1=16)) for y in range(2)])
        act(A("sS"), PS(2, 0, 256), AF.Sign, bias=yb_, scale=0.5)
        (act if "dx" in ON_S else cp)(A("dx"), IND(A("d16"), A("xl")))
        mm([(A("p2", 256, 272, 1, 32 * a, 32 * a + 32), A("W16", 16 - 16 * u, 48 - 16 * u), A("dx", 32 * a + 16 * u, 32 * a + 16 * u + 16)) for a in range(4) for u in range(2)], each=2)
        cp(A("dl"), PS(2, 256, 272))
        if t > 0:
            for y in range(2):
                sort(y, 3, 256 * y, 0, t in BY_DMA)
        elif t in BY_DMA:
            mms([(PS(3, 128 * y, 128 * y + 128), A("PMb"), view(t, y)) for y in range(2)])
            lin("Lp", A("Lf"), PS(3, 0, 256))
        line[0] = "K"
        for e in range(2):
            act(K2(t + 1, e, 512, 2), IND(K2(t, 0, 1024), A("cl", 88 * t + 40 + 16 * e, 88 * t + 56 + 16 * e)))
        if t < NS - 1:
            spread_K(t + 1)
        line[0] = "L"
        if t == NS - 1:
            if "Ko" in ON_S:
                act(A("Ko"), K2(NS), AF.Relu, bias=-2 * EPS)
            else:
                ts(A("Ko"), K2(NS), -2 * EPS, OP.add, 0.0, OP.max)
            hand_back("k", "Ko", 0, 512, (T["yk"][:, :], []), "g")
        spread_views(t)
        mm([(PS(2, 256, 512), A("nI"), A("ones")), (PS(2, 256, 512), A("nI"), A("sS"))], True, False)
        mm([(PS(2, 256, 512), A("PMt"), A("Lp"))] if t else [(PS(2, 256 + 128 * y, 384 + 128 * y), A("IDh"), view(t, y)) for y in range(2)], False, True)
        tt(A("ga"), IND(A("VT"), A("dl")), A("sS"), OP.min)
        if t < NS - 1:
            tt(A("LcB"), PS(2, 256, 512), A("ga"), OP.max)
        if t == 0:
            mark_constants()
            sort_constants()
        if t == NS - 1:
            for y in range(2):
                tt(A("Ls", y, 256, 2), PS(2, 256 + 128 * y, 384 + 128 * y), A("ga", 128 * y, 128 * y + 128), OP.max)
            trade(lambda q: A("Ls", 32 * q, 32 * q + 32), lambda q: A("R0", 32 * q, 32 * q + 32))
            cp(A("R0", 32 * r, 32 * r + 32), A("Ls", 32 * r, 32 * r + 32))
        lists(t + 1)
        line[0] = "K"
        mm([(PS(1, 400, 432), A("n8k"), A("sg")), (PS(1, 401, 432, 2), A("n8k"), A("sg", 0, 32, 2)), (PS(1, 400, 432, 2), A("n8k"), A("m05"))], True, False)
        for hs in (near, far):
            mm([(PS(1, 400 + e, 432, 2), A("nI"), A(rc, 16 * h, 16 * h + 16)) for e in range(2) for h in hs], False, hs == far)
        ts(A("sg"), PS(1, 400, 432), 0.5, OP.is_lt, -0.5, OP.add)
        sign_T()
        if t < NS - 1:
            cur_lists(t + 1)
            own_K(t + 1)
        on("V", values, t)

    step[0] = NS
    scores(NS)
    for y in range(2):
        digits(y, SB[y], 0, 1)
        marks(y, 0)
        powers(y, PS(KB[y], 256, 384))
    for y in range(2):
        sort(y, SB[y], 0, 1)
    swap(lambda x, p: B("p2", x, 16, 8, 0, 16, 1, p, p + 32), lambda q: A("Lp", 32 * q, 32 * q + 32), "IE2")
    lin("Lo", A("Lo"), PS(2, 0, 256), 2048.0, 2048.0)
    dma("s", [((T["yl"][:, :], []), A("Lo"))])
    emit(g, T, QU, ops, sent[0])


def arrange(ops):
    n, WAKE = len(ops), WAKES[0]
    other = [[o["other"][j] for o in ops] for j in range(2)]
    cost, lat, hold = [o["cost"] for o in ops], [o["lat"] for o in ops], [o["hold"] for o in ops]
    queue = [("pe", "v", "s", "g", "y", None).index(o["q"]) for o in ops]
    hard, soft, behind = [], [], []
    for o in ops:
        seen = 0
        for d in o["deps"] | o["order"]:
            seen |= behind[d]
        hard.append([d for d in sorted(o["deps"]) if not seen >> d & 1])
        soft.append([d for d in sorted(o["order"] - o["deps"]) if not seen >> d & 1])
        behind.append(seen | bits(o["deps"]))
    both = [h + s for h, s in zip(hard, soft)]
    after = [[] for o in ops]
    for i in range(n):
        for d in hard[i]:
            after[d].append((i, True))
        for d in soft[i]:
            after[d].append((i, False))

    def fit(st, en, t, c):
        j = m = len(st)
        while j and en[j - 1] > t:
            j -= 1
        while j < m and t + c > st[j]:
            if en[j] > t:
                t = en[j]
            j += 1
        st.insert(j, t)
        en.insert(j, t + c)
        return t

    def order(key):
        key = list(key)
        for i in range(n):
            k = key[i]
            for d in both[i]:
                if key[d] >= k:
                    k = key[d] + 1e-3
            key[i] = k
        return [j for k, j in sorted(zip(key, range(n)))]

    def forth(key):
        st, en, at, end = [[] for q in range(7)], [[] for q in range(7)], [0.0] * n, [0.0] * n
        for i in order(key):
            t = 0.0
            for d in hard[i]:
                x = end[d] + WAKE
                if x > t:
                    t = x
            for d in soft[i]:
                x = at[d] + cost[d]
                if x > t:
                    t = x
            q, c = queue[i], cost[i]
            if q < 5:
                s, e = st[q], en[q]
                if e and e[-1] > t:
                    t = fit(s, e, t, c)
                else:
                    s.append(t)
                    e.append(t + c)
            at[i] = t
            if hold[i]:
                q = 5 if q == 5 else 6
                end[i] = fit(st[q], en[q], t + c + 1400, hold[i]) + hold[i] + 600
            else:
                end[i] = t + c + lat[i]
        return max(end) + 1e-2 * sum(end) / n, at, end

    def back(at, end):
        st, en, lead = [[] for q in range(5)], [[] for q in range(5)], [0.0] * n
        for i in order(end)[::-1]:
            w = end[i] - at[i] - cost[i]
            t = 0.0 if after[i] else w
            for d, h in after[i]:
                x = lead[d] + (w + WAKE if h else 0.0)
                if x > t:
                    t = x
            if queue[i] < 5:
                t = fit(st[queue[i]], en[queue[i]], t, cost[i])
            lead[i] = t + cost[i]
        return [-x for x in lead]

    def lean(now, key, tries, kinds):
        best = now
        for it in range(tries):
            p = list(key if kinds else now[1])
            i = int(rng.integers(0, n))
            x, how = float(rng.normal()) * STEP * (1.0, 0.3)[it % 2], int(rng.integers(0, 4))
            if it % 8 == 4:
                for j in line[ops[i]["line"]]:
                    if how < 2 or seat[j][0] == seat[i][0]:
                        p[j] += x
            elif kinds:
                t, k = seat[i]
                for j in kin[ops[i]["tag"]]:
                    if how == 0 or (seat[j][1] >= k, seat[j][1] <= k, seat[j][1] == k)[how - 1]:
                        p[j] += x
            else:
                for j in kin[ops[i]["tag"]]:
                    if abs(j - i) <= (0, 8, 30, 60)[how]:
                        p[j] += x
            new = forth(p)
            if not kinds and it % 10 == 0:
                new = min(new, forth(back(new[1], new[2])), key=lambda z: z[0])
            room = SLACK * (1 - it / tries) * float(rng.exponential())
            if new[0] <= now[0] + room:
                now, key = new, p
                if new[0] < best[0]:
                    best = new
        return best

    seats = [(1 << q if q < 5 else 0) | (1 << 6 + (q != 5) if h else 0) for q, h in zip(queue, hold)]
    reach = [0] * n

    def spot(seq):
        for k, i in enumerate(seq):
            for d in both[i]:
                reach[d] = k

    def play(seq, j, p=0, old=None, stop=n):
        c_, f, wake = costs[j], LATE[j], WAKES[j]
        free, last = [0.0] * 8, [-1] * 8
        at, end, why = ([0.0] * n, [0.0] * n, [-1] * n) if old is None else (old[3][:], old[4][:], old[1][:])
        todo = {0, 1, 2, 3, 4, 6, 7}
        for k in range(p - 1, -1, -1):
            i = seq[k]
            q = queue[i]
            if q in todo:
                todo.remove(q)
                free[q], last[q] = at[i] + c_[i], i
            if hold[i] and 6 + (q != 5) in todo:
                todo.remove(6 + (q != 5))
                free[6 + (q != 5)], last[6 + (q != 5)] = end[i] - 600 * f, i
            if not todo:
                break
        odd, owed = 0, 0
        for k in range(p, n):
            i = seq[k]
            q, c = queue[i], c_[i]
            t, w = free[q], -2 - last[q]
            for d in hard[i]:
                x = end[d] + wake
                if x > t:
                    t, w = x, d
            for d in soft[i]:
                x = at[d] + c_[d]
                if x > t:
                    t, w = x, d
            if q < 5:
                free[q], last[q] = t + c, i
            if hold[i]:
                q = 6 + (q != 5)
                x = t + c + 1400 * f
                if free[q] > x:
                    x, w = free[q], -2 - last[q]
                free[q], last[q] = x + hold[i] * f, i
                e = free[q] + 600 * f
            else:
                e = t + c + lat[i] * f
            why[i] = w
            if t != at[i] or e != end[i]:
                at[i], end[i] = t, e
                odd |= seats[i]
                if reach[i] > owed:
                    owed = reach[i]
            elif k <= stop:
                odd |= seats[i]
            else:
                odd &= ~seats[i]
                if not odd and k >= owed:
                    break
        m = max(end)
        return m + 3e-3 * sum(end) / n, why, end.index(m), at, end

    def blocked(run):
        out, i = [], run[2]
        while i != -1:
            w = run[1][i]
            if w < -1:
                w = -2 - w
                if not needs[i] >> w & 1:
                    out.append((w, i))
            i = w
        return out

    def polish(seq, tries):
        now = [play(seq, j) for j in range(len(costs))]
        spot(seq)
        val = sum(w * x[0] for w, x in zip(weight, now))
        best, pairs, cum = (val, seq, now), [blocked(x) for x in now], np.cumsum(weight) / sum(weight)
        for it in range(tries):
            j = int(np.searchsorted(cum, rng.random()))
            if not pairs[j]:
                continue
            a, b = pairs[j][int(rng.integers(len(pairs[j])))]
            pa, pb, more = seq.index(a), seq.index(b), int(rng.integers(0, 3))
            if rng.random() < 0.5:
                while more and pa > 0 and not needs[b] >> seq[pa - 1] & (queue[seq[pa - 1]] == queue[b]):
                    pa -= 1
                    more -= queue[seq[pa]] == queue[b]
                first = [x for x in seq[pa:pb + 1] if x == b or needs[b] >> x & 1]
            else:
                while more and pb < n - 1 and not needs[seq[pb + 1]] >> a & (queue[seq[pb + 1]] == queue[a]):
                    pb += 1
                    more -= queue[seq[pb]] == queue[a]
                first = [x for x in seq[pa:pb + 1] if x != a and not needs[x] >> a & 1]
            moved = set(first)
            new = seq[:pa] + first + [x for x in seq[pa:pb + 1] if x not in moved] + seq[pb + 1:]
            room = SLACK * (1 - it / tries) * float(rng.exponential())
            one = play(new, j, pa, now[j], pb)
            if weight[j] * (one[0] - now[j][0]) > room + 400:
                continue
            runs = [one if k == j else play(new, k, pa, now[k], pb) for k in range(len(costs))]
            v = sum(w * x[0] for w, x in zip(weight, runs))
            if v <= val + room:
                seq, now, val, pairs = new, runs, v, [blocked(x) for x in runs]
                spot(seq)
                if v < best[0]:
                    best = (v, seq, now)
        return best

    if n not in KEPT:
        costs, weight, needs = [cost] + other, WEIGHTS, []
        for o in ops:
            m = bits(o["deps"] | o["order"])
            for d in o["deps"] | o["order"]:
                m |= needs[d]
            needs.append(m)
        rng = np.random.default_rng(SEED)
        kin, line, seat, met, ranks = {}, {}, [], {}, []
        for i in range(n):
            kin.setdefault(ops[i]["tag"], []).append(i)
            line.setdefault(ops[i]["line"], []).append(i)
        for x in (1.0, 1.25, 1.5, 1.75, 2.0, 2.5):
            for y in (1.0, 1.25, 1.5, 2.0):
                rank = [0.0] * n
                for i in range(n - 1, -1, -1):
                    rank[i] = -cost[i] * {"V": x, "L": y}.get(ops[i]["line"], 1.0) - lat[i] + min([rank[d] - WAKE for d, h in after[i]], default=0.0)
                ranks.append((forth(rank)[0], rank))
        ranks.sort()
        for o in ops:
            met[o["step"], o["tag"]] = met.get((o["step"], o["tag"]), -1) + 1
            seat.append((o["step"], met[o["step"], o["tag"]]))
        best = [lean(lean(forth(rank), rank, FIRST, True), None, FIRST, False) for _, rank in ranks[:STARTS]]
        best = min([polish(order(z[1]), MORE) for z in best], key=lambda z: z[0])
        best = polish(best[1], TRIES)
        KEPT[n] = best[1]
        KEPT["times"] = (best[0], best[2][0][3], best[2][0][4], best[2][0][0], [x[0] for x in best[2][1:]], best[2][0][1])
    seq = KEPT[n]
    place = {j: k for k, j in enumerate(seq)}
    for j, o in enumerate(ops):
        assert all(place[d] < place[j] for d in o["deps"] | o["order"])
        o["deps"] = {place[d] for d in o["deps"]}
    return [ops[j] for j in seq]


def emit(g, T, QU, ops, sent):
    ops = arrange(ops)
    clock = {q: {} for q in QU}
    marked = set()
    for i, o in enumerate(ops):
        o["waits"], o["snap"] = [], {}
        if o["q"] is None:
            continue
        ck = clock[o["q"]]
        for d in sorted(o["deps"], reverse=True):
            key = ops[d]["sem"] or ops[d]["q"]
            if ck.get(key, -1) >= d:
                continue
            o["waits"].append(d)
            marked.add(d)
            for k2, v2 in ops[d]["snap"].items():
                ck[k2] = max(ck.get(k2, -1), v2)
            ck[key] = d
        o["snap"] = dict(ck)
    last = {}
    for i, o in enumerate(ops):
        if o["sem"] is None:
            last[o["q"]] = i
    marked |= set(last.values())
    count, done = {}, {}
    for i, o in enumerate(ops):
        for d in o["waits"]:
            s = ops[d]["sem"] or ops[d]["q"]
            QU[o["q"]].wait_ge(T.sem[s], ops[d]["n"])
            done[s] = max(done.get(s, 0), ops[d]["n"])
        h = o["fn"]() if o["fn"] else None
        if o["sem"] is None:
            if i in marked:
                count[o["q"]] = o["n"] = count.get(o["q"], 0) + 1
                h.then_inc(T.sem[o["q"]], 1)
        elif o["sem"] != "-":
            count[o["sem"]] = o["n"]
    count["sent"] = sent
    for s, n in count.items():
        if done.get(s, 0) < n:
            g.wait_ge(T.sem[s], n)
